import numpy as np, ml_dtypes
CORES = [35,38,43,46]
N = 4
BF = ml_dtypes.bfloat16
D, T, L, RO, CM, SH = 4096, 1024, 3, 5, 255, 12
def at(c, p):
    return c.reshape(-1)[np.arange(N * 8).reshape((N, 8) + (1,) * (p.ndim - 2)) * D + p]
def grow(rng, c, p):
    e = at(c, p); u = rng.random(p.shape)
    e = np.where(u < 0.06, e + rng.integers(1, RO, p.shape), e)
    return np.where(u > 0.97, rng.integers(0, CM + 1, p.shape), e)
def parts(rng):
    c = rng.integers(0, CM - RO + 1, (N, 8, D)); p = rng.integers(0, D, (N, 8, 16, D)); hot = rng.integers(0, D, (N, 8, 32))
    for n in range(N):
        for g in range(8): p[n, g] = np.where(rng.random((16, D)) < 0.03, hot[n, g][rng.integers(0, 32, (16, D))], p[n, g])
    return c, p, rng.integers(0, 16, (N, 8, 16, D)), rng.integers(0, 16, (N, 8, 16, T))
def pack(k, x, c, z):
    return {"nkey": np.ascontiguousarray(k.reshape(N, 128, D)).astype(np.float32), "xreg": np.ascontiguousarray(x.reshape(N, 128, D)).astype(np.float32).astype(BF),
            "cnt": np.ascontiguousarray(c).astype(np.int32), "zin": np.ascontiguousarray(z.reshape(N, 128, T)).astype(np.float32).astype(BF)}
def setup_inputs(rng):
    c, p, x, z = parts(rng)
    return pack(np.where(rng.random(p.shape) < 0.04, -1, p + D * grow(rng, c, p)), x, c, z)
def setup_inputs_calm(rng):
    c, p, x, z = parts(rng)
    base = (np.arange(N)[:, None, None] + np.arange(8)[None, :, None]) & 3
    c = np.where(rng.random(c.shape) < 0.8, base, rng.integers(0, 4, c.shape))
    e = at(c, p); e = np.maximum(np.where(rng.random(p.shape) < 0.75, e, e + rng.integers(-3, 4, p.shape)), 0)
    return pack(np.where(rng.random(p.shape) < 0.02, -1, p + D * e), x, c, z)
def setup_inputs_corners(rng):
    c, p, x, z = parts(rng); k = np.where(rng.random(p.shape) < 0.04, -1, p + D * grow(rng, c, p)); col = np.arange(D); r16 = np.arange(16)[:, None]
    who = rng.permutation(N)
    for n in range(N):
        kinds = rng.permutation(8)
        for g in range(8):
            m = int(kinds[g]); w = c[n, g]
            if n == who[0]:
                if m < 4: k[n, g] = -1
                else:
                    q = p[n, g]; k[n, g] = np.where(rng.random((16, D)) < 0.1, -1, q + D * ((w[q] + rng.integers(1, CM + 1, (16, D))) & CM))
            elif n == who[1]:
                q = (col + (D >> 2) * ((r16 & 3) if m > 2 else 0 * r16)) & (D - 1); k[n, g] = q + D * w[q]
            elif m == 0: k[n, g] = col + D * (w[col] + (r16 >= 12))
            elif m == 1:
                q = (5 * col + int(rng.integers(0, D))) & (D - 1); k[n, g] = (q + D * w[q])[None, :]
            elif m == 2:
                k[n, g] = -1; k[n, g, :, T - 1] = T - 1 + D * w[T - 1]
            elif m == 3:
                q = np.array([0, 1, T - 1, T, D - 1])[rng.integers(0, 5, (16, D))]; k[n, g] = q + D * (w[q] + rng.integers(0, 3, (16, D)))
            elif m == 4:
                w = (CM - RO) * rng.integers(0, 2, D); c[n, g] = w; q = p[n, g]
                k[n, g] = q + D * np.maximum(w[q] + np.where(rng.random((16, D)) < 0.75, 0, rng.integers(-1, 2, (16, D))), 0)
            elif m == 5: k[n, g] = np.where((rng.random(D) < 0.5)[None, :], -1, k[n, g])
            elif m == 6:
                q = col ^ 1; k[n, g] = q + D * (w[q] + (r16 >= 13))
            else: z[n, g] = rng.integers(0, 16, (1, T)) + np.zeros((16, 1), np.int64)
    return pack(k, x, c, z)
def setup_inputs_crowd(rng):
    c, p, x, z = parts(rng); k = np.where(rng.random(p.shape) < 0.04, -1, p + D * grow(rng, c, p)); r16 = np.arange(16)
    for n in range(N):
        kinds = rng.permutation(8)
        for g in range(8):
            m = int(kinds[g]); w = c[n, g]
            if m > 5: continue
            h = T + rng.permutation(D - T)[:L + 7]; dd = h[L - 1:L + 3]; odd = int(rng.choice(np.array([0, T - 1])))
            k[n, g, :, :T] = h[0] + D * w[h[0]]
            for j in range(L - 2): k[n, g, :, h[j]] = h[j + 1] + D * w[h[j + 1]]
            to = dd[r16 & 3] if m == 2 else np.full(16, h[0] if m == 5 else dd[0])
            k[n, g, :, h[L - 2]] = to + D * (w[to] + ((r16 & 3) if m == 3 else 0))
            if m == 1: k[n, g, :, odd] = -1
            if m == 4: k[n, g, :, odd] = odd + D * w[odd]
    return pack(k, x, c, z)
def setup_inputs_ends(rng):
    F = D >> 4; M = 4; top = D * (CM + 1) - 1; last = np.arange(16) * F + F - 1
    c = (CM - RO) * rng.integers(0, 2, (N, 8, D)); x = 15 * rng.integers(0, 2, (N, 8, 16, D)); z = 15 * rng.integers(0, 2, (N, 8, 16, T))
    m = rng.integers(0, 3, (N, 8, 16, F)); m[:, :, 6:, F - 1] = 1; m[:, :, 6::2, 0] = 0; m[:, :, 7::2, 0] = 1
    m = np.tile(m, (1, 1, 1, 16)); k = np.where((m == 1) | ((m == 2) & (rng.random(m.shape) < 0.5)), top, -1)
    ti = np.concatenate([np.array([T - 1, 0]), 1 + rng.permutation(T - 2)[:M * RO - 2]]).reshape(M, RO); z[:, :, :, ti.reshape(-1)] = 0
    for n in range(N):
        for g in range(8):
            quiet = (n == N - 1 and g == 7) or (n + g) % 3 == 0
            cand = T + rng.permutation(D - T); cand = cand[(cand & (F - 1)) != F - 1][:M * (RO * (L - 1) + 1)]
            dd = cand[:M].copy(); nodes = cand[M:].reshape(M, RO, L - 1)
            if not quiet: dd[0] = D - 1
            c[n, g, dd] = (CM - RO) * ((np.arange(M) + g) & 1); x[n, g, :, dd] = 0
            tb = np.ones(D, bool); tb[cand] = False; tb[dd] = False; tb[ti.reshape(-1)] = False; tb[D - 1] = False
            if quiet:
                tb[last] = False; x[n, g, :, last] = 15
            lv = np.flatnonzero(tb)
            for s in (0, 15):
                q = np.where(rng.random(D) < 0.05, lv[rng.integers(0, 4, D)], lv[rng.integers(0, len(lv), D)])
                live = q + D * (c[n, g][q] + (rng.random(D) < 0.1)); k[n, g, s] = np.where(rng.random(D) < 0.1, k[n, g, s], live)
            if quiet: k[n, g, 15, last] = top
            for j in range(M):
                for t in range(RO):
                    v = ti[j, t]
                    for a in nodes[j, t]:
                        k[n, g, 0, v] = a + D * c[n, g, a]; v = a
                    k[n, g, 0, v] = dd[j] + D * (c[n, g, dd[j]] + t)
    return pack(k, x, c, z)
def setup_inputs_spread(rng):
    pw = rng.choice(np.array([0.3, 1.0, 4.0]), (N, 8, 1)); c = np.minimum(((CM - RO + 1) * rng.random((N, 8, D)) ** pw).astype(np.int64), CM - RO)
    pw = rng.choice(np.array([0.6, 1.0, 1.7]), (N, 8, 1, 1)); p = np.minimum((D * rng.random((N, 8, 16, D)) ** pw).astype(np.int64), D - 1)
    x = np.minimum((16 * rng.random((N, 8, 16, D)) ** rng.choice(np.array([0.4, 1.0, 2.5]), (N, 8, 1, D))).astype(np.int64), 15)
    z = np.minimum((16 * rng.random((N, 8, 16, T)) ** rng.choice(np.array([0.4, 1.0, 2.5]), (N, 8, 1, T))).astype(np.int64), 15)
    return pack(np.where(rng.random(p.shape) < 0.03, -1, p + D * grow(rng, c, p)), x, c, z)
def check_inputs(d):
    bad = []
    for k, lo, hi in (("nkey", -1, D * (CM + 1) - 1), ("xreg", 0, 15), ("cnt", 0, CM - RO), ("zin", 0, 15)):
        a = np.asarray(d[k]).astype(np.float64)
        if not (np.min(a) >= lo and np.max(a) <= hi): bad.append("range of " + k)
        elif np.any(a != np.floor(a)): bad.append("whole numbers in " + k)
    return bad
def reference(nkey, xreg, cnt, zin):
    K = nkey.astype(np.int64).reshape(N, 8, 16, D); X = xreg.astype(np.float32).astype(np.int64).reshape(N, 8, 16, D)
    C = cnt.astype(np.int64); Z = zin.astype(np.float32).astype(np.int64).reshape(N, 8, 16, T)
    for t in range(RO):
        if t > 0: Z = np.roll(Z, (1, t), axis=(0, 1))
        for q in range(N):
            for h in range(8):
                k, x, c, z = K[q, h], X[q, h], C[q, h], Z[q, h]
                v = np.arange(T); ok = np.ones(T, bool); key = None
                for m in range(L):
                    s = z[L * t + m].copy(); back = key
                    key = k[s, v]; v = key & (D - 1)
                    ok = ok & (key >= 0) & ((key >> SH) == c[v])
                w = np.flatnonzero(ok); d = v[w]
                u, first = np.unique(d, return_index=True); win = w[first]
                left = z[:, win]
                z[:, w] = x[:, d]
                x[:, u] = left
                c[u] += 1
                k[s[win], u] = back[win]
                k[t, w] = d + D * c[d]
    return {"yz": Z.reshape(N, 128, T).astype(np.float32).astype(BF), "yk": np.add.reduce(K.reshape(N, 128, 16, D >> 4), axis=2).astype(np.float32),
            "yx": np.add.reduce(X.reshape(N, 128, 16, D >> 4), axis=2).astype(np.float32).astype(BF), "yc": C.astype(np.float32)}

@@ -1,0 +1,542 @@
+from concourse.mybir import AluOpType as A, ActivationFunctionType as F
+
+D, TH, RO = 4096, 1024, 5
+BIG = float(1 << 21)
+KW = D + 64
+NR = TH // 64
+CUT = (0, 16, 24, 32)
+
+f32, bf, i32, u16, f16 = "float32", "bfloat16", "int32", "uint16", "float16"
+SCRATCH = {
+    "K": ("sbuf", [128, KW], f32), "XW": ("sbuf", [128, KW + TH], f32), "xb": ("sbuf", [128, D], bf),
+    "ci": ("sbuf", [128, 256], i32), "cj": ("sbuf", [128, 512], i32), "ch": ("sbuf", [128, 512], f16),
+    "Ga": ("sbuf", [128, TH], f32), "Gb": ("sbuf", [128, TH], f32), "Ab": ("sbuf", [128, TH], f32), "Bb": ("sbuf", [128, TH], f32),
+    "X1": ("sbuf", [128, TH], bf), "X2": ("sbuf", [128, TH], bf), "Cg0": ("sbuf", [128, TH], bf), "Cg1": ("sbuf", [128, TH], bf),
+    "Cg2": ("sbuf", [128, TH], bf), "eq": ("sbuf", [128, 2048], bf), "sq": ("sbuf", [128, TH], bf), "hi": ("sbuf", [128, TH], bf),
+    "T3": ("sbuf", [128, 256], f32), "ki": ("sbuf", [128, 192], i32), "pl": ("sbuf", [128, 192], i32),
+    "off": ("sbuf", [128, 192], u16), "cn": ("sbuf", [128, 192], i32), "tg": ("sbuf", [128, 192], f32),
+    "w": ("sbuf", [128, 8, 64], f32), "e01": ("sbuf", [128, 128], f32), "P12": ("sbuf", [128, 128], f16),
+    "Q": ("sbuf", [128, 64], f16), "Sx": ("sbuf", [128, 64], f16), "nok": ("sbuf", [128, 64], bf),
+    "nd": ("sbuf", [128, 64], bf), "xoff": ("sbuf", [128, 64], u16), "soff": ("sbuf", [128, 64], u16),
+    "oz": ("sbuf", [128, TH], bf), "okk": ("sbuf", [128, 512], f32), "ox": ("sbuf", [128, 256], bf), "oc": ("sbuf", [128, 512], f32),
+    "pi": ("sbuf", [128, 48], i32), "pj": ("sbuf", [128, 64], i32), "pc": ("sbuf", [128, 256], f32),
+    "n256": ("sbuf", [128, 256], bf), "io2": ("sbuf", [128, 512], bf),
+    "Sel": ("sbuf", [128, 32], f32), "Mq": ("sbuf", [128, 128], f32), "Rb": ("sbuf", [128, 32], f32), "BO": ("sbuf", [128, 128], f32),
+    "Y": ("sbuf", [128, 144], bf), "Z": ("sbuf", [128, 16, 160], f16), "SQ": ("sbuf", [128, RO, 64], bf),
+    "WB": ("sbuf", [128, 256], bf), "MK": ("sbuf", [128, 3, 128], bf), "HS": ("sbuf", [128, RO, 224], bf),
+    "HB": ("sbuf", [128, 5, 128], bf), "II": ("sbuf", [128, 256], bf), "C16": ("sbuf", [128, 128], bf), "I8": ("sbuf", [128, 128], bf),
+    "YC": ("sbuf", [128, 80], bf), "Dm": ("sbuf", [128, 32, 128], f16), "E": ("sbuf", [128, 32, 128], bf),
+    "Pm": ("sbuf", [128, 4, 224], f16), "Pt": ("sbuf", [128, 4, 224], bf), "JD": ("sbuf", [128, 128], f32),
+    "Pn": ("sbuf", [128, 4, 224], bf), "Ih": ("sbuf", [128, 128], f16), "nil": ("sbuf", [128, 128], bf),
+    "one": ("sbuf", [128, 128], bf), "big": ("sbuf", [128, 512], bf),
+}
+for _t in range(RO):
+    SCRATCH["s%d" % _t] = ("sbuf", [128, TH], bf)
+    for _h in range(2):
+        SCRATCH["z%d%d" % (_t, _h)] = ("sbuf", [128, TH // 2], bf)
+for _b in range(8):
+    SCRATCH["p%d" % _b] = ("psum", [128, 512], f32)
+SEMAPHORES = ["eV", "eS", "eP", "eG", "sent"] + ["arr%d%d" % (t, h) for t in range(1, RO) for h in range(2)] + ["d%d" % k for k in range(24)]
+
+
+def emit(g, T, ops):
+    q = {"V": g.vector, "S": g.scalar, "P": g.tensor, "G": g, "Y": g.sync}
+    lastw, readers, deps = {}, {}, []
+    for n, (e, fn, rd, wr, kind) in enumerate(ops):
+        d = set()
+        for k in rd:
+            if k in lastw: d.add(lastw[k])
+            if k[0] == "#": d.update(m for m in readers.get(k, []) if ops[m][0] != e)
+        for k in wr:
+            for m in readers.get(k, []) + ([lastw[k]] if k in lastw else []):
+                if ops[m][0] != e or e != "P" or ops[m][4]: d.add(m)
+        for k in rd: readers.setdefault(k, []).append(n)
+        for k in wr:
+            lastw[k] = n
+            readers[k] = []
+        last = {}
+        for m in d:
+            key = ops[m][0] if not ops[m][4] else ("x", m)
+            last[key] = max(last.get(key, -1), m)
+        deps.append(sorted(last.values()))
+    need = set(m for d in deps for m in d)
+    sig, cnt, nd, seen = {}, {"V": 0, "S": 0, "P": 0, "G": 0}, [0], {}
+    final = {}
+    for n, (e, fn, rd, wr, kind) in enumerate(ops):
+        for m in deps[n]:
+            s, v = sig[m]
+            if seen.get((e, s), 0) < v:
+                q[e].wait_ge(T.sem[s], v)
+                seen[(e, s)] = v
+        if kind == "dma":
+            s = "d%d" % nd[0]
+            nd[0] += 1
+            fn().then_inc(T.sem[s], 16)
+            sig[n] = (s, 16)
+            final[s] = 16
+        elif kind == "call":
+            fn()
+        elif kind:
+            sig[n] = kind
+            final[kind[0]] = kind[1]
+        else:
+            ins = fn()
+            if n in need:
+                cnt[e] += 1
+                ins.then_inc(T.sem["e" + e], 1)
+                sig[n] = ("e" + e, cnt[e])
+                final["e" + e] = cnt[e]
+    for s in final:
+        g.wait_ge(T.sem[s], final[s])
+
+
+def rank_program(g, core, T, topo):
+    rank = T.rank_of(core)
+    if rank is None:
+        return
+    cores = T.cores
+    nxt, prv = cores[(rank + 1) % len(cores)], cores[(rank - 1) % len(cores)]
+    rid, pid = topo.addr(nxt)[0], topo.addr(nxt)[1]
+    n_out, n_in = len(topo.engines(core, nxt)), len(topo.engines(prv, core))
+    ops = []
+    V, S, P = g.vector, g.scalar, g.tensor
+    ps = [T["p%d" % b] for b in range(8)]
+
+    def ts(out, in0, s1, o0, s2=None, o1=None, r=(), w=()):
+        if o1 is None: ops.append(("V", lambda: V.tensor_scalar(out, in0, s1, None, o0), list(r), list(w), None))
+        else: ops.append(("V", lambda: V.tensor_scalar(out, in0, s1, s2, o0, o1), list(r), list(w), None))
+
+    def tt(out, a, b, op, r, w): ops.append(("V", lambda: V.tensor_tensor(out, a, b, op), list(r), list(w), None))
+    def cp(out, a, r, w): ops.append(("V", lambda: V.tensor_copy(out, a), list(r), list(w), None))
+    def ms(ap, c, w): ops.append(("V", lambda: V.memset(ap, c), [], list(w), None))
+    def act(out, a, fn, r, w, **kw): ops.append(("S", lambda: S.activation(out, a, fn, **kw), list(r), list(w), None))
+    def mm(out, l, rh, st, sp, r, w): ops.append(("P", lambda: P.matmul(out, l, rh, st, sp), list(r), list(w), None))
+    def dma(e, out, a, r, w): ops.append((e, lambda: (g.sync if e == "Y" else S).dma_start(out, a), list(r), list(w), "dma"))
+
+    def iota(out, pat, base, cm, w, small=True):
+        if small: ops.append(("G", lambda: g.iota(out, pat, base, cm, allow_small_or_imprecise_dtypes=True), [], list(w), None))
+        else: ops.append(("G", lambda: g.iota(out, pat, base, cm), [], list(w), None))
+
+    K, XW, pc, pi, pj, w = T.K, T.XW, T.pc, T.pi, T.pj, T.w
+    KALL, H = ["K0", "K1", "K2", "K3", "K4", "K5"], [slice(0, 512), slice(512, 1024)]
+    XALL = ["XW%d" % c for c in range(8)]
+    col = lambda c, n=128: pc[0:n, c:c + 1]
+
+    dma("Y", K[:, 0:1024], T.nkey[:, 0:1024], [], ["K0", "K1"])
+    for h in range(2): dma("S", T["z0%d" % h][:], T.zin[:, H[h]], [], ["z0%d" % h])
+    dma("S", T.ci[:], T.cnt[:], [], ["ci"])
+    for c in range(4):
+        dma("Y", T.xb[:, 1024 * c:1024 * c + 1024], T.xreg[:, 1024 * c:1024 * c + 1024], [], ["xb%d" % c])
+        if c < 3: dma("Y", K[:, 1024 * c + 1024:1024 * c + 2048], T.nkey[:, 1024 * c + 1024:1024 * c + 2048], [], ["K%d" % (c + 2)] + (["K5"] if c == 2 else []))
+
+    io2, n256 = T.io2, T.n256
+    iota(pi[:, 0:1], [[0, 1]], 0, 1, ["pi0"], False)
+    iota(pi[:, 8:13], [[16, RO]], 0, 1, ["pi1"], False)
+    iota(n256[:], [[1, 256]], 0, 0, ["n256"])
+    iota(io2[:, 192:320], [[0, 8], [1, 16]], 0, 0, ["ioC"])
+    iota(io2[:, 64:192], [[1, 8], [0, 16]], 0, 0, ["ioB"])
+    iota(io2[:, 0:64], [[1, 32], [0, 2]], 0, 0, ["ioA"])
+    iota(pi[:, 16:48], [[2, 32]], 2, 1, ["pi2"], False)
+    iota(io2[:, 448:480], [[1, 8], [0, 4]], 0, 0, ["ioE"])
+    iota(io2[:, 320:448], [[0, 8], [1, 4], [0, 4]], 0, 0, ["ioD"])
+    iota(T.JD[:, 0:64], [[16, 64]], KW, 0, ["JD0"])
+    iota(T.JD[:, 64:128], [[0, 16], [16, 4]], D, 0, ["JD1"])
+    p0 = pi[:, 0:1]
+    bits = [(0, 127), (0, 15), (4, 7), (0, 3), (2, 31), (3, 7), (0, 1), (1, 3), (4, 1), (2, 7), (5, 3), (1, 15)]
+    cP, cA, cG, cM3, cP2, cGQ, cDUP, cMQ, cG1, cG4, cP5, cA2 = range(12)
+    for c, (sh, mk) in enumerate(bits): ts(pj[:, c:c + 1], p0, sh, A.arith_shift_right, mk, A.bitwise_and, ["pi0"], [])
+    ts(pj[:, 16:21], pi[:, 8:13], 4, A.arith_shift_right, 7, A.bitwise_and, ["pi1"], ["pjA"])
+    cp(pc[:, 0:12], pj[:, 0:12], ["pjA"], [])
+    cp(pc[:, 16:21], pj[:, 16:21], ["pjA"], ["c0"])
+    ts(pc[:, 24:29], n256[:, 0:5], -3.0, A.mult, col(cA), A.add, ["n256", "c0"], ["c1"])
+    ts(pc[:, 32:37], pc[:, 16:21], 4.0, A.mult, 300.0, A.add, ["c0"], ["c2"])
+    ts(pc[:, 14:15], col(cDUP), 2.0, A.mult, -1.0, A.add, ["c0"], [])
+    ts(pc[:, 15:16], col(cDUP), -1.0, A.add, r=["c0"], w=[])
+    ts(pc[:, 21:22], col(cA), 1.0, A.add, col(cA), A.mult, ["c0"], ["c3"])
+    ts(pc[:, 40:45], pc[:, 24:29], 0.0, A.is_ge, r=["c1"], w=[])
+    ts(pc[:, 48:53], pc[:, 24:29], 2.0, A.is_le, r=["c1"], w=["c4"])
+    ts(pc[:, 56:59], n256[:, 0:3], col(cMQ), A.is_equal, r=["c0"], w=["c5"])
+    tt(pc[:, 24:29], pc[:, 24:29], pc[:, 32:37], A.add, ["c1", "c2", "c4"], ["c1"])
+    ts(T.WB[:, 0:128], io2[:, 192:320], col(14), A.mult, col(15), A.add, ["ioC", "c3"], ["WB0"])
+    ts(T.WB[:, 128:256], io2[:, 64:192], col(cGQ), A.is_equal, r=["ioB", "c0"], w=["WB1"])
+    tt(pc[:, 40:45], pc[:, 40:45], pc[:, 48:53], A.mult, ["c4"], ["c4"])
+    ts(pc[:, 22:23], col(21), -BIG, A.mult, BIG, A.add, ["c3"], ["cMB"])
+    tt(T.WB[:, 0:128], T.WB[:, 0:128], T.WB[:, 128:256], A.mult, ["WB0", "WB1"], ["WB0"])
+    tt(pc[:, 24:29], pc[:, 24:29], pc[:, 40:45], A.mult, ["c1", "c4"], ["c1"])
+    ts(pj[:, 32:64], pi[:, 16:48], 127, A.bitwise_and, r=["pi2"], w=["pjB"])
+    ts(pc[:, 24:29], pc[:, 24:29], -300.0, A.add, r=["c1"], w=["c1"])
+    cp(pc[:, 192:224], pj[:, 32:64], ["pjB"], ["c11"])
+    ts(T.SQ[:, 0, :], io2[:, 0:64], col(24), A.is_equal, r=["ioA", "c1"], w=["SQ0"])
+    for m in range(3): ts(T.MK[:, m, :], T.WB[:, 0:128], col(56 + m), A.mult, r=["WB0", "c5"], w=["MK"] if m == 2 else [])
+
+    def front(t, h):
+        zn = "z%d%d" % (t, h)
+        mm(ps[7 - h][0:64, :], T.SQ[:, t, :], T[zn][:], True, True, [zn, "SQ%d" % t], ["#%d" % (7 - h)])
+        act(T.sq[0:64, H[h]], ps[7 - h][0:64, :], F.Square, ["#%d" % (7 - h), "c0", "c3"], ["sq%d" % h], bias=col(cDUP if t == 0 else 15, 64))
+
+    def front2(h):
+        mm(ps[2 + h][:, :], T.MK[0:64, 0, :], T.sq[0:64, H[h]], True, True, ["sq%d" % h, "MK"], ["#%d" % (2 + h)])
+        act(ps[2 + h][:, :], ps[2 + h][:, :], F.Relu, ["#%d" % (2 + h), "cMB"], ["#%d" % (2 + h)], bias=col(22), scale=BIG)
+
+    def plus_one(c0, c1, k, e="V"):
+        if e == "V": ts(K[:, c0:c1], K[:, c0:c1], 1.0, A.add, r=[k], w=[k])
+        else: act(K[:, c0:c1], K[:, c0:c1], F.Identity, [k], [k], bias=1.0)
+
+    front(0, 0)
+    front(0, 1)
+    front2(0)
+    front2(1)
+    for d in range(32): ts(T.Dm[:, d, :], n256[:, 0:128], col(192 + d), A.is_equal, -1.0, A.mult, ["c11"], ["Dm"] if d == 31 else [])
+    ops.append(("G", lambda: g.affine_select(T.Dm[:], T.Dm[:], [[0, 32], [1, 128]], A.not_equal, 1.0, 0, -1), ["Dm"], ["Dm"], None))
+    ts(T.Sel[:], io2[:, 448:480], col(cG), A.is_equal, r=["ioE", "c0"], w=["Sel"])
+    ts(T.Mq[:], io2[:, 320:448], col(cM3), A.is_equal, r=["ioD", "c0"], w=["Mq"])
+    ts(T.Rb[:], n256[:, 0:32], col(cP2), A.is_equal, r=["c0"], w=["Rb"])
+    ts(pc[:, 64:80], n256[:, 0:16], col(cA), A.is_equal, 64.0, A.mult, ["c0"], [])
+    ts(pc[:, 80:81], col(cP), 16.0, A.add, r=["c0"], w=[])
+    ts(pc[:, 81:82], col(cP), 128.0, A.add, r=["c0"], w=["c7"])
+    plus_one(0, 512, "K0")
+    plus_one(512, 1024, "K1")
+    ts(T.II[:, 0:128], n256[:, 0:128], col(cP), A.is_equal, r=["c0"], w=[])
+    ts(T.II[:, 128:256], n256[:, 128:256], col(81), A.is_equal, r=["c7"], w=["II"])
+    for a in range(16): ts(T.Z[:, a, :], n256[:, 0:160], col(80), A.is_equal, col(64 + a), A.mult, ["c7"], ["Z%d" % (a // 4)] if a % 4 == 3 else [])
+
+    def later_constants(part):
+        if part == 0:
+            ts(T.cj[:, 0:256], T.ci[:], 15, A.bitwise_and, r=["ci"], w=[])
+            ts(T.cj[:, 256:512], T.ci[:], 4, A.arith_shift_right, r=["ci"], w=["cj"])
+            ms(XW[:, D:KW], 32.0, ["XWd"])
+            ts(T.ch[:], T.cj[:], 0.25, A.mult, r=["cj"], w=["ch"])
+        if part == 1:
+            ts(pc[:, 82:83], col(cG), 16.0, A.mult, 16.0, A.add, ["c0"], [])
+            ts(pc[:, 83:84], col(cA), 3.0, A.is_lt, r=["c0"], w=[])
+            ts(pc[:, 84:85], col(cA), 1.0, A.is_equal, 15.0, A.mult, ["c0"], [])
+            ts(pc[:, 85:86], col(cA), 2.0, A.is_equal, 16.0, A.mult, ["c0"], ["c8"])
+            ts(pc[:, 96:128], n256[:, 1:33], 2.0, A.mult, col(cP), A.is_gt, ["c0"], [])
+            ts(pc[:, 224:256], n256[:, 1:33], -2.0, A.mult, 128.0, A.add, [], ["c9"])
+            ts(pc[:, 86:87], col(83), col(84), A.add, r=["c8"], w=[])
+            ts(pc[:, 87:88], col(83), 16.0, A.mult, r=["c8"], w=[])
+            ts(pc[:, 88:89], col(83), -2560.0, A.mult, col(85), A.add, ["c8"], ["c10"])
+            ts(pc[:, 89:90], col(85), 31.0, A.add, r=["c8"], w=[])
+            tt(pc[:, 96:128], pc[:, 96:128], pc[:, 224:256], A.mult, ["c9"], ["c9"])
+            ts(T.Y[:], n256[:, 0:144], col(82), A.is_equal, col(86), A.mult, ["c8", "c10"], ["Y"])
+            ts(T.C16[:], n256[:, 0:128], col(cP), A.is_equal, col(87), A.mult, ["c10"], ["C16"])
+            ts(pc[:, 88:89], col(88), 32.0, A.add, r=["c10"], w=["cSB"])
+            ts(T.BO[:], io2[:, 64:192], col(cG), A.is_equal, r=["ioB"], w=["BO"])
+            ts(pc[:, 96:128], pc[:, 96:128], col(cP), A.add, r=["c9"], w=["c9"])
+        if part == 2:
+            ts(pc[:, 90:91], col(cA), 2.0, A.mult, col(cG1), A.add, ["c0"], [])
+            ts(pc[:, 91:92], col(cDUP), 16.0, A.mult, col(cA2), A.add, ["c0"], [])
+            ts(pc[:, 128:132], n256[:, 0:4], col(cP5), A.is_equal, r=["c0"], w=["c12"])
+            ts(T.JD[:], T.JD[:], col(cA), A.add, r=["JD0", "JD1"], w=["JD"])
+            ts(pc[:, 90:92], pc[:, 90:92], 96.0, A.add, r=["c12"], w=["c13"])
+            ts(T.I8[:], n256[:, 0:128], col(cP), A.is_equal, 8192.0, A.mult, ["c0"], ["I8"])
+            ms(T.one[0:32, :], 1.0, [])
+            ms(T.nil[0:32, :], 0.0, [])
+            ms(T.big[0:32, :], BIG, ["big"])
+            for G in range(4): ts(T.Pm[:, G, :], n256[:, 0:224], col(90), A.is_equal, col(128 + G), A.mult, ["c13"], ["Pm"] if G == 3 else [])
+            ts(T.Ih[:], n256[:, 0:128], col(cP), A.is_equal, r=["c0"], w=["Ih"])
+            ts(T.JD[:, 64:128], T.JD[:, 64:128], -2048.0, A.add, r=["JD"], w=["JD"])
+            ts(T.Pn[:], T.Pm[:], 8192.0, A.mult, r=["Pm"], w=["Pn"])
+            for G in range(4): ts(T.Pt[:, G, :], n256[:, 0:224], col(91), A.is_equal, col(128 + G), A.mult, ["c13"], ["Pt"] if G == 3 else [])
+        if part == 3:
+            for d in range(32): ts(T.E[:, d, :], n256[:, 0:128], col(96 + d), A.is_equal, r=["c9"], w=["E"] if d == 31 else [])
+        if part == 4:
+            ts(pc[:, 144:149], pc[:, 32:37], col(cA), A.add, col(83), A.mult, ["c2", "c8"], ["c14"])
+            ts(pc[:, 150:151], col(cG4), 16.0, A.mult, col(cM3), A.add, ["c0"], [])
+            ts(pc[:, 151:152], col(cM3), 3.0, A.is_lt, -16.0, A.mult, ["c0"], [])
+            ts(pc[:, 152:153], col(cG4), 8.0, A.mult, col(cP5), A.add, ["c0"], [])
+            ts(pc[:, 153:154], col(cM3), 1.0, A.is_equal, 15.0, A.mult, ["c0"], ["c15"])
+            for t in range(1, RO): ts(T.SQ[:, t, :], io2[:, 0:64], col(24 + t), A.is_equal, r=["ioA", "c1"], w=["SQ%d" % t])
+            ts(pc[:, 154:155], col(83), 2560.0, A.mult, -1.0, A.add, ["c8"], [])
+            ts(pc[:, 155:156], col(83), 40960.0, A.mult, -16.0, A.add, ["c8"], ["cZB"])
+            ts(pc[:, 144:149], pc[:, 144:149], -204.0, A.add, r=["c14"], w=["c14"])
+            ts(pc[:, 156:160], pc[:, 128:132], col(151), A.mult, r=["c15", "c12"], w=[])
+            ts(pc[:, 160:161], col(151), -0.0625, A.mult, col(153), A.add, ["c15"], ["c16"])
+            ts(T.HB[:, 4, :], n256[:, 0:128], col(150), A.is_equal, col(151), A.mult, ["c15"], [])
+            for t in range(RO): ts(T.HS[:, t, :], n256[:, 0:224], col(144 + t), A.is_equal, r=["c14"], w=["HS"] if t == RO - 1 else [])
+            for b in range(4): ts(T.HB[:, b, :], n256[:, 0:128], col(150), A.is_equal, col(156 + b), A.mult, ["c16"], ["HB"] if b == 3 else [])
+            ts(T.YC[:, 0:16], n256[:, 0:16], 0.0, A.mult, r=[], w=[])
+            ts(T.YC[:, 16:80], n256[:, 0:64], col(152), A.is_equal, col(160), A.mult, ["c16"], ["YC"])
+
+    def build_xw(lo, hi):
+        for c in range(lo, hi):
+            bank = 6 + c % 2
+            for a in (2 * c, 2 * c + 1):
+                o = ps[bank][:, 256 * (a % 2):256 * (a % 2) + 256]
+                mm(o, T.II[:, 0:128], T.xb[:, 256 * a:256 * a + 256], True, False, ["II", "xb%d" % (c // 2)], ["#%d" % bank])
+                mm(o, T.Z[:, a, 16 + a:144 + a], T.ch[:, 0:256], False, False, ["Z%d" % (a // 4), "ch"], ["#%d" % bank])
+                mm(o, T.Z[:, a, 15 + a:143 + a], T.ch[:, 256:512], False, True, [], ["#%d" % bank])
+            act(XW[:, 512 * c:512 * c + 512], ps[bank][:, :], F.Identity, ["#%d" % bank], ["XW%d" % c], bias=32.0)
+
+    Gs, Gn = [T.Ga, T.Gb, T.Ga, T.Ab], ["Ga", "Gb", "Ga", "Ab"]
+    Xs = [None, T.X1, T.X2, T.X2]
+    Cg = [T.Cg0, T.Cg1, T.Cg2]
+    gk = lambda m, h: ["%s%d%d" % (Gn[m], h, i) for i in range(len(CUT) - 1)]
+
+    def piece(m, h, i):
+        a, b = 32 * h + CUT[i], 32 * h + CUT[i + 1]
+        c = 64 * (m - 1)
+        tt(Gs[m][:, 16 * a:16 * b], K[:, 0:D].indirect(T.off[:, c + a:c + b]), Xs[m][:, 16 * a:16 * b], A.min if m < 3 else A.subtract,
+           KALL + ["off%d%d" % (m - 1, h), "X%d%d" % (min(m, 2), h)], [gk(m, h)[i]])
+
+    def first(h):
+        tt(T.Ga[:, H[h]], K[:, H[h]], ps[2 + h][:, :], A.min, ["K%d" % h, "#%d" % (2 + h)], gk(0, h))
+
+    def mm1(m, h):
+        for c in range(4):
+            mm(ps[h][:, c:128:4], Gs[m][:, 512 * h + c:512 * h + 512:4], T.Sel[:], True, True, gk(m, h) + ["Sel"], ["#%d" % h])
+
+    def turn(m, h):
+        tt(T.T3[:, 128 * h:128 * h + 128], ps[h][:, 0:128], T.Mq[:], A.mult, ["#%d" % h, "Mq"], ["T3%d" % h])
+        mm(ps[h][:, 128:160], T.T3[:, 128 * h:128 * h + 128], T.Rb[:], True, True, ["T3%d" % h, "Rb"], ["#%d" % h])
+
+    def conv(m, h, i):
+        c = slice(64 * m + 32 * h, 64 * m + 32 * h + 32)
+        n = "%d%d" % (m, h)
+        if i == 0: ts(T.ki[:, c], ps[h][:, 128:160], -1.0, A.add, r=["#%d" % h], w=["ki" + n])
+        if i == 1: ts(T.pl[:, c], T.ki[:, c], D - 1, A.bitwise_and, r=["ki" + n], w=["pl" + n])
+        if i == 2: cp(T.off[:, c], T.pl[:, c], ["pl" + n], ["off" + n])
+
+    def half(x, y, extra=None, fill=(None, None, None)):
+        piece(x[0], x[1], 0)
+        turn(*y)
+        if extra: extra()
+        for i in range(3):
+            if i + 2 < len(CUT): piece(x[0], x[1], i + 1)
+            conv(y[0], y[1], i)
+            if fill[i]: fill[i]()
+        if x[0] < 3: mm1(*x)
+
+    def mask(m, b, bank, tensor=True, scalar=True):
+        if tensor: mm(ps[bank][:, :], T.MK[0:64, m, :], T.sq[0:64, H[b]], True, True, ["sq%d" % b, "MK"], ["#%d" % bank])
+        if scalar: act(Xs[m][:, H[b]], ps[bank][:, :], F.Relu, ["#%d" % bank, "cMB"], ["X%d%d" % (m, b)], bias=col(22), scale=BIG)
+
+    def cgather(m, hs):
+        for h in hs:
+            c = 64 * m + 32 * h
+            act(Cg[m][:, H[h]], XW[:, 0:D].indirect(T.off[:, c:c + 32]), F.Identity, XALL + ["off%d%d" % (m, h)], ["Cg%d%d" % (m, h)],
+                bias=160.0 - 39.5 / 16, scale=0.0625)
+
+    def count_w(m):
+        for a in range(16):
+            mm(ps[6][:, 64 * m:64 * m + 64], T.Y[:, 16 - a:144 - a], Cg[m][:, a:TH:16], a == 0, a == 15, ["Y", "Cg%d0" % m, "Cg%d1" % m, "Cg%d2" % m], ["#6"])
+
+    def k1r(qr):
+        bank = 4 + qr // 2
+        c = 256 * (qr % 2)
+        mm(ps[bank][:, c:c + 256], T.BO[:], T.Gb[:, 256 * qr:256 * qr + 256], True, True, ["BO"] + gk(1, qr // 2), ["#%d" % bank])
+
+    def high(src, t, bank, n, c0, down=False):
+        for b in range(4):
+            ap, name = src(b)
+            o = 32 * b if down else 96 - 32 * b
+            mm(ps[bank][:, 0:n], T.HS[:, t, o:o + 128], ap, b == 0, b == 3, ["HS", name], ["#%d" % bank])
+        act(T.hi[:, c0:c0 + n], ps[bank][:, 0:n], F.Identity, ["#%d" % bank], ["hi%d" % (c0 // 512)], bias=160.0 - 8.5 / 16, scale=0.0625)
+
+    def clean(src, t, strip, stop, move=True):
+        for b in range(2 if move else 0):
+            ap, name = src(b)
+            mm(ps[2 + b][:, :], T.II[:, 128 - 16 * t:256 - 16 * t], ap, True, stop and not strip, ["II", name], ["#%d" % (2 + b)])
+        if strip:
+            for b in range(4):
+                c = 256 * (b % 2)
+                mm(ps[2 + b // 2][:, c:c + 256], T.HB[:, b, :], T.hi[:, 0:256], False, stop and b % 2 == 1, ["HB", "hi0"], ["#%d" % (2 + b // 2)])
+
+    def xscatter(u):
+        act(XW[:, 0:KW].indirect(T.soff[:, 4 * u:4 * u + 4]), XW[:, KW + 64 * u:KW + 64 * u + 64], F.Silu, ["soff", "src0", "src1"], XALL + ["XWd"])
+
+    def diff(q):
+        bank = q % 2
+        for d in range(8 * q, 8 * q + 8):
+            mm(ps[bank][:, 64 * (d % 8):64 * (d % 8) + 64], T.Dm[:, d, :], T.Sx[:], True, True, ["Dm", "Sx"], ["#%d" % bank])
+
+    def equal(q):
+        ts(T.eq[:, 512 * q:512 * q + 512], ps[q % 2][:, :], 0.0, A.is_equal, r=["#%d" % (q % 2)], w=["eq%d" % q])
+
+    def fold(q):
+        for d in range(8 * q, 8 * q + 8):
+            mm(ps[7][:, 0:64], T.E[:, d, :], T.eq[:, 64 * d:64 * d + 64], d == 0, d == 31, ["E", "eq%d" % q], ["#7"])
+
+    def bpiece(u):
+        c = slice(64 * u, 64 * u + 64)
+        tt(T.Bb[:, c], ps[4 + u // 8][:, 64 * (u % 8):64 * (u % 8) + 64], T.X2[:, c], A.min, ["#%d" % (4 + u // 8), "X2%d" % (u // 8)], ["Bb%d" % u])
+
+    def new_key(b, t, bank):
+        mm(ps[bank][:, :], T.one[0:1, :], T.big[0:1, :], True, False, ["big"], ["#%d" % bank])
+        for a in range(16):
+            for part in (1, 0):
+                c = 64 * part + 32 * b
+                mm(ps[bank][:, a:512:16], T.Z[:, a, 16 + a - t:144 + a - t], T.P12[:, c:c + 32], False, a == 15 and part == 0,
+                   ["P1", "P2"], ["#%d" % bank])
+
+    for t in range(RO):
+        last = t == RO - 1
+        zh = lambda b, t=t: (T["z%d%d" % (t, b)][:], "z%d%d" % (t, b))
+        if t == 0:
+            for m in (1, 2):
+                for b in range(2): mask(m, b, 4 + b)
+            later_constants(0)
+            plus_one(1024, 2048, "K2", "S")
+            build_xw(0, 2)
+        first(0)
+        mm1(0, 0)
+        first(1)
+        if t == 0:
+            later_constants(1)
+            build_xw(2, 4)
+        turn(0, 0)
+        mm1(0, 1)
+        if t == 0:
+            later_constants(2)
+            build_xw(4, 6)
+        clean(zh, t, False, False)
+        for i in range(3): conv(0, 0, i)
+        if t == 0:
+            plus_one(2048, 3072, "K3")
+            later_constants(3)
+            plus_one(3072, 3584, "K4")
+            plus_one(3584, 4096, "K5", "S")
+            build_xw(6, 8)
+        half((1, 0), (0, 1), lambda: clean(zh, t, t > 0, False, False))
+        cgather(0, (0, 1))
+        half((1, 1), (1, 0), lambda: k1r(1))
+        cgather(1, (0,))
+        half((2, 0), (1, 1), lambda: k1r(3))
+        cgather(1, (1,))
+        half((2, 1), (2, 0), lambda: count_w(0),
+             (lambda: ts(T.cn[:, 0:128], T.ki[:, 0:128], 12, A.arith_shift_right, 255, A.bitwise_and, ["ki00", "ki01", "ki10", "ki11"], ["cn0"]),
+              lambda: ts(T.tg[:, 0:128], T.cn[:, 0:128], 2880.0, A.add, r=["cn0"], w=["tg0"]), None))
+        cgather(2, (0,))
+        half((3, 0), (2, 1), lambda: (count_w(1), k1r(2)),
+             (None,
+              lambda: ts(T.cn[:, 128:192], T.ki[:, 128:192], 12, A.arith_shift_right, 255, A.bitwise_and, ["ki20", "ki21"], ["cn2"]),
+              lambda: tt(T.e01[:], ps[6][:, 0:128], T.tg[:, 0:128], A.is_equal, ["#6", "tg0"], ["e01"])))
+        act(T.Cg2[:, 512:768], XW[:, 0:D].indirect(T.off[:, 160:176]), F.Identity, XALL + ["off21"], ["Cg21"], bias=160.0 - 39.5 / 16, scale=0.0625)
+        ts(T.Cg2[:, 768:TH], XW[:, 0:D].indirect(T.off[:, 176:192]), 0.0625, A.mult, 160.0 - 39.5 / 16, A.add, XALL + ["off21"], ["Cg22"])
+        ts(T.Q[:], T.pl[:, 128:192], -2048.0, A.add, r=["pl20", "pl21"], w=["Q"])
+        mm(ps[2][:, :], T.C16[:], T.Cg2[:, H[0]], False, True, ["C16", "Cg20"], ["#2"])
+        count_w(2)
+        mm(ps[7][:, 0:64], T.nil[0:1, :], T.big[0:1, 0:64], True, False, ["big"], ["#7"])
+        for G in range(4):
+            for h in range(4):
+                mm(ps[7][:, G:64:4], T.Pm[:, G, 96 - 32 * h:224 - 32 * h], T.Q[:, h:64:4], False, False, ["Pm", "Q"], ["#7"])
+        mm(ps[3][:, :], T.C16[:], T.Cg2[:, H[1]], False, True, ["C16", "Cg21", "Cg22"], ["#3"])
+        for b in range(2):
+            act(XW[:, KW + 512 * b:KW + 512 * b + 512], ps[2 + b][:, :], F.Identity, ["#%d" % (2 + b), "cSB"], ["src%d" % b], bias=col(88 if t == 0 else 89))
+        ts(T.tg[:, 128:192], T.cn[:, 128:192], 2880.0, A.add, r=["cn2"], w=["tg2"])
+        tt(w[:, 0, :], T.e01[:, 0:64], T.e01[:, 64:128], A.mult, ["e01"], ["w0"])
+        piece(3, 1, 0)
+        tt(T.tg[:, 128:192], T.tg[:, 128:192], w[:, 0, :], A.mult, ["w0", "tg2"], ["tg2"])
+        ts(w[:, 6, :], T.pl[:, 128:192], -1.0 / 64, A.mult, 2047.0 / 64, A.add, ["pl20", "pl21"], ["w6"])
+        ts(w[:, 7, :], T.cn[:, 128:192], -64.0, A.mult, -1027.0 * 32, A.add, ["cn2"], ["w7"])
+        tt(T.nok[:], ps[6][:, 128:192], T.tg[:, 128:192], A.not_equal, ["#6", "tg2"], ["nok"])
+        for G in range(4):
+            for h in range(4):
+                mm(ps[7][:, G:64:4], T.Pn[:, G, 96 - 32 * h:224 - 32 * h], T.nok[:, h:64:4], False, G + h == 6, ["Pn", "nok"], ["#7"])
+        tt(w[:, 4, :], ps[6][:, 128:192], T.tg[:, 128:192], A.is_equal, ["#6", "tg2"], ["w4"])
+        tt(w[:, 3, :], T.nok[:], T.JD[:, 0:64], A.mult, ["nok", "JD"], ["w3"])
+        piece(3, 1, 1)
+        tt(w[:, 3, :], w[:, 3, :], T.pl[:, 128:192], A.max, ["w3", "pl20", "pl21"], ["w3"])
+        bpiece(15)
+        cp(T.xoff[:], w[:, 3, :], ["w3"], ["xoff"])
+        cp(T.Sx[:], ps[7][:, 0:64], ["#7"], ["Sx"])
+        diff(0)
+        diff(1)
+        so = T["s%d" % t]
+        for h in range(2):
+            act(so[:, H[h]], XW[:, 0:KW + TH].indirect(T.xoff[:, 32 * h:32 * h + 32]), F.Identity, XALL + ["XWd", "src0", "src1", "xoff"],
+                ["s%d%d" % (t, h)], bias=-31.0)
+            if not last:
+                zn, sem = "z%d%d" % (t + 1, h), "arr%d%d" % (t + 1, h)
+                ops.append(("G", lambda zn=zn, sem=sem, src=so[:, H[h]]: g.remote_dma(T[zn][:], src, T.sem[sem], T.sem.sent, pid, rid, topo.mask(core, nxt)),
+                            ["s%d%d" % (t, h)], [], "call"))
+                ops.append(("P", None, [], [zn], (sem, n_in)))
+        for i in range(2, len(CUT) - 1): piece(3, 1, i)
+        equal(0)
+        diff(2)
+        fold(0)
+        equal(1)
+        diff(3)
+        fold(1)
+        equal(2)
+        fold(2)
+        equal(3)
+        fold(3)
+        tt(T.P12[:, 0:64], w[:, 6, :], w[:, 4, :], A.mult, ["w6", "w4"], ["P1"])
+        tt(T.P12[:, 64:128], w[:, 7, :], w[:, 4, :], A.mult, ["w7", "w4"], ["P2"])
+        mm(ps[6][:, 0:64], T.Ih[:], T.Q[:], True, False, ["Ih", "Q"], ["#6"])
+        mm(ps[6][:, 0:64], T.I8[:], T.nok[:], False, False, ["I8", "nok"], ["#6"])
+        ts(T.nd[:], ps[7][:, 0:64], 0.0, A.is_gt, 8192.0, A.mult, ["#7"], ["nd"])
+        for h in range(4):
+            for G in range(4):
+                mm(ps[6][:, h:64:4], T.Pt[:, h, 96 - 32 * G:224 - 32 * G], T.nd[:, G:64:4], False, G + h == 6, ["Pt", "nd"], ["#6"])
+        k1r(0)
+        for u in range(14, 8, -1): bpiece(u)
+        if last:
+            high(lambda b: (so[:, 256 * b:256 * b + 256], "s4%d" % (b // 2)), 0, 7, 256, 0)
+            new_key(0, t, 0)
+            clean(lambda b: (so[:, H[b]], "s4%d" % b), 0, True, True)
+            new_key(1, t, 1)
+        tt(w[:, 5, :], ps[6][:, 0:64], T.JD[:, 64:128], A.min, ["JD", "#6"], ["w5"])
+        bpiece(8)
+        ts(T.soff[:], w[:, 5, :], 2048.0, A.add, r=["w5"], w=["soff"])
+        s0 = len(ops)
+        if t == 0: later_constants(4)
+        fill = ops[s0:]
+        del ops[s0:]
+        for u in range(NR - 1, -1, -1):
+            c = slice(64 * u, 64 * u + 64)
+            tt(K[:, 0:KW].indirect(T.soff[:, 4 * u:4 * u + 4]), T.Ab[:, c], T.Bb[:, c], A.max, ["soff", "Bb%d" % u] + gk(3, u // 8), KALL)
+            if 6 < u < 15: bpiece(u - 7)
+            ops.extend(fill[2 * (NR - 1 - u):2 * (NR - u)])
+        zq = lambda b, t=t + 1: (T["z%d%d" % (t, b // 2)][:, 256 * (b % 2):256 * (b % 2) + 256], "z%d%d" % (t, b // 2))
+        absk = lambda b: act(K[:, H[b]], K[:, H[b]], F.Abs, ["K%d" % b], ["K%d" % b])
+
+        def new_row():
+            for b in range(2):
+                tt(K[:, H[b]], K[:, H[b]], ps[b][:, :], A.min, ["K%d" % b, "#%d" % b], ["K%d" % b])
+            absk(0)
+
+        if not last:
+            steps = {0: lambda: new_key(0, t, 0), 3: lambda: front(t + 1, 0), 4: lambda: (front(t + 1, 1), front2(0)), 5: lambda: front2(1),
+                     6: lambda: (mask(1, 0, 4), mask(1, 1, 5, True, False), new_key(1, t, 1), mask(2, 0, 6, True, False), mask(2, 1, 7, True, False)),
+                     7: lambda: (new_row(), absk(1), mask(1, 1, 5, False)), 8: lambda: high(zq, t + 1, 4, 256, 0),
+                     10: lambda: mask(2, 0, 6, False), 12: lambda: mask(2, 1, 7, False)}
+        else:
+            oz = lambda b: act(T.oz[:, H[b]], ps[2 + b][:, :], F.Identity, ["#%d" % (2 + b), "cZB"], ["oz%d" % b], bias=col(154))
+            steps = {4: lambda: oz(0), 5: lambda: (oz(1), dma("Y", T.yz[:], T.oz[:], ["oz0", "oz1"], [])), 12: new_row, 13: lambda: absk(1)}
+        for n in range(NR):
+            xscatter(NR - 1 - n)
+            if n in steps: steps[n]()
+
+    vb = lambda c: (T.xb[:, 512 * c:512 * c + 512], "v%d" % (c // 2))
+    for b in range(2): cp(ps[4 + b][:, 0:256], K[:, 1024 + 256 * b:1280 + 256 * b], ["K2"], ["#%d" % (4 + b)])
+    for c in list(range(6, 16)) + [0, 1, 2, 3]:
+        b = 4 + c % 2
+        if c == 0: ts(T.xb[:, 0:1024], XW[:, 0:1024], -31.0, A.add, r=XALL, w=["v0", "xb0"])
+        tt(ps[b][:, 0:256], K[:, 256 * c:256 * c + 256], ps[b][:, 0:256], A.add, ["#%d" % b] + (["K%d" % (c // 2)] if c < 4 else []), ["#%d" % b])
+    ts(T.okk[:, 0:256], ps[4][:, 0:256], -16.0, A.add, r=["#4"], w=["ok0"])
+    tt(T.okk[:, 256:512], T.okk[:, 0:256], ps[5][:, 0:256], A.add, ["ok0", "#5"], ["ok1"])
+    dma("Y", T.yk[:], T.okk[:, 256:512], ["ok1"], [])
+
+    def sum_x(a0, a1):
+        for a in range(a0, a1):
+            mm(ps[0][:, 0:256], T.II[:, 0:128], T.xb[:, 256 * a:256 * a + 256], a == 12, False, ["v%d" % (a // 4)], ["#0"])
+
+    for b in (3, 2, 1):
+        act(T.xb[:, 1024 * b:1024 * b + 1024], XW[:, 1024 * b:1024 * b + 1024], F.Identity, XALL, ["v%d" % b, "xb%d" % b], bias=-31.0)
+        if b == 3: sum_x(12, 16)
+    high(lambda c: vb(7 - c), 0, 7, 512, 512, True)
+    high(vb, 0, 6, 512, 0)
+    sum_x(4, 12)
+    for b in (1, 0):
+        mm(ps[2][0:64, :], T.YC[:, 16 - 4 * b:80 - 4 * b], T.hi[:, H[b]], b == 1, b == 0, ["YC", "hi%d" % b], ["#2"])
+    sum_x(0, 4)
+    for b in (3, 2, 1, 0):
+        mm(ps[0][:, 0:256], T.HB[:, 4, :], T.hi[:, 256 * b:256 * b + 256], False, b == 0, ["HB", "hi%d" % (b // 2)], ["#0"])
+    act(T.oc[0:64, :], ps[2][0:64, :], F.Identity, ["#2"], ["oc"], bias=-2880.0)
+    ts(T.ox[:], ps[0][:, 0:256], col(155), A.add, r=["#0", "cZB"], w=["ox"])
+    dma("S", T.yc[:], T.oc[0:64, :], ["oc"], [])
+    dma("Y", T.yx[:], T.ox[:], ["ox"], [])
+    emit(g, T, ops)
+    g.wait_ge(T.sem.sent, 2 * n_out * (RO - 1))

@@ -1,91 +1,170 @@
 from concourse.mybir import AluOpType as A, ActivationFunctionType as F
 
 D, TH, RO = 4096, 1024, 5
-BIG = float(1 << 21)
 KW = D + 64
-NR = TH // 64
-CUT = (0, 16, 24, 32)
+BIG = float(1 << 22)
+HB = 1600
+PB = float(HB * D)
+PAIRS = ((1, 0), (2, 1), (3, 2), (2, 0), (3, 1), (3, 0))
+TURNS = ((1, 2, 3, 4, 5, 6), (7, 8, 0, 9, 10), (11, 12, 13, 14, 15))
+NOM = dict(cyc=0.83, pe=0.42, gather=1.5, scatter=3.5, wake=220.0, dma=1800.0, rate=200.0, hop=3400.0)
+OPT = dict(cgv=1, gp=2, mp=2, fp=2, passes=4, wV=0.7, wS=1.5, wP=1.0, wG=1.0, wY=1.0, wX=1.0)
 
 f32, bf, i32, u16, f16 = "float32", "bfloat16", "int32", "uint16", "float16"
-SCRATCH = {
-    "K": ("sbuf", [128, KW], f32), "XW": ("sbuf", [128, KW + TH], f32), "xb": ("sbuf", [128, D], bf),
-    "ci": ("sbuf", [128, 256], i32), "cj": ("sbuf", [128, 512], i32), "ch": ("sbuf", [128, 512], f16),
-    "Ga": ("sbuf", [128, TH], f32), "Gb": ("sbuf", [128, TH], f32), "Ab": ("sbuf", [128, TH], f32), "Bb": ("sbuf", [128, TH], f32),
-    "X1": ("sbuf", [128, TH], bf), "X2": ("sbuf", [128, TH], bf), "Cg0": ("sbuf", [128, TH], bf), "Cg1": ("sbuf", [128, TH], bf),
-    "Cg2": ("sbuf", [128, TH], bf), "eq": ("sbuf", [128, 2048], bf), "sq": ("sbuf", [128, TH], bf), "hi": ("sbuf", [128, TH], bf),
-    "T3": ("sbuf", [128, 256], f32), "ki": ("sbuf", [128, 192], i32), "pl": ("sbuf", [128, 192], i32),
-    "off": ("sbuf", [128, 192], u16), "cn": ("sbuf", [128, 192], i32), "tg": ("sbuf", [128, 192], f32),
-    "w": ("sbuf", [128, 8, 64], f32), "e01": ("sbuf", [128, 128], f32), "P12": ("sbuf", [128, 128], f16),
-    "Q": ("sbuf", [128, 64], f16), "Sx": ("sbuf", [128, 64], f16), "nok": ("sbuf", [128, 64], bf),
-    "nd": ("sbuf", [128, 64], bf), "xoff": ("sbuf", [128, 64], u16), "soff": ("sbuf", [128, 64], u16),
-    "oz": ("sbuf", [128, TH], bf), "okk": ("sbuf", [128, 512], f32), "ox": ("sbuf", [128, 256], bf), "oc": ("sbuf", [128, 512], f32),
-    "pi": ("sbuf", [128, 48], i32), "pj": ("sbuf", [128, 64], i32), "pc": ("sbuf", [128, 256], f32),
-    "n256": ("sbuf", [128, 256], bf), "io2": ("sbuf", [128, 512], bf),
-    "Sel": ("sbuf", [128, 32], f32), "Mq": ("sbuf", [128, 128], f32), "Rb": ("sbuf", [128, 32], f32), "BO": ("sbuf", [128, 128], f32),
-    "Y": ("sbuf", [128, 144], bf), "Z": ("sbuf", [128, 16, 160], f16), "SQ": ("sbuf", [128, RO, 64], bf),
-    "WB": ("sbuf", [128, 256], bf), "MK": ("sbuf", [128, 3, 128], bf), "HS": ("sbuf", [128, RO, 224], bf),
-    "HB": ("sbuf", [128, 5, 128], bf), "II": ("sbuf", [128, 256], bf), "C16": ("sbuf", [128, 128], bf), "I8": ("sbuf", [128, 128], bf),
-    "YC": ("sbuf", [128, 80], bf), "Dm": ("sbuf", [128, 32, 128], f16), "E": ("sbuf", [128, 32, 128], bf),
-    "Pm": ("sbuf", [128, 4, 224], f16), "Pt": ("sbuf", [128, 4, 224], bf), "JD": ("sbuf", [128, 128], f32),
-    "Pn": ("sbuf", [128, 4, 224], bf), "Ih": ("sbuf", [128, 128], f16), "nil": ("sbuf", [128, 128], bf),
-    "one": ("sbuf", [128, 128], bf), "big": ("sbuf", [128, 512], bf),
+SB = {
+    "K": (KW, f32), "XW": (KW + TH, f32), "xb": (D, bf), "CT": (D, bf), "ci": (256, i32), "ch": (256, bf),
+    "Ga": (TH, f32), "Gb": (TH, f32), "Ab": (TH, f32), "Bb": (TH, f32), "X1": (TH, bf), "X2": (TH, bf),
+    "Cg0": (TH, bf), "Cg1": (TH, bf), "Cg2": (TH, bf), "eq": (2560, bf), "sq": (512, bf), "hi": (TH, bf),
+    "T3": (256, f32), "H3": (256, f16), "off": (192, u16), "cab": (192, bf), "P1": (64, f16), "cB": (64, f16),
+    "e01": (64, bf), "nok": (64, bf), "AR": (320, f16), "nd": (160, bf), "pk": (64, bf), "w": (64, f32),
+    "xoff": (64, u16), "soff": (64, u16), "Hk": (TH, f16), "Hn": (TH, f16),
+    "oz": (TH, bf), "okk": (512, f32), "ox": (256, bf), "oc": (TH, f32),
+    "pi": (48, i32), "pj": (48, i32), "pc": (160, f32), "n256": (256, bf), "io": (576, bf), "JX": (64, f32),
+    "Sel": (128, f32), "Mq": (128, f32), "Rb": (32, f32), "Rh": (64, bf), "RA": (160, f32), "RH": (160, bf),
+    "crow": (256, bf), "one": (512, bf), "nil": (128, bf), "PI": (RO * 128, bf), "WB": (256, bf), "MK": (768, bf),
+    "SQ": (RO * 64, bf), "Y": (288, bf), "Id": (8 * 128, bf), "II": (256, bf), "PK": (128, bf), "Z": (16 * 160, bf),
+    "L": (16 * 128, bf), "SH": (16 * 128, bf), "E": (8 * 128, bf), "HX": (4 * 96, bf), "HR": (6 * 128, bf),
 }
 for _t in range(RO):
-    SCRATCH["s%d" % _t] = ("sbuf", [128, TH], bf)
+    SB["s%d" % _t] = (TH, bf)
     for _h in range(2):
-        SCRATCH["z%d%d" % (_t, _h)] = ("sbuf", [128, TH // 2], bf)
+        SB["z%d%d" % (_t, _h)] = (TH // 2, bf)
+SCRATCH = {n: ("sbuf", [128, c], d) for n, (c, d) in SB.items()}
 for _b in range(8):
     SCRATCH["p%d" % _b] = ("psum", [128, 512], f32)
 SEMAPHORES = ["eV", "eS", "eP", "eG", "sent"] + ["arr%d%d" % (t, h) for t in range(1, RO) for h in range(2)] + ["d%d" % k for k in range(24)]
+PLAN = []
+
+
+def v(name, c0=0, c1=None, step=1, p0=0, p1=128):
+    return (name, c0, SCRATCH[name][1][1] if c1 is None else c1, step, p0, p1)
+
+
+def meet(a, b):
+    if a[2] <= b[1] or b[2] <= a[1] or a[5] <= b[4] or b[5] <= a[4]: return False
+    return not (a[3] == b[3] > 1 and (a[1] - b[1]) % a[3])
+
+
+def covers(a, b):
+    return a == b or (a[3] == 1 and a[1] <= b[1] and b[2] <= a[2] and a[4] <= b[4] and b[5] <= a[5])
+
+
+def needs(ops):
+    reads, writes, banks, loads, deps = {}, {}, {}, {}, []
+    for n, (e, fn, rd, wr, kind, cost, lag) in enumerate(ops):
+        d = set()
+        for name in set(x[0] for x in rd + wr if SCRATCH[x[0]][0] == "psum"):
+            b = banks.setdefault(name, [e, [], []])
+            if b[0] != e: b[:] = [e, [], b[1]]
+            d.update(b[2])
+            if e == "P":
+                d.update(b[1])
+                b[1] = []
+            b[1].append(n)
+        for x in rd: d.update(m for m, old in writes.get(x[0], []) if meet(x, old))
+        for x in wr:
+            for book in (reads, writes):
+                d.update(m for m, old in book.get(x[0], []) if meet(x, old))
+                book[x[0]] = [(m, old) for m, old in book.get(x[0], []) if not covers(x, old)]
+        for x in rd: reads.setdefault(x[0], []).append((n, x))
+        for x in wr: writes.setdefault(x[0], []).append((n, x))
+        if kind and kind[0] == "arrival": d.add(n - 1)
+        if kind == "dma" and wr:
+            if e in loads: d.add(loads[e])
+            loads[e] = n
+        d.discard(n)
+        deps.append(d)
+    return deps
+
+
+def free(ops, m, n):
+    return ops[m][0] == ops[n][0] and (ops[m][0] == "P" and ops[n][4] is None or ops[m][4] == ops[n][4] == "dma")
+
+
+def plan(ops, deps):
+    N = len(ops)
+    gap = lambda m, n: 0.0 if free(ops, m, n) else ops[m][6] + (0.0 if ops[n][0] == "X" else NOM["wake"])
+    way = [ops[n][5] + ops[n][6] for n in range(N)]
+    for n in range(N - 1, -1, -1):
+        for m in deps[n]: way[m] = max(way[m], ops[m][5] * OPT["w" + ops[m][0]] + gap(m, n) + way[n])
+    before = [[(m, gap(m, n)) for m in deps[n]] for n in range(N)]
+    after = [[] for n in range(N)]
+    for n in range(N):
+        for m, x in before[n]: after[m].append((n, x))
+
+    def lay(order, links, least):
+        end, taken = [0.0] * N, {}
+        for n in order:
+            t, c = max([end[m] + x for m, x in links[n]] + [least[n]]), ops[n][5]
+            slots = taken.setdefault(ops[n][0], [])
+            lo, hi = 0, len(slots)
+            while lo < hi:
+                mid = (lo + hi) // 2
+                if slots[mid][1] <= t: lo = mid + 1
+                else: hi = mid
+            while lo < len(slots) and slots[lo][0] < t + c:
+                t = max(t, slots[lo][1])
+                lo += 1
+            slots.insert(lo, (t, t + c))
+            end[n] = t + c
+        return end
+
+    order, best = sorted(range(N), key=lambda n: (-way[n], n)), None
+    for _ in range(OPT["passes"]):
+        end = lay(order, before, [0.0] * N)
+        total = max(end[n] + ops[n][6] for n in range(N))
+        if best is None or total < best[0]: best = (total, end)
+        back = lay(sorted(range(N), key=lambda n: (-end[n], -n)), after, [ops[n][6] for n in range(N)])
+        order = sorted(range(N), key=lambda n: (-back[n], n))
+    return sorted(range(N), key=lambda n: (best[1][n] - ops[n][5], n))
 
 
 def emit(g, T, ops):
     q = {"V": g.vector, "S": g.scalar, "P": g.tensor, "G": g, "Y": g.sync}
-    lastw, readers, deps = {}, {}, []
-    for n, (e, fn, rd, wr, kind) in enumerate(ops):
-        d = set()
-        for k in rd:
-            if k in lastw: d.add(lastw[k])
-            if k[0] == "#": d.update(m for m in readers.get(k, []) if ops[m][0] != e)
-        for k in wr:
-            for m in readers.get(k, []) + ([lastw[k]] if k in lastw else []):
-                if ops[m][0] != e or e != "P" or ops[m][4]: d.add(m)
-        for k in rd: readers.setdefault(k, []).append(n)
-        for k in wr:
-            lastw[k] = n
-            readers[k] = []
-        last = {}
-        for m in d:
-            key = ops[m][0] if not ops[m][4] else ("x", m)
-            last[key] = max(last.get(key, -1), m)
-        deps.append(sorted(last.values()))
-    need = set(m for d in deps for m in d)
-    sig, cnt, nd, seen = {}, {"V": 0, "S": 0, "P": 0, "G": 0}, [0], {}
-    final = {}
-    for n, (e, fn, rd, wr, kind) in enumerate(ops):
-        for m in deps[n]:
-            s, v = sig[m]
-            if seen.get((e, s), 0) < v:
-                q[e].wait_ge(T.sem[s], v)
-                seen[(e, s)] = v
+    if not PLAN:
+        deps = needs(ops)
+        order = plan(ops, deps)
+        place = {n: k for k, n in enumerate(order)}
+        waits = []
+        for n in range(len(ops)):
+            last = {}
+            for m in deps[n]:
+                if free(ops, m, n) or ops[n][0] == "X": continue
+                key = ("x", m) if ops[m][4] else ops[m][0]
+                if place[m] > place.get(last.get(key), -1): last[key] = m
+            waits.append(sorted(last.values(), key=lambda m: -place[m]))
+        PLAN.extend([order, waits])
+    order, waits = PLAN
+    need = set(m for d in waits for m in d)
+    sig, cnt, nd, final = {}, {"V": 0, "S": 0, "P": 0, "G": 0}, [0], {}
+    seen, knew = {e: {} for e in q}, {}
+    for n in order:
+        e, fn, kind = ops[n][0], ops[n][1], ops[n][4]
+        for m in waits[n]:
+            s, val = sig[m]
+            if seen[e].get(s, 0) < val:
+                q[e].wait_ge(T.sem[s], val)
+                seen[e][s] = val
+                for s2, v2 in knew[m].items():
+                    seen[e][s2] = max(seen[e].get(s2, 0), v2)
         if kind == "dma":
             s = "d%d" % nd[0]
             nd[0] += 1
             fn().then_inc(T.sem[s], 16)
             sig[n] = (s, 16)
-            final[s] = 16
         elif kind == "call":
             fn()
         elif kind:
-            sig[n] = kind
-            final[kind[0]] = kind[1]
+            sig[n] = kind[1:]
         else:
             ins = fn()
             if n in need:
                 cnt[e] += 1
                 ins.then_inc(T.sem["e" + e], 1)
                 sig[n] = ("e" + e, cnt[e])
-                final["e" + e] = cnt[e]
+        if n in sig:
+            final[sig[n][0]] = sig[n][1]
+            knew[n] = dict(seen[e]) if e != "X" else {}
     for s in final:
         g.wait_ge(T.sem[s], final[s])
 
@@ -98,445 +177,369 @@ def rank_program(g, core, T, topo):
     nxt, prv = cores[(rank + 1) % len(cores)], cores[(rank - 1) % len(cores)]
     rid, pid = topo.addr(nxt)[0], topo.addr(nxt)[1]
     n_out, n_in = len(topo.engines(core, nxt)), len(topo.engines(prv, core))
-    ops = []
+    ops, loaded = [], [0.0]
     V, S, P = g.vector, g.scalar, g.tensor
-    ps = [T["p%d" % b] for b in range(8)]
 
-    def ts(out, in0, s1, o0, s2=None, o1=None, r=(), w=()):
-        if o1 is None: ops.append(("V", lambda: V.tensor_scalar(out, in0, s1, None, o0), list(r), list(w), None))
-        else: ops.append(("V", lambda: V.tensor_scalar(out, in0, s1, s2, o0, o1), list(r), list(w), None))
+    def ap(x):
+        if not isinstance(x, tuple): return x
+        if x[0] == "at": return ap(x[1]).indirect(ap(x[2]))
+        return T[x[0]][x[4]:x[5], x[1]:x[2]:x[3]] if x[3] > 1 else T[x[0]][x[4]:x[5], x[1]:x[2]]
 
-    def tt(out, a, b, op, r, w): ops.append(("V", lambda: V.tensor_tensor(out, a, b, op), list(r), list(w), None))
-    def cp(out, a, r, w): ops.append(("V", lambda: V.tensor_copy(out, a), list(r), list(w), None))
-    def ms(ap, c, w): ops.append(("V", lambda: V.memset(ap, c), [], list(w), None))
-    def act(out, a, fn, r, w, **kw): ops.append(("S", lambda: S.activation(out, a, fn, **kw), list(r), list(w), None))
-    def mm(out, l, rh, st, sp, r, w): ops.append(("P", lambda: P.matmul(out, l, rh, st, sp), list(r), list(w), None))
-    def dma(e, out, a, r, w): ops.append((e, lambda: (g.sync if e == "Y" else S).dma_start(out, a), list(r), list(w), "dma"))
+    size = lambda x: 16 * size(x[2]) if x[0] == "at" else len(range(x[1], x[2], x[3]))
+    short = lambda x: SCRATCH[x[0]][2] in (bf, f16, u16)
 
-    def iota(out, pat, base, cm, w, small=True):
-        if small: ops.append(("G", lambda: g.iota(out, pat, base, cm, allow_small_or_imprecise_dtypes=True), [], list(w), None))
-        else: ops.append(("G", lambda: g.iota(out, pat, base, cm), [], list(w), None))
+    def add(e, fn, out, ins, kind=None, cost=None, lag=0.0, per=None):
+        rd, wr = [], []
+        for x in ins:
+            if isinstance(x, tuple): rd += [x[1], x[2]] if x[0] == "at" else [x]
+        if isinstance(out, tuple):
+            if out[0] == "at":
+                wr, rd = [out[1]], rd + [out[2]]
+            else: wr = [out]
+        if cost is None:
+            if out[0] == "at": cost = 55 + size(out) * NOM["scatter"] * NOM["cyc"]
+            elif ins and ins[0][0] == "at": cost = 55 + size(out) * NOM["gather"] * NOM["cyc"]
+            else:
+                if per is None: per = 0.5 if e == "V" and all(short(x) for x in [out] + ins[:1]) else 1.0
+                cost = max(64, size(out) * per) * NOM["cyc"]
+        ops.append((e, fn, rd, wr, kind, cost, lag))
 
-    K, XW, pc, pi, pj, w = T.K, T.XW, T.pc, T.pi, T.pj, T.w
-    KALL, H = ["K0", "K1", "K2", "K3", "K4", "K5"], [slice(0, 512), slice(512, 1024)]
-    XALL = ["XW%d" % c for c in range(8)]
-    col = lambda c, n=128: pc[0:n, c:c + 1]
+    def ts(out, a, s1, o0, s2=None, o1=None):
+        if o1 is None: add("V", lambda: V.tensor_scalar(ap(out), ap(a), ap(s1), None, o0), out, [a, s1])
+        else: add("V", lambda: V.tensor_scalar(ap(out), ap(a), ap(s1), ap(s2), o0, o1), out, [a, s1, s2])
 
-    dma("Y", K[:, 0:1024], T.nkey[:, 0:1024], [], ["K0", "K1"])
-    for h in range(2): dma("S", T["z0%d" % h][:], T.zin[:, H[h]], [], ["z0%d" % h])
-    dma("S", T.ci[:], T.cnt[:], [], ["ci"])
-    for c in range(4):
-        dma("Y", T.xb[:, 1024 * c:1024 * c + 1024], T.xreg[:, 1024 * c:1024 * c + 1024], [], ["xb%d" % c])
-        if c < 3: dma("Y", K[:, 1024 * c + 1024:1024 * c + 2048], T.nkey[:, 1024 * c + 1024:1024 * c + 2048], [], ["K%d" % (c + 2)] + (["K5"] if c == 2 else []))
+    def tt(out, a, b, op): add("V", lambda: V.tensor_tensor(ap(out), ap(a), ap(b), op), out, [a, b], per=2.0 if a[0] in SB and b[0] in SB else 1.0)
+    def cp(out, a): add("V", lambda: V.tensor_copy(ap(out), ap(a)), out, [a])
+    def ms(out, c): add("V", lambda: V.memset(ap(out), c), out, [])
 
-    io2, n256 = T.io2, T.n256
-    iota(pi[:, 0:1], [[0, 1]], 0, 1, ["pi0"], False)
-    iota(pi[:, 8:13], [[16, RO]], 0, 1, ["pi1"], False)
-    iota(n256[:], [[1, 256]], 0, 0, ["n256"])
-    iota(io2[:, 192:320], [[0, 8], [1, 16]], 0, 0, ["ioC"])
-    iota(io2[:, 64:192], [[1, 8], [0, 16]], 0, 0, ["ioB"])
-    iota(io2[:, 0:64], [[1, 32], [0, 2]], 0, 0, ["ioA"])
-    iota(pi[:, 16:48], [[2, 32]], 2, 1, ["pi2"], False)
-    iota(io2[:, 448:480], [[1, 8], [0, 4]], 0, 0, ["ioE"])
-    iota(io2[:, 320:448], [[0, 8], [1, 4], [0, 4]], 0, 0, ["ioD"])
-    iota(T.JD[:, 0:64], [[16, 64]], KW, 0, ["JD0"])
-    iota(T.JD[:, 64:128], [[0, 16], [16, 4]], D, 0, ["JD1"])
-    p0 = pi[:, 0:1]
-    bits = [(0, 127), (0, 15), (4, 7), (0, 3), (2, 31), (3, 7), (0, 1), (1, 3), (4, 1), (2, 7), (5, 3), (1, 15)]
-    cP, cA, cG, cM3, cP2, cGQ, cDUP, cMQ, cG1, cG4, cP5, cA2 = range(12)
-    for c, (sh, mk) in enumerate(bits): ts(pj[:, c:c + 1], p0, sh, A.arith_shift_right, mk, A.bitwise_and, ["pi0"], [])
-    ts(pj[:, 16:21], pi[:, 8:13], 4, A.arith_shift_right, 7, A.bitwise_and, ["pi1"], ["pjA"])
-    cp(pc[:, 0:12], pj[:, 0:12], ["pjA"], [])
-    cp(pc[:, 16:21], pj[:, 16:21], ["pjA"], ["c0"])
-    ts(pc[:, 24:29], n256[:, 0:5], -3.0, A.mult, col(cA), A.add, ["n256", "c0"], ["c1"])
-    ts(pc[:, 32:37], pc[:, 16:21], 4.0, A.mult, 300.0, A.add, ["c0"], ["c2"])
-    ts(pc[:, 14:15], col(cDUP), 2.0, A.mult, -1.0, A.add, ["c0"], [])
-    ts(pc[:, 15:16], col(cDUP), -1.0, A.add, r=["c0"], w=[])
-    ts(pc[:, 21:22], col(cA), 1.0, A.add, col(cA), A.mult, ["c0"], ["c3"])
-    ts(pc[:, 40:45], pc[:, 24:29], 0.0, A.is_ge, r=["c1"], w=[])
-    ts(pc[:, 48:53], pc[:, 24:29], 2.0, A.is_le, r=["c1"], w=["c4"])
-    ts(pc[:, 56:59], n256[:, 0:3], col(cMQ), A.is_equal, r=["c0"], w=["c5"])
-    tt(pc[:, 24:29], pc[:, 24:29], pc[:, 32:37], A.add, ["c1", "c2", "c4"], ["c1"])
-    ts(T.WB[:, 0:128], io2[:, 192:320], col(14), A.mult, col(15), A.add, ["ioC", "c3"], ["WB0"])
-    ts(T.WB[:, 128:256], io2[:, 64:192], col(cGQ), A.is_equal, r=["ioB", "c0"], w=["WB1"])
-    tt(pc[:, 40:45], pc[:, 40:45], pc[:, 48:53], A.mult, ["c4"], ["c4"])
-    ts(pc[:, 22:23], col(21), -BIG, A.mult, BIG, A.add, ["c3"], ["cMB"])
-    tt(T.WB[:, 0:128], T.WB[:, 0:128], T.WB[:, 128:256], A.mult, ["WB0", "WB1"], ["WB0"])
-    tt(pc[:, 24:29], pc[:, 24:29], pc[:, 40:45], A.mult, ["c1", "c4"], ["c1"])
-    ts(pj[:, 32:64], pi[:, 16:48], 127, A.bitwise_and, r=["pi2"], w=["pjB"])
-    ts(pc[:, 24:29], pc[:, 24:29], -300.0, A.add, r=["c1"], w=["c1"])
-    cp(pc[:, 192:224], pj[:, 32:64], ["pjB"], ["c11"])
-    ts(T.SQ[:, 0, :], io2[:, 0:64], col(24), A.is_equal, r=["ioA", "c1"], w=["SQ0"])
-    for m in range(3): ts(T.MK[:, m, :], T.WB[:, 0:128], col(56 + m), A.mult, r=["WB0", "c5"], w=["MK"] if m == 2 else [])
+    def act(out, a, fn, bias=None, scale=None):
+        kw = {k: x for k, x in (("bias", bias), ("scale", scale)) if x is not None}
+        add("S", lambda: S.activation(ap(out), ap(a), fn, **{k: ap(x) for k, x in kw.items()}), out, [a, bias, scale])
+
+    def mm(out, l, r, st, sp):
+        add("P", lambda: P.matmul(ap(out), ap(l), ap(r), st, sp), out, [l, r], cost=max(64, size(r)) * (1 if short(l) else 4) * NOM["pe"])
+
+    def dma(e, out, a):
+        x = out if isinstance(out, tuple) else a
+        n = size(x) * (x[5] - x[4]) * (2 if short(x) else 4) / NOM["rate"]
+        if x is out: loaded[0] += n
+        add(e, lambda: (g.sync if e == "Y" else S).dma_start(ap(out), ap(a)), out, [a], "dma", 50.0, NOM["dma"] + (loaded[0] if x is out else n))
+
+    def iota(out, pat, base, cm=0):
+        kw = {} if SB[out[0]][1] == i32 else {"allow_small_or_imprecise_dtypes": True}
+        add("G", lambda: g.iota(ap(out), pat, base, cm, **kw), out, [], cost=130 + 2 * size(out) * NOM["cyc"])
+
+    at = lambda win, off: ("at", win, off)
+    ps = lambda b, c0=0, c1=512, step=1, p0=0, p1=128: v("p%d" % b, c0, c1, step, p0, p1)
+    R = lambda name, h: v(name, 512 * h, 512 * h + 512)
+    W = lambda name, h, m=0: v(name, 64 * m + 32 * h, 64 * m + 32 * h + 32)
+    blk = lambda name, k, n: v(name, k * n, k * n + n)
+    part = lambda x, i, n: (x[0], x[1] + (x[2] - x[1]) // n * i, x[1] + (x[2] - x[1]) // n * (i + 1)) + x[3:]
+    col = lambda c: v("pc", c, c + 1)
+    pcs = lambda c, n: v("pc", c, c + n)
+    num = lambda a, b: v("n256", a, b)
+    z = lambda t, h: v("z%d%d" % (t, h))
+
+    for h in (1, 0):
+        dma("S", z(0, h), T.zin[:, 512 * h:512 * h + 512])
+        dma("Y", R("K", h), T.nkey[:, 512 * h:512 * h + 512])
+    dma("S", v("ci"), T.cnt[:])
+    for c in range(1, 4): dma("Y", blk("K", c, 1024), T.nkey[:, 1024 * c:1024 * c + 1024])
+    for c in range(4): dma("Y", blk("xb", c, 1024), T.xreg[:, 1024 * c:1024 * c + 1024])
+
+    ioA, ioB, ioC, ioD, ioE, ioR = v("io", 0, 64), v("io", 64, 192), v("io", 192, 320), v("io", 320, 448), v("io", 448, 480), 480
+    iota(v("pi", 0, 1), [[0, 1]], 0, 1)
+    iota(v("pi", 8, 13), [[16, RO]], 0, 1)
+    iota(v("n256"), [[1, 256]], 0)
+    iota(ioC, [[0, 8], [1, 16]], 0)
+    iota(ioB, [[1, 8], [0, 16]], 0)
+    iota(ioA, [[1, 32], [0, 2]], 0)
+    iota(ioE, [[1, 8], [0, 4]], 0)
+    iota(ioD, [[0, 8], [1, 4], [0, 4]], 0)
+    iota(v("pi", 16, 32), [[-1, 16]], 16, 1)
+    iota(v("pi", 32, 40), [[1, 8]], 1, 1)
+    for k, (c, n) in enumerate(((0, 3), (24, 2), (40, 1))):
+        iota(v("io", ioR + c, ioR + c + 8 * n), [[1, n], [4, 8]], k + 1)
+        iota(v("io", ioR + 48 + c, ioR + 48 + c + 8 * n), [[1, n], [4, 8]], 0)
+    for h in range(2): iota(W("JX", h), [[16, 32]], KW - D // 2 + 512 * (1 - h), 1)
+    bits = [(0, 127), (0, 15), (4, 7), (0, 3), (2, 31), (3, 7), (0, 1), (1, 3), (4, 3), (1, 7)]
+    cP, cA, cG, cM3, cP2, cGQ, cDUP, cMQ, cQ, cG2 = range(10)
+    for c, (sh, mk) in enumerate(bits): ts(v("pj", c, c + 1), v("pi", 0, 1), sh, A.arith_shift_right, mk, A.bitwise_and)
+    ts(v("pj", 10, 15), v("pi", 8, 13), 4, A.arith_shift_right, 7, A.bitwise_and)
+    ts(v("pj", 15, 16), v("pi", 0, 1), 6, A.arith_shift_right, 1, A.bitwise_and)
+    ts(v("pj", 16, 40), v("pi", 16, 40), 15, A.bitwise_and)
+    cp(pcs(0, 16), v("pj", 0, 16))
+    cp(pcs(96, 24), v("pj", 16, 40))
+    ts(pcs(64, 16), num(0, 16), col(cA), A.is_equal)
+    ts(col(21), col(cG), 16.0, A.mult)
+    ts(pcs(24, 5), num(0, 5), -3.0, A.mult, col(cA), A.add)
+    ts(pcs(32, 5), pcs(10, 5), 4.0, A.mult, 300.0, A.add)
+    ts(pcs(40, 5), pcs(24, 5), 0.0, A.is_ge)
+    ts(pcs(48, 5), pcs(24, 5), 2.0, A.is_le)
+    tt(pcs(32, 5), pcs(24, 5), pcs(32, 5), A.add)
+    tt(pcs(40, 5), pcs(40, 5), pcs(48, 5), A.mult)
+    tt(pcs(32, 5), pcs(32, 5), pcs(40, 5), A.mult)
+    ts(pcs(24, 5), pcs(32, 5), -300.0, A.add)
+    for t in range(RO): ts(blk("SQ", t, 64), ioA, col(24 + t), A.is_equal)
+    ts(col(16), col(cDUP), 2.0, A.mult, -1.0, A.add)
+    ts(col(17), col(cDUP), -1.0, A.add)
+    ts(col(18), col(cA), 1.0, A.add, col(cA), A.mult)
+    ts(col(19), col(18), -1.0, A.mult, 1.0, A.add)
+    ts(col(20), col(18), -BIG, A.mult, BIG, A.add)
+    ts(col(23), col(15), 4.0, A.mult, col(cMQ), A.add)
+    ts(pcs(56, 7), num(0, 7), col(23), A.is_equal)
+    ts(blk("WB", 0, 128), ioC, col(16), A.mult, col(17), A.add)
+    ts(blk("WB", 1, 128), ioB, col(cGQ), A.is_equal)
+    tt(blk("WB", 0, 128), blk("WB", 0, 128), blk("WB", 1, 128), A.mult)
+    for m in range(6): ts(blk("MK", m, 128), blk("WB", 0, 128), col(56 + m // 2 + 4 * (m % 2)), A.mult)
+    for k, wt in enumerate((1.0, 1.0 / D, 1.0 / BIG, 1.0 / BIG / D)): ts(blk("Sel", k, 32), ioE, col(cG), A.is_equal, wt, A.mult)
+    ts(v("Mq"), ioD, col(cM3), A.is_equal)
+    ts(v("Rb"), num(0, 32), col(cP2), A.is_equal)
+    ts(blk("Rh", 0, 32), num(0, 32), col(cP2), A.is_equal, -float(D), A.mult)
+    ts(blk("Rh", 1, 32), num(0, 32), col(cP2), A.is_equal)
+    ms(v("one", p1=32), 1.0)
+    ms(v("nil", p1=32), 0.0)
+    ts(pcs(80, 3), num(0, 3), col(cP), A.is_equal)
+    ts(col(83), col(80), float(HB), A.mult)
+    ts(col(84), col(81), -0.5, A.mult, col(83), A.add)
+    ts(col(85), col(82), 0.5 / D, A.mult, col(84), A.add)
+    ts(v("crow"), num(0, 256), 127.5, A.is_gt, col(85), A.mult)
+    ts(col(22), col(cP), 16.0, A.add)
+    for a in range(16): ts(blk("Z", a, 160), num(0, 160), col(22), A.is_equal, col(64 + a), A.mult)
+    cp(v("ch"), v("ci"))
+    ts(col(86), col(21), 16.0, A.add)
+    ts(col(87), col(cP), 128.0, A.add)
+    ts(col(88), col(64), -1.0, A.mult, 1.0, A.add)
+    ts(col(89), col(64), 512.0, A.mult)
+    ts(col(90), col(64), 15.0, A.mult, col(cP), A.add)
+    ts(col(91), col(64), col(66), A.add, 15.0, A.mult)
+    ts(col(92), col(64), 31.0, A.add)
+    ts(col(93), col(90), col(66), A.subtract)
+    ts(col(94), col(91), 1.0, A.add)
+    for k, wt in enumerate((1.0, -1.0 / D, -512.0 / D, 8192.0 / BIG, -8192.0 / BIG, -8192.0)):
+        ts(blk("Id", k, 128), num(0, 128), col(cP), A.is_equal, wt, A.mult)
+    ts(blk("Id", 6, 128), num(0, 128), col(cP), A.is_equal, col(64), A.mult)
+    ts(blk("Id", 7, 128), ioB, col(cG), A.is_equal, float(D), A.mult)
+    ts(blk("Y", 0, 144), num(0, 144), col(86), A.is_equal, col(64), A.mult)
+    ts(blk("Y", 1, 144), num(0, 144), col(86), A.is_equal, col(89), A.mult)
+    ts(blk("II", 0, 128), num(0, 128), col(cP), A.is_equal, col(88), A.mult)
+    ts(blk("II", 1, 128), num(128, 256), col(87), A.is_equal, col(88), A.mult)
+    ts(v("PK"), num(0, 128), col(93), A.is_equal, col(94), A.mult)
+    for a in range(16): ts(blk("L", a, 128), blk("Id", 7, 128), col(64 + a), A.mult)
+    for k in range(2):
+        for out, wt in (("RA", 1.0), ("RH", -float(D))):
+            ts(v(out, 80 * k, 80 * k + 48), v("io", ioR + 48 * k, ioR + 48 * k + 48), col(cP2), A.is_equal, wt, A.mult)
+            ts(v(out, 80 * k + 48, 80 * k + 80), num(0, 32), col(cP2), A.is_equal, wt, A.mult)
+    ts(v("JX"), v("JX"), col(21), A.subtract)
+    ts(pcs(120, 4), num(0, 4), 16.0, A.mult, col(cA), A.add)
+    ts(pcs(120, 4), pcs(120, 4), float(D // 2), A.add)
+    for t in range(RO): ts(v("PI", 128 * t, 128 * t + 128, p1=32), v("io", 192, 320, p1=32), float(t), A.not_equal, BIG, A.mult)
+    ts(v("PI", p1=32), v("PI", p1=32), -1.5 * D, A.add)
+    ms(v("XW", D, KW), 32.0)
+    ts(pcs(96, 16), pcs(96, 16), col(21), A.add)
+    ts(pcs(112, 8), pcs(112, 8), col(cA), A.max, col(21), A.add)
+    for s in range(16): ts(blk("SH", s, 128), num(0, 128), col(96 + s), A.is_equal)
+    for s in range(8): ts(blk("E", s, 128), num(0, 128), col(112 + s), A.is_equal)
+    ts(col(124), col(65), col(79), A.add)
+    ts(col(125), col(cG), 2.0, A.mult, col(79), A.add)
+    ts(col(126), col(cG), 4.0, A.mult, 1.0, A.add)
+    ts(pcs(136, 4), num(0, 4), 16.0, A.mult, col(125), A.add)
+    ts(pcs(136, 4), pcs(136, 4), 33.0, A.add, col(124), A.mult)
+    ts(pcs(140, 4), num(0, 4), col(126), A.add, col(64), A.mult)
+    tt(pcs(136, 4), pcs(136, 4), pcs(140, 4), A.add)
+    ts(pcs(136, 4), pcs(136, 4), -1.0, A.add)
+    for b in range(4): ts(blk("HX", b, 96), num(0, 96), col(136 + b), A.is_equal)
+    ts(col(127), col(cG2), 16.0, A.mult, 1.0, A.add)
+    ts(col(128), col(cP), 32.0, A.is_ge)
+    ts(col(144), col(cDUP), 14.0, A.mult, col(127), A.add)
+    ts(col(145), col(16), -1.0, A.mult, col(127), A.add)
+    ts(col(146), col(128), -16.0, A.mult)
+    ts(blk("HR", 4, 128), num(0, 128), col(144), A.is_equal, col(146), A.mult)
+    ts(blk("HR", 5, 128), num(0, 128), col(145), A.is_equal, col(128), A.mult)
+    tt(blk("HR", 4, 128), blk("HR", 4, 128), blk("HR", 5, 128), A.add)
+    ts(pcs(148, 4), num(0, 4), 2.0, A.add, col(cQ), A.subtract)
+    ts(pcs(152, 4), pcs(148, 4), 0.0, A.is_equal)
+    ts(pcs(156, 4), pcs(148, 4), 4.0, A.is_equal)
+    tt(pcs(152, 4), pcs(152, 4), pcs(156, 4), A.add)
+    for b in range(4): ts(blk("HR", b, 128), blk("HR", 4, 128), col(152 + b), A.mult)
+    ts(col(129), col(124), 2560.0, A.mult, -1.0, A.add)
+    ts(col(130), col(64), col(66), A.add, -160.0, A.mult)
+    ts(col(131), col(64), col(129), A.add, col(130), A.add)
+    ts(col(147), col(131), 16.0, A.mult)
+
+    Id = lambda k: blk("Id", k, 128)
 
     def front(t, h):
-        zn = "z%d%d" % (t, h)
-        mm(ps[7 - h][0:64, :], T.SQ[:, t, :], T[zn][:], True, True, [zn, "SQ%d" % t], ["#%d" % (7 - h)])
-        act(T.sq[0:64, H[h]], ps[7 - h][0:64, :], F.Square, ["#%d" % (7 - h), "c0", "c3"], ["sq%d" % h], bias=col(cDUP if t == 0 else 15, 64))
+        for q in range(2): mm(ps(7, 256 * h, 256 * h + 256, 1, 64 * q, 64 * q + 64), blk("SQ", t, 64), part(z(t, h), q, 2), True, True)
+        act(blk("sq", h, 256), ps(7, 256 * h, 256 * h + 256), F.Square, bias=col(cDUP if t == 0 else 17))
 
-    def front2(h):
-        mm(ps[2 + h][:, :], T.MK[0:64, 0, :], T.sq[0:64, H[h]], True, True, ["sq%d" % h, "MK"], ["#%d" % (2 + h)])
-        act(ps[2 + h][:, :], ps[2 + h][:, :], F.Relu, ["#%d" % (2 + h), "cMB"], ["#%d" % (2 + h)], bias=col(22), scale=BIG)
+    def mask(m, h, bank):
+        for q in range(2): mm(part(ps(bank), q, 2), blk("MK", 2 * m + q, 128), blk("sq", h, 256), True, True)
+        n = OPT["mp"]
+        for q in range(n):
+            if m < 2: act(part(ps(bank) if m == 0 else R("X1", h), q, n), part(ps(bank), q, n), F.Relu, bias=col(19))
+            else: act(part(R("X2", h), q, n), part(ps(bank), q, n), F.Relu, bias=col(20), scale=BIG)
 
-    def plus_one(c0, c1, k, e="V"):
-        if e == "V": ts(K[:, c0:c1], K[:, c0:c1], 1.0, A.add, r=[k], w=[k])
-        else: act(K[:, c0:c1], K[:, c0:c1], F.Identity, [k], [k], bias=1.0)
+    def masks(t):
+        for h in (1, 0):
+            front(t, h)
+            mask(0, h, 2 + h)
+        for m in (1, 2):
+            for h in (1, 0): mask(m, h, 7 - h)
 
-    front(0, 0)
-    front(0, 1)
-    front2(0)
-    front2(1)
-    for d in range(32): ts(T.Dm[:, d, :], n256[:, 0:128], col(192 + d), A.is_equal, -1.0, A.mult, ["c11"], ["Dm"] if d == 31 else [])
-    ops.append(("G", lambda: g.affine_select(T.Dm[:], T.Dm[:], [[0, 32], [1, 128]], A.not_equal, 1.0, 0, -1), ["Dm"], ["Dm"], None))
-    ts(T.Sel[:], io2[:, 448:480], col(cG), A.is_equal, r=["ioE", "c0"], w=["Sel"])
-    ts(T.Mq[:], io2[:, 320:448], col(cM3), A.is_equal, r=["ioD", "c0"], w=["Mq"])
-    ts(T.Rb[:], n256[:, 0:32], col(cP2), A.is_equal, r=["c0"], w=["Rb"])
-    ts(pc[:, 64:80], n256[:, 0:16], col(cA), A.is_equal, 64.0, A.mult, ["c0"], [])
-    ts(pc[:, 80:81], col(cP), 16.0, A.add, r=["c0"], w=[])
-    ts(pc[:, 81:82], col(cP), 128.0, A.add, r=["c0"], w=["c7"])
-    plus_one(0, 512, "K0")
-    plus_one(512, 1024, "K1")
-    ts(T.II[:, 0:128], n256[:, 0:128], col(cP), A.is_equal, r=["c0"], w=[])
-    ts(T.II[:, 128:256], n256[:, 128:256], col(81), A.is_equal, r=["c7"], w=["II"])
-    for a in range(16): ts(T.Z[:, a, :], n256[:, 0:160], col(80), A.is_equal, col(64 + a), A.mult, ["c7"], ["Z%d" % (a // 4)] if a % 4 == 3 else [])
+    def table(name, c, bank):
+        for a in (2 * c, 2 * c + 1):
+            o = part(ps(bank), a % 2, 2)
+            if name == "XW": mm(o, v("PK"), blk("xb", a, 256), True, False)
+            mm(o, v("Z", 160 * a + 16 + a, 160 * a + 144 + a), v("ch"), name == "CT", True)
+        act(blk(name, c, 512), ps(bank), F.Identity, bias=32.0 if name == "XW" else 1.0)
 
-    def later_constants(part):
-        if part == 0:
-            ts(T.cj[:, 0:256], T.ci[:], 15, A.bitwise_and, r=["ci"], w=[])
-            ts(T.cj[:, 256:512], T.ci[:], 4, A.arith_shift_right, r=["ci"], w=["cj"])
-            ms(XW[:, D:KW], 32.0, ["XWd"])
-            ts(T.ch[:], T.cj[:], 0.25, A.mult, r=["cj"], w=["ch"])
-        if part == 1:
-            ts(pc[:, 82:83], col(cG), 16.0, A.mult, 16.0, A.add, ["c0"], [])
-            ts(pc[:, 83:84], col(cA), 3.0, A.is_lt, r=["c0"], w=[])
-            ts(pc[:, 84:85], col(cA), 1.0, A.is_equal, 15.0, A.mult, ["c0"], [])
-            ts(pc[:, 85:86], col(cA), 2.0, A.is_equal, 16.0, A.mult, ["c0"], ["c8"])
-            ts(pc[:, 96:128], n256[:, 1:33], 2.0, A.mult, col(cP), A.is_gt, ["c0"], [])
-            ts(pc[:, 224:256], n256[:, 1:33], -2.0, A.mult, 128.0, A.add, [], ["c9"])
-            ts(pc[:, 86:87], col(83), col(84), A.add, r=["c8"], w=[])
-            ts(pc[:, 87:88], col(83), 16.0, A.mult, r=["c8"], w=[])
-            ts(pc[:, 88:89], col(83), -2560.0, A.mult, col(85), A.add, ["c8"], ["c10"])
-            ts(pc[:, 89:90], col(85), 31.0, A.add, r=["c8"], w=[])
-            tt(pc[:, 96:128], pc[:, 96:128], pc[:, 224:256], A.mult, ["c9"], ["c9"])
-            ts(T.Y[:], n256[:, 0:144], col(82), A.is_equal, col(86), A.mult, ["c8", "c10"], ["Y"])
-            ts(T.C16[:], n256[:, 0:128], col(cP), A.is_equal, col(87), A.mult, ["c10"], ["C16"])
-            ts(pc[:, 88:89], col(88), 32.0, A.add, r=["c10"], w=["cSB"])
-            ts(T.BO[:], io2[:, 64:192], col(cG), A.is_equal, r=["ioB"], w=["BO"])
-            ts(pc[:, 96:128], pc[:, 96:128], col(cP), A.add, r=["c9"], w=["c9"])
-        if part == 2:
-            ts(pc[:, 90:91], col(cA), 2.0, A.mult, col(cG1), A.add, ["c0"], [])
-            ts(pc[:, 91:92], col(cDUP), 16.0, A.mult, col(cA2), A.add, ["c0"], [])
-            ts(pc[:, 128:132], n256[:, 0:4], col(cP5), A.is_equal, r=["c0"], w=["c12"])
-            ts(T.JD[:], T.JD[:], col(cA), A.add, r=["JD0", "JD1"], w=["JD"])
-            ts(pc[:, 90:92], pc[:, 90:92], 96.0, A.add, r=["c12"], w=["c13"])
-            ts(T.I8[:], n256[:, 0:128], col(cP), A.is_equal, 8192.0, A.mult, ["c0"], ["I8"])
-            ms(T.one[0:32, :], 1.0, [])
-            ms(T.nil[0:32, :], 0.0, [])
-            ms(T.big[0:32, :], BIG, ["big"])
-            for G in range(4): ts(T.Pm[:, G, :], n256[:, 0:224], col(90), A.is_equal, col(128 + G), A.mult, ["c13"], ["Pm"] if G == 3 else [])
-            ts(T.Ih[:], n256[:, 0:128], col(cP), A.is_equal, r=["c0"], w=["Ih"])
-            ts(T.JD[:, 64:128], T.JD[:, 64:128], -2048.0, A.add, r=["JD"], w=["JD"])
-            ts(T.Pn[:], T.Pm[:], 8192.0, A.mult, r=["Pm"], w=["Pn"])
-            for G in range(4): ts(T.Pt[:, G, :], n256[:, 0:224], col(91), A.is_equal, col(128 + G), A.mult, ["c13"], ["Pt"] if G == 3 else [])
-        if part == 3:
-            for d in range(32): ts(T.E[:, d, :], n256[:, 0:128], col(96 + d), A.is_equal, r=["c9"], w=["E"] if d == 31 else [])
-        if part == 4:
-            ts(pc[:, 144:149], pc[:, 32:37], col(cA), A.add, col(83), A.mult, ["c2", "c8"], ["c14"])
-            ts(pc[:, 150:151], col(cG4), 16.0, A.mult, col(cM3), A.add, ["c0"], [])
-            ts(pc[:, 151:152], col(cM3), 3.0, A.is_lt, -16.0, A.mult, ["c0"], [])
-            ts(pc[:, 152:153], col(cG4), 8.0, A.mult, col(cP5), A.add, ["c0"], [])
-            ts(pc[:, 153:154], col(cM3), 1.0, A.is_equal, 15.0, A.mult, ["c0"], ["c15"])
-            for t in range(1, RO): ts(T.SQ[:, t, :], io2[:, 0:64], col(24 + t), A.is_equal, r=["ioA", "c1"], w=["SQ%d" % t])
-            ts(pc[:, 154:155], col(83), 2560.0, A.mult, -1.0, A.add, ["c8"], [])
-            ts(pc[:, 155:156], col(83), 40960.0, A.mult, -16.0, A.add, ["c8"], ["cZB"])
-            ts(pc[:, 144:149], pc[:, 144:149], -204.0, A.add, r=["c14"], w=["c14"])
-            ts(pc[:, 156:160], pc[:, 128:132], col(151), A.mult, r=["c15", "c12"], w=[])
-            ts(pc[:, 160:161], col(151), -0.0625, A.mult, col(153), A.add, ["c15"], ["c16"])
-            ts(T.HB[:, 4, :], n256[:, 0:128], col(150), A.is_equal, col(151), A.mult, ["c15"], [])
-            for t in range(RO): ts(T.HS[:, t, :], n256[:, 0:224], col(144 + t), A.is_equal, r=["c14"], w=["HS"] if t == RO - 1 else [])
-            for b in range(4): ts(T.HB[:, b, :], n256[:, 0:128], col(150), A.is_equal, col(156 + b), A.mult, ["c16"], ["HB"] if b == 3 else [])
-            ts(T.YC[:, 0:16], n256[:, 0:16], 0.0, A.mult, r=[], w=[])
-            ts(T.YC[:, 16:80], n256[:, 0:64], col(152), A.is_equal, col(160), A.mult, ["c16"], ["YC"])
+    Gs = ["Ga", "Gb", "Ga", "Ab"]
 
-    def build_xw(lo, hi):
-        for c in range(lo, hi):
-            bank = 6 + c % 2
-            for a in (2 * c, 2 * c + 1):
-                o = ps[bank][:, 256 * (a % 2):256 * (a % 2) + 256]
-                mm(o, T.II[:, 0:128], T.xb[:, 256 * a:256 * a + 256], True, False, ["II", "xb%d" % (c // 2)], ["#%d" % bank])
-                mm(o, T.Z[:, a, 16 + a:144 + a], T.ch[:, 0:256], False, False, ["Z%d" % (a // 4), "ch"], ["#%d" % bank])
-                mm(o, T.Z[:, a, 15 + a:143 + a], T.ch[:, 256:512], False, True, [], ["#%d" % bank])
-            act(XW[:, 512 * c:512 * c + 512], ps[bank][:, :], F.Identity, ["#%d" % bank], ["XW%d" % c], bias=32.0)
+    def gather(m, h):
+        n = OPT["fp"] if m == 0 else OPT["gp"]
+        for i in range(n):
+            if m == 0: tt(part(R("Ga", h), i, n), part(R("K", h), i, n), part(ps(2 + h), i, n), A.mult)
+            else: tt(part(R(Gs[m], h), i, n), at(v("K", 0, D), part(W("off", h, m - 1), i, n)), part(R("X1" if m == 1 else "X2", h), i, n),
+                     A.mult if m < 3 else A.subtract)
 
-    Gs, Gn = [T.Ga, T.Gb, T.Ga, T.Ab], ["Ga", "Gb", "Ga", "Ab"]
-    Xs = [None, T.X1, T.X2, T.X2]
-    Cg = [T.Cg0, T.Cg1, T.Cg2]
-    gk = lambda m, h: ["%s%d%d" % (Gn[m], h, i) for i in range(len(CUT) - 1)]
+    def turn(t, m, h):
+        mm(ps(h, 0, 256), v("one", 0, 128, p1=3), v("crow", p1=3), True, False)
+        for c in range(4): mm(ps(h, c, 256, 4), v(Gs[m], 512 * h + c, 512 * h + 512, 4), blk("Sel", m // 2, 64), False, c == 3)
+        tt(blk("H3", h, 128), ps(h, 128, 256), v("Mq"), A.mult)
+        tt(blk("T3", h, 128), ps(h, 0, 128), v("Mq"), A.mult)
+        mm(ps(h, 256, 288), blk("H3", h, 128), blk("Rh", 0, 32), True, False)
+        mm(ps(h, 256, 288), blk("T3", h, 128), v("Rb"), False, True)
+        mm(ps(2 + h, 0, 32), blk("H3", h, 128), blk("Rh", 1, 32), True, True)
+        ts(W("off", h, m), ps(h, 256, 288), PB, A.add)
+        if m == 1: ts(W("P1", h), ps(h, 256, 288), PB - D // 2, A.add, 1.0 / D, A.mult)
+        act(W("cab", h, m), ps(2 + h, 0, 32), F.Abs, bias=-(HB - 1.0) * D, scale=float(D))
+        win, b = (v("CT"), 0.0) if t == 0 else (v("XW", 0, D), -31.0)
+        if m == 2 and h == 1 and OPT["cgv"]:
+            act(part(R("Cg2", h), 0, 2), at(win, part(W("off", h, m), 0, 2)), F.Identity, bias=b)
+            ts(part(R("Cg2", h), 1, 2), at(win, part(W("off", h, m), 1, 2)), b, A.add)
+        else: act(R("Cg%d" % m, h), at(win, W("off", h, m)), F.Identity, bias=b)
 
-    def piece(m, h, i):
-        a, b = 32 * h + CUT[i], 32 * h + CUT[i + 1]
-        c = 64 * (m - 1)
-        tt(Gs[m][:, 16 * a:16 * b], K[:, 0:D].indirect(T.off[:, c + a:c + b]), Xs[m][:, 16 * a:16 * b], A.min if m < 3 else A.subtract,
-           KALL + ["off%d%d" % (m - 1, h), "X%d%d" % (min(m, 2), h)], [gk(m, h)[i]])
+    def check01(m):
+        for a in range(16): mm(ps(6, 0, 64), v("Y", 144 * m + 16 - a, 144 * m + 144 - a), v("Cg%d" % m, a, TH, 16), m == 0 and a == 0, False)
+        mm(ps(6, 0, 64), Id(1 + m), blk("cab", m, 64), False, m == 1)
 
-    def first(h):
-        tt(T.Ga[:, H[h]], K[:, H[h]], ps[2 + h][:, :], A.min, ["K%d" % h, "#%d" % (2 + h)], gk(0, h))
+    own = lambda h: v("AR", 160 * h + 128, 160 * h + 160)
+    wide = lambda s: 80 if 1 <= s <= 8 else 48
 
-    def mm1(m, h):
-        for c in range(4):
-            mm(ps[h][:, c:128:4], Gs[m][:, 512 * h + c:512 * h + 512:4], T.Sel[:], True, True, gk(m, h) + ["Sel"], ["#%d" % h])
+    def verdict(t, h):
+        o = ps(6, 64 + 32 * h, 96 + 32 * h)
+        mm(o, Id(1), W("cab", h, 2), True, False)
+        mm(o, Id(0), W("e01", h), False, False)
+        for a in range(16): mm(o, v("Y", 16 - a, 144 - a), v("Cg2", 512 * h + a, 512 * h + 512, 16), False, a == 15)
+        ts(W("nok", h), o, 0.0, A.not_equal, BIG, A.mult)
+        mm(ps(h, 320, 480), blk("T3", h, 128), v("RA"), True, False)
+        mm(ps(h, 320, 480), blk("H3", h, 128), v("RH"), False, False)
+        for k, (_, lo) in enumerate(PAIRS): mm(ps(h, 400 + 8 * k, 408 + 8 * k), Id(3), v("nok", 32 * h + lo, 32 * h + 32, 4), False, False)
+        mm(ps(h, 448, 480), Id(3), W("nok", h), False, False)
+        mm(ps(h, 368, 400), Id(4), W("nok", h), False, True)
+        ts(blk("AR", h, 160), ps(h, 320, 480), PB - D // 2, A.add)
+        mm(ps(2 + h), v("PK") if t == 0 else v("II", 128 - 16 * t, 256 - 16 * t), z(t, h), True, False)
+        mm(ps(2 + h), Id(6), R("Cg2", h), False, True)
+        act(v("XW", KW + 512 * (1 - h), KW + 512 * (2 - h)), ps(2 + h), F.Identity, bias=32.0 if t == 0 else col(92))
+        tt(W("w", h), own(h), W("JX", h), A.min)
+        ts(W("xoff", h), W("w", h), float(D // 2), A.add)
+        so = R("s%d" % t, h)
+        act(so, at(v("XW", 0, KW + 512 * (2 - h)), W("xoff", h)), F.Identity, bias=-31.0)
+        if t < RO - 1:
+            sem = "arr%d%d" % (t + 1, h)
+            add("G", lambda: g.remote_dma(ap(z(t + 1, h)), ap(so), T.sem[sem], T.sem.sent, pid, rid, topo.mask(core, nxt)), None, [so], "call", 600.0, NOM["hop"] - 600)
+            add("X", None, z(t + 1, h), [], ("arrival", sem, n_in), 1.0)
+        tt(W("pk", h), W("nok", h), W("cab", h, 2), A.subtract)
 
-    def turn(m, h):
-        tt(T.T3[:, 128 * h:128 * h + 128], ps[h][:, 0:128], T.Mq[:], A.mult, ["#%d" % h, "Mq"], ["T3%d" % h])
-        mm(ps[h][:, 128:160], T.T3[:, 128 * h:128 * h + 128], T.Rb[:], True, True, ["T3%d" % h, "Rb"], ["#%d" % h])
+    def winners(h, banks):
+        mm(ps(h, 0, 80), v("nil", p1=1), v("one", 0, 80, p1=1), True, False)
+        for k, bank in enumerate(banks):
+            for i, s in enumerate(TURNS[k]):
+                mm(ps(bank, 80 * i, 80 * i + wide(s)), blk("SH", s, 128), v("AR", 160 * h + 80, 160 * h + 80 + wide(s)), True, True)
+            for i, s in enumerate(TURNS[k]):
+                c = 1280 * h + 80 * s
+                tt(v("eq", c, c + wide(s)), ps(bank, 80 * i, 80 * i + wide(s)), v("AR", 160 * h, 160 * h + wide(s)), A.is_equal)
+                if wide(s) == 80: mm(ps(h, 48, 80), blk("E", s - 1, 128), v("eq", c + 48, c + 80), False, False)
+                mm(ps(h, 0, 48), Id(0), v("eq", c, c + 48), False, s == 15)
+        ts(blk("nd", h, 80), ps(h, 0, 80), 0.0, A.is_gt, 8192.0, A.mult)
+        mm(ps(h, 96, 128), Id(0), own(h), True, False)
+        for k, (hi, _) in enumerate(PAIRS): mm(ps(h, 96 + hi, 128, 4), Id(0), v("nd", 80 * h + 8 * k, 80 * h + 8 * k + 8), False, False)
+        mm(ps(h, 96, 128), Id(0), v("nd", 80 * h + 48, 80 * h + 80), False, True)
+        for i in range(4): ts(v("soff", 32 * h + i, 32 * h + 32, 4), ps(h, 96 + i, 128, 4), col(120 + i), A.min, float(D // 2), A.add)
 
-    def conv(m, h, i):
-        c = slice(64 * m + 32 * h, 64 * m + 32 * h + 32)
-        n = "%d%d" % (m, h)
-        if i == 0: ts(T.ki[:, c], ps[h][:, 128:160], -1.0, A.add, r=["#%d" % h], w=["ki" + n])
-        if i == 1: ts(T.pl[:, c], T.ki[:, c], D - 1, A.bitwise_and, r=["ki" + n], w=["pl" + n])
-        if i == 2: cp(T.off[:, c], T.pl[:, c], ["pl" + n], ["off" + n])
-
-    def half(x, y, extra=None, fill=(None, None, None)):
-        piece(x[0], x[1], 0)
-        turn(*y)
-        if extra: extra()
-        for i in range(3):
-            if i + 2 < len(CUT): piece(x[0], x[1], i + 1)
-            conv(y[0], y[1], i)
-            if fill[i]: fill[i]()
-        if x[0] < 3: mm1(*x)
-
-    def mask(m, b, bank, tensor=True, scalar=True):
-        if tensor: mm(ps[bank][:, :], T.MK[0:64, m, :], T.sq[0:64, H[b]], True, True, ["sq%d" % b, "MK"], ["#%d" % bank])
-        if scalar: act(Xs[m][:, H[b]], ps[bank][:, :], F.Relu, ["#%d" % bank, "cMB"], ["X%d%d" % (m, b)], bias=col(22), scale=BIG)
-
-    def cgather(m, hs):
-        for h in hs:
-            c = 64 * m + 32 * h
-            act(Cg[m][:, H[h]], XW[:, 0:D].indirect(T.off[:, c:c + 32]), F.Identity, XALL + ["off%d%d" % (m, h)], ["Cg%d%d" % (m, h)],
-                bias=160.0 - 39.5 / 16, scale=0.0625)
-
-    def count_w(m):
-        for a in range(16):
-            mm(ps[6][:, 64 * m:64 * m + 64], T.Y[:, 16 - a:144 - a], Cg[m][:, a:TH:16], a == 0, a == 15, ["Y", "Cg%d0" % m, "Cg%d1" % m, "Cg%d2" % m], ["#6"])
-
-    def k1r(qr):
-        bank = 4 + qr // 2
-        c = 256 * (qr % 2)
-        mm(ps[bank][:, c:c + 256], T.BO[:], T.Gb[:, 256 * qr:256 * qr + 256], True, True, ["BO"] + gk(1, qr // 2), ["#%d" % bank])
-
-    def high(src, t, bank, n, c0, down=False):
-        for b in range(4):
-            ap, name = src(b)
-            o = 32 * b if down else 96 - 32 * b
-            mm(ps[bank][:, 0:n], T.HS[:, t, o:o + 128], ap, b == 0, b == 3, ["HS", name], ["#%d" % bank])
-        act(T.hi[:, c0:c0 + n], ps[bank][:, 0:n], F.Identity, ["#%d" % bank], ["hi%d" % (c0 // 512)], bias=160.0 - 8.5 / 16, scale=0.0625)
-
-    def clean(src, t, strip, stop, move=True):
-        for b in range(2 if move else 0):
-            ap, name = src(b)
-            mm(ps[2 + b][:, :], T.II[:, 128 - 16 * t:256 - 16 * t], ap, True, stop and not strip, ["II", name], ["#%d" % (2 + b)])
-        if strip:
-            for b in range(4):
-                c = 256 * (b % 2)
-                mm(ps[2 + b // 2][:, c:c + 256], T.HB[:, b, :], T.hi[:, 0:256], False, stop and b % 2 == 1, ["HB", "hi0"], ["#%d" % (2 + b // 2)])
-
-    def xscatter(u):
-        act(XW[:, 0:KW].indirect(T.soff[:, 4 * u:4 * u + 4]), XW[:, KW + 64 * u:KW + 64 * u + 64], F.Silu, ["soff", "src0", "src1"], XALL + ["XWd"])
-
-    def diff(q):
-        bank = q % 2
-        for d in range(8 * q, 8 * q + 8):
-            mm(ps[bank][:, 64 * (d % 8):64 * (d % 8) + 64], T.Dm[:, d, :], T.Sx[:], True, True, ["Dm", "Sx"], ["#%d" % bank])
-
-    def equal(q):
-        ts(T.eq[:, 512 * q:512 * q + 512], ps[q % 2][:, :], 0.0, A.is_equal, r=["#%d" % (q % 2)], w=["eq%d" % q])
-
-    def fold(q):
-        for d in range(8 * q, 8 * q + 8):
-            mm(ps[7][:, 0:64], T.E[:, d, :], T.eq[:, 64 * d:64 * d + 64], d == 0, d == 31, ["E", "eq%d" % q], ["#7"])
-
-    def bpiece(u):
-        c = slice(64 * u, 64 * u + 64)
-        tt(T.Bb[:, c], ps[4 + u // 8][:, 64 * (u % 8):64 * (u % 8) + 64], T.X2[:, c], A.min, ["#%d" % (4 + u // 8), "X2%d" % (u // 8)], ["Bb%d" % u])
-
-    def new_key(b, t, bank):
-        mm(ps[bank][:, :], T.one[0:1, :], T.big[0:1, :], True, False, ["big"], ["#%d" % bank])
-        for a in range(16):
-            for part in (1, 0):
-                c = 64 * part + 32 * b
-                mm(ps[bank][:, a:512:16], T.Z[:, a, 16 + a - t:144 + a - t], T.P12[:, c:c + 32], False, a == 15 and part == 0,
-                   ["P1", "P2"], ["#%d" % bank])
-
-    for t in range(RO):
-        last = t == RO - 1
-        zh = lambda b, t=t: (T["z%d%d" % (t, b)][:], "z%d%d" % (t, b))
-        if t == 0:
-            for m in (1, 2):
-                for b in range(2): mask(m, b, 4 + b)
-            later_constants(0)
-            plus_one(1024, 2048, "K2", "S")
-            build_xw(0, 2)
-        first(0)
-        mm1(0, 0)
-        first(1)
-        if t == 0:
-            later_constants(1)
-            build_xw(2, 4)
-        turn(0, 0)
-        mm1(0, 1)
-        if t == 0:
-            later_constants(2)
-            build_xw(4, 6)
-        clean(zh, t, False, False)
-        for i in range(3): conv(0, 0, i)
-        if t == 0:
-            plus_one(2048, 3072, "K3")
-            later_constants(3)
-            plus_one(3072, 3584, "K4")
-            plus_one(3584, 4096, "K5", "S")
-            build_xw(6, 8)
-        half((1, 0), (0, 1), lambda: clean(zh, t, t > 0, False, False))
-        cgather(0, (0, 1))
-        half((1, 1), (1, 0), lambda: k1r(1))
-        cgather(1, (0,))
-        half((2, 0), (1, 1), lambda: k1r(3))
-        cgather(1, (1,))
-        half((2, 1), (2, 0), lambda: count_w(0),
-             (lambda: ts(T.cn[:, 0:128], T.ki[:, 0:128], 12, A.arith_shift_right, 255, A.bitwise_and, ["ki00", "ki01", "ki10", "ki11"], ["cn0"]),
-              lambda: ts(T.tg[:, 0:128], T.cn[:, 0:128], 2880.0, A.add, r=["cn0"], w=["tg0"]), None))
-        cgather(2, (0,))
-        half((3, 0), (2, 1), lambda: (count_w(1), k1r(2)),
-             (None,
-              lambda: ts(T.cn[:, 128:192], T.ki[:, 128:192], 12, A.arith_shift_right, 255, A.bitwise_and, ["ki20", "ki21"], ["cn2"]),
-              lambda: tt(T.e01[:], ps[6][:, 0:128], T.tg[:, 0:128], A.is_equal, ["#6", "tg0"], ["e01"])))
-        act(T.Cg2[:, 512:768], XW[:, 0:D].indirect(T.off[:, 160:176]), F.Identity, XALL + ["off21"], ["Cg21"], bias=160.0 - 39.5 / 16, scale=0.0625)
-        ts(T.Cg2[:, 768:TH], XW[:, 0:D].indirect(T.off[:, 176:192]), 0.0625, A.mult, 160.0 - 39.5 / 16, A.add, XALL + ["off21"], ["Cg22"])
-        ts(T.Q[:], T.pl[:, 128:192], -2048.0, A.add, r=["pl20", "pl21"], w=["Q"])
-        mm(ps[2][:, :], T.C16[:], T.Cg2[:, H[0]], False, True, ["C16", "Cg20"], ["#2"])
-        count_w(2)
-        mm(ps[7][:, 0:64], T.nil[0:1, :], T.big[0:1, 0:64], True, False, ["big"], ["#7"])
-        for G in range(4):
-            for h in range(4):
-                mm(ps[7][:, G:64:4], T.Pm[:, G, 96 - 32 * h:224 - 32 * h], T.Q[:, h:64:4], False, False, ["Pm", "Q"], ["#7"])
-        mm(ps[3][:, :], T.C16[:], T.Cg2[:, H[1]], False, True, ["C16", "Cg21", "Cg22"], ["#3"])
+    def back():
+        ts(v("cB"), blk("cab", 1, 64), 1.0 / D, A.mult, -1024.5, A.add)
         for b in range(2):
-            act(XW[:, KW + 512 * b:KW + 512 * b + 512], ps[2 + b][:, :], F.Identity, ["#%d" % (2 + b), "cSB"], ["src%d" % b], bias=col(88 if t == 0 else 89))
-        ts(T.tg[:, 128:192], T.cn[:, 128:192], 2880.0, A.add, r=["cn2"], w=["tg2"])
-        tt(w[:, 0, :], T.e01[:, 0:64], T.e01[:, 64:128], A.mult, ["e01"], ["w0"])
-        piece(3, 1, 0)
-        tt(T.tg[:, 128:192], T.tg[:, 128:192], w[:, 0, :], A.mult, ["w0", "tg2"], ["tg2"])
-        ts(w[:, 6, :], T.pl[:, 128:192], -1.0 / 64, A.mult, 2047.0 / 64, A.add, ["pl20", "pl21"], ["w6"])
-        ts(w[:, 7, :], T.cn[:, 128:192], -64.0, A.mult, -1027.0 * 32, A.add, ["cn2"], ["w7"])
-        tt(T.nok[:], ps[6][:, 128:192], T.tg[:, 128:192], A.not_equal, ["#6", "tg2"], ["nok"])
-        for G in range(4):
-            for h in range(4):
-                mm(ps[7][:, G:64:4], T.Pn[:, G, 96 - 32 * h:224 - 32 * h], T.nok[:, h:64:4], False, G + h == 6, ["Pn", "nok"], ["#7"])
-        tt(w[:, 4, :], ps[6][:, 128:192], T.tg[:, 128:192], A.is_equal, ["#6", "tg2"], ["w4"])
-        tt(w[:, 3, :], T.nok[:], T.JD[:, 0:64], A.mult, ["nok", "JD"], ["w3"])
-        piece(3, 1, 1)
-        tt(w[:, 3, :], w[:, 3, :], T.pl[:, 128:192], A.max, ["w3", "pl20", "pl21"], ["w3"])
-        bpiece(15)
-        cp(T.xoff[:], w[:, 3, :], ["w3"], ["xoff"])
-        cp(T.Sx[:], ps[7][:, 0:64], ["#7"], ["Sx"])
-        diff(0)
-        diff(1)
-        so = T["s%d" % t]
-        for h in range(2):
-            act(so[:, H[h]], XW[:, 0:KW + TH].indirect(T.xoff[:, 32 * h:32 * h + 32]), F.Identity, XALL + ["XWd", "src0", "src1", "xoff"],
-                ["s%d%d" % (t, h)], bias=-31.0)
-            if not last:
-                zn, sem = "z%d%d" % (t + 1, h), "arr%d%d" % (t + 1, h)
-                ops.append(("G", lambda zn=zn, sem=sem, src=so[:, H[h]]: g.remote_dma(T[zn][:], src, T.sem[sem], T.sem.sent, pid, rid, topo.mask(core, nxt)),
-                            ["s%d%d" % (t, h)], [], "call"))
-                ops.append(("P", None, [], [zn], (sem, n_in)))
-        for i in range(2, len(CUT) - 1): piece(3, 1, i)
-        equal(0)
-        diff(2)
-        fold(0)
-        equal(1)
-        diff(3)
-        fold(1)
-        equal(2)
-        fold(2)
-        equal(3)
-        fold(3)
-        tt(T.P12[:, 0:64], w[:, 6, :], w[:, 4, :], A.mult, ["w6", "w4"], ["P1"])
-        tt(T.P12[:, 64:128], w[:, 7, :], w[:, 4, :], A.mult, ["w7", "w4"], ["P2"])
-        mm(ps[6][:, 0:64], T.Ih[:], T.Q[:], True, False, ["Ih", "Q"], ["#6"])
-        mm(ps[6][:, 0:64], T.I8[:], T.nok[:], False, False, ["I8", "nok"], ["#6"])
-        ts(T.nd[:], ps[7][:, 0:64], 0.0, A.is_gt, 8192.0, A.mult, ["#7"], ["nd"])
-        for h in range(4):
-            for G in range(4):
-                mm(ps[6][:, h:64:4], T.Pt[:, h, 96 - 32 * G:224 - 32 * G], T.nd[:, G:64:4], False, G + h == 6, ["Pt", "nd"], ["#6"])
-        k1r(0)
-        for u in range(14, 8, -1): bpiece(u)
-        if last:
-            high(lambda b: (so[:, 256 * b:256 * b + 256], "s4%d" % (b // 2)), 0, 7, 256, 0)
-            new_key(0, t, 0)
-            clean(lambda b: (so[:, H[b]], "s4%d" % b), 0, True, True)
-            new_key(1, t, 1)
-        tt(w[:, 5, :], ps[6][:, 0:64], T.JD[:, 64:128], A.min, ["JD", "#6"], ["w5"])
-        bpiece(8)
-        ts(T.soff[:], w[:, 5, :], 2048.0, A.add, r=["w5"], w=["soff"])
-        s0 = len(ops)
-        if t == 0: later_constants(4)
-        fill = ops[s0:]
-        del ops[s0:]
-        for u in range(NR - 1, -1, -1):
-            c = slice(64 * u, 64 * u + 64)
-            tt(K[:, 0:KW].indirect(T.soff[:, 4 * u:4 * u + 4]), T.Ab[:, c], T.Bb[:, c], A.max, ["soff", "Bb%d" % u] + gk(3, u // 8), KALL)
-            if 6 < u < 15: bpiece(u - 7)
-            ops.extend(fill[2 * (NR - 1 - u):2 * (NR - u)])
-        zq = lambda b, t=t + 1: (T["z%d%d" % (t, b // 2)][:, 256 * (b % 2):256 * (b % 2) + 256], "z%d%d" % (t, b // 2))
-        absk = lambda b: act(K[:, H[b]], K[:, H[b]], F.Abs, ["K%d" % b], ["K%d" % b])
+            for a in range(8):
+                mm(part(ps(4 + b), a, 8), blk("L", 8 * b + a, 128), v("P1"), True, False)
+                mm(part(ps(4 + b), a, 8), blk("L", 8 * b + a, 128), v("cB"), False, True)
+            for a in range(8): tt(v("Bb", 8 * b + a, TH, 16), part(ps(4 + b), a, 8), v("X2", 8 * b + a, TH, 16), A.add)
 
-        def new_row():
-            for b in range(2):
-                tt(K[:, H[b]], K[:, H[b]], ps[b][:, :], A.min, ["K%d" % b, "#%d" % b], ["K%d" % b])
-            absk(0)
+    def new_key(t, h):
+        mm(ps(4 + h), v("PI", 128 * t, 128 * t + 128, p1=1), v("one", p1=1), True, False)
+        for a in range(16):
+            l = v("Z", 160 * a + 16 + a - t, 160 * a + 144 + a - t)
+            mm(ps(4 + h, a, 512, 16), l, own(h), False, False)
+            mm(ps(4 + h, a, 512, 16), l, W("pk", h), False, a == 15)
 
-        if not last:
-            steps = {0: lambda: new_key(0, t, 0), 3: lambda: front(t + 1, 0), 4: lambda: (front(t + 1, 1), front2(0)), 5: lambda: front2(1),
-                     6: lambda: (mask(1, 0, 4), mask(1, 1, 5, True, False), new_key(1, t, 1), mask(2, 0, 6, True, False), mask(2, 1, 7, True, False)),
-                     7: lambda: (new_row(), absk(1), mask(1, 1, 5, False)), 8: lambda: high(zq, t + 1, 4, 256, 0),
-                     10: lambda: mask(2, 0, 6, False), 12: lambda: mask(2, 1, 7, False)}
-        else:
-            oz = lambda b: act(T.oz[:, H[b]], ps[2 + b][:, :], F.Identity, ["#%d" % (2 + b), "cZB"], ["oz%d" % b], bias=col(154))
-            steps = {4: lambda: oz(0), 5: lambda: (oz(1), dma("Y", T.yz[:], T.oz[:], ["oz0", "oz1"], [])), 12: new_row, 13: lambda: absk(1)}
-        for n in range(NR):
-            xscatter(NR - 1 - n)
-            if n in steps: steps[n]()
+    def stack(src, n, bank, c0, order=(0, 1, 2, 3)):
+        for b in order: mm(ps(bank, 0, n, 1, 0, 96), blk("HX", b, 96), src(b), b == order[0], b == order[3])
+        act(v("hi", c0, c0 + n, 1, 0, 96), ps(bank, 0, n, 1, 0, 96), F.Identity, bias=160.0 - 8.5 / 16, scale=0.0625)
 
-    vb = lambda c: (T.xb[:, 512 * c:512 * c + 512], "v%d" % (c // 2))
-    for b in range(2): cp(ps[4 + b][:, 0:256], K[:, 1024 + 256 * b:1280 + 256 * b], ["K2"], ["#%d" % (4 + b)])
-    for c in list(range(6, 16)) + [0, 1, 2, 3]:
-        b = 4 + c % 2
-        if c == 0: ts(T.xb[:, 0:1024], XW[:, 0:1024], -31.0, A.add, r=XALL, w=["v0", "xb0"])
-        tt(ps[b][:, 0:256], K[:, 256 * c:256 * c + 256], ps[b][:, 0:256], A.add, ["#%d" % b] + (["K%d" % (c // 2)] if c < 4 else []), ["#%d" % b])
-    ts(T.okk[:, 0:256], ps[4][:, 0:256], -16.0, A.add, r=["#4"], w=["ok0"])
-    tt(T.okk[:, 256:512], T.okk[:, 0:256], ps[5][:, 0:256], A.add, ["ok0", "#5"], ["ok1"])
-    dma("Y", T.yk[:], T.okk[:, 256:512], ["ok1"], [])
+    masks(0)
+    for c in range(8): table("CT", c, 4 + c % 2)
+    for t in range(RO):
+        for m in range(3):
+            for h in (1, 0):
+                gather(m, h)
+                turn(t, m, h)
+            if m < 2: check01(m)
+            if m == 1:
+                ts(v("e01"), ps(6, 0, 64), 0.0, A.not_equal, 1024.0, A.mult)
+                back()
+            if t == 0 and m == 0:
+                for c in range(8): table("XW", c, (7, 4, 5)[c % 3] if c < 6 else 7)
+        for h in (1, 0):
+            gather(3, h)
+            verdict(t, h)
+        winners(1, (7, 4, 5))
+        winners(0, (7, 4, 5))
+        for h in (1, 0): new_key(t, h)
+        for u in range(15, -1, -1):
+            tt(at(v("K"), blk("soff", u, 4)), blk("Ab", u, 64), blk("Bb", u, 64), A.max)
+            c = KW + (64 * u + 512) % TH
+            act(at(v("XW", 0, KW), blk("soff", u, 4)), v("XW", c, c + 64), F.Silu)
+        for h in (1, 0):
+            for i in range(OPT["fp"]): tt(part(R("K", h), i, OPT["fp"]), part(R("K", h), i, OPT["fp"]), part(ps(4 + h), i, OPT["fp"]), A.min)
+        if t < RO - 1: masks(t + 1)
 
-    def sum_x(a0, a1):
-        for a in range(a0, a1):
-            mm(ps[0][:, 0:256], T.II[:, 0:128], T.xb[:, 256 * a:256 * a + 256], a == 12, False, ["v%d" % (a // 4)], ["#0"])
-
-    for b in (3, 2, 1):
-        act(T.xb[:, 1024 * b:1024 * b + 1024], XW[:, 1024 * b:1024 * b + 1024], F.Identity, XALL, ["v%d" % b, "xb%d" % b], bias=-31.0)
-        if b == 3: sum_x(12, 16)
-    high(lambda c: vb(7 - c), 0, 7, 512, 512, True)
-    high(vb, 0, 6, 512, 0)
-    sum_x(4, 12)
-    for b in (1, 0):
-        mm(ps[2][0:64, :], T.YC[:, 16 - 4 * b:80 - 4 * b], T.hi[:, H[b]], b == 1, b == 0, ["YC", "hi%d" % b], ["#2"])
-    sum_x(0, 4)
-    for b in (3, 2, 1, 0):
-        mm(ps[0][:, 0:256], T.HB[:, 4, :], T.hi[:, 256 * b:256 * b + 256], False, b == 0, ["HB", "hi%d" % (b // 2)], ["#0"])
-    act(T.oc[0:64, :], ps[2][0:64, :], F.Identity, ["#2"], ["oc"], bias=-2880.0)
-    ts(T.ox[:], ps[0][:, 0:256], col(155), A.add, r=["#0", "cZB"], w=["ox"])
-    dma("S", T.yc[:], T.oc[0:64, :], ["oc"], [])
-    dma("Y", T.yx[:], T.ox[:], ["ox"], [])
+    stack(lambda b: blk("s4", b, 256), 256, 7, 0)
+    for h in (1, 0):
+        mm(ps(2 + h), blk("II", 1, 128), R("s4", h), True, False)
+        for b in range(2): mm(part(ps(2 + h), b, 2), v("HR", 128 * (2 * h + b), 128 * (2 * h + b + 1), p1=96), v("hi", 0, 256, p1=96), False, b == 1)
+        for b in range(2): act(part(R("oz", h), b, 2), part(ps(2 + h), b, 2), F.Identity, bias=col(131))
+    dma("Y", T.yz[:], v("oz"))
+    for h in (1, 0):
+        ts(R("Hk", h), R("K", h), 1.0 / D, A.mult, HB - 0.5 + 0.5 / D, A.add)
+        ts(R("Hn", h), R("Hk", h), 1.0 - HB, A.add, 0.0, A.min)
+    for b in (3, 2, 1, 0): mm(ps(4, 0, 256), Id(5), blk("Hn", b, 256), b == 3, b == 0)
+    cp(ps(1, 0, 256), blk("K", 15, 256))
+    for b in range(14, 5, -1): tt(ps(1, 0, 256), blk("K", b, 256), ps(1, 0, 256), A.add)
+    cp(blk("okk", 0, 256), ps(1, 0, 256))
+    for b in range(6): tt(ps(4, 0, 256), blk("K", b, 256), ps(4, 0, 256), A.add)
+    tt(blk("okk", 1, 256), blk("okk", 0, 256), ps(4, 0, 256), A.add)
+    dma("Y", T.yk[:], blk("okk", 1, 256))
+    ts(blk("xb", 0, 1024), blk("XW", 0, 1024), -31.0, A.add)
+    for b in (3, 2, 1): act(blk("xb", b, 1024), blk("XW", b, 1024), F.Identity, bias=-31.0)
+    for e in range(2):
+        stack(lambda b: blk("xb", 2 * b + e, 512), 512, 6 + e, 512 * e, (3, 2, 0, 1))
+        ts(v("oc", 512 * e, 512 * e + 512, p1=32), ps(6 + e, p1=32), -1.0, A.add)
+    dma("S", T.yc[:], v("oc", p1=32))
+    for b in (3, 2, 0, 1):
+        for a in range(4 * b, 4 * b + 4): mm(ps(0, 0, 256), blk("II", 1, 128), blk("xb", a, 256), a == 12, False)
+    for b in range(4): mm(ps(0, 0, 256), v("HR", 512, 640, p1=96), v("hi", 256 * b, 256 * b + 256, p1=96), False, b == 3)
+    ts(v("ox"), ps(0, 0, 256), col(147), A.add)
+    dma("Y", T.yx[:], v("ox"))
     emit(g, T, ops)
     g.wait_ge(T.sem.sent, 2 * n_out * (RO - 1))

@@ -7,32 +7,36 @@ HB = 1600
 PB = float(HB * D)
 PAIRS = ((1, 0), (2, 1), (3, 2), (2, 0), (3, 1), (3, 0))
 TURNS = ((1, 2, 3, 4, 5, 6), (7, 8, 0, 9, 10), (11, 12, 13, 14, 15))
-NOM = dict(cyc=0.83, pe=0.42, gather=1.5, scatter=3.5, wake=220.0, dma=1800.0, rate=200.0, hop=3400.0)
-OPT = dict(cgv=1, gp=2, mp=2, fp=2, passes=4, wV=0.7, wS=1.5, wP=1.0, wG=1.0, wY=1.0, wX=1.0)
+NOM = dict(cyc=0.83, pe=0.42, gather=1.5, scatter=3.5, wake=220.0, dma=1800.0, rate=300.0, hop=3400.0, once=2000.0)
+OPT = dict(x0=1, xs=1.0, ar=2, hp=1, xl=4, sh=0, ga=2, sq=1, xq=0, sb=2, bb=(4, 5), wb=((7, 4, 5), (7, 4, 5)), xw=((7, 4, 5), (7,), (2, 3, 6, 2)), ls=0, bs=0, ns=0, es=0, bg=0, nw=0, two=0, mv=0, cap=230, eh=0, npe=4, xv=1, ocv=0, cgv=1, gp=2, mp=2, fp=2, passes=4, wV=0.7, wS=1.5, wP=1.0, wG=1.0, wY=1.0, wX=1.0)
 
 f32, bf, i32, u16, f16 = "float32", "bfloat16", "int32", "uint16", "float16"
 SB = {
-    "K": (KW, f32), "XW": (KW + TH, f32), "xb": (D, bf), "CT": (D, bf), "ci": (256, i32), "ch": (256, bf),
+    "K": (KW, f32), "XW": (KW + TH, f32), "xb": (KW + TH, bf), "CT": (D, bf), "ci": (256, i32), "ch": (256, bf),
     "Ga": (TH, f32), "Gb": (TH, f32), "Ab": (TH, f32), "Bb": (TH, f32), "X1": (TH, bf), "X2": (TH, bf),
     "Cg0": (TH, bf), "Cg1": (TH, bf), "Cg2": (TH, bf), "eq": (2560, bf), "sq": (512, bf), "hi": (TH, bf),
-    "T3": (256, f32), "H3": (256, f16), "off": (192, u16), "cab": (192, bf), "P1": (64, f16), "cB": (64, f16),
-    "e01": (64, bf), "nok": (64, bf), "AR": (320, f16), "nd": (160, bf), "pk": (64, bf), "w": (64, f32),
+    "T3": (256, f32), "H3": (768, f16), "off": (192, u16), "cab": (192, bf), "P1": (64, f16), "cB": (64, f16),
+    "e01": (64, bf), "nok": (64, bf), "AR": (320, f16), "nd": (160, bf), "pk": (64, bf), "w": (128, f32),
+    "Qn": (64, f16), "e0": (64, bf), "nk8": (64, bf), "CA": (320, bf), "XH": (160, f32), "IF": (128, f32),
     "xoff": (64, u16), "soff": (64, u16), "Hk": (TH, f16), "Hn": (TH, f16),
-    "oz": (TH, bf), "okk": (512, f32), "ox": (256, bf), "oc": (TH, f32),
-    "pi": (48, i32), "pj": (48, i32), "pc": (160, f32), "n256": (256, bf), "io": (576, bf), "JX": (64, f32),
-    "Sel": (128, f32), "Mq": (128, f32), "Rb": (32, f32), "Rh": (64, bf), "RA": (160, f32), "RH": (160, bf),
+    "oz": (TH, bf), "okk": (512, f32), "ox": (256, bf), "oc": (512, f32),
+    "pi": (48, i32), "pj": (48, i32), "pc": (192, f32), "n256": (256, bf), "io": (576, bf), "JX": (64, f32),
+    "Sel": (128, f32), "Mq": (128, f32), "Rb": (32, f32), "Rh": (64, bf), "RA": (160, f32), "RH": (320, bf),
     "crow": (256, bf), "one": (512, bf), "nil": (128, bf), "PI": (RO * 128, bf), "WB": (256, bf), "MK": (768, bf),
-    "SQ": (RO * 64, bf), "Y": (288, bf), "Id": (8 * 128, bf), "II": (256, bf), "PK": (128, bf), "Z": (16 * 160, bf),
-    "L": (16 * 128, bf), "SH": (16 * 128, bf), "E": (8 * 128, bf), "HX": (4 * 96, bf), "HR": (6 * 128, bf),
+    "SQ": (RO * 64, bf), "Y": (288, bf), "Id": (8 * 128, bf), "II": (256, bf), "PK": (256, bf), "Z": (16 * 160, bf),
+    "BR": (512, bf), "L": (16 * 128, bf), "SH": (16 * 128, bf), "E": (15 * 128, bf), "HX": (136, bf), "HR": (10 * 128, bf),
 }
 for _t in range(RO):
     SB["s%d" % _t] = (TH, bf)
-    for _h in range(2):
+    for _h in range(2 if _t else 0):
         SB["z%d%d" % (_t, _h)] = (TH // 2, bf)
 SCRATCH = {n: ("sbuf", [128, c], d) for n, (c, d) in SB.items()}
 for _b in range(8):
     SCRATCH["p%d" % _b] = ("psum", [128, 512], f32)
-SEMAPHORES = ["eV", "eS", "eP", "eG", "sent"] + ["arr%d%d" % (t, h) for t in range(1, RO) for h in range(2)] + ["d%d" % k for k in range(24)]
+SEMAPHORES = ["eV", "eS", "eP", "eG", "sent"] + ["arr%d%d%d" % (t, h, q) for t in range(1, RO) for h in range(2) for q in range(2)] + ["d%d" % k for k in range(24)]
+RANK = ["hop", "count", "last1", "fault1", "win1", "last0", "fault0", "old", "back", "leave1", "leave0", "win0", "run", "row", "xrun", "mask0", "mask", "end"]
+LEAD = {'run': -500, 'back': 500, 'endP': -500, 'xrunS': -500, 'win0P': 500, 'leave1S': -500, 'table': 500, 'leave0P': -500, 'backP': 500, 'fault1V': 500, 'win1': -500, 'fault0': 1000, 'mask0': -1000, 'hop': 1000, 'leave0V': 1000, 'fault0P': -1000, 'hopV': -1000, 'win1P': -1000, 'clear': 1000, 'fault0V': -1000, 'last0P': -1000, 'endS': -1000, 'leave1': 1500, 'last1': -1500, 'endV': -1500, 'oldS': 1500, 'backV': -2000, 'rowP': 2000, 'xrun': 2000, 'old': -2000, 'count': -2000, 'last0': 3000, 'end': 4000}
+DBG = []
 PLAN = []
 
 
@@ -51,7 +55,7 @@ def covers(a, b):
 
 def needs(ops):
     reads, writes, banks, loads, deps = {}, {}, {}, {}, []
-    for n, (e, fn, rd, wr, kind, cost, lag) in enumerate(ops):
+    for n, (e, fn, rd, wr, kind, cost, lag, stage) in enumerate(ops):
         d = set()
         for name in set(x[0] for x in rd + wr if SCRATCH[x[0]][0] == "psum"):
             b = banks.setdefault(name, [e, [], []])
@@ -86,7 +90,7 @@ def plan(ops, deps):
     gap = lambda m, n: 0.0 if free(ops, m, n) else ops[m][6] + (0.0 if ops[n][0] == "X" else NOM["wake"])
     way = [ops[n][5] + ops[n][6] for n in range(N)]
     for n in range(N - 1, -1, -1):
-        for m in deps[n]: way[m] = max(way[m], ops[m][5] * OPT["w" + ops[m][0]] + gap(m, n) + way[n])
+        for m in deps[n]: way[m] = max(way[m], ops[m][5] + gap(m, n) + way[n])
     before = [[(m, gap(m, n)) for m in deps[n]] for n in range(N)]
     after = [[] for n in range(N)]
     for n in range(N):
@@ -109,13 +113,12 @@ def plan(ops, deps):
             end[n] = t + c
         return end
 
-    order, best = sorted(range(N), key=lambda n: (-way[n], n)), None
-    for _ in range(OPT["passes"]):
-        end = lay(order, before, [0.0] * N)
-        total = max(end[n] + ops[n][6] for n in range(N))
-        if best is None or total < best[0]: best = (total, end)
-        back = lay(sorted(range(N), key=lambda n: (-end[n], -n)), after, [ops[n][6] for n in range(N)])
-        order = sorted(range(N), key=lambda n: (-back[n], n))
+    key = [way[n] + (LEAD.get(ops[n][7][1], 0.0) + LEAD.get(ops[n][7][1] + ops[n][0], 0.0) if ops[n][7] else 0.0) for n in range(N)]
+    for n in range(N - 1, -1, -1):
+        for m in deps[n]: key[m] = max(key[m], key[n] + 1.0)
+    end = lay(sorted(range(N), key=lambda n: (-key[n], n)), before, [0.0] * N)
+    best = (max(end[n] + ops[n][6] for n in range(N)), end)
+    DBG[:] = [ops, before, best]
     return sorted(range(N), key=lambda n: (best[1][n] - ops[n][5], n))
 
 
@@ -177,7 +180,7 @@ def rank_program(g, core, T, topo):
     nxt, prv = cores[(rank + 1) % len(cores)], cores[(rank - 1) % len(cores)]
     rid, pid = topo.addr(nxt)[0], topo.addr(nxt)[1]
     n_out, n_in = len(topo.engines(core, nxt)), len(topo.engines(prv, core))
-    ops, loaded = [], [0.0]
+    ops, loaded, now = [], [0.0], [0, None]
     V, S, P = g.vector, g.scalar, g.tensor
 
     def ap(x):
@@ -202,7 +205,9 @@ def rank_program(g, core, T, topo):
             else:
                 if per is None: per = 0.5 if e == "V" and all(short(x) for x in [out] + ins[:1]) else 1.0
                 cost = max(64, size(out) * per) * NOM["cyc"]
-        ops.append((e, fn, rd, wr, kind, cost, lag))
+        ops.append((e, fn, rd, wr, kind, cost, lag, now[1] and tuple(now)))
+
+    def stage(name, t=None): now[:] = [now[0] if t is None else t, name]
 
     def ts(out, a, s1, o0, s2=None, o1=None):
         if o1 is None: add("V", lambda: V.tensor_scalar(ap(out), ap(a), ap(s1), None, o0), out, [a, s1])
@@ -217,13 +222,16 @@ def rank_program(g, core, T, topo):
         add("S", lambda: S.activation(ap(out), ap(a), fn, **{k: ap(x) for k, x in kw.items()}), out, [a, bias, scale])
 
     def mm(out, l, r, st, sp):
-        add("P", lambda: P.matmul(ap(out), ap(l), ap(r), st, sp), out, [l, r], cost=max(64, size(r)) * (1 if short(l) else 4) * NOM["pe"])
+        add("P", lambda: P.matmul(ap(out), ap(l), ap(r), bool(st), bool(sp)), out, [l, r], cost=max(64, size(r)) * (1 if short(l) else 4) * NOM["pe"])
+        a, b = ops[-2], ops[-1]
+        if a[0] == "P" and a[3][0][0] == out[0] and (a[2][-2][0] == l[0] or a[2][-1][0] == r[0]) and a[5] + b[5] <= (OPT["cap"] if now[1] != "end" else 120):
+            ops[-2:] = [("P", lambda: (a[1](), b[1]())[1], a[2] + b[2], a[3] + b[3], None, a[5] + b[5], 0.0, a[7])]
 
     def dma(e, out, a):
         x = out if isinstance(out, tuple) else a
         n = size(x) * (x[5] - x[4]) * (2 if short(x) else 4) / NOM["rate"]
         if x is out: loaded[0] += n
-        add(e, lambda: (g.sync if e == "Y" else S).dma_start(ap(out), ap(a)), out, [a], "dma", 50.0, NOM["dma"] + (loaded[0] if x is out else n))
+        add(e, lambda: (g.sync if e == "Y" else S).dma_start(ap(out), ap(a)), out, [a], "dma", 50.0, NOM["dma"] + (loaded[0] * (OPT["xs"] if x[0] == "xb" else 1) if x is out else n))
 
     def iota(out, pat, base, cm=0):
         kw = {} if SB[out[0]][1] == i32 else {"allow_small_or_imprecise_dtypes": True}
@@ -238,14 +246,14 @@ def rank_program(g, core, T, topo):
     col = lambda c: v("pc", c, c + 1)
     pcs = lambda c, n: v("pc", c, c + n)
     num = lambda a, b: v("n256", a, b)
-    z = lambda t, h: v("z%d%d" % (t, h))
+    z = lambda t, h: v("z%d%d" % (t, h)) if t else v("xb", KW + 512 * (1 - h), KW + 512 * (2 - h))
 
     for h in (1, 0):
         dma("S", z(0, h), T.zin[:, 512 * h:512 * h + 512])
         dma("Y", R("K", h), T.nkey[:, 512 * h:512 * h + 512])
     dma("S", v("ci"), T.cnt[:])
-    for c in range(1, 4): dma("Y", blk("K", c, 1024), T.nkey[:, 1024 * c:1024 * c + 1024])
-    for c in range(4): dma("Y", blk("xb", c, 1024), T.xreg[:, 1024 * c:1024 * c + 1024])
+    dma("Y", v("K", TH, D), T.nkey[:, TH:D])
+    for c in range(OPT["xl"]): dma("Y", part(v("xb", 0, D), c, OPT["xl"]), T.xreg[:, D // OPT["xl"] * c:D // OPT["xl"] * (c + 1)])
 
     ioA, ioB, ioC, ioD, ioE, ioR = v("io", 0, 64), v("io", 64, 192), v("io", 192, 320), v("io", 320, 448), v("io", 448, 480), 480
     iota(v("pi", 0, 1), [[0, 1]], 0, 1)
@@ -262,8 +270,8 @@ def rank_program(g, core, T, topo):
         iota(v("io", ioR + c, ioR + c + 8 * n), [[1, n], [4, 8]], k + 1)
         iota(v("io", ioR + 48 + c, ioR + 48 + c + 8 * n), [[1, n], [4, 8]], 0)
     for h in range(2): iota(W("JX", h), [[16, 32]], KW - D // 2 + 512 * (1 - h), 1)
-    bits = [(0, 127), (0, 15), (4, 7), (0, 3), (2, 31), (3, 7), (0, 1), (1, 3), (4, 3), (1, 7)]
-    cP, cA, cG, cM3, cP2, cGQ, cDUP, cMQ, cQ, cG2 = range(10)
+    bits = [(0, 127), (0, 15), (4, 7), (0, 3), (2, 31), (3, 7), (0, 1), (1, 3), (0, 7), (0, 7)]
+    cP, cA, cG, cM3, cP2, cGQ, cDUP, cMQ, c7 = range(9)
     for c, (sh, mk) in enumerate(bits): ts(v("pj", c, c + 1), v("pi", 0, 1), sh, A.arith_shift_right, mk, A.bitwise_and)
     ts(v("pj", 10, 15), v("pi", 8, 13), 4, A.arith_shift_right, 7, A.bitwise_and)
     ts(v("pj", 15, 16), v("pi", 0, 1), 6, A.arith_shift_right, 1, A.bitwise_and)
@@ -292,6 +300,8 @@ def rank_program(g, core, T, topo):
     ts(blk("WB", 1, 128), ioB, col(cGQ), A.is_equal)
     tt(blk("WB", 0, 128), blk("WB", 0, 128), blk("WB", 1, 128), A.mult)
     for m in range(6): ts(blk("MK", m, 128), blk("WB", 0, 128), col(56 + m // 2 + 4 * (m % 2)), A.mult)
+    ts(col(95), col(cA), 1.0, A.add)
+    for t in range(1, RO): ts(blk("BR", t - 1, 128), ioB, col(10 + t), A.is_equal, col(64 + 3 * t), A.mult)
     for k, wt in enumerate((1.0, 1.0 / D, 1.0 / BIG, 1.0 / BIG / D)): ts(blk("Sel", k, 32), ioE, col(cG), A.is_equal, wt, A.mult)
     ts(v("Mq"), ioD, col(cM3), A.is_equal)
     ts(v("Rb"), num(0, 32), col(cP2), A.is_equal)
@@ -311,12 +321,10 @@ def rank_program(g, core, T, topo):
     ts(col(87), col(cP), 128.0, A.add)
     ts(col(88), col(64), -1.0, A.mult, 1.0, A.add)
     ts(col(89), col(64), 512.0, A.mult)
-    ts(col(90), col(64), 15.0, A.mult, col(cP), A.add)
-    ts(col(91), col(64), col(66), A.add, 15.0, A.mult)
     ts(col(92), col(64), 31.0, A.add)
-    ts(col(93), col(90), col(66), A.subtract)
-    ts(col(94), col(91), 1.0, A.add)
-    for k, wt in enumerate((1.0, -1.0 / D, -512.0 / D, 8192.0 / BIG, -8192.0 / BIG, -8192.0)):
+    ts(col(93), col(64), col(cP), A.add)
+    ts(col(94), col(64), 15.0, A.mult, 1.0, A.add)
+    for k, wt in enumerate((1.0, -1.0 / D, -2048.0 / BIG, 2048.0 / BIG, 2.0 if OPT["two"] else -512.0 / D, -8192.0)):
         ts(blk("Id", k, 128), num(0, 128), col(cP), A.is_equal, wt, A.mult)
     ts(blk("Id", 6, 128), num(0, 128), col(cP), A.is_equal, col(64), A.mult)
     ts(blk("Id", 7, 128), ioB, col(cG), A.is_equal, float(D), A.mult)
@@ -324,48 +332,46 @@ def rank_program(g, core, T, topo):
     ts(blk("Y", 1, 144), num(0, 144), col(86), A.is_equal, col(89), A.mult)
     ts(blk("II", 0, 128), num(0, 128), col(cP), A.is_equal, col(88), A.mult)
     ts(blk("II", 1, 128), num(128, 256), col(87), A.is_equal, col(88), A.mult)
-    ts(v("PK"), num(0, 128), col(93), A.is_equal, col(94), A.mult)
-    for a in range(16): ts(blk("L", a, 128), blk("Id", 7, 128), col(64 + a), A.mult)
+    for k in range(2): ts(blk("PK", k, 128), num(0, 128), col(93), A.is_equal, col(94), A.mult)
+    ts(col(90), col(65), -16.0, A.mult, col(92), A.add)
+    ms(v("xb", D, KW), 0.0)
+    for a in range(16):
+        if a < OPT["ls"]: act(blk("L", a, 128), blk("Id", 7, 128), F.Identity, scale=col(64 + a))
+        else: ts(blk("L", a, 128), blk("Id", 7, 128), col(64 + a), A.mult)
     for k in range(2):
-        for out, wt in (("RA", 1.0), ("RH", -float(D))):
-            ts(v(out, 80 * k, 80 * k + 48), v("io", ioR + 48 * k, ioR + 48 * k + 48), col(cP2), A.is_equal, wt, A.mult)
-            ts(v(out, 80 * k + 48, 80 * k + 80), num(0, 32), col(cP2), A.is_equal, wt, A.mult)
+        ts(v("RA", 80 * k, 80 * k + 48), v("io", ioR + 48 * k, ioR + 48 * k + 48), col(cP2), A.is_equal)
+        ts(v("RA", 80 * k + 48, 80 * k + 80), num(0, 32), col(cP2), A.is_equal)
+    for k, wt in enumerate((-float(D), 1.0)): act(blk("RH", k, 160), v("RA"), F.Identity, scale=wt)
     ts(v("JX"), v("JX"), col(21), A.subtract)
     ts(pcs(120, 4), num(0, 4), 16.0, A.mult, col(cA), A.add)
     ts(pcs(120, 4), pcs(120, 4), float(D // 2), A.add)
     for t in range(RO): ts(v("PI", 128 * t, 128 * t + 128, p1=32), v("io", 192, 320, p1=32), float(t), A.not_equal, BIG, A.mult)
     ts(v("PI", p1=32), v("PI", p1=32), -1.5 * D, A.add)
-    ms(v("XW", D, KW), 32.0)
+    act(v("XW", D, KW), num(64, 128), F.Silu)
     ts(pcs(96, 16), pcs(96, 16), col(21), A.add)
     ts(pcs(112, 8), pcs(112, 8), col(cA), A.max, col(21), A.add)
     for s in range(16): ts(blk("SH", s, 128), num(0, 128), col(96 + s), A.is_equal)
-    for s in range(8): ts(blk("E", s, 128), num(0, 128), col(112 + s), A.is_equal)
-    ts(col(124), col(65), col(79), A.add)
-    ts(col(125), col(cG), 2.0, A.mult, col(79), A.add)
-    ts(col(126), col(cG), 4.0, A.mult, 1.0, A.add)
-    ts(pcs(136, 4), num(0, 4), 16.0, A.mult, col(125), A.add)
-    ts(pcs(136, 4), pcs(136, 4), 33.0, A.add, col(124), A.mult)
-    ts(pcs(140, 4), num(0, 4), col(126), A.add, col(64), A.mult)
-    tt(pcs(136, 4), pcs(136, 4), pcs(140, 4), A.add)
-    ts(pcs(136, 4), pcs(136, 4), -1.0, A.add)
-    for b in range(4): ts(blk("HX", b, 96), num(0, 96), col(136 + b), A.is_equal)
-    ts(col(127), col(cG2), 16.0, A.mult, 1.0, A.add)
-    ts(col(128), col(cP), 32.0, A.is_ge)
-    ts(col(144), col(cDUP), 14.0, A.mult, col(127), A.add)
-    ts(col(145), col(16), -1.0, A.mult, col(127), A.add)
-    ts(col(146), col(128), -16.0, A.mult)
-    ts(blk("HR", 4, 128), num(0, 128), col(144), A.is_equal, col(146), A.mult)
-    ts(blk("HR", 5, 128), num(0, 128), col(145), A.is_equal, col(128), A.mult)
-    tt(blk("HR", 4, 128), blk("HR", 4, 128), blk("HR", 5, 128), A.add)
-    ts(pcs(148, 4), num(0, 4), 2.0, A.add, col(cQ), A.subtract)
-    ts(pcs(152, 4), pcs(148, 4), 0.0, A.is_equal)
-    ts(pcs(156, 4), pcs(148, 4), 4.0, A.is_equal)
-    tt(pcs(152, 4), pcs(152, 4), pcs(156, 4), A.add)
-    for b in range(4): ts(blk("HR", b, 128), blk("HR", 4, 128), col(152 + b), A.mult)
-    ts(col(129), col(124), 2560.0, A.mult, -1.0, A.add)
-    ts(col(130), col(64), col(66), A.add, -160.0, A.mult)
-    ts(col(131), col(64), col(129), A.add, col(130), A.add)
+    if OPT["sh"]:
+        ts(pcs(160, 15), num(1, 16), col(cA), A.add, 16.0, A.is_lt)
+        ts(pcs(176, 15), num(2, 17), col(cP), A.add)
+        tt(pcs(160, 15), pcs(160, 15), pcs(176, 15), A.mult)
+        for s in range(15): ts(blk("E", s, 128), num(1, 129), col(160 + s), A.is_equal)
+    for s in range(0 if OPT["sh"] else 8): ts(blk("E", s, 128), num(0, 128), col(112 + s), A.is_equal)
+    ts(col(124), col(cA), 8.0, A.mult, col(cG), A.add)
+    ts(col(124), col(124), 8.0, A.mult, 8.0, A.add)
+    ts(v("HX"), num(0, 136), col(124), A.is_equal)
+    ts(col(127), col(cGQ), 16.0, A.mult)
+    ts(col(128), col(127), 1.0, A.add)
+    ts(col(146), col(15), -16.0, A.mult)
+    ts(blk("HR", 8, 128), num(0, 128), col(128), A.is_equal, col(146), A.mult)
+    ts(blk("HR", 9, 128), num(0, 128), col(127), A.is_equal, col(15), A.mult)
+    tt(blk("HR", 8, 128), blk("HR", 8, 128), blk("HR", 9, 128), A.add)
+    ts(pcs(148, 8), num(0, 8), col(c7), A.is_equal)
+    for b in range(8): ts(blk("HR", b, 128), blk("HR", 8, 128), col(148 + b), A.mult)
+    ts(col(129), col(65), 2560.0, A.mult, -1.0, A.add)
+    ts(col(131), col(64), -159.0, A.mult, col(129), A.add)
     ts(col(147), col(131), 16.0, A.mult)
+    act(v("IF"), blk("Id", 0, 128), F.Identity)
 
     Id = lambda k: blk("Id", k, 128)
 
@@ -381,89 +387,182 @@ def rank_program(g, core, T, topo):
             else: act(part(R("X2", h), q, n), part(ps(bank), q, n), F.Relu, bias=col(20), scale=BIG)
 
     def masks(t):
+        if t: stage("mask0")
         for h in (1, 0):
-            front(t, h)
-            mask(0, h, 2 + h)
+            if OPT["mv"] and t:
+                for q in range(2): mm(part(ps(2 + h), q, 2), blk("BR", t - 1, 128), part(z(t, h), q, 2), True, True)
+                for q in range(2): ts(part(ps(2 + h), q, 2), part(ps(2 + h), q, 2), col(95), A.is_equal)
+                stage("mask")
+                front(t, h)
+                stage("mask0")
+            else:
+                front(t, h)
+                mask(0, h, 2 + h)
+        if t: stage("mask")
         for m in (1, 2):
             for h in (1, 0): mask(m, h, 7 - h)
 
     def table(name, c, bank):
         for a in (2 * c, 2 * c + 1):
             o = part(ps(bank), a % 2, 2)
-            if name == "XW": mm(o, v("PK"), blk("xb", a, 256), True, False)
+            if name == "XW": mm(o, blk("PK", 0, 128), blk("xb", a, 256), True, False)
             mm(o, v("Z", 160 * a + 16 + a, 160 * a + 144 + a), v("ch"), name == "CT", True)
         act(blk(name, c, 512), ps(bank), F.Identity, bias=32.0 if name == "XW" else 1.0)
 
     Gs = ["Ga", "Gb", "Ga", "Ab"]
 
     def gather(m, h):
-        n = OPT["fp"] if m == 0 else OPT["gp"]
+        n = OPT["fp"] if m == 0 else OPT["gp"] if m < 3 else OPT["ga"]
+        if m == 3 and OPT["ar"] > 2 * h:
+            k = min(2, OPT["ar"] - 2 * h)
+            a, b = 32 * h, 32 * h + 16 * k
+            act(v("Gb", 16 * a, 16 * b), at(v("K", 0, D), v("off", 128 + a, 128 + b)), F.Identity)
+            if k == 1: tt(part(R("Ab", h), 1, 2), at(v("K", 0, D), part(W("off", h, 2), 1, 2)), part(R("X2", h), 1, 2), A.subtract)
+            stage("clear")
+            for u in range(b // 4 - 1, a // 4 - 1, -1): tt(blk("Ab", u, 64), blk("Gb", u, 64), blk("X2", u, 64), A.subtract)
+            return
         for i in range(n):
             if m == 0: tt(part(R("Ga", h), i, n), part(R("K", h), i, n), part(ps(2 + h), i, n), A.mult)
             else: tt(part(R(Gs[m], h), i, n), at(v("K", 0, D), part(W("off", h, m - 1), i, n)), part(R("X1" if m == 1 else "X2", h), i, n),
                      A.mult if m < 3 else A.subtract)
 
     def turn(t, m, h):
-        mm(ps(h, 0, 256), v("one", 0, 128, p1=3), v("crow", p1=3), True, False)
-        for c in range(4): mm(ps(h, c, 256, 4), v(Gs[m], 512 * h + c, 512 * h + 512, 4), blk("Sel", m // 2, 64), False, c == 3)
-        tt(blk("H3", h, 128), ps(h, 128, 256), v("Mq"), A.mult)
-        tt(blk("T3", h, 128), ps(h, 0, 128), v("Mq"), A.mult)
-        mm(ps(h, 256, 288), blk("H3", h, 128), blk("Rh", 0, 32), True, False)
-        mm(ps(h, 256, 288), blk("T3", h, 128), v("Rb"), False, True)
-        mm(ps(2 + h, 0, 32), blk("H3", h, 128), blk("Rh", 1, 32), True, True)
+        if not OPT["bg"]: mm(ps(h, 0, 256), v("one", 0, 128, p1=3), v("crow", p1=3), True, False)
+        for c in range(4): mm(ps(h, c, 256, 4), v(Gs[m], 512 * h + c, 512 * h + 512, 4), blk("Sel", m // 2, 64), OPT["bg"] and c == 0, c == 3 and not OPT["bg"])
+        if OPT["bg"]: mm(ps(h, 128, 256), v("one", 0, 128, p1=3), v("crow", 128, p1=3), False, True)
+        H3, T3 = blk("H3", 2 * m + h, 128), blk("T3", h, 128)
+        tt(H3, ps(h, 128, 256), v("Mq"), A.mult)
+        tt(T3, ps(h, 0, 128), v("Mq"), A.mult)
+        mm(ps(h, 256, 288), H3, blk("Rh", 0, 32), True, False)
+        mm(ps(h, 256, 288), T3, v("Rb"), False, True)
         ts(W("off", h, m), ps(h, 256, 288), PB, A.add)
         if m == 1: ts(W("P1", h), ps(h, 256, 288), PB - D // 2, A.add, 1.0 / D, A.mult)
-        act(W("cab", h, m), ps(2 + h, 0, 32), F.Abs, bias=-(HB - 1.0) * D, scale=float(D))
+        if m == 2 and OPT["xq"]: ts(W("Qn", h), ps(h, 256, 288), PB - D // 2, A.add)
+        stage("count" if m < 2 else "last%d" % h)
+        if m < 2 or not OPT["two"]:
+            mm(ps(2 + h, 0, 32), H3, blk("Rh", 1, 32), True, True)
+            act(W("cab", h, m), ps(2 + h, 0, 32), F.Abs, bias=-(HB - 1.0) * D, scale=float(D))
+            if m == 2 and OPT["sh"]:
+                mm(ps(h, 320, 400), T3, v("RA", 0, 80), True, False)
+                mm(ps(h, 320, 400), H3, v("RH", 0, 80), False, True)
+                ts(v("AR", 160 * h, 160 * h + 80), ps(h, 320, 400), PB - D // 2, A.add)
+        else:
+            mm(ps(h, 320, 480), T3, v("RA"), True, False)
+            mm(ps(h, 320, 480), H3, blk("RH", 0, 160), False, True)
+            ts(blk("AR", h, 160), ps(h, 320, 480), PB - D // 2, A.add)
+            mm(ps(2 + h, 0, 160), H3, blk("RH", 1, 160), True, False)
+            for k, (_, lo) in enumerate(PAIRS): mm(ps(2 + h, 80 + 8 * k, 88 + 8 * k), Id(0), v("e01", 32 * h + lo, 32 * h + 32, 4), False, False)
+            mm(ps(2 + h, 128, 160), Id(0), W("e01", h), False, False)
+            mm(ps(2 + h, 48, 80), Id(4), W("e01", h), False, True)
+            act(blk("CA", h, 160), ps(2 + h, 0, 160), F.Abs, bias=-(HB - 1.0) * D, scale=float(D))
+            tt(blk("XH", h, 80), v("AR", 160 * h, 160 * h + 80), v("CA", 160 * h, 160 * h + 80), A.add)
+        if m == 2: stage("fault%d" % h)
         win, b = (v("CT"), 0.0) if t == 0 else (v("XW", 0, D), -31.0)
-        if m == 2 and h == 1 and OPT["cgv"]:
+        if m == 2 and OPT["cgv"] >> (1 - h) & 1:
             act(part(R("Cg2", h), 0, 2), at(win, part(W("off", h, m), 0, 2)), F.Identity, bias=b)
             ts(part(R("Cg2", h), 1, 2), at(win, part(W("off", h, m), 1, 2)), b, A.add)
         else: act(R("Cg%d" % m, h), at(win, W("off", h, m)), F.Identity, bias=b)
 
     def check01(m):
-        for a in range(16): mm(ps(6, 0, 64), v("Y", 144 * m + 16 - a, 144 * m + 144 - a), v("Cg%d" % m, a, TH, 16), m == 0 and a == 0, False)
-        mm(ps(6, 0, 64), Id(1 + m), blk("cab", m, 64), False, m == 1)
+        if OPT["eh"] == 0:
+            for a in range(16): mm(ps(6, 0, 64), v("Y", 144 * m + 16 - a, 144 * m + 144 - a), v("Cg%d" % m, a, TH, 16), m == 0 and a == 0, False)
+            mm(ps(6, 0, 64), Id(1 + 3 * m), blk("cab", m, 64), False, m == 1)
+            if m == 1 and OPT["es"]: act(v("e01"), ps(6, 0, 64), F.Abs, scale=1024.0)
+            elif m == 1: ts(v("e01"), ps(6, 0, 64), 0.0, A.not_equal, 1024.0, A.mult)
+        elif m == 0 and OPT["eh"] == 1:
+            for a in range(16): mm(ps(6, 0, 64), v("Y", 16 - a, 144 - a), v("Cg0", a, TH, 16), a == 0, False)
+            mm(ps(6, 0, 64), Id(1), blk("cab", 0, 64), False, True)
+            ts(v("e0"), ps(6, 0, 64), 0.0, A.not_equal, 1024.0, A.mult)
 
-    own = lambda h: v("AR", 160 * h + 128, 160 * h + 160)
+    def check0(h):
+        o = ps(6, 32 * h, 32 + 32 * h)
+        mm(o, Id(1), W("cab", h, 0), True, False)
+        for a in range(16): mm(o, v("Y", 16 - a, 144 - a), v("Cg0", 512 * h + a, 512 * h + 512, 16), False, a == 15)
+        ts(W("e0", h), o, 0.0, A.not_equal, 1024.0, A.mult)
+
+    def check1(h):
+        stage("count")
+        o = ps(6, 128 + 32 * h, 160 + 32 * h)
+        mm(o, Id(0), W("e0", h), True, False)
+        mm(o, Id(1), W("cab", h, 1), False, False)
+        for a in range(16): mm(o, v("Y", 16 - a, 144 - a), v("Cg1", 512 * h + a, 512 * h + 512, 16), False, a == 15)
+        ts(W("e01", h), o, 0.0, A.not_equal, 1024.0, A.mult)
+
+    two = OPT["two"]
+    own = lambda h: v("AR", 160 * h + 48, 160 * h + 80) if two else v("AR", 160 * h + 128, 160 * h + 160)
+    cab2 = lambda h: v("CA", 160 * h + 48, 160 * h + 80) if two else W("cab", h, 2)
     wide = lambda s: 80 if 1 <= s <= 8 else 48
 
+    def moved(t, h): mm(ps(OPT["sb"] + h), v("PK" if t <= OPT["x0"] else "II", 128 - 16 * t, 256 - 16 * t), z(t, h), True, False)
+
     def verdict(t, h):
+        stage("fault%d" % h)
         o = ps(6, 64 + 32 * h, 96 + 32 * h)
-        mm(o, Id(1), W("cab", h, 2), True, False)
-        mm(o, Id(0), W("e01", h), False, False)
-        for a in range(16): mm(o, v("Y", 16 - a, 144 - a), v("Cg2", 512 * h + a, 512 * h + 512, 16), False, a == 15)
-        ts(W("nok", h), o, 0.0, A.not_equal, BIG, A.mult)
-        mm(ps(h, 320, 480), blk("T3", h, 128), v("RA"), True, False)
-        mm(ps(h, 320, 480), blk("H3", h, 128), v("RH"), False, False)
-        for k, (_, lo) in enumerate(PAIRS): mm(ps(h, 400 + 8 * k, 408 + 8 * k), Id(3), v("nok", 32 * h + lo, 32 * h + 32, 4), False, False)
-        mm(ps(h, 448, 480), Id(3), W("nok", h), False, False)
-        mm(ps(h, 368, 400), Id(4), W("nok", h), False, True)
-        ts(blk("AR", h, 160), ps(h, 320, 480), PB - D // 2, A.add)
-        mm(ps(2 + h), v("PK") if t == 0 else v("II", 128 - 16 * t, 256 - 16 * t), z(t, h), True, False)
-        mm(ps(2 + h), Id(6), R("Cg2", h), False, True)
-        act(v("XW", KW + 512 * (1 - h), KW + 512 * (2 - h)), ps(2 + h), F.Identity, bias=32.0 if t == 0 else col(92))
-        tt(W("w", h), own(h), W("JX", h), A.min)
-        ts(W("xoff", h), W("w", h), float(D // 2), A.add)
-        so = R("s%d" % t, h)
-        act(so, at(v("XW", 0, KW + 512 * (2 - h)), W("xoff", h)), F.Identity, bias=-31.0)
-        if t < RO - 1:
-            sem = "arr%d%d" % (t + 1, h)
-            add("G", lambda: g.remote_dma(ap(z(t + 1, h)), ap(so), T.sem[sem], T.sem.sent, pid, rid, topo.mask(core, nxt)), None, [so], "call", 600.0, NOM["hop"] - 600)
-            add("X", None, z(t + 1, h), [], ("arrival", sem, n_in), 1.0)
-        tt(W("pk", h), W("nok", h), W("cab", h, 2), A.subtract)
+        if not two:
+            mm(o, Id(1), cab2(h), True, False)
+            mm(o, Id(0), W("e01", h), False, False)
+        for a in range(16): mm(o, v("Y", 16 - a, 144 - a), v("Cg2", 512 * h + a, 512 * h + 512, 16), two and a == 0, a == 15 and not two)
+        if two: mm(o, Id(1), cab2(h), False, True)
+        ts(W("nok", h), o, 0.0, A.not_equal, 4 * BIG, A.mult)
+        if OPT["sh"]:
+            mm(ps(h, 400, 480), blk("T3", h, 128), v("RA", 80), True, False)
+            mm(ps(h, 400, 480), blk("H3", 4 + h, 128), v("RH", 80, 160), False, False)
+            for k, (_, lo) in enumerate(PAIRS): mm(ps(h, 400 + 8 * k, 408 + 8 * k), Id(3), v("nok", 32 * h + lo, 32 * h + 32, 4), False, False)
+            mm(ps(h, 448, 480), Id(3), W("nok", h), False, True)
+            ts(v("AR", 160 * h + 80, 160 * h + 160), ps(h, 400, 480), PB - D // 2, A.add)
+        elif not two:
+            mm(ps(h, 320, 480), blk("T3", h, 128), v("RA"), True, False)
+            mm(ps(h, 320, 480), blk("H3", 4 + h, 128), blk("RH", 0, 160), False, False)
+            for k, (_, lo) in enumerate(PAIRS): mm(ps(h, 400 + 8 * k, 408 + 8 * k), Id(3), v("nok", 32 * h + lo, 32 * h + 32, 4), False, False)
+            mm(ps(h, 448, 480), Id(3), W("nok", h), False, False)
+            mm(ps(h, 368, 400), Id(2), W("nok", h), False, True)
+            ts(blk("AR", h, 160), ps(h, 320, 480), PB - D // 2, A.add)
+        stage("leave%d" % h)
+        if two or OPT["xq"]: ts(W("nk8", h), o, 0.0, A.not_equal, 8192.0, A.mult)
+        if OPT["sb"] == 2: moved(t, h)
+        mm(ps(OPT["sb"] + h), Id(6), R("Cg2", h), False, True)
+        act(v("XW", KW + 512 * (1 - h), KW + 512 * (2 - h)), ps(OPT["sb"] + h), F.Identity, bias=32.0 if t == 0 else col(90 if t == OPT["x0"] else 92))
+        if two or OPT["xq"]: tt(W("w", h), own(h) if two else W("Qn", h), W("nk8", h), A.add)
+        tt(W("w", h, 1), W("w", h) if two or OPT["xq"] else own(h), W("JX", h), A.min)
+        ts(W("xoff", h), W("w", h, 1), float(D // 2), A.add)
+        n = OPT["sq"]
+        for q in range(n):
+            so = part(R("s%d" % t, h), q, n)
+            name, b = ("xb", 1.0) if t < OPT["x0"] else ("XW", -31.0)
+            act(so, at(v(name, 0, KW + 512 * (2 - h)), part(W("xoff", h), q, n)), F.Identity, bias=b)
+            if t < RO - 1:
+                sem, to = "arr%d%d%d" % (t + 1, h, q), part(z(t + 1, h), q, n)
+                add("G", lambda so=so, sem=sem, to=to: g.remote_dma(ap(to), ap(so), T.sem[sem], T.sem.sent, pid, rid, topo.mask(core, nxt)), None, [so], "call", 600.0,
+                    NOM["hop"] - 600 - 650 * (n - 1) + (NOM["once"] if t == 0 else 0))
+                add("X", None, to, [], ("arrival", sem, n_in), 1.0)
+        stage("row")
+        tt(W("pk", h), W("nok", h), cab2(h), A.subtract)
+        if OPT["nw"]: cp(W("Qn", h), own(h))
 
     def winners(h, banks):
+        stage("win%d" % h)
         mm(ps(h, 0, 80), v("nil", p1=1), v("one", 0, 80, p1=1), True, False)
-        for k, bank in enumerate(banks):
+        for k, bank in enumerate(banks if OPT["sh"] else ()):
+            stage("last%d" % h)
+            for i, s in enumerate(TURNS[k]): mm(ps(bank, 80 * i, 80 * i + (80 if s else 48)), blk("SH", s, 128), v("AR", 160 * h, 160 * h + (80 if s else 48)), True, True)
+            stage("win%d" % h)
             for i, s in enumerate(TURNS[k]):
-                mm(ps(bank, 80 * i, 80 * i + wide(s)), blk("SH", s, 128), v("AR", 160 * h + 80, 160 * h + 80 + wide(s)), True, True)
+                c, n = 1280 * h + 80 * s, 80 if s else 48
+                tt(v("eq", c, c + n), ps(bank, 80 * i, 80 * i + n), v("AR", 160 * h + 80, 160 * h + 80 + n), A.is_equal)
+                if s: mm(ps(h, 48, 80), blk("E", s - 1, 128), v("eq", c + 48, c + 80), False, False)
+                mm(ps(h, 0, 48), blk("SH", -s % 16, 128), v("eq", c, c + 48), False, s == 15)
+        for k, bank in enumerate(() if OPT["sh"] else banks):
+            for i, s in enumerate(TURNS[k]):
+                for x in ("AR", "CA")[:1 + two]: mm(ps(bank, 80 * i, 80 * i + wide(s)), blk("SH", s, 128), v(x, 160 * h + 80, 160 * h + 80 + wide(s)), x == "AR", x == "CA" or not two)
             for i, s in enumerate(TURNS[k]):
                 c = 1280 * h + 80 * s
-                tt(v("eq", c, c + wide(s)), ps(bank, 80 * i, 80 * i + wide(s)), v("AR", 160 * h, 160 * h + wide(s)), A.is_equal)
+                tt(v("eq", c, c + wide(s)), ps(bank, 80 * i, 80 * i + wide(s)), v("XH", 80 * h, 80 * h + wide(s)) if two else v("AR", 160 * h, 160 * h + wide(s)), A.is_equal)
                 if wide(s) == 80: mm(ps(h, 48, 80), blk("E", s - 1, 128), v("eq", c + 48, c + 80), False, False)
                 mm(ps(h, 0, 48), Id(0), v("eq", c, c + 48), False, s == 15)
-        ts(blk("nd", h, 80), ps(h, 0, 80), 0.0, A.is_gt, 8192.0, A.mult)
+        if OPT["ns"] >> h & 1: act(blk("nd", h, 80), ps(h, 0, 80), F.Identity, scale=8192.0)
+        else: ts(blk("nd", h, 80), ps(h, 0, 80), 0.0, A.is_gt, 8192.0, A.mult)
         mm(ps(h, 96, 128), Id(0), own(h), True, False)
+        if two: mm(ps(h, 96, 128), Id(3), W("nok", h), False, False)
         for k, (hi, _) in enumerate(PAIRS): mm(ps(h, 96 + hi, 128, 4), Id(0), v("nd", 80 * h + 8 * k, 80 * h + 8 * k + 8), False, False)
         mm(ps(h, 96, 128), Id(0), v("nd", 80 * h + 48, 80 * h + 80), False, True)
         for i in range(4): ts(v("soff", 32 * h + i, 32 * h + 32, 4), ps(h, 96 + i, 128, 4), col(120 + i), A.min, float(D // 2), A.add)
@@ -472,74 +571,106 @@ def rank_program(g, core, T, topo):
         ts(v("cB"), blk("cab", 1, 64), 1.0 / D, A.mult, -1024.5, A.add)
         for b in range(2):
             for a in range(8):
-                mm(part(ps(4 + b), a, 8), blk("L", 8 * b + a, 128), v("P1"), True, False)
-                mm(part(ps(4 + b), a, 8), blk("L", 8 * b + a, 128), v("cB"), False, True)
-            for a in range(8): tt(v("Bb", 8 * b + a, TH, 16), part(ps(4 + b), a, 8), v("X2", 8 * b + a, TH, 16), A.add)
+                o = part(ps(OPT["bb"][b]), a, 8)
+                mm(o, blk("L", 8 * b + a, 128), v("P1"), True, False)
+                mm(o, blk("L", 8 * b + a, 128), v("cB"), False, b >= OPT["bs"])
+                if b < OPT["bs"]: mm(o, Id(0), v("X2", 8 * b + a, TH, 16), False, True)
+            for a in range(8):
+                o = part(ps(OPT["bb"][b]), a, 8)
+                if b < OPT["bs"]: act(v("Bb", 8 * b + a, TH, 16), o, F.Identity)
+                else: tt(v("Bb", 8 * b + a, TH, 16), o, v("X2", 8 * b + a, TH, 16), A.add)
 
     def new_key(t, h):
         mm(ps(4 + h), v("PI", 128 * t, 128 * t + 128, p1=1), v("one", p1=1), True, False)
         for a in range(16):
             l = v("Z", 160 * a + 16 + a - t, 160 * a + 144 + a - t)
-            mm(ps(4 + h, a, 512, 16), l, own(h), False, False)
-            mm(ps(4 + h, a, 512, 16), l, W("pk", h), False, a == 15)
+            if not OPT["nw"]:
+                mm(ps(4 + h, a, 512, 16), l, own(h), False, False)
+                mm(ps(4 + h, a, 512, 16), l, W("pk", h), False, a == 15)
+            elif a // 8 == h:
+                mm(part(ps(4 + h), a % 8, 8), l, v("Qn"), False, False)
+                mm(part(ps(4 + h), a % 8, 8), l, v("pk"), False, a % 8 == 7)
 
-    def stack(src, n, bank, c0, order=(0, 1, 2, 3)):
-        for b in order: mm(ps(bank, 0, n, 1, 0, 96), blk("HX", b, 96), src(b), b == order[0], b == order[3])
-        act(v("hi", c0, c0 + n, 1, 0, 96), ps(bank, 0, n, 1, 0, 96), F.Identity, bias=160.0 - 8.5 / 16, scale=0.0625)
+    def stack(name, n, bank, c0, order):
+        for b in order: mm(ps(bank, 0, n), v("HX", 8 - b, 136 - b), blk(name, b, n), b == order[0], b == order[7])
+        k = n // 128 if OPT["hp"] else 1
+        for i in range(k): act(part(v("hi", c0, c0 + n), i, k), part(ps(bank, 0, n), i, k), F.Identity, bias=160.0 - 8.5 / 16, scale=0.0625)
 
     masks(0)
     for c in range(8): table("CT", c, 4 + c % 2)
     for t in range(RO):
         for m in range(3):
             for h in (1, 0):
+                stage("hop", t)
                 gather(m, h)
                 turn(t, m, h)
+                if m == 1 and OPT["eh"] and (h or OPT["eh"] < 3): check1(h)
+                if m == 0 and OPT["eh"] > 1: check0(h)
+            stage("count")
             if m < 2: check01(m)
-            if m == 1:
-                ts(v("e01"), ps(6, 0, 64), 0.0, A.not_equal, 1024.0, A.mult)
-                back()
-            if t == 0 and m == 0:
-                for c in range(8): table("XW", c, (7, 4, 5)[c % 3] if c < 6 else 7)
+            stage("back")
+            if m == 1: back()
+            if t == 0 and m < 2:
+                stage("table")
+                for c, bank in enumerate(OPT["xw"][m]): table("XW", c + m * len(OPT["xw"][0]), bank)
+            if t == 1 and m == 5: pass
+            if OPT["sb"] == 4 and m == (1 if t == 0 else 0):
+                stage("moved")
+                for h in (1, 0): moved(t, h)
         for h in (1, 0):
+            stage("old")
             gather(3, h)
             verdict(t, h)
-        winners(1, (7, 4, 5))
-        winners(0, (7, 4, 5))
+            if h and OPT["eh"] == 3: check1(0)
+        winners(1, OPT["wb"][1])
+        winners(0, OPT["wb"][0])
+        stage("table")
+        for c, bank in enumerate(OPT["xw"][2] if t == 0 else ()): table("XW", c + len(OPT["xw"][0] + OPT["xw"][1]), bank)
+        stage("row")
         for h in (1, 0): new_key(t, h)
         for u in range(15, -1, -1):
+            stage("run")
             tt(at(v("K"), blk("soff", u, 4)), blk("Ab", u, 64), blk("Bb", u, 64), A.max)
             c = KW + (64 * u + 512) % TH
+            stage("xrun")
             act(at(v("XW", 0, KW), blk("soff", u, 4)), v("XW", c, c + 64), F.Silu)
+        stage("row")
         for h in (1, 0):
-            for i in range(OPT["fp"]): tt(part(R("K", h), i, OPT["fp"]), part(R("K", h), i, OPT["fp"]), part(ps(4 + h), i, OPT["fp"]), A.min)
+            for a in range(8 * OPT["nw"]): tt(v("K", 8 * h + a, TH, 16), v("K", 8 * h + a, TH, 16), part(ps(4 + h), a, 8), A.min)
+            for i in range(OPT["fp"] * (1 - OPT["nw"])): tt(part(R("K", h), i, OPT["fp"]), part(R("K", h), i, OPT["fp"]), part(ps(4 + h), i, OPT["fp"]), A.min)
         if t < RO - 1: masks(t + 1)
 
-    stack(lambda b: blk("s4", b, 256), 256, 7, 0)
+    stage("end")
+    stack("s4", 128, 7, 512, range(8))
     for h in (1, 0):
         mm(ps(2 + h), blk("II", 1, 128), R("s4", h), True, False)
-        for b in range(2): mm(part(ps(2 + h), b, 2), v("HR", 128 * (2 * h + b), 128 * (2 * h + b + 1), p1=96), v("hi", 0, 256, p1=96), False, b == 1)
+        for b in range(4): mm(part(ps(2 + h), b, 4), blk("HR", 4 * h + b, 128), v("hi", 512, 640), False, b == 3)
         for b in range(2): act(part(R("oz", h), b, 2), part(ps(2 + h), b, 2), F.Identity, bias=col(131))
     dma("Y", T.yz[:], v("oz"))
     for h in (1, 0):
         ts(R("Hk", h), R("K", h), 1.0 / D, A.mult, HB - 0.5 + 0.5 / D, A.add)
         ts(R("Hn", h), R("Hk", h), 1.0 - HB, A.add, 0.0, A.min)
-    for b in (3, 2, 1, 0): mm(ps(4, 0, 256), Id(5), blk("Hn", b, 256), b == 3, b == 0)
-    cp(ps(1, 0, 256), blk("K", 15, 256))
-    for b in range(14, 5, -1): tt(ps(1, 0, 256), blk("K", b, 256), ps(1, 0, 256), A.add)
-    cp(blk("okk", 0, 256), ps(1, 0, 256))
-    for b in range(6): tt(ps(4, 0, 256), blk("K", b, 256), ps(4, 0, 256), A.add)
-    tt(blk("okk", 1, 256), blk("okk", 0, 256), ps(4, 0, 256), A.add)
+    top = 16 - OPT["npe"]
+    for b in range(top, 16): mm(ps(1, 0, 256), v("IF"), blk("K", b, 256), b == top, False)
+    for b in (3, 2, 1, 0): mm(ps(1, 0, 256), Id(5), blk("Hn", b, 256), top == 16 and b == 3, b == 0)
+    cp(ps(0, 256, 512), blk("K", top - 1, 256))
+    for b in range(top - 2, 3, -1): tt(ps(0, 256, 512), blk("K", b, 256), ps(0, 256, 512), A.add)
+    cp(blk("okk", 0, 256), ps(0, 256, 512))
+    for b in range(4): tt(ps(1, 0, 256), blk("K", b, 256), ps(1, 0, 256), A.add)
+    tt(blk("okk", 1, 256), blk("okk", 0, 256), ps(1, 0, 256), A.add)
     dma("Y", T.yk[:], blk("okk", 1, 256))
-    ts(blk("xb", 0, 1024), blk("XW", 0, 1024), -31.0, A.add)
-    for b in (3, 2, 1): act(blk("xb", b, 1024), blk("XW", b, 1024), F.Identity, bias=-31.0)
-    for e in range(2):
-        stack(lambda b: blk("xb", 2 * b + e, 512), 512, 6 + e, 512 * e, (3, 2, 0, 1))
-        ts(v("oc", 512 * e, 512 * e + 512, p1=32), ps(6 + e, p1=32), -1.0, A.add)
-    dma("S", T.yc[:], v("oc", p1=32))
-    for b in (3, 2, 0, 1):
-        for a in range(4 * b, 4 * b + 4): mm(ps(0, 0, 256), blk("II", 1, 128), blk("xb", a, 256), a == 12, False)
-    for b in range(4): mm(ps(0, 0, 256), v("HR", 512, 640, p1=96), v("hi", 256 * b, 256 * b + 256, p1=96), False, b == 3)
-    ts(v("ox"), ps(0, 0, 256), col(147), A.add)
+    for b in range(7, -1, -1):
+        if b in (0, 1, 2, 3)[:OPT["xv"]]: ts(blk("xb", b, 512), blk("XW", b, 512), -31.0, A.add)
+        else: act(blk("xb", b, 512), blk("XW", b, 512), F.Identity, bias=-31.0)
+    turns = [7, 6, 5, 0, 4, 3, 1, 2] if OPT["xv"] == 2 else [7, 6, 5, 4, 0, 3, 2, 1] if OPT["xv"] == 1 else [7, 6, 0, 5, 1, 4, 2, 3] if OPT["xv"] == 3 else [7, 6, 5, 4, 3, 2, 1, 0]
+    stack("xb", 512, 6, 0, turns)
+    if OPT["ocv"]: ts(v("oc", p1=64), ps(6, p1=64), -1.0, A.add)
+    else: act(v("oc", p1=64), ps(6, p1=64), F.Identity, bias=-1.0)
+    dma("S", T.yc[:], v("oc", p1=64))
+    for b in turns:
+        for a in (2 * b, 2 * b + 1): mm(ps(2, 0, 256), blk("II", 1, 128), blk("xb", a, 256), a == 14, False)
+    for b in range(2): mm(ps(2, 0, 256), blk("HR", 8, 128), blk("hi", b, 256), False, b == 1)
+    ts(v("ox"), ps(2, 0, 256), col(147), A.add)
     dma("Y", T.yx[:], v("ox"))
     emit(g, T, ops)
-    g.wait_ge(T.sem.sent, 2 * n_out * (RO - 1))
+    g.wait_ge(T.sem.sent, 2 * OPT["sq"] * n_out * (RO - 1))

@@ -1,42 +1,46 @@
+import math
 from concourse.mybir import AluOpType as A, ActivationFunctionType as F
 
 D, TH, RO = 4096, 1024, 5
-KW = D + 64
+KW = D + 128
 BIG = float(1 << 22)
 HB = 1600
 PB = float(HB * D)
-PAIRS = ((1, 0), (2, 1), (3, 2), (2, 0), (3, 1), (3, 0))
-TURNS = ((1, 2, 3, 4, 5, 6), (7, 8, 0, 9, 10), (11, 12, 13, 14, 15))
-NOM = dict(cyc=0.83, pe=0.42, gather=1.5, scatter=3.5, wake=220.0, dma=1800.0, rate=300.0, hop=3400.0, once=2000.0)
-OPT = dict(x0=1, xs=1.0, ar=2, hp=1, xl=4, sh=0, ga=2, sq=1, xq=0, sb=2, bb=(4, 5), wb=((7, 4, 5), (7, 4, 5)), xw=((7, 4, 5), (7,), (2, 3, 6, 2)), ls=0, bs=0, ns=0, es=0, bg=0, nw=0, two=0, mv=0, cap=230, eh=0, npe=4, xv=1, ocv=0, cgv=1, gp=2, mp=2, fp=2, passes=4, wV=0.7, wS=1.5, wP=1.0, wG=1.0, wY=1.0, wX=1.0)
+RUN = (8, 4)
+NOM = dict(cyc=0.83, pe=0.42, gather=1.5, scatter=3.5, wake=220.0, dma=1800.0, rate=300.0, hop=4500.0, once=2000.0, gdma=1000.0, glag=1500.0)
+OPT = dict(npe=3, cap=230, seed=3, turns=500, shifts=4000, polish=2500, heat=100.0, heat2=60.0)
+LEAD = dict(win0=1500.0, clear=-2000.0, soon=30000.0)
+OTHER = ((1.4, 1.3, 1.6, 1.8, 1.3), (0.7, 1.0, 0.8, 0.6, 0.8), (1.5, 1.0, 1.0, 0.9, 1.6))
 
 f32, bf, i32, u16, f16 = "float32", "bfloat16", "int32", "uint16", "float16"
 SB = {
-    "K": (KW, f32), "XW": (KW + TH, f32), "xb": (KW + TH, bf), "CT": (D, bf), "ci": (256, i32), "ch": (256, bf),
+    "K": (KW, f32), "XW": (KW + TH, f32), "CT": (D, bf), "xb": (D, bf), "NC": (TH, f32),
+    "ci": (256, i32), "ch": (256, bf), "d0": (256, bf), "d1": (256, bf), "r0": (256, f32), "r1": (256, f32), "z3": (TH, bf),
     "Ga": (TH, f32), "Gb": (TH, f32), "Ab": (TH, f32), "Bb": (TH, f32), "X1": (TH, bf), "X2": (TH, bf),
-    "Cg0": (TH, bf), "Cg1": (TH, bf), "Cg2": (TH, bf), "eq": (2560, bf), "sq": (512, bf), "hi": (TH, bf),
+    "Cg0": (TH, bf), "Cg1": (TH, bf), "Cg2": (TH, bf), "sq": (512, bf), "hi": (TH, bf),
     "T3": (256, f32), "H3": (768, f16), "off": (192, u16), "cab": (192, bf), "P1": (64, f16), "cB": (64, f16),
-    "e01": (64, bf), "nok": (64, bf), "AR": (320, f16), "nd": (160, bf), "pk": (64, bf), "w": (128, f32),
-    "Qn": (64, f16), "e0": (64, bf), "nk8": (64, bf), "CA": (320, bf), "XH": (160, f32), "IF": (128, f32),
-    "xoff": (64, u16), "soff": (64, u16), "Hk": (TH, f16), "Hn": (TH, f16),
+    "e01": (64, bf), "nok": (64, bf), "pk": (64, bf), "w": (64, f32), "xoff": (64, u16), "Qn": (64, f16),
+    "Qc": (64, f16), "CA": (32, bf), "XH": (32, f32), "own0": (256, f32), "own1": (288, f32), "eq0": (2048, bf), "eq1": (1152, bf),
+    "nd": (288, bf), "wl": (32, f32), "soff": (64, u16), "Hk": (TH, f16), "Hn": (TH, f16),
     "oz": (TH, bf), "okk": (512, f32), "ox": (256, bf), "oc": (512, f32),
-    "pi": (48, i32), "pj": (48, i32), "pc": (192, f32), "n256": (256, bf), "io": (576, bf), "JX": (64, f32),
-    "Sel": (128, f32), "Mq": (128, f32), "Rb": (32, f32), "Rh": (64, bf), "RA": (160, f32), "RH": (320, bf),
-    "crow": (256, bf), "one": (512, bf), "nil": (128, bf), "PI": (RO * 128, bf), "WB": (256, bf), "MK": (768, bf),
-    "SQ": (RO * 64, bf), "Y": (288, bf), "Id": (8 * 128, bf), "II": (256, bf), "PK": (256, bf), "Z": (16 * 160, bf),
-    "BR": (512, bf), "L": (16 * 128, bf), "SH": (16 * 128, bf), "E": (15 * 128, bf), "HX": (136, bf), "HR": (10 * 128, bf),
+    "pi": (48, i32), "pj": (48, i32), "pc": (192, f32), "n256": (256, bf), "io": (480, bf), "JX": (64, f32),
+    "SP": (32, f32), "ri": (48, i32), "rf": (34, f32), "ro0": (16, u16), "ro1": (18, u16), "qo": (2, u16), "so": (2, u16),
+    "Sel": (64, f32), "Mq": (128, f32), "Mh": (128, f32),
+    "Rb": (32, f32), "Rh": (64, bf), "RP": (32, f32), "RQ": (64, bf), "IF": (128, f32),
+    "crow": (128, bf), "one": (512, bf), "PI": (RO * 128, bf), "WB": (256, bf), "MK": (768, bf),
+    "SQ": (RO * 64, bf), "Y": (288, bf), "Id": (8 * 128, bf), "II": (256, bf), "PK": (128, bf), "Zb": (160, bf), "Z": (16 * 160, bf),
+    "L": (16 * 128, bf), "SH": (16 * 128, bf), "E": (8 * 128, bf), "HX": (136, bf), "HR": (10 * 128, bf),
 }
 for _t in range(RO):
     SB["s%d" % _t] = (TH, bf)
-    for _h in range(2 if _t else 0):
+    for _h in range(2):
         SB["z%d%d" % (_t, _h)] = (TH // 2, bf)
 SCRATCH = {n: ("sbuf", [128, c], d) for n, (c, d) in SB.items()}
 for _b in range(8):
     SCRATCH["p%d" % _b] = ("psum", [128, 512], f32)
-SEMAPHORES = ["eV", "eS", "eP", "eG", "sent"] + ["arr%d%d%d" % (t, h, q) for t in range(1, RO) for h in range(2) for q in range(2)] + ["d%d" % k for k in range(24)]
-RANK = ["hop", "count", "last1", "fault1", "win1", "last0", "fault0", "old", "back", "leave1", "leave0", "win0", "run", "row", "xrun", "mask0", "mask", "end"]
-LEAD = {'run': -500, 'back': 500, 'endP': -500, 'xrunS': -500, 'win0P': 500, 'leave1S': -500, 'table': 500, 'leave0P': -500, 'backP': 500, 'fault1V': 500, 'win1': -500, 'fault0': 1000, 'mask0': -1000, 'hop': 1000, 'leave0V': 1000, 'fault0P': -1000, 'hopV': -1000, 'win1P': -1000, 'clear': 1000, 'fault0V': -1000, 'last0P': -1000, 'endS': -1000, 'leave1': 1500, 'last1': -1500, 'endV': -1500, 'oldS': 1500, 'backV': -2000, 'rowP': 2000, 'xrun': 2000, 'old': -2000, 'count': -2000, 'last0': 3000, 'end': 4000}
+SEMAPHORES = ["eV", "eS", "eP", "eG", "sent"] + ["arr%d%d" % (t, h) for t in range(1, RO) for h in range(2)] + ["d%d" % k for k in range(32)]
 DBG = []
+LAND = {}
 PLAN = []
 
 
@@ -46,7 +50,7 @@ def v(name, c0=0, c1=None, step=1, p0=0, p1=128):
 
 def meet(a, b):
     if a[2] <= b[1] or b[2] <= a[1] or a[5] <= b[4] or b[5] <= a[4]: return False
-    return not (a[3] == b[3] > 1 and (a[1] - b[1]) % a[3])
+    return (a[1] - b[1]) % math.gcd(a[3], b[3]) == 0
 
 
 def covers(a, b):
@@ -88,38 +92,150 @@ def free(ops, m, n):
 def plan(ops, deps):
     N = len(ops)
     gap = lambda m, n: 0.0 if free(ops, m, n) else ops[m][6] + (0.0 if ops[n][0] == "X" else NOM["wake"])
-    way = [ops[n][5] + ops[n][6] for n in range(N)]
+    before = [[(m, gap(m, n)) for m in sorted(deps[n])] for n in range(N)]
+    cost, eng, lag = [o[5] for o in ops], [o[0] for o in ops], [o[6] for o in ops]
+    for n in range(N):
+        land = [LAND[m] for m in deps[n] if m in LAND and not free(ops, m, n)]
+        if land: before[n].append((0, max(land) + NOM["wake"] - cost[0]))
+    way = [cost[n] + lag[n] for n in range(N)]
     for n in range(N - 1, -1, -1):
-        for m in deps[n]: way[m] = max(way[m], ops[m][5] + gap(m, n) + way[n])
-    before = [[(m, gap(m, n)) for m in deps[n]] for n in range(N)]
+        for m, x in before[n]: way[m] = max(way[m], cost[m] + x + way[n])
+    kind, seen, one, many = [], {}, {}, {}
+    for n, o in enumerate(ops):
+        k, t = (o[7] and o[7][1], o[0], o[3][0][0] if o[3] and o[3][0][0][0] not in "sz" else ""), o[7] and o[7][0]
+        seen[k, t] = seen.get((k, t), 0) + 1
+        kind.append(k + (seen[k, t],))
+        one.setdefault(kind[n], []).append(n)
+        many.setdefault(k, []).append(n)
+
+    way = [way[n] + LEAD.get(kind[n][0], 0.0) for n in range(N)]
     after = [[] for n in range(N)]
     for n in range(N):
-        for m, x in before[n]: after[m].append((n, x))
+        for m, x in before[n]: after[m].append(n)
+    tails = [n for n in range(N) if not after[n]]
 
-    def lay(order, links, least):
-        end, taken = [0.0] * N, {}
-        for n in order:
-            t, c = max([end[m] + x for m, x in links[n]] + [least[n]]), ops[n][5]
-            slots = taken.setdefault(ops[n][0], [])
-            lo, hi = 0, len(slots)
+    def lay(key, moved=None, up=True):
+        for n in range(N - 1, -1, -1) if moved is None else ():
+            for m, x in before[n]:
+                if key[m] <= key[n]: key[m] = key[n] + 1.0
+        todo = list(moved or ())
+        while todo:
+            n = todo.pop()
+            for m in [m for m, x in before[n] if key[m] <= key[n]] if up else [m for m in after[n] if key[m] >= key[n]]:
+                key[m] = key[n] + (1.0 if up else -1.0)
+                todo.append(m)
+        end, taken = [0.0] * N, {e: ([], []) for e in eng}
+        for n in sorted(range(N), key=lambda n: key[n], reverse=True):
+            t, c, (s, f) = 0.0, cost[n], taken[eng[n]]
+            for m, x in before[n]:
+                x += end[m]
+                if x > t: t = x
+            lo, hi = (len(s), 0) if not f or f[-1] <= t else (0, len(s))
             while lo < hi:
                 mid = (lo + hi) // 2
-                if slots[mid][1] <= t: lo = mid + 1
+                if f[mid] <= t: lo = mid + 1
                 else: hi = mid
-            while lo < len(slots) and slots[lo][0] < t + c:
-                t = max(t, slots[lo][1])
+            hi = len(s)
+            while lo < hi and s[lo] < t + c:
+                t = f[lo]
                 lo += 1
-            slots.insert(lo, (t, t + c))
+            s.insert(lo, t)
+            f.insert(lo, t + c)
             end[n] = t + c
-        return end
+        return max(end[n] + lag[n] for n in tails), end, key
 
-    key = [way[n] + (LEAD.get(ops[n][7][1], 0.0) + LEAD.get(ops[n][7][1] + ops[n][0], 0.0) if ops[n][7] else 0.0) for n in range(N)]
-    for n in range(N - 1, -1, -1):
-        for m in deps[n]: key[m] = max(key[m], key[n] + 1.0)
-    end = lay(sorted(range(N), key=lambda n: (-key[n], n)), before, [0.0] * N)
-    best = (max(end[n] + ops[n][6] for n in range(N)), end)
+    def bound(end, before=before):
+        last, prev, out = {}, {}, []
+        for n in sorted(range(N), key=lambda n: end[n]):
+            prev[n] = last.get(eng[n])
+            last[eng[n]] = n
+        n = max(range(N), key=lambda n: end[n] + lag[n])
+        while n is not None:
+            t, m = max([(end[k] + x, k) for k, x in before[n]] + [(-1.0, None)], key=lambda p: p[0])
+            if prev[n] is not None and end[prev[n]] > t + 1:
+                m = prev[n]
+                out.append((m, n))
+            n = m
+        return out
+
+    state = [OPT["seed"]]
+
+    def pick(k):
+        state[0] = (state[0] * 6364136223846793005 + 1442695040888963407) % (1 << 64)
+        return (state[0] >> 33) % k
+
+    lead = {}
+    now = best = lay(list(way))
+    pairs = bound(now[1])
+    for it in range(OPT["turns"]):
+        new = dict(lead)
+        for k in range(1 + (pick(3) == 0)):
+            m, n = pairs[pick(len(pairs))]
+            x = now[2][m] - now[2][n]
+            if x <= 0: new[kind[n]] = new.get(kind[n], 0.0) + (100, 300, 1000)[pick(3)]
+            elif pick(2): new[kind[n]] = new.get(kind[n], 0.0) + x + (10, 100, 300)[pick(3)]
+            else: new[kind[m]] = new.get(kind[m], 0.0) - x - (10, 100, 300)[pick(3)]
+        y = lay([way[n] + new.get(kind[n], 0.0) for n in range(N)])
+        if y[0] <= now[0] + OPT["heat"] * (1 - it / OPT["turns"]) * pick(1000) / 1000:
+            now, lead = y, new
+            pairs = bound(now[1])
+            if y[0] < best[0]: best = y
+
+    def shift(now, pairs):
+        key = [cost[n] - now[1][n] - 1e-6 * n for n in range(N)]
+        m, n = pairs[pick(len(pairs))]
+        how = pick(4)
+        if how == 0: n, x = m, -(cost[n] + 10, 300, 600, 1200)[pick(4)]
+        elif how == 1: x = (cost[m] + 10, 300, 600, 1200)[pick(4)]
+        else: n, x = pick(N), (-1500, -800, -400, -200, 200, 400, 800, 1500)[pick(8)]
+        group = one[kind[n]] if pick(2) else many[kind[n][:3]]
+        for k in group: key[k] += x
+        return lay(key, group, x > 0)
+
+    now = best
+    pairs = bound(now[1])
+    for it in range(OPT["shifts"]):
+        y = shift(now, pairs)
+        if y[0] <= now[0] + OPT["heat2"] * (1 - it / OPT["shifts"]) * pick(1000) / 1000:
+            now = y
+            pairs = bound(now[1])
+            if y[0] < best[0]: best = y
+
+    sort = ["s" if o[7] and o[7][1] in ("run", "xrun") else "g" if o[2][1:] and SCRATCH[o[2][1][0]][2] == u16 else "d" if o[4] else "c" for o in ops]
+    other = []
+    for wake, fc, fg, fs, fr in OTHER:
+        f = dict(s=fs, g=fg, d=1.0, c=fc)
+        other.append(([cost[n] * f[sort[n]] for n in range(N)],
+                      [[(m, x and x + lag[m] * (fr - 1.0) * (ops[m][4] == "call") + NOM["wake"] * (wake - 1.0)) for m, x in before[n]] for n in range(N)]))
+
+    def judge(y):
+        order, ends = sorted(range(N), key=lambda n: (y[1][n] - cost[n], n)), [y[1]]
+        for c, b in other:
+            end, busy = [0.0] * N, {e: 0.0 for e in eng}
+            for n in order:
+                t = busy[eng[n]]
+                for m, x in b[n]:
+                    x += end[m]
+                    if x > t: t = x
+                end[n] = busy[eng[n]] = t + c[n]
+            ends.append(end)
+        return [max(e[n] + lag[n] for n in tails) for e in ends], ends
+
+    bounds = lambda ends: [p for e, b in zip(ends, [before] + [b for c, b in other]) for p in bound(e, b)]
+    now = best
+    unit, ends = judge(now)
+    mark = top = float(len(unit))
+    pairs = bounds(ends)
+    for it in range(OPT["polish"]):
+        y = shift(now, pairs)
+        if y[0] > now[0] + 600: continue
+        times, ends = judge(y)
+        got = sum(a / b for a, b in zip(times, unit))
+        if got <= mark + 0.002 * (1 - it / OPT["polish"]) * pick(1000) / 1000:
+            now, mark, pairs = y, got, bounds(ends)
+            if got < top: best, top = y, got
     DBG[:] = [ops, before, best]
-    return sorted(range(N), key=lambda n: (best[1][n] - ops[n][5], n))
+    return sorted(range(N), key=lambda n: (best[1][n] - cost[n], n))
 
 
 def emit(g, T, ops):
@@ -217,21 +333,25 @@ def rank_program(g, core, T, topo):
     def cp(out, a): add("V", lambda: V.tensor_copy(ap(out), ap(a)), out, [a])
     def ms(out, c): add("V", lambda: V.memset(ap(out), c), out, [])
 
-    def act(out, a, fn, bias=None, scale=None):
+    def act(out, a, fn=F.Identity, bias=None, scale=None):
         kw = {k: x for k, x in (("bias", bias), ("scale", scale)) if x is not None}
         add("S", lambda: S.activation(ap(out), ap(a), fn, **{k: ap(x) for k, x in kw.items()}), out, [a, bias, scale])
 
-    def mm(out, l, r, st, sp):
+    def mm(out, l, r, st, sp, alone=False):
         add("P", lambda: P.matmul(ap(out), ap(l), ap(r), bool(st), bool(sp)), out, [l, r], cost=max(64, size(r)) * (1 if short(l) else 4) * NOM["pe"])
         a, b = ops[-2], ops[-1]
-        if a[0] == "P" and a[3][0][0] == out[0] and (a[2][-2][0] == l[0] or a[2][-1][0] == r[0]) and a[5] + b[5] <= (OPT["cap"] if now[1] != "end" else 120):
+        if not alone and a[0] == "P" and a[3][0][0] == out[0] and (a[2][-2][0] == l[0] or a[2][-1][0] == r[0]) and a[5] + b[5] <= (OPT["cap"] if now[1] != "end" else 120):
             ops[-2:] = [("P", lambda: (a[1](), b[1]())[1], a[2] + b[2], a[3] + b[3], None, a[5] + b[5], 0.0, a[7])]
 
-    def dma(e, out, a):
-        x = out if isinstance(out, tuple) else a
+    def dma(e, out, a, row=None, after=()):
+        x = a if row is not None or not isinstance(out, tuple) else out
         n = size(x) * (x[5] - x[4]) * (2 if short(x) else 4) / NOM["rate"]
-        if x is out: loaded[0] += n
-        add(e, lambda: (g.sync if e == "Y" else S).dma_start(ap(out), ap(a)), out, [a], "dma", 50.0, NOM["dma"] + (loaded[0] * (OPT["xs"] if x[0] == "xb" else 1) if x is out else n))
+        if isinstance(out, tuple):
+            loaded[0] += n
+            LAND[len(ops)] = NOM["dma"] + loaded[0]
+        to = (lambda: ap(out)) if row is None else (lambda: T[out[0]][row:128:16, out[1]:out[2]])
+        add(e, lambda: {"Y": g.sync, "S": S, "G": g}[e].dma_start(to(), ap(a)), out, [a] + list(after), "dma", NOM["gdma"] if e == "G" else 50.0,
+            NOM["glag" if e == "G" else "dma"] + n)
 
     def iota(out, pat, base, cm=0):
         kw = {} if SB[out[0]][1] == i32 else {"allow_small_or_imprecise_dtypes": True}
@@ -239,23 +359,22 @@ def rank_program(g, core, T, topo):
 
     at = lambda win, off: ("at", win, off)
     ps = lambda b, c0=0, c1=512, step=1, p0=0, p1=128: v("p%d" % b, c0, c1, step, p0, p1)
-    R = lambda name, h: v(name, 512 * h, 512 * h + 512)
+    R = lambda name, h, i=0, n=1: v(name, 512 * h + i, 512 * h + 512, n)
     W = lambda name, h, m=0: v(name, 64 * m + 32 * h, 64 * m + 32 * h + 32)
     blk = lambda name, k, n: v(name, k * n, k * n + n)
     part = lambda x, i, n: (x[0], x[1] + (x[2] - x[1]) // n * i, x[1] + (x[2] - x[1]) // n * (i + 1)) + x[3:]
     col = lambda c: v("pc", c, c + 1)
     pcs = lambda c, n: v("pc", c, c + n)
     num = lambda a, b: v("n256", a, b)
-    z = lambda t, h: v("z%d%d" % (t, h)) if t else v("xb", KW + 512 * (1 - h), KW + 512 * (2 - h))
+    z = lambda t, h: v("z%d%d" % (t, h))
+    Id = lambda k: blk("Id", k, 128)
 
-    for h in (1, 0):
-        dma("S", z(0, h), T.zin[:, 512 * h:512 * h + 512])
-        dma("Y", R("K", h), T.nkey[:, 512 * h:512 * h + 512])
+    for k in range(3): dma("S", v("z3", p0=8 * k, p1=8 * k + 8), T.zin[k:128:16, :])
     dma("S", v("ci"), T.cnt[:])
+    for h in (1, 0): dma("Y", R("K", h), T.nkey[:, 512 * h:512 * h + 512])
     dma("Y", v("K", TH, D), T.nkey[:, TH:D])
-    for c in range(OPT["xl"]): dma("Y", part(v("xb", 0, D), c, OPT["xl"]), T.xreg[:, D // OPT["xl"] * c:D // OPT["xl"] * (c + 1)])
 
-    ioA, ioB, ioC, ioD, ioE, ioR = v("io", 0, 64), v("io", 64, 192), v("io", 192, 320), v("io", 320, 448), v("io", 448, 480), 480
+    ioA, ioB, ioC, ioD, ioE = v("io", 0, 64), v("io", 64, 192), v("io", 192, 320), v("io", 320, 448), v("io", 448, 480)
     iota(v("pi", 0, 1), [[0, 1]], 0, 1)
     iota(v("pi", 8, 13), [[16, RO]], 0, 1)
     iota(v("n256"), [[1, 256]], 0)
@@ -266,10 +385,9 @@ def rank_program(g, core, T, topo):
     iota(ioD, [[0, 8], [1, 4], [0, 4]], 0)
     iota(v("pi", 16, 32), [[-1, 16]], 16, 1)
     iota(v("pi", 32, 40), [[1, 8]], 1, 1)
-    for k, (c, n) in enumerate(((0, 3), (24, 2), (40, 1))):
-        iota(v("io", ioR + c, ioR + c + 8 * n), [[1, n], [4, 8]], k + 1)
-        iota(v("io", ioR + 48 + c, ioR + 48 + c + 8 * n), [[1, n], [4, 8]], 0)
-    for h in range(2): iota(W("JX", h), [[16, 32]], KW - D // 2 + 512 * (1 - h), 1)
+    iota(v("SP"), [[16, RUN[0]], [0, 32 // RUN[0]]], D // 2, 1)
+    iota(v("rf", 0, 18), [[16, 18]], 0, 1)
+    for h in range(2): iota(W("JX", h), [[16, 32]], KW - D // 2 + 512 * h, 1)
     bits = [(0, 127), (0, 15), (4, 7), (0, 3), (2, 31), (3, 7), (0, 1), (1, 3), (0, 7), (0, 7)]
     cP, cA, cG, cM3, cP2, cGQ, cDUP, cMQ, c7 = range(9)
     for c, (sh, mk) in enumerate(bits): ts(v("pj", c, c + 1), v("pi", 0, 1), sh, A.arith_shift_right, mk, A.bitwise_and)
@@ -288,9 +406,11 @@ def rank_program(g, core, T, topo):
     tt(pcs(40, 5), pcs(40, 5), pcs(48, 5), A.mult)
     tt(pcs(32, 5), pcs(32, 5), pcs(40, 5), A.mult)
     ts(pcs(24, 5), pcs(32, 5), -300.0, A.add)
-    for t in range(RO): ts(blk("SQ", t, 64), ioA, col(24 + t), A.is_equal)
+    ts(col(30), col(c7), 4.0, A.mult, col(cGQ), A.add)
+    for t in range(RO): ts(blk("SQ", t, 64), ioA, col(24 + t if t else 30), A.is_equal)
     ts(col(16), col(cDUP), 2.0, A.mult, -1.0, A.add)
     ts(col(17), col(cDUP), -1.0, A.add)
+    ts(col(169), col(cDUP), -128.0, A.add)
     ts(col(18), col(cA), 1.0, A.add, col(cA), A.mult)
     ts(col(19), col(18), -1.0, A.mult, 1.0, A.add)
     ts(col(20), col(18), -BIG, A.mult, BIG, A.add)
@@ -299,64 +419,72 @@ def rank_program(g, core, T, topo):
     ts(blk("WB", 0, 128), ioC, col(16), A.mult, col(17), A.add)
     ts(blk("WB", 1, 128), ioB, col(cGQ), A.is_equal)
     tt(blk("WB", 0, 128), blk("WB", 0, 128), blk("WB", 1, 128), A.mult)
-    for m in range(6): ts(blk("MK", m, 128), blk("WB", 0, 128), col(56 + m // 2 + 4 * (m % 2)), A.mult)
-    ts(col(95), col(cA), 1.0, A.add)
-    for t in range(1, RO): ts(blk("BR", t - 1, 128), ioB, col(10 + t), A.is_equal, col(64 + 3 * t), A.mult)
-    for k, wt in enumerate((1.0, 1.0 / D, 1.0 / BIG, 1.0 / BIG / D)): ts(blk("Sel", k, 32), ioE, col(cG), A.is_equal, wt, A.mult)
+    for m in range(6): act(blk("MK", m, 128), blk("WB", 0, 128), scale=col(56 + m // 2 + 4 * (m % 2)))
+    for k, wt in enumerate((1.0, 1.0 / BIG)): ts(blk("Sel", k, 32), ioE, col(cG), A.is_equal, wt, A.mult)
     ts(v("Mq"), ioD, col(cM3), A.is_equal)
+    ts(v("Mh"), ioD, col(cM3), A.is_equal, 1.0 / D, A.mult)
     ts(v("Rb"), num(0, 32), col(cP2), A.is_equal)
     ts(blk("Rh", 0, 32), num(0, 32), col(cP2), A.is_equal, -float(D), A.mult)
     ts(blk("Rh", 1, 32), num(0, 32), col(cP2), A.is_equal)
     ms(v("one", p1=32), 1.0)
-    ms(v("nil", p1=32), 0.0)
     ts(pcs(80, 3), num(0, 3), col(cP), A.is_equal)
-    ts(col(83), col(80), float(HB), A.mult)
-    ts(col(84), col(81), -0.5, A.mult, col(83), A.add)
-    ts(col(85), col(82), 0.5 / D, A.mult, col(84), A.add)
-    ts(v("crow"), num(0, 256), 127.5, A.is_gt, col(85), A.mult)
+    ts(col(83), col(80), PB, A.mult)
+    ts(col(84), col(81), -float(D // 2), A.mult, col(83), A.add)
+    ts(col(85), col(82), 0.5, A.mult, col(84), A.add)
+    ts(v("crow"), num(0, 128), 0.0, A.mult, col(85), A.add)
     ts(col(22), col(cP), 16.0, A.add)
-    for a in range(16): ts(blk("Z", a, 160), num(0, 160), col(22), A.is_equal, col(64 + a), A.mult)
-    cp(v("ch"), v("ci"))
+    stage("soon", 0)
+    ts(v("Zb"), num(0, 160), col(22), A.is_equal)
+    stage(None)
+    for a in range(16): act(blk("Z", a, 160), v("Zb"), scale=col(64 + a))
     ts(col(86), col(21), 16.0, A.add)
-    ts(col(87), col(cP), 128.0, A.add)
     ts(col(88), col(64), -1.0, A.mult, 1.0, A.add)
-    ts(col(89), col(64), 512.0, A.mult)
-    ts(col(92), col(64), 31.0, A.add)
+    ts(col(89), col(64), 16.0, A.mult)
+    ts(col(91), col(64), 1.0 / 32, A.mult)
+    ts(col(92), col(65), 159.0, A.mult, -128.0, A.add)
+    ts(col(95), col(64), 128.0, A.mult, col(92), A.add)
+    ts(col(90), col(95), -1.0, A.mult)
+    ts(col(168), col(65), 32.0, A.mult)
     ts(col(93), col(64), col(cP), A.add)
     ts(col(94), col(64), 15.0, A.mult, 1.0, A.add)
-    for k, wt in enumerate((1.0, -1.0 / D, -2048.0 / BIG, 2048.0 / BIG, 2.0 if OPT["two"] else -512.0 / D, -8192.0)):
-        ts(blk("Id", k, 128), num(0, 128), col(cP), A.is_equal, wt, A.mult)
-    ts(blk("Id", 6, 128), num(0, 128), col(cP), A.is_equal, col(64), A.mult)
-    ts(blk("Id", 7, 128), ioB, col(cG), A.is_equal, float(D), A.mult)
-    ts(blk("Y", 0, 144), num(0, 144), col(86), A.is_equal, col(64), A.mult)
+    ts(Id(0), num(0, 128), col(cP), A.is_equal)
+    for k, wt in enumerate((-1.0 / D, 16.0, 2048.0 / BIG, -512.0 / D, -8192.0)): act(Id(k + 1), Id(0), scale=wt)
+    act(Id(6), Id(0), scale=col(64))
+    ts(Id(7), ioB, col(cG), A.is_equal, float(D), A.mult)
+    ts(blk("Y", 0, 144), num(0, 144), col(86), A.is_equal, col(91), A.mult)
     ts(blk("Y", 1, 144), num(0, 144), col(86), A.is_equal, col(89), A.mult)
-    ts(blk("II", 0, 128), num(0, 128), col(cP), A.is_equal, col(88), A.mult)
-    ts(blk("II", 1, 128), num(128, 256), col(87), A.is_equal, col(88), A.mult)
-    for k in range(2): ts(blk("PK", k, 128), num(0, 128), col(93), A.is_equal, col(94), A.mult)
-    ts(col(90), col(65), -16.0, A.mult, col(92), A.add)
-    ms(v("xb", D, KW), 0.0)
-    for a in range(16):
-        if a < OPT["ls"]: act(blk("L", a, 128), blk("Id", 7, 128), F.Identity, scale=col(64 + a))
-        else: ts(blk("L", a, 128), blk("Id", 7, 128), col(64 + a), A.mult)
-    for k in range(2):
-        ts(v("RA", 80 * k, 80 * k + 48), v("io", ioR + 48 * k, ioR + 48 * k + 48), col(cP2), A.is_equal)
-        ts(v("RA", 80 * k + 48, 80 * k + 80), num(0, 32), col(cP2), A.is_equal)
-    for k, wt in enumerate((-float(D), 1.0)): act(blk("RH", k, 160), v("RA"), F.Identity, scale=wt)
+    for k in range(2): act(blk("II", k, 128), Id(0), scale=col(88))
+    ts(v("PK"), num(0, 128), col(93), A.is_equal, col(94), A.mult)
+    for a in range(16): act(blk("L", a, 128), Id(7), scale=col(64 + a))
+    for k, (sh, mk) in enumerate(((2, 3), (3, 1))): ts(v("pj", 40 + k, 41 + k), v("pi", 0, 1), sh, A.arith_shift_right, mk, A.bitwise_and)
+    cp(pcs(160, 2), v("pj", 40, 42))
+    ts(col(164), col(160), 8.0, A.mult, col(cG), A.add)
+    ts(v("RP"), num(0, 32), col(164), A.is_equal)
+    ts(blk("RQ", 0, 32), num(0, 32), col(164), A.is_equal, -float(D), A.mult)
+    ts(blk("RQ", 1, 32), num(0, 32), col(164), A.is_equal)
+    ts(col(165), col(cM3), 8.0, A.mult, col(160), A.add)
+    ts(v("qo"), num(0, 2), 4.0, A.mult, col(165), A.add)
+    ts(col(166), col(c7), 4.0, A.mult, col(161), A.add)
+    ts(v("so"), num(0, 2), 2.0, A.mult, col(166), A.add)
+    ts(v("rf", 0, 18), v("rf", 0, 18), col(21), A.subtract)
+    ts(v("ro1"), v("rf", 0, 18), 1.0 / 9, A.mult, -4.0 / 9, A.add)
+    ts(v("ri", 0, 16), v("rf", 0, 16), 1.0 / 8, A.mult, -3.5 / 8, A.add)
+    ts(v("ri", 16, 32), v("ri", 0, 16), 3, A.bitwise_and)
+    ts(v("ri", 32, 48), v("ri", 0, 16), 2, A.arith_shift_right)
+    ts(v("rf", 18, 34), v("ri", 16, 32), 8.0, A.mult)
+    tt(v("rf", 18, 34), v("rf", 18, 34), v("ri", 32, 48), A.add)
+    cp(v("ro0"), v("rf", 18, 34))
+    ts(v("SP"), v("SP"), col(21), A.subtract)
     ts(v("JX"), v("JX"), col(21), A.subtract)
     ts(pcs(120, 4), num(0, 4), 16.0, A.mult, col(cA), A.add)
     ts(pcs(120, 4), pcs(120, 4), float(D // 2), A.add)
     for t in range(RO): ts(v("PI", 128 * t, 128 * t + 128, p1=32), v("io", 192, 320, p1=32), float(t), A.not_equal, BIG, A.mult)
     ts(v("PI", p1=32), v("PI", p1=32), -1.5 * D, A.add)
-    act(v("XW", D, KW), num(64, 128), F.Silu)
+    add("S", lambda: S.activation(ap(v("XW", D, KW)), ap(num(64, 192)), F.Silu), v("XW", D, KW), [num(64, 192)], cost=1400.0)
     ts(pcs(96, 16), pcs(96, 16), col(21), A.add)
     ts(pcs(112, 8), pcs(112, 8), col(cA), A.max, col(21), A.add)
     for s in range(16): ts(blk("SH", s, 128), num(0, 128), col(96 + s), A.is_equal)
-    if OPT["sh"]:
-        ts(pcs(160, 15), num(1, 16), col(cA), A.add, 16.0, A.is_lt)
-        ts(pcs(176, 15), num(2, 17), col(cP), A.add)
-        tt(pcs(160, 15), pcs(160, 15), pcs(176, 15), A.mult)
-        for s in range(15): ts(blk("E", s, 128), num(1, 129), col(160 + s), A.is_equal)
-    for s in range(0 if OPT["sh"] else 8): ts(blk("E", s, 128), num(0, 128), col(112 + s), A.is_equal)
+    for s in range(8): ts(blk("E", s, 128), num(0, 128), col(112 + s), A.is_equal)
     ts(col(124), col(cA), 8.0, A.mult, col(cG), A.add)
     ts(col(124), col(124), 8.0, A.mult, 8.0, A.add)
     ts(v("HX"), num(0, 136), col(124), A.is_equal)
@@ -367,277 +495,234 @@ def rank_program(g, core, T, topo):
     ts(blk("HR", 9, 128), num(0, 128), col(127), A.is_equal, col(15), A.mult)
     tt(blk("HR", 8, 128), blk("HR", 8, 128), blk("HR", 9, 128), A.add)
     ts(pcs(148, 8), num(0, 8), col(c7), A.is_equal)
-    for b in range(8): ts(blk("HR", b, 128), blk("HR", 8, 128), col(148 + b), A.mult)
-    ts(col(129), col(65), 2560.0, A.mult, -1.0, A.add)
-    ts(col(131), col(64), -159.0, A.mult, col(129), A.add)
+    for b in range(8): act(blk("HR", b, 128), blk("HR", 8, 128), scale=col(148 + b))
+    ts(col(129), col(65), 2687.0, A.mult, -128.0, A.add)
+    ts(col(131), col(64), -32.0, A.mult, col(129), A.add)
     ts(col(147), col(131), 16.0, A.mult)
-    act(v("IF"), blk("Id", 0, 128), F.Identity)
-
-    Id = lambda k: blk("Id", k, 128)
+    act(v("IF"), Id(0))
 
     def front(t, h):
-        for q in range(2): mm(ps(7, 256 * h, 256 * h + 256, 1, 64 * q, 64 * q + 64), blk("SQ", t, 64), part(z(t, h), q, 2), True, True)
-        act(blk("sq", h, 256), ps(7, 256 * h, 256 * h + 256), F.Square, bias=col(cDUP if t == 0 else 17))
+        src = z(t, h) if t else v("z3", 512 * h, 512 * h + 512, p1=24)
+        for q in range(2): mm(ps(7, 256 * h, 256 * h + 256, 1, 64 * q, 64 * q + 64), v("SQ", 64 * t, 64 * t + 64, p1=src[5]), part(src, q, 2), True, True)
+        act(blk("sq", h, 256), ps(7, 256 * h, 256 * h + 256), F.Square, bias=col(169 if t else cDUP))
 
     def mask(m, h, bank):
         for q in range(2): mm(part(ps(bank), q, 2), blk("MK", 2 * m + q, 128), blk("sq", h, 256), True, True)
-        n = OPT["mp"]
-        for q in range(n):
-            if m < 2: act(part(ps(bank) if m == 0 else R("X1", h), q, n), part(ps(bank), q, n), F.Relu, bias=col(19))
-            else: act(part(R("X2", h), q, n), part(ps(bank), q, n), F.Relu, bias=col(20), scale=BIG)
+        for q in range(2):
+            if m < 2: act(part(ps(bank) if m == 0 else R("X1", h), q, 2), part(ps(bank), q, 2), F.Relu, bias=col(19))
+            else: act(part(R("X2", h), q, 2), part(ps(bank), q, 2), F.Relu, bias=col(20), scale=BIG)
 
     def masks(t):
-        if t: stage("mask0")
         for h in (1, 0):
-            if OPT["mv"] and t:
-                for q in range(2): mm(part(ps(2 + h), q, 2), blk("BR", t - 1, 128), part(z(t, h), q, 2), True, True)
-                for q in range(2): ts(part(ps(2 + h), q, 2), part(ps(2 + h), q, 2), col(95), A.is_equal)
-                stage("mask")
-                front(t, h)
-                stage("mask0")
-            else:
-                front(t, h)
-                mask(0, h, 2 + h)
-        if t: stage("mask")
+            if t: stage("mask0%d" % h)
+            front(t, h)
+            mask(0, h, 2 + h)
         for m in (1, 2):
-            for h in (1, 0): mask(m, h, 7 - h)
+            for h in (1, 0):
+                if t: stage("mask%d%d" % (m, h))
+                mask(m, h, 7 - h)
 
-    def table(name, c, bank):
-        for a in (2 * c, 2 * c + 1):
-            o = part(ps(bank), a % 2, 2)
-            if name == "XW": mm(o, blk("PK", 0, 128), blk("xb", a, 256), True, False)
-            mm(o, v("Z", 160 * a + 16 + a, 160 * a + 144 + a), v("ch"), name == "CT", True)
-        act(blk(name, c, 512), ps(bank), F.Identity, bias=32.0 if name == "XW" else 1.0)
+    def tables():
+        stage("table", 0)
+        for c in range(6): act(blk("CT", c, 256), v("n256"))
+        ms(v("CT", 6 * 256), 0.0)
+        ts(v("ch"), v("ci"), 32.0, A.mult, 64.0, A.add)
+        add("S", lambda: S.activation(ap(v("r0")), ap(v("ch")), F.Identity, bias=-32.0), v("r0"), [v("ch"), v("CT")])
+        dma("Y", v("CT"), v("ch"), 0)
+        for k in range(2): dma("Y", v("d%d" % k), T.xreg[k:128:16, :])
+        for h in (1, 0): dma("Y", z(0, h), T.zin[:, 512 * h:512 * h + 512])
+        dma("Y", v("XW", 0, D, 1, 0, 1), v("r0"), 0)
+        for k in range(8):
+            dma("G", v("XW", 0, D, 1, 16 * k + 2, 16 * k + 16), T.xreg[16 * k + 2:16 * k + 16, :],
+                after=[v(x) for x in ("pi", "n256", "io", "SP", "rf", "JX", "r0")])
+        mm(ps(5, 0, 256), Id(2), v("d0"), True, False)
+        mm(ps(5, 0, 256), Id(0), v("d1"), False, True)
+        act(v("r1"), ps(5, 0, 256), bias=32.0)
+        dma("Y", v("XW", 0, D, 1, 1, 2), v("r1"), 1)
 
     Gs = ["Ga", "Gb", "Ga", "Ab"]
 
     def gather(m, h):
-        n = OPT["fp"] if m == 0 else OPT["gp"] if m < 3 else OPT["ga"]
-        if m == 3 and OPT["ar"] > 2 * h:
-            k = min(2, OPT["ar"] - 2 * h)
-            a, b = 32 * h, 32 * h + 16 * k
-            act(v("Gb", 16 * a, 16 * b), at(v("K", 0, D), v("off", 128 + a, 128 + b)), F.Identity)
-            if k == 1: tt(part(R("Ab", h), 1, 2), at(v("K", 0, D), part(W("off", h, 2), 1, 2)), part(R("X2", h), 1, 2), A.subtract)
+        if m == 3 and h == 0:
+            act(R("Gb", h), at(v("K", 0, D), W("off", h, 2)))
             stage("clear")
-            for u in range(b // 4 - 1, a // 4 - 1, -1): tt(blk("Ab", u, 64), blk("Gb", u, 64), blk("X2", u, 64), A.subtract)
+            for i in (3, 2, 1, 0): tt(part(R("Ab", h), i, 4), part(R("Gb", h), i, 4), part(R("X2", h), i, 4), A.subtract)
             return
-        for i in range(n):
-            if m == 0: tt(part(R("Ga", h), i, n), part(R("K", h), i, n), part(ps(2 + h), i, n), A.mult)
-            else: tt(part(R(Gs[m], h), i, n), at(v("K", 0, D), part(W("off", h, m - 1), i, n)), part(R("X1" if m == 1 else "X2", h), i, n),
+        for i in range(4 if m == 0 else 2):
+            if m == 0: tt(R("Ga", h, i, 4), R("K", h, i, 4), ps(2 + h, i, 512, 4), A.mult)
+            else: tt(part(R(Gs[m], h), i, 2), at(v("K", 0, D), part(W("off", h, m - 1), i, 2)), part(R("X1" if m == 1 else "X2", h), i, 2),
                      A.mult if m < 3 else A.subtract)
 
     def turn(t, m, h):
-        if not OPT["bg"]: mm(ps(h, 0, 256), v("one", 0, 128, p1=3), v("crow", p1=3), True, False)
-        for c in range(4): mm(ps(h, c, 256, 4), v(Gs[m], 512 * h + c, 512 * h + 512, 4), blk("Sel", m // 2, 64), OPT["bg"] and c == 0, c == 3 and not OPT["bg"])
-        if OPT["bg"]: mm(ps(h, 128, 256), v("one", 0, 128, p1=3), v("crow", 128, p1=3), False, True)
+        mm(ps(h, 0, 128), v("one", 0, 128, p1=3), v("crow", p1=3), True, False)
+        for c in range(4): mm(ps(h, c, 128, 4), R(Gs[m], h, c, 4), blk("Sel", m // 2, 32), False, c == 3, True)
         H3, T3 = blk("H3", 2 * m + h, 128), blk("T3", h, 128)
-        tt(H3, ps(h, 128, 256), v("Mq"), A.mult)
         tt(T3, ps(h, 0, 128), v("Mq"), A.mult)
-        mm(ps(h, 256, 288), H3, blk("Rh", 0, 32), True, False)
-        mm(ps(h, 256, 288), T3, v("Rb"), False, True)
-        ts(W("off", h, m), ps(h, 256, 288), PB, A.add)
-        if m == 1: ts(W("P1", h), ps(h, 256, 288), PB - D // 2, A.add, 1.0 / D, A.mult)
-        if m == 2 and OPT["xq"]: ts(W("Qn", h), ps(h, 256, 288), PB - D // 2, A.add)
-        stage("count" if m < 2 else "last%d" % h)
-        if m < 2 or not OPT["two"]:
-            mm(ps(2 + h, 0, 32), H3, blk("Rh", 1, 32), True, True)
-            act(W("cab", h, m), ps(2 + h, 0, 32), F.Abs, bias=-(HB - 1.0) * D, scale=float(D))
-            if m == 2 and OPT["sh"]:
-                mm(ps(h, 320, 400), T3, v("RA", 0, 80), True, False)
-                mm(ps(h, 320, 400), H3, v("RH", 0, 80), False, True)
-                ts(v("AR", 160 * h, 160 * h + 80), ps(h, 320, 400), PB - D // 2, A.add)
-        else:
-            mm(ps(h, 320, 480), T3, v("RA"), True, False)
-            mm(ps(h, 320, 480), H3, blk("RH", 0, 160), False, True)
-            ts(blk("AR", h, 160), ps(h, 320, 480), PB - D // 2, A.add)
-            mm(ps(2 + h, 0, 160), H3, blk("RH", 1, 160), True, False)
-            for k, (_, lo) in enumerate(PAIRS): mm(ps(2 + h, 80 + 8 * k, 88 + 8 * k), Id(0), v("e01", 32 * h + lo, 32 * h + 32, 4), False, False)
-            mm(ps(2 + h, 128, 160), Id(0), W("e01", h), False, False)
-            mm(ps(2 + h, 48, 80), Id(4), W("e01", h), False, True)
-            act(blk("CA", h, 160), ps(2 + h, 0, 160), F.Abs, bias=-(HB - 1.0) * D, scale=float(D))
-            tt(blk("XH", h, 80), v("AR", 160 * h, 160 * h + 80), v("CA", 160 * h, 160 * h + 80), A.add)
-        if m == 2: stage("fault%d" % h)
-        win, b = (v("CT"), 0.0) if t == 0 else (v("XW", 0, D), -31.0)
-        if m == 2 and OPT["cgv"] >> (1 - h) & 1:
-            act(part(R("Cg2", h), 0, 2), at(win, part(W("off", h, m), 0, 2)), F.Identity, bias=b)
-            ts(part(R("Cg2", h), 1, 2), at(win, part(W("off", h, m), 1, 2)), b, A.add)
-        else: act(R("Cg%d" % m, h), at(win, W("off", h, m)), F.Identity, bias=b)
+        tt(H3, ps(h, 0, 128), v("Mh"), A.mult)
+        mm(ps(h, 256, 288), T3, v("Rb"), True, False, True)
+        mm(ps(h, 256, 288), H3, blk("Rh", 0, 32), False, True, True)
+        ts(W("off", h, m), ps(h, 256, 288), D // 2 - 0.5, A.add)
+        if m == 1: ts(W("P1", h), ps(h, 256, 288), -0.5, A.add, 1.0 / D, A.mult)
+        if m == 2: ts(W("Qn", h), ps(h, 256, 288), -0.5, A.add)
+        if m == 2 and h:
+            stage("first")
+            mm(ps(6, 288, 320), T3, v("RP"), True, False)
+            mm(ps(6, 288, 320), H3, blk("RQ", 0, 32), False, True)
+            ts(W("Qc", h), ps(6, 288, 320), -0.5, A.add)
+            o = ps(7, 96, 128)
+            mm(o, H3, blk("RQ", 1, 32), True, False)
+            for i in range(RUN[h]): mm(part(o, i, RUN[h]), Id(0), v("e01", 32 * h + i, 32 * h + 32, RUN[h]), False, i == RUN[h] - 1)
+            act(v("CA"), o, F.Abs, bias=-(HB - 1.0) * D, scale=float(D))
+            tt(v("XH"), W("Qc", h), v("CA"), A.add)
+        stage("cab%d%d" % (m, h))
+        o = ps(5 + 2 * h, 0, 32)
+        mm(o, H3, blk("Rh", 1, 32), True, True)
+        act(W("cab", h, m), o, F.Abs, bias=-(HB - 1.0) * D, scale=float(D))
+        stage("count%d%d" % (m, h))
+        win, b = (v("XW", 0, D), 32.0) if t else (v("CT"), 0.0)
+        if m == 2 and h == 0:
+            ts(part(R("Cg2", h), 0, 2), at(win, part(W("off", h, m), 0, 2)), b, A.add)
+            act(part(R("Cg2", h), 1, 2), at(win, part(W("off", h, m), 1, 2)), bias=b)
+        else: act(R("Cg%d" % m, h), at(win, W("off", h, m)), bias=b)
 
-    def check01(m):
-        if OPT["eh"] == 0:
-            for a in range(16): mm(ps(6, 0, 64), v("Y", 144 * m + 16 - a, 144 * m + 144 - a), v("Cg%d" % m, a, TH, 16), m == 0 and a == 0, False)
-            mm(ps(6, 0, 64), Id(1 + 3 * m), blk("cab", m, 64), False, m == 1)
-            if m == 1 and OPT["es"]: act(v("e01"), ps(6, 0, 64), F.Abs, scale=1024.0)
-            elif m == 1: ts(v("e01"), ps(6, 0, 64), 0.0, A.not_equal, 1024.0, A.mult)
-        elif m == 0 and OPT["eh"] == 1:
-            for a in range(16): mm(ps(6, 0, 64), v("Y", 16 - a, 144 - a), v("Cg0", a, TH, 16), a == 0, False)
-            mm(ps(6, 0, 64), Id(1), blk("cab", 0, 64), False, True)
-            ts(v("e0"), ps(6, 0, 64), 0.0, A.not_equal, 1024.0, A.mult)
+    def check(m):
+        o = ps(4, 0, 64) if m < 2 else ps(6, 320, 384)
+        if m == 2: mm(o, Id(0), v("e01"), True, False)
+        if m != 1: mm(o, Id(1), blk("cab", m, 64), m == 0, False)
+        for a in range(16): mm(o, v("Y", 144 * (m % 2) + 16 - a, 144 * (m % 2) + 144 - a), v("Cg%d" % m, a, TH, 16), False, m == 2 and a == 15)
+        if m == 1:
+            mm(o, Id(4), blk("cab", m, 64), False, True)
+            ts(v("e01"), o, 513.0, A.not_equal, 1024.0, A.mult)
+        if m == 2: ts(v("nok"), o, 1.0, A.not_equal, 4 * BIG, A.mult)
 
-    def check0(h):
-        o = ps(6, 32 * h, 32 + 32 * h)
-        mm(o, Id(1), W("cab", h, 0), True, False)
-        for a in range(16): mm(o, v("Y", 16 - a, 144 - a), v("Cg0", 512 * h + a, 512 * h + 512, 16), False, a == 15)
-        ts(W("e0", h), o, 0.0, A.not_equal, 1024.0, A.mult)
+    def moved(t, h, stop): mm(ps(2 + h), v("II", 128 - 16 * t, 256 - 16 * t) if t else v("PK"), z(t, h), True, stop)
 
-    def check1(h):
-        stage("count")
-        o = ps(6, 128 + 32 * h, 160 + 32 * h)
-        mm(o, Id(0), W("e0", h), True, False)
-        mm(o, Id(1), W("cab", h, 1), False, False)
-        for a in range(16): mm(o, v("Y", 16 - a, 144 - a), v("Cg1", 512 * h + a, 512 * h + 512, 16), False, a == 15)
-        ts(W("e01", h), o, 0.0, A.not_equal, 1024.0, A.mult)
-
-    two = OPT["two"]
-    own = lambda h: v("AR", 160 * h + 48, 160 * h + 80) if two else v("AR", 160 * h + 128, 160 * h + 160)
-    cab2 = lambda h: v("CA", 160 * h + 48, 160 * h + 80) if two else W("cab", h, 2)
-    wide = lambda s: 80 if 1 <= s <= 8 else 48
-
-    def moved(t, h): mm(ps(OPT["sb"] + h), v("PK" if t <= OPT["x0"] else "II", 128 - 16 * t, 256 - 16 * t), z(t, h), True, False)
-
-    def verdict(t, h):
-        stage("fault%d" % h)
-        o = ps(6, 64 + 32 * h, 96 + 32 * h)
-        if not two:
-            mm(o, Id(1), cab2(h), True, False)
-            mm(o, Id(0), W("e01", h), False, False)
-        for a in range(16): mm(o, v("Y", 16 - a, 144 - a), v("Cg2", 512 * h + a, 512 * h + 512, 16), two and a == 0, a == 15 and not two)
-        if two: mm(o, Id(1), cab2(h), False, True)
-        ts(W("nok", h), o, 0.0, A.not_equal, 4 * BIG, A.mult)
-        if OPT["sh"]:
-            mm(ps(h, 400, 480), blk("T3", h, 128), v("RA", 80), True, False)
-            mm(ps(h, 400, 480), blk("H3", 4 + h, 128), v("RH", 80, 160), False, False)
-            for k, (_, lo) in enumerate(PAIRS): mm(ps(h, 400 + 8 * k, 408 + 8 * k), Id(3), v("nok", 32 * h + lo, 32 * h + 32, 4), False, False)
-            mm(ps(h, 448, 480), Id(3), W("nok", h), False, True)
-            ts(v("AR", 160 * h + 80, 160 * h + 160), ps(h, 400, 480), PB - D // 2, A.add)
-        elif not two:
-            mm(ps(h, 320, 480), blk("T3", h, 128), v("RA"), True, False)
-            mm(ps(h, 320, 480), blk("H3", 4 + h, 128), blk("RH", 0, 160), False, False)
-            for k, (_, lo) in enumerate(PAIRS): mm(ps(h, 400 + 8 * k, 408 + 8 * k), Id(3), v("nok", 32 * h + lo, 32 * h + 32, 4), False, False)
-            mm(ps(h, 448, 480), Id(3), W("nok", h), False, False)
-            mm(ps(h, 368, 400), Id(2), W("nok", h), False, True)
-            ts(blk("AR", h, 160), ps(h, 320, 480), PB - D // 2, A.add)
-        stage("leave%d" % h)
-        if two or OPT["xq"]: ts(W("nk8", h), o, 0.0, A.not_equal, 8192.0, A.mult)
-        if OPT["sb"] == 2: moved(t, h)
-        mm(ps(OPT["sb"] + h), Id(6), R("Cg2", h), False, True)
-        act(v("XW", KW + 512 * (1 - h), KW + 512 * (2 - h)), ps(OPT["sb"] + h), F.Identity, bias=32.0 if t == 0 else col(90 if t == OPT["x0"] else 92))
-        if two or OPT["xq"]: tt(W("w", h), own(h) if two else W("Qn", h), W("nk8", h), A.add)
-        tt(W("w", h, 1), W("w", h) if two or OPT["xq"] else own(h), W("JX", h), A.min)
-        ts(W("xoff", h), W("w", h, 1), float(D // 2), A.add)
-        n = OPT["sq"]
-        for q in range(n):
-            so = part(R("s%d" % t, h), q, n)
-            name, b = ("xb", 1.0) if t < OPT["x0"] else ("XW", -31.0)
-            act(so, at(v(name, 0, KW + 512 * (2 - h)), part(W("xoff", h), q, n)), F.Identity, bias=b)
-            if t < RO - 1:
-                sem, to = "arr%d%d%d" % (t + 1, h, q), part(z(t + 1, h), q, n)
-                add("G", lambda so=so, sem=sem, to=to: g.remote_dma(ap(to), ap(so), T.sem[sem], T.sem.sent, pid, rid, topo.mask(core, nxt)), None, [so], "call", 600.0,
-                    NOM["hop"] - 600 - 650 * (n - 1) + (NOM["once"] if t == 0 else 0))
-                add("X", None, to, [], ("arrival", sem, n_in), 1.0)
+    def leave(t):
+        stage("leave")
+        o = ps(6, 384, 448)
+        mm(o, Id(0), v("Qn"), True, False)
+        mm(o, Id(3), v("nok"), False, True)
+        tt(v("w"), o, v("JX"), A.min)
+        ts(v("xoff"), v("w"), float(D // 2), A.add)
+        for h in (1, 0):
+            stage("leave%d" % h)
+            send(t, h)
         stage("row")
-        tt(W("pk", h), W("nok", h), cab2(h), A.subtract)
-        if OPT["nw"]: cp(W("Qn", h), own(h))
+        tt(v("pk"), v("nok"), blk("cab", 2, 64), A.subtract)
 
-    def winners(h, banks):
+    def send(t, h):
+        so = R("s%d" % t, h)
+        act(so, at(v("XW"), W("xoff", h)), bias=col(90))
+        if t < RO - 1:
+            sem, to = "arr%d%d" % (t + 1, h), z(t + 1, h)
+            add("G", lambda: g.remote_dma(ap(to), ap(so), T.sem[sem], T.sem.sent, pid, rid, topo.mask(core, nxt)), None, [so], "call", 600.0,
+                NOM["hop"] - 600 + (NOM["once"] if t == 0 else 0))
+            add("X", None, to, [], ("arrival", sem, n_in), 1.0)
+
+    def column(t, h):
+        moved(t, h, False)
+        mm(ps(2 + h), Id(6), R("Cg2", h), False, True)
+        act(R("NC", h), ps(2 + h), bias=col(95 if t else 168))
+
+    def winners(h):
+        c, eq = RUN[h], "eq%d" % h
+        nr = 32 // c
         stage("win%d" % h)
-        mm(ps(h, 0, 80), v("nil", p1=1), v("one", 0, 80, p1=1), True, False)
-        for k, bank in enumerate(banks if OPT["sh"] else ()):
-            stage("last%d" % h)
-            for i, s in enumerate(TURNS[k]): mm(ps(bank, 80 * i, 80 * i + (80 if s else 48)), blk("SH", s, 128), v("AR", 160 * h, 160 * h + (80 if s else 48)), True, True)
-            stage("win%d" % h)
-            for i, s in enumerate(TURNS[k]):
-                c, n = 1280 * h + 80 * s, 80 if s else 48
-                tt(v("eq", c, c + n), ps(bank, 80 * i, 80 * i + n), v("AR", 160 * h + 80, 160 * h + 80 + n), A.is_equal)
-                if s: mm(ps(h, 48, 80), blk("E", s - 1, 128), v("eq", c + 48, c + 80), False, False)
-                mm(ps(h, 0, 48), blk("SH", -s % 16, 128), v("eq", c, c + 48), False, s == 15)
-        for k, bank in enumerate(() if OPT["sh"] else banks):
-            for i, s in enumerate(TURNS[k]):
-                for x in ("AR", "CA")[:1 + two]: mm(ps(bank, 80 * i, 80 * i + wide(s)), blk("SH", s, 128), v(x, 160 * h + 80, 160 * h + 80 + wide(s)), x == "AR", x == "CA" or not two)
-            for i, s in enumerate(TURNS[k]):
-                c = 1280 * h + 80 * s
-                tt(v("eq", c, c + wide(s)), ps(bank, 80 * i, 80 * i + wide(s)), v("XH", 80 * h, 80 * h + wide(s)) if two else v("AR", 160 * h, 160 * h + wide(s)), A.is_equal)
-                if wide(s) == 80: mm(ps(h, 48, 80), blk("E", s - 1, 128), v("eq", c + 48, c + 80), False, False)
-                mm(ps(h, 0, 48), Id(0), v("eq", c, c + 48), False, s == 15)
-        if OPT["ns"] >> h & 1: act(blk("nd", h, 80), ps(h, 0, 80), F.Identity, scale=8192.0)
-        else: ts(blk("nd", h, 80), ps(h, 0, 80), 0.0, A.is_gt, 8192.0, A.mult)
-        mm(ps(h, 96, 128), Id(0), own(h), True, False)
-        if two: mm(ps(h, 96, 128), Id(3), W("nok", h), False, False)
-        for k, (hi, _) in enumerate(PAIRS): mm(ps(h, 96 + hi, 128, 4), Id(0), v("nd", 80 * h + 8 * k, 80 * h + 8 * k + 8), False, False)
-        mm(ps(h, 96, 128), Id(0), v("nd", 80 * h + 48, 80 * h + 80), False, True)
-        for i in range(4): ts(v("soff", 32 * h + i, 32 * h + 32, 4), ps(h, 96 + i, 128, 4), col(120 + i), A.min, float(D // 2), A.add)
+        sizes = [(c - d) * nr for d in range(1, c)]
+        npair = sum(sizes)
+        n = 8 + h
+        own = lambda a, b=32: v("own%d" % h, n * a, n * b)
+        SH = lambda s: blk("SH", s % 16, 128)
+        if h == 0: cp(W("Qc", h), at(W("w", h), v("qo")))
+        act(own(0), at(v("XH") if h else W("w", h), v("ro%d" % h)))
+        for r in range(2):
+            bank = 4 + r * (1 - h)
+            for k in range(n * (1 - r * h)):
+                mm(ps(bank, k, 32 * n, n), SH(k if h else k + 1 + 8 * r), W("Qc", h), True, not h)
+                if h: mm(ps(bank, k, 32 * n, n), SH(k), v("CA"), False, True)
+            e0 = n * (32 + npair * r)
+            if r == 0:
+                tt(v(eq, 0, 32 * n), ps(bank, 0, 32 * n), own(0), A.is_equal)
+                for k in range(8): mm(ps(h, npair, npair + 32), blk("E", k, 128), v(eq, k + h, 32 * n, n), k == 0, k == 7)
+            for d in range(1, c):
+                x, a = sizes[d - 1], e0 + n * sum(sizes[:d - 1])
+                if r * h: tt(v(eq, a, a + n * x), ps(bank, n * d * nr, 32 * n), own(0, x), A.is_equal)
+                else: tt(v(eq, a, a + n * x), ps(bank, 0, n * x), own(d * nr), A.is_equal)
+            for k in range(r * h, n - r * h): mm(ps(h, 0, npair), SH(-k * r * h), v(eq, e0 + k, e0 + n * npair, n), r == 0 and k == 0, r == 1 and k == 7)
+        nd = lambda a, b: v("nd", 144 * h + a, 144 * h + b)
+        ts(nd(0, npair + 32), ps(h, 0, npair + 32), 0.0, A.is_gt, 8192.0, A.mult)
+        o = ps(h, 352, 384)
+        mm(o, Id(0), W("Qc", h), True, False)
+        for i in range(c * h): mm(part(o, i, c), Id(3), v("nok", 32 * h + i, 32 * h + 32, c), False, False)
+        for d in range(1, c): mm(ps(h, 352 + d * nr, 384), Id(0), nd(sum(sizes[:d - 1]), sum(sizes[:d])), False, False)
+        mm(o, Id(0), nd(npair, npair + 32), False, True)
+        if h:
+            for i in range(c): ts(v("soff", 32 * h + i, 32 * h + 32, c), part(o, i, c), col(120 + i), A.min, float(D // 2), A.add)
+        else:
+            tt(v("wl"), o, v("SP"), A.min)
+            ts(W("soff", h), at(v("wl"), v("so")), float(D // 2), A.add)
 
     def back():
         ts(v("cB"), blk("cab", 1, 64), 1.0 / D, A.mult, -1024.5, A.add)
         for b in range(2):
             for a in range(8):
-                o = part(ps(OPT["bb"][b]), a, 8)
+                o = part(ps(2 + b), a, 8)
                 mm(o, blk("L", 8 * b + a, 128), v("P1"), True, False)
-                mm(o, blk("L", 8 * b + a, 128), v("cB"), False, b >= OPT["bs"])
-                if b < OPT["bs"]: mm(o, Id(0), v("X2", 8 * b + a, TH, 16), False, True)
+                mm(o, blk("L", 8 * b + a, 128), v("cB"), False, b)
+                if b == 0: mm(o, Id(0), v("X2", a, TH, 16), False, True)
             for a in range(8):
-                o = part(ps(OPT["bb"][b]), a, 8)
-                if b < OPT["bs"]: act(v("Bb", 8 * b + a, TH, 16), o, F.Identity)
-                else: tt(v("Bb", 8 * b + a, TH, 16), o, v("X2", 8 * b + a, TH, 16), A.add)
+                if b == 0: act(v("Bb", a, TH, 16), part(ps(2), a, 8))
+                else: tt(v("Bb", 8 + a, TH, 16), part(ps(3), a, 8), v("X2", 8 + a, TH, 16), A.add)
 
     def new_key(t, h):
         mm(ps(4 + h), v("PI", 128 * t, 128 * t + 128, p1=1), v("one", p1=1), True, False)
         for a in range(16):
             l = v("Z", 160 * a + 16 + a - t, 160 * a + 144 + a - t)
-            if not OPT["nw"]:
-                mm(ps(4 + h, a, 512, 16), l, own(h), False, False)
-                mm(ps(4 + h, a, 512, 16), l, W("pk", h), False, a == 15)
-            elif a // 8 == h:
-                mm(part(ps(4 + h), a % 8, 8), l, v("Qn"), False, False)
-                mm(part(ps(4 + h), a % 8, 8), l, v("pk"), False, a % 8 == 7)
+            mm(ps(4 + h, a, 512, 16), l, W("Qn", h), False, False)
+            mm(ps(4 + h, a, 512, 16), l, W("pk", h), False, a == 15)
 
     def stack(name, n, bank, c0, order):
         for b in order: mm(ps(bank, 0, n), v("HX", 8 - b, 136 - b), blk(name, b, n), b == order[0], b == order[7])
-        k = n // 128 if OPT["hp"] else 1
-        for i in range(k): act(part(v("hi", c0, c0 + n), i, k), part(ps(bank, 0, n), i, k), F.Identity, bias=160.0 - 8.5 / 16, scale=0.0625)
+        for i in range(n // 128): act(v("hi", c0 + 128 * i, c0 + 128 * i + 128), part(ps(bank, 0, n), i, n // 128), bias=160.0 - 8.5 / 16, scale=0.0625)
 
     masks(0)
-    for c in range(8): table("CT", c, 4 + c % 2)
+    tables()
     for t in range(RO):
         for m in range(3):
             for h in (1, 0):
-                stage("hop", t)
+                stage("hop%d" % h, t)
                 gather(m, h)
                 turn(t, m, h)
-                if m == 1 and OPT["eh"] and (h or OPT["eh"] < 3): check1(h)
-                if m == 0 and OPT["eh"] > 1: check0(h)
-            stage("count")
-            if m < 2: check01(m)
+            stage("check%d" % m)
+            check(m)
+            stage("moved")
+            for h in (1, 0) if m == 0 else ():
+                moved(t, h, True)
+                act(v("XW", KW + 512 * h, KW + 512 * h + 512), ps(2 + h), bias=col(95 if t else 168))
             stage("back")
             if m == 1: back()
-            if t == 0 and m < 2:
-                stage("table")
-                for c, bank in enumerate(OPT["xw"][m]): table("XW", c + m * len(OPT["xw"][0]), bank)
-            if t == 1 and m == 5: pass
-            if OPT["sb"] == 4 and m == (1 if t == 0 else 0):
-                stage("moved")
-                for h in (1, 0): moved(t, h)
         for h in (1, 0):
-            stage("old")
+            stage("old%d" % h)
             gather(3, h)
-            verdict(t, h)
-            if h and OPT["eh"] == 3: check1(0)
-        winners(1, OPT["wb"][1])
-        winners(0, OPT["wb"][0])
-        stage("table")
-        for c, bank in enumerate(OPT["xw"][2] if t == 0 else ()): table("XW", c + len(OPT["xw"][0] + OPT["xw"][1]), bank)
-        stage("row")
-        for h in (1, 0): new_key(t, h)
-        for u in range(15, -1, -1):
-            stage("run")
-            tt(at(v("K"), blk("soff", u, 4)), blk("Ab", u, 64), blk("Bb", u, 64), A.max)
-            c = KW + (64 * u + 512) % TH
-            stage("xrun")
-            act(at(v("XW", 0, KW), blk("soff", u, 4)), v("XW", c, c + 64), F.Silu)
-        stage("row")
+        leave(t)
+        for h in (1, 0): winners(h)
         for h in (1, 0):
-            for a in range(8 * OPT["nw"]): tt(v("K", 8 * h + a, TH, 16), v("K", 8 * h + a, TH, 16), part(ps(4 + h), a, 8), A.min)
-            for i in range(OPT["fp"] * (1 - OPT["nw"])): tt(part(R("K", h), i, OPT["fp"]), part(R("K", h), i, OPT["fp"]), part(ps(4 + h), i, OPT["fp"]), A.min)
+            stage("column%d" % h)
+            column(t, h)
+        for h in (1, 0):
+            stage("row%d" % h)
+            new_key(t, h)
+        for h in (1, 0):
+            nr = 32 // RUN[h]
+            for r in range(nr - 1, -1, -1):
+                so = part(W("soff", h), r, nr)
+                stage("run")
+                tt(at(v("K"), so), part(R("Ab", h), r, nr), part(R("Bb", h), r, nr), A.max)
+                stage("xrun")
+                act(at(v("XW", 0, KW), so), part(R("NC", h), r, nr), F.Silu)
+        for h in (1, 0):
+            stage("min%d" % h)
+            for i in range(4): tt(R("K", h, i, 4), R("K", h, i, 4), ps(4 + h, i, 512, 4), A.min)
         if t < RO - 1: masks(t + 1)
 
     stage("end")
@@ -645,32 +730,28 @@ def rank_program(g, core, T, topo):
     for h in (1, 0):
         mm(ps(2 + h), blk("II", 1, 128), R("s4", h), True, False)
         for b in range(4): mm(part(ps(2 + h), b, 4), blk("HR", 4 * h + b, 128), v("hi", 512, 640), False, b == 3)
-        for b in range(2): act(part(R("oz", h), b, 2), part(ps(2 + h), b, 2), F.Identity, bias=col(131))
+        for b in range(2): act(part(R("oz", h), b, 2), part(ps(2 + h), b, 2), bias=col(131))
     dma("Y", T.yz[:], v("oz"))
     for h in (1, 0):
         ts(R("Hk", h), R("K", h), 1.0 / D, A.mult, HB - 0.5 + 0.5 / D, A.add)
         ts(R("Hn", h), R("Hk", h), 1.0 - HB, A.add, 0.0, A.min)
     top = 16 - OPT["npe"]
     for b in range(top, 16): mm(ps(1, 0, 256), v("IF"), blk("K", b, 256), b == top, False)
-    for b in (3, 2, 1, 0): mm(ps(1, 0, 256), Id(5), blk("Hn", b, 256), top == 16 and b == 3, b == 0)
+    for b in (3, 2, 1, 0): mm(ps(1, 0, 256), Id(5), blk("Hn", b, 256), False, b == 0)
     cp(ps(0, 256, 512), blk("K", top - 1, 256))
-    for b in range(top - 2, 3, -1): tt(ps(0, 256, 512), blk("K", b, 256), ps(0, 256, 512), A.add)
-    cp(blk("okk", 0, 256), ps(0, 256, 512))
-    for b in range(4): tt(ps(1, 0, 256), blk("K", b, 256), ps(1, 0, 256), A.add)
+    for b in range(top - 2, 3, -1): tt(ps(0, 256, 512) if b > 4 else blk("okk", 0, 256), blk("K", b, 256), ps(0, 256, 512), A.add)
+    for b in (3, 2, 1, 0): tt(ps(1, 0, 256), blk("K", b, 256), ps(1, 0, 256), A.add)
     tt(blk("okk", 1, 256), blk("okk", 0, 256), ps(1, 0, 256), A.add)
     dma("Y", T.yk[:], blk("okk", 1, 256))
-    for b in range(7, -1, -1):
-        if b in (0, 1, 2, 3)[:OPT["xv"]]: ts(blk("xb", b, 512), blk("XW", b, 512), -31.0, A.add)
-        else: act(blk("xb", b, 512), blk("XW", b, 512), F.Identity, bias=-31.0)
-    turns = [7, 6, 5, 0, 4, 3, 1, 2] if OPT["xv"] == 2 else [7, 6, 5, 4, 0, 3, 2, 1] if OPT["xv"] == 1 else [7, 6, 0, 5, 1, 4, 2, 3] if OPT["xv"] == 3 else [7, 6, 5, 4, 3, 2, 1, 0]
+    turns = range(7, -1, -1)
+    for b in turns: act(blk("xb", b, 512), blk("XW", b, 512), bias=col(90))
     stack("xb", 512, 6, 0, turns)
-    if OPT["ocv"]: ts(v("oc", p1=64), ps(6, p1=64), -1.0, A.add)
-    else: act(v("oc", p1=64), ps(6, p1=64), F.Identity, bias=-1.0)
+    act(v("oc", p1=64), ps(6, p1=64), bias=-1.0, scale=1.0 / 32)
     dma("S", T.yc[:], v("oc", p1=64))
     for b in turns:
         for a in (2 * b, 2 * b + 1): mm(ps(2, 0, 256), blk("II", 1, 128), blk("xb", a, 256), a == 14, False)
     for b in range(2): mm(ps(2, 0, 256), blk("HR", 8, 128), blk("hi", b, 256), False, b == 1)
-    ts(v("ox"), ps(2, 0, 256), col(147), A.add)
+    act(v("ox"), ps(2, 0, 256), bias=col(147))
     dma("Y", T.yx[:], v("ox"))
     emit(g, T, ops)
-    g.wait_ge(T.sem.sent, 2 * OPT["sq"] * n_out * (RO - 1))
+    g.wait_ge(T.sem.sent, 2 * n_out * (RO - 1))

@@ -8,7 +8,20 @@ HB = 1600
 PB = float(HB * D)
 RUN = (8, 4)
 NOM = dict(cyc=0.83, pe=0.42, gather=1.5, scatter=3.5, wake=220.0, dma=1800.0, rate=300.0, hop=4500.0, once=2000.0, gdma=1000.0, glag=1500.0)
-OPT = dict(npe=3, cap=230, seed=3, turns=500, shifts=4000, polish=2500, heat=100.0, heat2=60.0)
+OPT = dict(npe=3, cap=230, seed=3, turns=700, shifts=3000, polish=600, heat=100.0, heat2=60.0)
+OPT.update(tile="SS", nd="VV", soff="tc", dmacol=True, vcount=False, split=True, back=(1, 0), bcopy="SSSS")
+BK = dict(two=(5, 7), mask=(6, 6), cab=(5, 7), nok=(6, 6), win=(5, 4), back=(2, 3))
+FREE = "hop01 hop00 hop11 hop10 cab01 cab00 cab11 cab10 count01 count00 count11 count10 check0 moved back1 back0".split()
+LOOSE = "old1 old0 leave1 leave0 xoff1 xoff0 check21 check20 win1 win0 lose1 lose0 clear row back1 back0 run1 run0 xrun1 xrun0 min1 min0 count20 cab20 column1 column0".split()
+ORDER = {
+    'V': '<min1:3,1,2 <min0 hop01*4 <min0*2 hop00*4 hop01*2 hop00 hop01 hop00 hop11 hop00 hop11 hop10*2 hop11*2 hop10 hop11 hop10 hop11 hop21:0 hop10 hop21:1 hop10 hop20:0,1 hop21:2,3,5,4 check1 hop20:2,3 old1 cab21 hop20:5,4 old1 win1:0 cab20 win1:3 check21 win1:2,1,4,6 xoff1 win1:5 xoff1 win0:3,1,2,11 check20 lose1:0 win0:13,0 xoff0 win0:14,12,7 xoff0 lose1:1,4,3,2 win0:5,4 run1 win0:8 run1 win0:6,9 run1 win0:10 run1 clear run1 lose0 run1 row run1 lose0 run1 lose0 clear run0 clear run0 clear run0*2 min1:0 min0',
+    'S': '<mask10:1,0 <xrun0 <mask21*2 count01 cab00 cab01 <mask20:1 count00 moved <mask20:0 count11 count10 cab11 cab10 moved cab21 count21 win1*8 cab20 count20 win0*8 back1*2 leave1 old0 leave0 back0 xrun1*2 back0 xrun1*6 mask01 xrun0 mask01 xrun0 mask00:0 mask11*2 mask01 mask00:1,2 xrun0',
+    'P': 'hop01 <mask11 <mask00*2 hop00 <mask10 hop01*4 hop00*4 hop01*2 <mask21 moved:1 hop00*2 hop11 cab01 <mask20 cab00 moved:0 hop10 hop11*4 hop10*4 hop11*2 check0*2 hop10*2 back1*2 hop21 check0 back1 cab11 hop20 hop21 cab10 hop21*3 check1*2 hop21*2 check1 hop20*4 cab21*2 back1 hop20*2 win1*3 cab20*2 check21*3 win0 win1 xoff1 win0*2 win1 check20*3 win1 back0 xoff0 lose1 back0*2 row:0 back0 win0*5 row:3 lose0*2 row:1,4,2,5 mask01*2',
+    'G': 'column1 column0 leave1 leave0'}
+ORDER = {'V': '<min0:2 hop01*3 <min0:0 hop01 <min0:3 hop00*4 hop01*2 hop00 hop01 hop00 hop11 hop00 hop11 hop10:1,0 hop11*4 hop10:2,3 hop21:0 hop10:4 hop21:1 hop10:5 hop20:0,1 hop21:2,3 check1 hop21:5,4 hop20:2,3 old1:1 cab21 hop20:5,4 old1:0 win1:0 cab20 check21 win1:3,1,2,5 xoff1 win1:6,4 xoff1 win0:7,1,3,4,11 check20 win0:2 lose1:0 win0:0 xoff0 win0:12,13 xoff0 lose1:1,3,2,4 win0:14,5,6 run1 win0:8 run1 win0:9 run1 win0:10 run1 clear run1 lose0 run1 clear run1 row lose0 run1 lose0 clear run0*2 clear run0*2 min1:0,2,1,3 min0:1', 'S': '<mask21*2 count01 cab01 count00 moved <mask20 cab00 <mask20 count11 count10 cab11 cab10 moved cab21 count21 win1*8 cab20 count20 win0*8 back1:1 leave1 old0 leave0 xrun1 back0:1 xrun1 back1:0 xrun1 back0:0 xrun1*5 mask01 xrun0 mask11 mask01 mask00 mask01 mask11 mask00*2 xrun0 mask10:1,0 xrun0*2', 'P': '<row:5 hop01 <mask00 hop00 <mask10 hop01*4 hop00*4 hop01*2 <mask21 hop00 hop11 hop00 hop10 cab01 moved:1,0 <mask20 hop11*4 cab00 hop10*3 hop11*2 hop10 hop21 check0*3 hop10*2 cab11 back1*3 hop21*4 cab10 check1*3 hop21*2 hop20*5 cab21*2 back1 hop20*2 win1*3 cab20*2 check21*3 win0*2 xoff1 win0 win1*2 check20*3 win1 back0 xoff0 lose1 win0 back0*3 win0*2 row:0 win0*2 row:3 lose0*2 row:1,2 mask01 row:4 mask11 mask01 mask00', 'G': 'column1 column0 leave1 leave0'}
+FIRST = {'V': 'hop01*4 hop00:0,1,2,3 hop01*2 hop00:5,4 hop01 hop11 hop00:6 hop11 hop10*2 hop11*4 hop10*2 hop21 hop10 hop21 hop10 hop20*2 hop21*4 check1 hop20*4 old1 cab21 check21 old1 xoff1 cab20 xoff1 win1:0,3,1,6,2 check20 win1:5,4 win0:12,3 xoff0 win0:8,13 xoff0 win0:5 lose1:0 win0:0,10,6,4,7,14 lose1:1,2,4,3 win0:1 run1 win0:2 run1 row win0:11 run1 win0:9 run1 clear run1 lose0 run1 clear run1 lose0 run1 lose0 clear run0 clear run0*3 min1:2,0 min0:1 min1:1,3', 'S': 'count01 count00 cab00 cab01 moved count11 count10 cab11 cab10 moved count21 cab21 count20 cab20 win1*8 back1:1 win0*8 leave1 old0 leave0 xrun1 back1:0 xrun1*5 back0:1 xrun1*2 back0:0 xrun0 mask01 xrun0 mask11:1 mask01 mask00 mask11:0 mask01 mask00*2 mask10:1 xrun0 mask10:0 xrun0', 'P': 'hop01 hop00 hop01*4 hop00*4 hop01*2 hop00 hop10 hop00 cab01 cab00 hop11*5 moved hop10*2 hop11*2 hop10*2 hop21 check0*2 cab11 check0 hop10*2 moved back1*3 hop21*4 hop20 cab10 check1*2 hop21*2 hop20*2 check1 hop20*2 back1 cab21 hop20*2 cab21 check21*3 cab20*2 win1 xoff1 win1*2 win0 check20*3 win0*2 win1 xoff0 win1*2 lose1 back0 win0 row:0 win0 back0 win0 back0 win0*2 row:1 lose0 back0 lose0 row:3,2 mask01 mask11 mask01 mask00 row:4', 'G': 'column1 column0 leave1 leave0'}
+LAST = {'V': 'hop01*2 <min0:0 hop01*2 <min0:2,3 hop00*4 hop01*2 hop00 hop01 hop00 hop11:0 hop00 hop11:1 hop10:1,0 hop11:2,3,5,4 hop10:2,3 hop21:0 hop10:4 hop21:1 hop10:5 hop20:1,0 hop21:2,3 check1 hop21:5,4 hop20:2,3 cab21 hop20:5,4 old1*2 win1:0,3 check21 cab20 win1:1,2,6 xoff1 win1:4 xoff1 win1:5 win0:11,2,7,3 check20 win0:13,4 lose1:0 win0:14,0 xoff0 win0:1 xoff0 lose1:2,1,4,3 win0:8 run1 win0:6,9 run1 win0:5,10 run1 win0:12 row run1 clear run1 lose0 run1 clear run1 lose0 run1 lose0 clear run0 clear run0*3 ksum min1:1,0 ksum min1:3,2 ksum min0*2 ksum min0*2 ksum mirror:0 ksum mirror:2,1 ksum mirror:4 ksum mirror:3,5 ksum mirror:6 ksum mirror:7 ksum*2', 'S': '<mask21:1,0 cab01 count01 count00 <mask20:1 cab00 moved <mask20:0 count11 count10 cab11 cab10 moved cab21 count21 win1*8 cab20 count20 win0*8 back1:1 old0 leave1 leave0 xrun1 back0:1 xrun1 back1:0 xrun1 back0:0 xrun1*3 zout:0 xrun1*2 xrun0 zout:1 xrun0 zout:3 xrun0 zout:4 xrun0 zout:2 xsum*6 rows:1 xsum rows:0 xsum*2', 'P': 'hop01 hop00 <row:5 <mask00:1 <mask10 hop01*4 hop00*4 hop01*2 <mask21 hop11 hop00*2 cab01 moved:1 <mask20 hop11*4 hop10 moved:0 cab00 hop10*2 hop11*2 hop10*2 check0*2 hop10*2 back1*2 check0 hop21 cab11 back1 hop20 hop21*3 cab10 hop21 check1*3 hop21*2 hop20*4 cab21*2 back1 hop20*2 win1*3 cab20*2 check21*3 win0*3 xoff1 win1*2 check20*3 win1 xoff0 lose1 row:0 back0*4 zout:0 win0*5 row:3 zout:1,7 lose0*2 zout:2,3,4 row:1,4,2 zout:5,6,8 row:5 zout:9 mirror*4 xsum mirror xsum mirror xsum*4 mirror*2 xsum mirror xsum*2', 'G': 'column1 column0 rows'}
+OPT.update(npe=5)
 LEAD = dict(win0=1500.0, clear=-2000.0, soon=30000.0)
 OTHER = ((1.4, 1.3, 1.6, 1.8, 1.3), (0.7, 1.0, 0.8, 0.6, 0.8), (1.5, 1.0, 1.0, 0.9, 1.6))
 
@@ -20,15 +33,15 @@ SB = {
     "Cg0": (TH, bf), "Cg1": (TH, bf), "Cg2": (TH, bf), "sq": (512, bf), "hi": (TH, bf),
     "T3": (256, f32), "H3": (768, f16), "off": (192, u16), "cab": (192, bf), "P1": (64, f16), "cB": (64, f16),
     "e01": (64, bf), "nok": (64, bf), "pk": (64, bf), "w": (64, f32), "xoff": (64, u16), "Qn": (64, f16),
-    "Qc": (64, f16), "CA": (32, bf), "XH": (32, f32), "own0": (256, f32), "own1": (288, f32), "eq0": (2048, bf), "eq1": (1152, bf),
-    "nd": (288, bf), "wl": (32, f32), "soff": (64, u16), "Hk": (TH, f16), "Hn": (TH, f16),
+    "XH": (64, f32), "own0": (288, f32), "own1": (288, f32), "eq0": (2048, bf), "eq1": (2048, bf),
+    "nd": (288, bf), "wl": (64, f32), "soff": (64, u16), "Hk": (TH, f16), "Hn": (TH, f16),
     "oz": (TH, bf), "okk": (512, f32), "ox": (256, bf), "oc": (512, f32),
     "pi": (48, i32), "pj": (48, i32), "pc": (192, f32), "n256": (256, bf), "io": (480, bf), "JX": (64, f32),
-    "SP": (32, f32), "ri": (48, i32), "rf": (34, f32), "ro0": (16, u16), "ro1": (18, u16), "qo": (2, u16), "so": (2, u16),
+    "SP": (64, f32),
     "Sel": (64, f32), "Mq": (128, f32), "Mh": (128, f32),
-    "Rb": (32, f32), "Rh": (64, bf), "RP": (32, f32), "RQ": (64, bf), "IF": (128, f32),
+    "Rb": (32, f32), "Rh": (64, bf), "IF": (128, f32),
     "crow": (128, bf), "one": (512, bf), "PI": (RO * 128, bf), "WB": (256, bf), "MK": (768, bf),
-    "SQ": (RO * 64, bf), "Y": (288, bf), "Id": (8 * 128, bf), "II": (256, bf), "PK": (128, bf), "Zb": (160, bf), "Z": (16 * 160, bf),
+    "SQ": (RO * 64, bf), "Y": (288, bf), "Id": (9 * 128, bf), "II": (256, bf), "PK": (128, bf), "Zb": (160, bf), "Z": (16 * 160, bf),
     "L": (16 * 128, bf), "SH": (16 * 128, bf), "E": (8 * 128, bf), "HX": (136, bf), "HR": (10 * 128, bf),
 }
 for _t in range(RO):
@@ -38,14 +51,37 @@ for _t in range(RO):
 SCRATCH = {n: ("sbuf", [128, c], d) for n, (c, d) in SB.items()}
 for _b in range(8):
     SCRATCH["p%d" % _b] = ("psum", [128, 512], f32)
-SEMAPHORES = ["eV", "eS", "eP", "eG", "sent"] + ["arr%d%d" % (t, h) for t in range(1, RO) for h in range(2)] + ["d%d" % k for k in range(32)]
+DIMS = {}
+for _h in range(2):
+    DIMS["p%d" % _h] = [512 // RUN[_h], RUN[_h]]
+    DIMS["p%d" % BK["win"][_h]] = [32 // RUN[_h], RUN[_h], 16]
+    DIMS["own%d" % _h] = [32 // RUN[_h], RUN[_h], 8]
+for _n in DIMS:
+    SCRATCH[_n] = (SCRATCH[_n][0], [128] + DIMS[_n], f32)
+SEMAPHORES = ["eV", "eS", "eP", "eG", "sent"] + ["arr%d%d" % (t, h) for t in range(1, RO) for h in range(2)] + ["d%d" % k for k in range(56)]
 DBG = []
+RAW = set()
 LAND = {}
 PLAN = []
 
 
 def v(name, c0=0, c1=None, step=1, p0=0, p1=128):
-    return (name, c0, SCRATCH[name][1][1] if c1 is None else c1, step, p0, p1)
+    return (name, c0, math.prod(SCRATCH[name][1][1:]) if c1 is None else c1, step, p0, p1)
+
+
+def split(x):
+    out, cols, inner = [], list(range(x[1], x[2], x[3])), math.prod(DIMS[x[0]])
+    for d in DIMS[x[0]]:
+        inner //= d
+        k = sorted(set(c // inner % d for c in cols))
+        out.append(range(k[0], k[-1] + 1, k[1] - k[0] if k[1:] else 1))
+    assert math.prod(len(r) for r in out) == len(cols)
+    return out
+
+
+def box(name, *ranges):
+    at = lambda f: sum(f(r) * math.prod(DIMS[name][k + 1:]) for k, r in enumerate(ranges))
+    return (name, at(min), at(max) + 1, 1, 0, 128, ranges)
 
 
 def meet(a, b):
@@ -54,7 +90,7 @@ def meet(a, b):
 
 
 def covers(a, b):
-    return a == b or (a[3] == 1 and a[1] <= b[1] and b[2] <= a[2] and a[4] <= b[4] and b[5] <= a[5])
+    return a == b or (a[3] == 1 and not a[6:] and a[1] <= b[1] and b[2] <= a[2] and a[4] <= b[4] and b[5] <= a[5])
 
 
 def needs(ops):
@@ -70,6 +106,7 @@ def needs(ops):
                 b[1] = []
             b[1].append(n)
         for x in rd: d.update(m for m, old in writes.get(x[0], []) if meet(x, old))
+        RAW.update((m, n) for m in d)
         for x in wr:
             for book in (reads, writes):
                 d.update(m for m, old in book.get(x[0], []) if meet(x, old))
@@ -89,6 +126,20 @@ def free(ops, m, n):
     return ops[m][0] == ops[n][0] and (ops[m][0] == "P" and ops[n][4] is None or ops[m][4] == ops[n][4] == "dma")
 
 
+def sequence(text):
+    words, used = [], {}
+    for w in text.split():
+        dt, w = -(w[0] == "<"), w.lstrip("<")
+        if ":" in w: words += [(w.split(":")[0], int(k), dt) for k in w.split(":")[1].split(",")]
+        else: words += [(w.split("*")[0], None, dt)] * int((w + "*1").split("*")[1])
+    for want in (0, -1):
+        for i, (step, k, dt) in enumerate(words):
+            if k is None and dt == want:
+                words[i] = (step, used.get(step, 0), dt)
+                used[step] = used.get(step, 0) + 1
+    return words
+
+
 def plan(ops, deps):
     N = len(ops)
     gap = lambda m, n: 0.0 if free(ops, m, n) else ops[m][6] + (0.0 if ops[n][0] == "X" else NOM["wake"])
@@ -97,8 +148,27 @@ def plan(ops, deps):
     for n in range(N):
         land = [LAND[m] for m in deps[n] if m in LAND and not free(ops, m, n)]
         if land: before[n].append((0, max(land) + NOM["wake"] - cost[0]))
+    calls, soft = {}, []
+    for n, o in enumerate(ops): calls.setdefault((o[0], o[7]), []).append(n)
+    for e in ORDER:
+        last = None
+        for t in range(RO):
+            for step, k, dt in sequence((FIRST if t == 0 else LAST if t == RO - 1 else ORDER)[e]):
+                here = calls.get((e, (t + dt, step)), [])
+                if t or step not in FREE:
+                    if last is not None: before[here[k]].append((last, 0.0))
+                    last = here[k]
+    topo, todo, after = [], [len(b) for b in before], [[] for n in range(N)]
+    for n in range(N):
+        for m, x in before[n]: after[m].append(n)
+        if not todo[n]: topo.append(n)
+    for n in topo:
+        for m in after[n]:
+            todo[m] -= 1
+            if not todo[m]: topo.append(m)
+    assert len(topo) == N
     way = [cost[n] + lag[n] for n in range(N)]
-    for n in range(N - 1, -1, -1):
+    for n in topo[::-1]:
         for m, x in before[n]: way[m] = max(way[m], cost[m] + x + way[n])
     kind, seen, one, many = [], {}, {}, {}
     for n, o in enumerate(ops):
@@ -109,13 +179,10 @@ def plan(ops, deps):
         many.setdefault(k, []).append(n)
 
     way = [way[n] + LEAD.get(kind[n][0], 0.0) for n in range(N)]
-    after = [[] for n in range(N)]
-    for n in range(N):
-        for m, x in before[n]: after[m].append(n)
     tails = [n for n in range(N) if not after[n]]
 
     def lay(key, moved=None, up=True):
-        for n in range(N - 1, -1, -1) if moved is None else ():
+        for n in topo[::-1] if moved is None else ():
             for m, x in before[n]:
                 if key[m] <= key[n]: key[m] = key[n] + 1.0
         todo = list(moved or ())
@@ -156,7 +223,7 @@ def plan(ops, deps):
                 m = prev[n]
                 out.append((m, n))
             n = m
-        return out
+        return out or [(0, 1)]
 
     state = [OPT["seed"]]
 
@@ -201,7 +268,7 @@ def plan(ops, deps):
             pairs = bound(now[1])
             if y[0] < best[0]: best = y
 
-    sort = ["s" if o[7] and o[7][1] in ("run", "xrun") else "g" if o[2][1:] and SCRATCH[o[2][1][0]][2] == u16 else "d" if o[4] else "c" for o in ops]
+    sort = ["s" if o[7] and "run" in o[7][1] else "g" if o[2][1:] and SCRATCH[o[2][1][0]][2] == u16 else "d" if o[4] else "c" for o in ops]
     other = []
     for wake, fc, fg, fs, fr in OTHER:
         f = dict(s=fs, g=fg, d=1.0, c=fc)
@@ -302,9 +369,10 @@ def rank_program(g, core, T, topo):
     def ap(x):
         if not isinstance(x, tuple): return x
         if x[0] == "at": return ap(x[1]).indirect(ap(x[2]))
+        if x[0] in DIMS: return T[x[0]][(slice(x[4], x[5]),) + tuple(slice(r.start, r.stop, r.step) for r in (x[6] if x[6:] else split(x)))]
         return T[x[0]][x[4]:x[5], x[1]:x[2]:x[3]] if x[3] > 1 else T[x[0]][x[4]:x[5], x[1]:x[2]]
 
-    size = lambda x: 16 * size(x[2]) if x[0] == "at" else len(range(x[1], x[2], x[3]))
+    size = lambda x: 16 * size(x[2]) if x[0] == "at" else math.prod(len(r) for r in x[6]) if x[6:] else len(range(x[1], x[2], x[3]))
     short = lambda x: SCRATCH[x[0]][2] in (bf, f16, u16)
 
     def add(e, fn, out, ins, kind=None, cost=None, lag=0.0, per=None):
@@ -340,7 +408,7 @@ def rank_program(g, core, T, topo):
     def mm(out, l, r, st, sp, alone=False):
         add("P", lambda: P.matmul(ap(out), ap(l), ap(r), bool(st), bool(sp)), out, [l, r], cost=max(64, size(r)) * (1 if short(l) else 4) * NOM["pe"])
         a, b = ops[-2], ops[-1]
-        if not alone and a[0] == "P" and a[3][0][0] == out[0] and (a[2][-2][0] == l[0] or a[2][-1][0] == r[0]) and a[5] + b[5] <= (OPT["cap"] if now[1] != "end" else 120):
+        if not alone and a[0] == "P" and a[3][0][0] == out[0] and (a[2][-2][0] == l[0] or a[2][-1][0] == r[0]) and a[5] + b[5] <= (OPT["cap"] if now[1] not in ("zout", "mirror") else 120):
             ops[-2:] = [("P", lambda: (a[1](), b[1]())[1], a[2] + b[2], a[3] + b[3], None, a[5] + b[5], 0.0, a[7])]
 
     def dma(e, out, a, row=None, after=()):
@@ -385,8 +453,7 @@ def rank_program(g, core, T, topo):
     iota(ioD, [[0, 8], [1, 4], [0, 4]], 0)
     iota(v("pi", 16, 32), [[-1, 16]], 16, 1)
     iota(v("pi", 32, 40), [[1, 8]], 1, 1)
-    iota(v("SP"), [[16, RUN[0]], [0, 32 // RUN[0]]], D // 2, 1)
-    iota(v("rf", 0, 18), [[16, 18]], 0, 1)
+    for h in range(2): iota(W("SP", h), [[0, 32 // RUN[h]], [16, RUN[h]]], D // 2, 1)
     for h in range(2): iota(W("JX", h), [[16, 32]], KW - D // 2 + 512 * h, 1)
     bits = [(0, 127), (0, 15), (4, 7), (0, 3), (2, 31), (3, 7), (0, 1), (1, 3), (0, 7), (0, 7)]
     cP, cA, cG, cM3, cP2, cGQ, cDUP, cMQ, c7 = range(9)
@@ -450,37 +517,21 @@ def rank_program(g, core, T, topo):
     ts(Id(0), num(0, 128), col(cP), A.is_equal)
     for k, wt in enumerate((-1.0 / D, 16.0, 2048.0 / BIG, -512.0 / D, -8192.0)): act(Id(k + 1), Id(0), scale=wt)
     act(Id(6), Id(0), scale=col(64))
-    ts(Id(7), ioB, col(cG), A.is_equal, float(D), A.mult)
+    ts(Id(7), ioB, col(cG), A.is_equal)
     ts(blk("Y", 0, 144), num(0, 144), col(86), A.is_equal, col(91), A.mult)
     ts(blk("Y", 1, 144), num(0, 144), col(86), A.is_equal, col(89), A.mult)
     for k in range(2): act(blk("II", k, 128), Id(0), scale=col(88))
     ts(v("PK"), num(0, 128), col(93), A.is_equal, col(94), A.mult)
     for a in range(16): act(blk("L", a, 128), Id(7), scale=col(64 + a))
-    for k, (sh, mk) in enumerate(((2, 3), (3, 1))): ts(v("pj", 40 + k, 41 + k), v("pi", 0, 1), sh, A.arith_shift_right, mk, A.bitwise_and)
-    cp(pcs(160, 2), v("pj", 40, 42))
-    ts(col(164), col(160), 8.0, A.mult, col(cG), A.add)
-    ts(v("RP"), num(0, 32), col(164), A.is_equal)
-    ts(blk("RQ", 0, 32), num(0, 32), col(164), A.is_equal, -float(D), A.mult)
-    ts(blk("RQ", 1, 32), num(0, 32), col(164), A.is_equal)
-    ts(col(165), col(cM3), 8.0, A.mult, col(160), A.add)
-    ts(v("qo"), num(0, 2), 4.0, A.mult, col(165), A.add)
-    ts(col(166), col(c7), 4.0, A.mult, col(161), A.add)
-    ts(v("so"), num(0, 2), 2.0, A.mult, col(166), A.add)
-    ts(v("rf", 0, 18), v("rf", 0, 18), col(21), A.subtract)
-    ts(v("ro1"), v("rf", 0, 18), 1.0 / 9, A.mult, -4.0 / 9, A.add)
-    ts(v("ri", 0, 16), v("rf", 0, 16), 1.0 / 8, A.mult, -3.5 / 8, A.add)
-    ts(v("ri", 16, 32), v("ri", 0, 16), 3, A.bitwise_and)
-    ts(v("ri", 32, 48), v("ri", 0, 16), 2, A.arith_shift_right)
-    ts(v("rf", 18, 34), v("ri", 16, 32), 8.0, A.mult)
-    tt(v("rf", 18, 34), v("rf", 18, 34), v("ri", 32, 48), A.add)
-    cp(v("ro0"), v("rf", 18, 34))
+    act(Id(8), blk("L", 0, 128), scale=128.0)
     ts(v("SP"), v("SP"), col(21), A.subtract)
     ts(v("JX"), v("JX"), col(21), A.subtract)
-    ts(pcs(120, 4), num(0, 4), 16.0, A.mult, col(cA), A.add)
-    ts(pcs(120, 4), pcs(120, 4), float(D // 2), A.add)
+    ts(pcs(170, 8), num(128, 136), 16.0, A.mult, col(cA), A.add)
     for t in range(RO): ts(v("PI", 128 * t, 128 * t + 128, p1=32), v("io", 192, 320, p1=32), float(t), A.not_equal, BIG, A.mult)
     ts(v("PI", p1=32), v("PI", p1=32), -1.5 * D, A.add)
+    stage("soon", 0)
     add("S", lambda: S.activation(ap(v("XW", D, KW)), ap(num(64, 192)), F.Silu), v("XW", D, KW), [num(64, 192)], cost=1400.0)
+    stage(None)
     ts(pcs(96, 16), pcs(96, 16), col(21), A.add)
     ts(pcs(112, 8), pcs(112, 8), col(cA), A.max, col(21), A.add)
     for s in range(16): ts(blk("SH", s, 128), num(0, 128), col(96 + s), A.is_equal)
@@ -498,7 +549,12 @@ def rank_program(g, core, T, topo):
     for b in range(8): act(blk("HR", b, 128), blk("HR", 8, 128), scale=col(148 + b))
     ts(col(129), col(65), 2687.0, A.mult, -128.0, A.add)
     ts(col(131), col(64), -32.0, A.mult, col(129), A.add)
-    ts(col(147), col(131), 16.0, A.mult)
+    ts(col(126), col(65), 42992.0, A.mult, -2048.0, A.add)
+    ts(col(147), col(64), -512.0, A.mult, col(126), A.add)
+    ts(col(125), col(21), 1.0, A.add)
+    ts(blk("HR", 9, 128), num(0, 128), col(125), A.is_equal, -16.0, A.mult)
+    ts(blk("WB", 1, 128), num(0, 128), col(21), A.is_equal)
+    tt(blk("HR", 9, 128), blk("HR", 9, 128), blk("WB", 1, 128), A.add)
     act(v("IF"), Id(0))
 
     def front(t, h):
@@ -520,7 +576,7 @@ def rank_program(g, core, T, topo):
         for m in (1, 2):
             for h in (1, 0):
                 if t: stage("mask%d%d" % (m, h))
-                mask(m, h, 7 - h)
+                mask(m, h, BK["mask"][h])
 
     def tables():
         stage("table", 0)
@@ -534,10 +590,10 @@ def rank_program(g, core, T, topo):
         dma("Y", v("XW", 0, D, 1, 0, 1), v("r0"), 0)
         for k in range(8):
             dma("G", v("XW", 0, D, 1, 16 * k + 2, 16 * k + 16), T.xreg[16 * k + 2:16 * k + 16, :],
-                after=[v(x) for x in ("pi", "n256", "io", "SP", "rf", "JX", "r0")])
-        mm(ps(5, 0, 256), Id(2), v("d0"), True, False)
-        mm(ps(5, 0, 256), Id(0), v("d1"), False, True)
-        act(v("r1"), ps(5, 0, 256), bias=32.0)
+                after=[v(x) for x in ("pi", "n256", "io", "SP", "JX", "r0")])
+        mm(ps(4, 0, 256), Id(2), v("d0"), True, False)
+        mm(ps(4, 0, 256), Id(0), v("d1"), False, True)
+        act(v("r1"), ps(4, 0, 256), bias=32.0)
         dma("Y", v("XW", 0, D, 1, 1, 2), v("r1"), 1)
 
     Gs = ["Ga", "Gb", "Ga", "Ab"]
@@ -559,56 +615,45 @@ def rank_program(g, core, T, topo):
         H3, T3 = blk("H3", 2 * m + h, 128), blk("T3", h, 128)
         tt(T3, ps(h, 0, 128), v("Mq"), A.mult)
         tt(H3, ps(h, 0, 128), v("Mh"), A.mult)
-        mm(ps(h, 256, 288), T3, v("Rb"), True, False, True)
-        mm(ps(h, 256, 288), H3, blk("Rh", 0, 32), False, True, True)
-        ts(W("off", h, m), ps(h, 256, 288), D // 2 - 0.5, A.add)
-        if m == 1: ts(W("P1", h), ps(h, 256, 288), -0.5, A.add, 1.0 / D, A.mult)
-        if m == 2: ts(W("Qn", h), ps(h, 256, 288), -0.5, A.add)
-        if m == 2 and h:
-            stage("first")
-            mm(ps(6, 288, 320), T3, v("RP"), True, False)
-            mm(ps(6, 288, 320), H3, blk("RQ", 0, 32), False, True)
-            ts(W("Qc", h), ps(6, 288, 320), -0.5, A.add)
-            o = ps(7, 96, 128)
-            mm(o, H3, blk("RQ", 1, 32), True, False)
-            for i in range(RUN[h]): mm(part(o, i, RUN[h]), Id(0), v("e01", 32 * h + i, 32 * h + 32, RUN[h]), False, i == RUN[h] - 1)
-            act(v("CA"), o, F.Abs, bias=-(HB - 1.0) * D, scale=float(D))
-            tt(v("XH"), W("Qc", h), v("CA"), A.add)
+        o = ps(BK["two"][h], 256, 288)
+        mm(o, T3, v("Rb"), True, False, True)
+        mm(o, H3, blk("Rh", 0, 32), False, True, True)
+        ts(W("off", h, m), o, D // 2 - 0.5, A.add)
+        if m: ts(W(("P1", "Qn")[m - 1], h), o, -0.5, A.add)
         stage("cab%d%d" % (m, h))
-        o = ps(5 + 2 * h, 0, 32)
-        mm(o, H3, blk("Rh", 1, 32), True, True)
+        o = ps(BK["cab"][h], 0, 32)
+        mm(o, H3, blk("Rh", 1, 32), True, m < 2)
+        if m == 2: mm(o, Id(0), W("e01", h), False, True)
         act(W("cab", h, m), o, F.Abs, bias=-(HB - 1.0) * D, scale=float(D))
+        if m == 2: tt(W("XH", h), W("Qn", h), W("cab", h, m), A.add)
         stage("count%d%d" % (m, h))
         win, b = (v("XW", 0, D), 32.0) if t else (v("CT"), 0.0)
-        if m == 2 and h == 0:
+        if m == 2 and h == 0 and OPT["vcount"]:
             ts(part(R("Cg2", h), 0, 2), at(win, part(W("off", h, m), 0, 2)), b, A.add)
             act(part(R("Cg2", h), 1, 2), at(win, part(W("off", h, m), 1, 2)), bias=b)
         else: act(R("Cg%d" % m, h), at(win, W("off", h, m)), bias=b)
 
-    def check(m):
-        o = ps(4, 0, 64) if m < 2 else ps(6, 320, 384)
-        if m == 2: mm(o, Id(0), v("e01"), True, False)
-        if m != 1: mm(o, Id(1), blk("cab", m, 64), m == 0, False)
-        for a in range(16): mm(o, v("Y", 144 * (m % 2) + 16 - a, 144 * (m % 2) + 144 - a), v("Cg%d" % m, a, TH, 16), False, m == 2 and a == 15)
-        if m == 1:
-            mm(o, Id(4), blk("cab", m, 64), False, True)
-            ts(v("e01"), o, 513.0, A.not_equal, 1024.0, A.mult)
-        if m == 2: ts(v("nok"), o, 1.0, A.not_equal, 4 * BIG, A.mult)
+    def check(m, h=None):
+        c0, c1 = (0, 64) if h is None else (32 * h, 32 * h + 32)
+        o = ps(4, c0, c1) if m < 2 else ps(BK["nok"][h or 0], 320 + c0, 320 + c1)
+        for a in range(16): mm(o, v("Y", 144 * (m % 2) + 16 - a, 144 * (m % 2) + 144 - a), v("Cg%d" % m, 16 * c0 + a, 16 * c1, 16), a == 0 and m != 1, False)
+        mm(o, Id(4 if m == 1 else 1), v("cab", 64 * m + c0, 64 * m + c1), False, m > 0, True)
+        if m == 1: ts(v("e01"), o, 513.0, A.not_equal, 1024.0, A.mult)
+        if m == 2: ts(v("nok", c0, c1), o, 1.0, A.not_equal, 4 * BIG, A.mult)
 
     def moved(t, h, stop): mm(ps(2 + h), v("II", 128 - 16 * t, 256 - 16 * t) if t else v("PK"), z(t, h), True, stop)
 
-    def leave(t):
-        stage("leave")
-        o = ps(6, 384, 448)
-        mm(o, Id(0), v("Qn"), True, False)
-        mm(o, Id(3), v("nok"), False, True)
-        tt(v("w"), o, v("JX"), A.min)
-        ts(v("xoff"), v("w"), float(D // 2), A.add)
-        for h in (1, 0):
-            stage("leave%d" % h)
-            send(t, h)
-        stage("row")
-        tt(v("pk"), v("nok"), blk("cab", 2, 64), A.subtract)
+    def leave(t, h=None):
+        c0, c1 = (0, 64) if h is None else (32 * h, 32 * h + 32)
+        stage("xoff%s" % h)
+        o = ps(BK["nok"][h or 0], 384 + c0, 384 + c1)
+        mm(o, Id(0), v("Qn", c0, c1), True, False)
+        mm(o, Id(3), v("nok", c0, c1), False, True)
+        tt(v("w", c0, c1), o, v("JX", c0, c1), A.min)
+        ts(v("xoff", c0, c1), v("w", c0, c1), float(D // 2), A.add)
+        for x in (1, 0) if h is None else (h,):
+            stage("leave%d" % x)
+            send(t, x)
 
     def send(t, h):
         so = R("s%d" % t, h)
@@ -619,7 +664,15 @@ def rank_program(g, core, T, topo):
                 NOM["hop"] - 600 + (NOM["once"] if t == 0 else 0))
             add("X", None, to, [], ("arrival", sem, n_in), 1.0)
 
+    def twin(h):
+        own = v("XW", KW + 512 * h, KW + 512 * h + 512)
+        add("Y", lambda: g.sync.dma_start(ap(R("NC", h)), ap(own)), R("NC", h), [own], "dma", 50.0, NOM["dma"] + 128 * 2048 / NOM["rate"])
+
     def column(t, h):
+        if OPT["dmacol"]:
+            add("G", lambda: g.dma_start(T.NC[0:128:16, 512 * h:512 * h + 512], T.Cg2[0:128:16, 512 * h:512 * h + 512]), R("NC", h), [R("Cg2", h)],
+                "dma", NOM["gdma"], NOM["glag"])
+            return
         moved(t, h, False)
         mm(ps(2 + h), Id(6), R("Cg2", h), False, True)
         act(R("NC", h), ps(2 + h), bias=col(95 if t else 168))
@@ -630,56 +683,66 @@ def rank_program(g, core, T, topo):
         stage("win%d" % h)
         sizes = [(c - d) * nr for d in range(1, c)]
         npair = sum(sizes)
-        n = 8 + h
-        own = lambda a, b=32: v("own%d" % h, n * a, n * b)
         SH = lambda s: blk("SH", s % 16, 128)
-        if h == 0: cp(W("Qc", h), at(W("w", h), v("qo")))
-        act(own(0), at(v("XH") if h else W("w", h), v("ro%d" % h)))
+        for k in range(8): act(v("own%d" % h, k, 256, 8), W("XH", h))
+        bank = BK["win"][h]
+        own = lambda i0, i1: box("own%d" % h, range(nr), range(i0, i1), range(8))
+        far = lambda i0, i1, k0, k1: box("p%d" % bank, range(nr), range(i0, i1), range(k0, k1))
+        for k in range(9):
+            mm(ps(bank, k, 512, 16), SH(k), W("Qn", h), True, False)
+            mm(ps(bank, k, 512, 16), SH(k), W("cab", h, 2), False, True)
+        tt(v(eq, 0, 256), far(0, c, 1, 9), own(0, c), A.is_equal)
+        for k in range(8): mm(ps(h, npair, npair + 32), blk("E", k, 128), v(eq, k, 256, 8), k == 0, k == 7)
         for r in range(2):
-            bank = 4 + r * (1 - h)
-            for k in range(n * (1 - r * h)):
-                mm(ps(bank, k, 32 * n, n), SH(k if h else k + 1 + 8 * r), W("Qc", h), True, not h)
-                if h: mm(ps(bank, k, 32 * n, n), SH(k), v("CA"), False, True)
-            e0 = n * (32 + npair * r)
-            if r == 0:
-                tt(v(eq, 0, 32 * n), ps(bank, 0, 32 * n), own(0), A.is_equal)
-                for k in range(8): mm(ps(h, npair, npair + 32), blk("E", k, 128), v(eq, k + h, 32 * n, n), k == 0, k == 7)
+            e0 = 256 + 8 * npair * r
             for d in range(1, c):
-                x, a = sizes[d - 1], e0 + n * sum(sizes[:d - 1])
-                if r * h: tt(v(eq, a, a + n * x), ps(bank, n * d * nr, 32 * n), own(0, x), A.is_equal)
-                else: tt(v(eq, a, a + n * x), ps(bank, 0, n * x), own(d * nr), A.is_equal)
-            for k in range(r * h, n - r * h): mm(ps(h, 0, npair), SH(-k * r * h), v(eq, e0 + k, e0 + n * npair, n), r == 0 and k == 0, r == 1 and k == 7)
+                x, a = sizes[d - 1], e0 + 8 * sum(sizes[:d - 1])
+                if r: tt(v(eq, a, a + 8 * x), far(d, c, 0, 8), own(0, c - d), A.is_equal)
+                else: tt(v(eq, a, a + 8 * x), far(0, c - d, 1, 9), own(d, c), A.is_equal)
+            for k in range(8): mm(ps(h, 0, npair), SH(-k * r), v(eq, e0 + k, e0 + 8 * npair, 8), r == 0 and k == 0, r == 1 and k == 7)
+        stage("lose%d" % h)
         nd = lambda a, b: v("nd", 144 * h + a, 144 * h + b)
-        ts(nd(0, npair + 32), ps(h, 0, npair + 32), 0.0, A.is_gt, 8192.0, A.mult)
+        if OPT["nd"][h] == "V": ts(nd(0, npair + 32), ps(h, 0, npair + 32), 8192.0, A.mult)
+        else: act(nd(0, npair + 32), ps(h, 0, npair + 32), scale=8192.0)
         o = ps(h, 352, 384)
-        mm(o, Id(0), W("Qc", h), True, False)
-        for i in range(c * h): mm(part(o, i, c), Id(3), v("nok", 32 * h + i, 32 * h + 32, c), False, False)
-        for d in range(1, c): mm(ps(h, 352 + d * nr, 384), Id(0), nd(sum(sizes[:d - 1]), sum(sizes[:d])), False, False)
+        mm(o, Id(0), W("Qn", h), True, False)
+        mm(o, Id(3), W("nok", h), False, False)
+        for d in range(1, c): mm(box("p%d" % h, range(352 // c, 384 // c), range(d, c)), Id(0), nd(sum(sizes[:d - 1]), sum(sizes[:d])), False, False)
         mm(o, Id(0), nd(npair, npair + 32), False, True)
-        if h:
-            for i in range(c): ts(v("soff", 32 * h + i, 32 * h + 32, c), part(o, i, c), col(120 + i), A.min, float(D // 2), A.add)
+        if OPT["soff"][h] == "c":
+            for i in range(c): ts(v("soff", 32 * h + i, 32 * h + 32, c), ps(h, 352 + i, 384, c), col(170 + i), A.min, float(D // 2), A.add)
         else:
-            tt(v("wl"), o, v("SP"), A.min)
-            ts(W("soff", h), at(v("wl"), v("so")), float(D // 2), A.add)
+            tt(W("wl", h), o, W("SP", h), A.min)
+            ts(W("soff", h), W("wl", h), float(D // 2), A.add)
 
-    def back():
-        ts(v("cB"), blk("cab", 1, 64), 1.0 / D, A.mult, -1024.5, A.add)
-        for b in range(2):
-            for a in range(8):
-                o = part(ps(2 + b), a, 8)
-                mm(o, blk("L", 8 * b + a, 128), v("P1"), True, False)
-                mm(o, blk("L", 8 * b + a, 128), v("cB"), False, b)
-                if b == 0: mm(o, Id(0), v("X2", a, TH, 16), False, True)
-            for a in range(8):
-                if b == 0: act(v("Bb", a, TH, 16), part(ps(2), a, 8))
-                else: tt(v("Bb", 8 + a, TH, 16), part(ps(3), a, 8), v("X2", 8 + a, TH, 16), A.add)
+    def copy(e, out, a, b):
+        if e == "S": act(out, a, bias=b)
+        else: ts(out, a, b, A.add)
 
-    def new_key(t, h):
-        mm(ps(4 + h), v("PI", 128 * t, 128 * t + 128, p1=1), v("one", p1=1), True, False)
-        for a in range(16):
-            l = v("Z", 160 * a + 16 + a - t, 160 * a + 144 + a - t)
-            mm(ps(4 + h, a, 512, 16), l, W("Qn", h), False, False)
-            mm(ps(4 + h, a, 512, 16), l, W("pk", h), False, a == 15)
+    def back(h=None):
+        if h is None:
+            for e in range(2):
+                mm(ps(2 + e), Id(0), v("X2", e, TH, 2), True, False)
+                for a in range(e, 16, 2):
+                    mm(ps(2 + e, a // 2, 512, 8), blk("L", a, 128), v("P1"), False, False)
+                    mm(ps(2 + e, a // 2, 512, 8), blk("L", a, 128), blk("cab", 1, 64), False, a >= 14)
+            for x in (1, 0):
+                for e in range(2): copy(OPT["bcopy"][2 * x + e], R("Bb", x, e, 2), part(ps(2 + e), x, 2), -BIG - D // 2)
+            return
+        b = BK["back"][h]
+        mm(ps(b), Id(0), R("X2", h), True, False)
+        for a in range(16): mm(ps(b, a, 512, 16), blk("L", a, 128), W("P1", h), False, False)
+        mm(ps(b), Id(8), R("Cg1", h), False, True, True)
+        for e in range(2): copy(OPT["bcopy"][2 * h + e], part(R("Bb", h), e, 2), part(ps(b), e, 2), -BIG - 1.5 * D)
+
+    def new_key(t):
+        tt(v("pk"), v("nok"), blk("cab", 2, 64), A.subtract)
+        for e in range(2):
+            mm(ps(4 + e), v("PI", 128 * t, 128 * t + 128, p1=1), v("one", p1=1), True, False)
+            for a in range(e, 16, 2):
+                l = v("Z", 160 * a + 16 + a - t, 160 * a + 144 + a - t)
+                mm(ps(4 + e, a // 2, 512, 8), l, v("Qn"), False, False)
+                mm(ps(4 + e, a // 2, 512, 8), l, v("pk"), False, a >= 14)
 
     def stack(name, n, bank, c0, order):
         for b in order: mm(ps(bank, 0, n), v("HX", 8 - b, 136 - b), blk(name, b, n), b == order[0], b == order[7])
@@ -690,67 +753,78 @@ def rank_program(g, core, T, topo):
     for t in range(RO):
         for m in range(3):
             for h in (1, 0):
-                stage("hop%d" % h, t)
+                stage("hop%d%d" % (m, h), t)
                 gather(m, h)
                 turn(t, m, h)
             stage("check%d" % m)
-            check(m)
+            if m < 2 or not OPT["split"]: check(m)
             stage("moved")
             for h in (1, 0) if m == 0 else ():
                 moved(t, h, True)
                 act(v("XW", KW + 512 * h, KW + 512 * h + 512), ps(2 + h), bias=col(95 if t else 168))
-            stage("back")
-            if m == 1: back()
+                if OPT["dmacol"]: twin(h)
+            for h in OPT["back"] if m == 1 else ():
+                stage("back%s" % h)
+                back(h)
         for h in (1, 0):
             stage("old%d" % h)
             gather(3, h)
-        leave(t)
+        for h in (1, 0) if OPT["split"] else ():
+            stage("check2%d" % h)
+            check(2, h)
+            leave(t, h)
+        if not OPT["split"]: leave(t)
         for h in (1, 0): winners(h)
         for h in (1, 0):
             stage("column%d" % h)
             column(t, h)
-        for h in (1, 0):
-            stage("row%d" % h)
-            new_key(t, h)
+        stage("row")
+        new_key(t)
         for h in (1, 0):
             nr = 32 // RUN[h]
             for r in range(nr - 1, -1, -1):
                 so = part(W("soff", h), r, nr)
-                stage("run")
+                stage("run%d" % h)
                 tt(at(v("K"), so), part(R("Ab", h), r, nr), part(R("Bb", h), r, nr), A.max)
-                stage("xrun")
+                stage("xrun%d" % h)
                 act(at(v("XW", 0, KW), so), part(R("NC", h), r, nr), F.Silu)
         for h in (1, 0):
             stage("min%d" % h)
-            for i in range(4): tt(R("K", h, i, 4), R("K", h, i, 4), ps(4 + h, i, 512, 4), A.min)
+            for i in range(4): tt(R("K", h, i, 4), R("K", h, i, 4), ps(4 + i % 2, 256 * h + i // 2, 256 * h + 256, 2), A.min)
         if t < RO - 1: masks(t + 1)
 
-    stage("end")
+    stage("zout")
     stack("s4", 128, 7, 512, range(8))
     for h in (1, 0):
         mm(ps(2 + h), blk("II", 1, 128), R("s4", h), True, False)
         for b in range(4): mm(part(ps(2 + h), b, 4), blk("HR", 4 * h + b, 128), v("hi", 512, 640), False, b == 3)
         for b in range(2): act(part(R("oz", h), b, 2), part(ps(2 + h), b, 2), bias=col(131))
     dma("Y", T.yz[:], v("oz"))
-    for h in (1, 0):
-        ts(R("Hk", h), R("K", h), 1.0 / D, A.mult, HB - 0.5 + 0.5 / D, A.add)
-        ts(R("Hn", h), R("Hk", h), 1.0 - HB, A.add, 0.0, A.min)
+    stage("ksum")
     top = 16 - OPT["npe"]
+    cp(ps(0, 256, 512), blk("K", top - 1, 256))
+    for b in range(top - 2, -1, -1): tt(ps(0, 256, 512) if b else blk("okk", 0, 256), blk("K", b, 256), ps(0, 256, 512), A.add)
+    stage("mirror")
+    for b in (3, 2, 1, 0):
+        ts(blk("Hk", b, 256), blk("K", b, 256), 1.0 / D, A.mult, HB - 0.5 + 0.5 / D, A.add)
+        ts(blk("Hn", b, 256), blk("Hk", b, 256), 1.0 - HB, A.add, 0.0, A.min)
     for b in range(top, 16): mm(ps(1, 0, 256), v("IF"), blk("K", b, 256), b == top, False)
     for b in (3, 2, 1, 0): mm(ps(1, 0, 256), Id(5), blk("Hn", b, 256), False, b == 0)
-    cp(ps(0, 256, 512), blk("K", top - 1, 256))
-    for b in range(top - 2, 3, -1): tt(ps(0, 256, 512) if b > 4 else blk("okk", 0, 256), blk("K", b, 256), ps(0, 256, 512), A.add)
-    for b in (3, 2, 1, 0): tt(ps(1, 0, 256), blk("K", b, 256), ps(1, 0, 256), A.add)
+    stage("ksum")
     tt(blk("okk", 1, 256), blk("okk", 0, 256), ps(1, 0, 256), A.add)
     dma("Y", T.yk[:], blk("okk", 1, 256))
-    turns = range(7, -1, -1)
-    for b in turns: act(blk("xb", b, 512), blk("XW", b, 512), bias=col(90))
-    stack("xb", 512, 6, 0, turns)
-    act(v("oc", p1=64), ps(6, p1=64), bias=-1.0, scale=1.0 / 32)
-    dma("S", T.yc[:], v("oc", p1=64))
-    for b in turns:
-        for a in (2 * b, 2 * b + 1): mm(ps(2, 0, 256), blk("II", 1, 128), blk("xb", a, 256), a == 14, False)
-    for b in range(2): mm(ps(2, 0, 256), blk("HR", 8, 128), blk("hi", b, 256), False, b == 1)
+    stage("rows")
+    for k in range(2):
+        add("Y", lambda k=k: g.sync.dma_start(ap(v("r%d" % k)), T.XW[k:128:16, 0:D]), v("r%d" % k), [v("XW", 0, D)], "dma", 50.0, NOM["dma"] + 128 * 1024 / NOM["rate"])
+    tile = lambda e, out, a, x, y: act(out, a, bias=y, scale=x) if e == "S" else ts(out, a, x, A.mult, y, A.add)
+    tile(OPT["tile"][0], v("d1"), v("r1"), 0.0625, 158.0 - 7.5 / 16)
+    tile(OPT["tile"][1], v("d0"), v("r0"), 1.0 / 32, -1.0)
+    dma("G", T.yc[:], v("d0"))
+    stage("xsum")
+    for b in range(8): act(blk("xb", b, 512), blk("XW", b, 512), bias=col(90))
+    for a in range(16):
+        mm(ps(2, 0, 256), blk("II", 1, 128), blk("xb", a, 256), a == 0, a == 15)
+        if a == 13: mm(ps(2, 0, 256), blk("HR", 9, 128), v("d1"), False, False, True)
     act(v("ox"), ps(2, 0, 256), bias=col(147))
     dma("Y", T.yx[:], v("ox"))
     emit(g, T, ops)

@@ -6,11 +6,13 @@ KW = D + 128
 BIG = float(1 << 22)
 HB = 1600
 PB = float(HB * D)
+GOOD = 513.0 * 1024
+PIECES = (("1", 1, 0, 8, False, 1), ("0", 0, 0, 8, True, 0))
 RUN = (8, 4)
-NOM = dict(cyc=0.83, pe=0.42, gather=1.5, scatter=3.5, wake=220.0, dma=1800.0, rate=300.0, hop=4500.0, once=2000.0, gdma=1000.0, glag=1500.0)
-OPT = dict(npe=3, cap=230, seed=3, turns=700, shifts=3000, polish=600, heat=100.0, heat2=60.0)
-OPT.update(tile="SS", nd="VV", soff="tc", dmacol=True, vcount=False, split=True, back=(1, 0), bcopy="SSSS")
-BK = dict(two=(5, 7), mask=(6, 6), cab=(5, 7), nok=(6, 6), win=(5, 4), back=(2, 3))
+NOM = dict(cyc=0.83, pe=0.42, gather=1.5, scatter=3.5, wake=220.0, dma=1800.0, rate=300.0, hop=4500.0, less=700.0, once=2000.0, gdma=1000.0, glag=1500.0)
+OPT = dict(npe=3, cap=230, seed=3, turns=800, shifts=6000, polish=1500, heat=100.0, heat2=60.0)
+OPT.update(mk="SSSSSSSSSSSS", mv="SSSS", e1=False, tile="SS", u16=True, cut=2, late=(3, 0), own="SV", old0="S", soff="tc", nd="VV", pclear=True, sq="VVVVV", dmacol=True, vcount=False, split=True, back=(1, 0), bcopy="SSSS")
+BK = dict(front=(7, 4), two=(5, 7), mask=(6, 6), cab=(5, 7), nok=(7, 6), win=(5, 4), back=(2, 3))
 FREE = "hop01 hop00 hop11 hop10 cab01 cab00 cab11 cab10 count01 count00 count11 count10 check0 moved back1 back0".split()
 LOOSE = "old1 old0 leave1 leave0 xoff1 xoff0 check21 check20 win1 win0 lose1 lose0 clear row back1 back0 run1 run0 xrun1 xrun0 min1 min0 count20 cab20 column1 column0".split()
 ORDER = {
@@ -21,7 +23,27 @@ ORDER = {
 ORDER = {'V': '<min0:2 hop01*3 <min0:0 hop01 <min0:3 hop00*4 hop01*2 hop00 hop01 hop00 hop11 hop00 hop11 hop10:1,0 hop11*4 hop10:2,3 hop21:0 hop10:4 hop21:1 hop10:5 hop20:0,1 hop21:2,3 check1 hop21:5,4 hop20:2,3 old1:1 cab21 hop20:5,4 old1:0 win1:0 cab20 check21 win1:3,1,2,5 xoff1 win1:6,4 xoff1 win0:7,1,3,4,11 check20 win0:2 lose1:0 win0:0 xoff0 win0:12,13 xoff0 lose1:1,3,2,4 win0:14,5,6 run1 win0:8 run1 win0:9 run1 win0:10 run1 clear run1 lose0 run1 clear run1 row lose0 run1 lose0 clear run0*2 clear run0*2 min1:0,2,1,3 min0:1', 'S': '<mask21*2 count01 cab01 count00 moved <mask20 cab00 <mask20 count11 count10 cab11 cab10 moved cab21 count21 win1*8 cab20 count20 win0*8 back1:1 leave1 old0 leave0 xrun1 back0:1 xrun1 back1:0 xrun1 back0:0 xrun1*5 mask01 xrun0 mask11 mask01 mask00 mask01 mask11 mask00*2 xrun0 mask10:1,0 xrun0*2', 'P': '<row:5 hop01 <mask00 hop00 <mask10 hop01*4 hop00*4 hop01*2 <mask21 hop00 hop11 hop00 hop10 cab01 moved:1,0 <mask20 hop11*4 cab00 hop10*3 hop11*2 hop10 hop21 check0*3 hop10*2 cab11 back1*3 hop21*4 cab10 check1*3 hop21*2 hop20*5 cab21*2 back1 hop20*2 win1*3 cab20*2 check21*3 win0*2 xoff1 win0 win1*2 check20*3 win1 back0 xoff0 lose1 win0 back0*3 win0*2 row:0 win0*2 row:3 lose0*2 row:1,2 mask01 row:4 mask11 mask01 mask00', 'G': 'column1 column0 leave1 leave0'}
 FIRST = {'V': 'hop01*4 hop00:0,1,2,3 hop01*2 hop00:5,4 hop01 hop11 hop00:6 hop11 hop10*2 hop11*4 hop10*2 hop21 hop10 hop21 hop10 hop20*2 hop21*4 check1 hop20*4 old1 cab21 check21 old1 xoff1 cab20 xoff1 win1:0,3,1,6,2 check20 win1:5,4 win0:12,3 xoff0 win0:8,13 xoff0 win0:5 lose1:0 win0:0,10,6,4,7,14 lose1:1,2,4,3 win0:1 run1 win0:2 run1 row win0:11 run1 win0:9 run1 clear run1 lose0 run1 clear run1 lose0 run1 lose0 clear run0 clear run0*3 min1:2,0 min0:1 min1:1,3', 'S': 'count01 count00 cab00 cab01 moved count11 count10 cab11 cab10 moved count21 cab21 count20 cab20 win1*8 back1:1 win0*8 leave1 old0 leave0 xrun1 back1:0 xrun1*5 back0:1 xrun1*2 back0:0 xrun0 mask01 xrun0 mask11:1 mask01 mask00 mask11:0 mask01 mask00*2 mask10:1 xrun0 mask10:0 xrun0', 'P': 'hop01 hop00 hop01*4 hop00*4 hop01*2 hop00 hop10 hop00 cab01 cab00 hop11*5 moved hop10*2 hop11*2 hop10*2 hop21 check0*2 cab11 check0 hop10*2 moved back1*3 hop21*4 hop20 cab10 check1*2 hop21*2 hop20*2 check1 hop20*2 back1 cab21 hop20*2 cab21 check21*3 cab20*2 win1 xoff1 win1*2 win0 check20*3 win0*2 win1 xoff0 win1*2 lose1 back0 win0 row:0 win0 back0 win0 back0 win0*2 row:1 lose0 back0 lose0 row:3,2 mask01 mask11 mask01 mask00 row:4', 'G': 'column1 column0 leave1 leave0'}
 LAST = {'V': 'hop01*2 <min0:0 hop01*2 <min0:2,3 hop00*4 hop01*2 hop00 hop01 hop00 hop11:0 hop00 hop11:1 hop10:1,0 hop11:2,3,5,4 hop10:2,3 hop21:0 hop10:4 hop21:1 hop10:5 hop20:1,0 hop21:2,3 check1 hop21:5,4 hop20:2,3 cab21 hop20:5,4 old1*2 win1:0,3 check21 cab20 win1:1,2,6 xoff1 win1:4 xoff1 win1:5 win0:11,2,7,3 check20 win0:13,4 lose1:0 win0:14,0 xoff0 win0:1 xoff0 lose1:2,1,4,3 win0:8 run1 win0:6,9 run1 win0:5,10 run1 win0:12 row run1 clear run1 lose0 run1 clear run1 lose0 run1 lose0 clear run0 clear run0*3 ksum min1:1,0 ksum min1:3,2 ksum min0*2 ksum min0*2 ksum mirror:0 ksum mirror:2,1 ksum mirror:4 ksum mirror:3,5 ksum mirror:6 ksum mirror:7 ksum*2', 'S': '<mask21:1,0 cab01 count01 count00 <mask20:1 cab00 moved <mask20:0 count11 count10 cab11 cab10 moved cab21 count21 win1*8 cab20 count20 win0*8 back1:1 old0 leave1 leave0 xrun1 back0:1 xrun1 back1:0 xrun1 back0:0 xrun1*3 zout:0 xrun1*2 xrun0 zout:1 xrun0 zout:3 xrun0 zout:4 xrun0 zout:2 xsum*6 rows:1 xsum rows:0 xsum*2', 'P': 'hop01 hop00 <row:5 <mask00:1 <mask10 hop01*4 hop00*4 hop01*2 <mask21 hop11 hop00*2 cab01 moved:1 <mask20 hop11*4 hop10 moved:0 cab00 hop10*2 hop11*2 hop10*2 check0*2 hop10*2 back1*2 check0 hop21 cab11 back1 hop20 hop21*3 cab10 hop21 check1*3 hop21*2 hop20*4 cab21*2 back1 hop20*2 win1*3 cab20*2 check21*3 win0*3 xoff1 win1*2 check20*3 win1 xoff0 lose1 row:0 back0*4 zout:0 win0*5 row:3 zout:1,7 lose0*2 zout:2,3,4 row:1,4,2 zout:5,6,8 row:5 zout:9 mirror*4 xsum mirror xsum mirror xsum*4 mirror*2 xsum mirror xsum*2', 'G': 'column1 column0 rows'}
-OPT.update(npe=5)
+OPT.update(npe=5, bcopy="SSVV", sq="VVVVS")
+FREE = "hop01 hop00 hop11 hop10 cab01 cab00 cab11 cab10 count01 count00 count11 count10 check0 moved1 moved0 back1 back0".split()
+ORDER = {'V': '<min1*3 hop01 <min0 hop01*3 <min0*3 hop00*4 hop01*2 hop00 hop01 hop00 hop11 hop00 hop11 hop10*2 hop11*2 hop10 hop11 hop10 hop11 hop21 hop10 hop21 hop10 hop20*2 hop21*2 back1*2 hop21*2 win1:4,3,7 hop20*2 win1:2,6,1,0,5,10 hop20*2 win1:11,8 cab20 win1:14,9,12,13 check21 old1*2 lose1 xoff1 win0:0,1 check20 win0:3,7 soff1 win0:4,2 xoff0 run1 win0:5 late0:4 win0:6 run1 late0:5,1 run1 late0:0 run1 late0:2 lose0 run1 late0:3,6 run1 row clear run1 clear*2 run1 soff0 clear run0*4 min1', 'S': '<mask00 <xrun0 <mask10*2 <xrun0 <mask21*2 moved1*2 cab01 count01 count00 cab00 <mask20*2 count11 count10 cab11 moved0*2 cab10 cab21*2 count21 cab20 count20 win0*8 old0 leave1 leave0 front1 xrun1 back0 front0 xrun1 back0 xrun1*6 xrun0*2 mask01*2 mask11*2 mask00', 'P': '<row hop01 hop00 <row*5 <mask01 <mask11 <mask00 <mask10 hop01*4 hop00*4 hop01*2 <mask21 moved1 hop00 hop11 cab01 hop00 moved0 hop10 <mask20 cab00 hop11*4 back1 hop10*4 hop11*2 hop21 check0*3 hop10*2 cab11 back1 hop20 back1*2 hop21*4 cab10 check1*2 hop21*2 check1 cab21 hop20*4 clear win1*3 hop20*2 cab20*2 check21*3 win0*2 win1*2 win0 win1 xoff1*3 check20*3 lose1*2 lose0*2 lose1 back0 xoff0*3 back0*2 lose0 win0 front1 back0 win0 front0 win0 late0*3 lose0 late0*4', 'G': 'column1 column0 front1 front0 leave1 leave0'}
+FIRST = {'V': 'hop01*4 hop00*4 hop01*2 hop00*2 hop01 hop11 hop00 hop11 hop10:1,0 hop11*2 hop10:2 hop11 hop10:3 hop11 hop21 hop10:4 hop21 hop10:5 hop20*2 hop21*2 back1*2 hop21*2 hop20*2 win1:2,0,4,7,3,6,1,5 hop20*2 cab20 win1:11,8,10 check21 win1:12,14,13,9 old1 xoff1 check20 old1 lose1 xoff0 clear:1 win0:5,4 late0:0 soff1 win0:2,3 run1 win0:6,0 run1 win0:7,1 run1 late0:2,1 run1 late0:3 lose0 run1 late0:5,6,4 run1 row clear:2 run1 clear:0 soff0 run1 run0 clear:3 run0*3 min1', 'S': 'cab01 count01 cab00 count00 moved1*2 count11 count10 cab11 moved0*2 cab10 cab21*2 count21 cab20 count20 win0*8 old0 leave1 leave0 front1 xrun1 front0 xrun1*4 back0 xrun1*2 back0 xrun1 xrun0*2 mask01*2 mask11*2 mask00', 'P': 'hop00 hop01*5 hop00*4 hop01*2 hop00*2 hop11 cab01 cab00 hop11*4 moved1 hop10*5 hop11*2 moved0 hop21 back1 hop10*2 check0 cab11 check0*2 hop20 back1*2 hop21*4 cab10 back1 check1*2 hop20 hop21*2 hop20 check1 cab21 hop20*2 clear win1 hop20*2 cab20*2 win1*2 check21*3 win0 win1 xoff1*3 check20*3 win1*2 lose0 xoff0*3 win0*2 lose0 lose1*3 front1 back0 lose0 back0 front0 late0 back0 win0*3 back0 late0*2 lose0 late0*4', 'G': 'column1 column0 front1 front0 leave1 leave0'}
+LAST = {'V': '<min1:1,2,3 <min0 hop01*4 <min0*3 hop00*4 hop01*2 hop00 hop01 hop00 hop11 hop00 hop11 hop10:1,0 hop11*4 hop10:2,3 hop21 hop10:4 hop21 hop20:1 hop10:5 hop20:0 hop21*2 back1*2 hop21*2 win1:5,4,1 hop20:2,3 win1:2,6,0,3,7,10 hop20:4,5 win1:9,11,8,12 cab20 win1:13,14 check21 old1*2 lose1 xoff1 win0:0,1 check20 win0:3 soff1 xoff0 win0:7,2,4 run1 late0:5,4 win0:5 run1 win0:6 late0:1 run1 late0:0 run1 late0:2 lose0 run1 late0:3 clear run1 row late0:6 run1 clear*2 run1 soff0 clear run0*4 ksum min1:0,1 ksum min0:3 min1:3,2 ksum min0:0,1 ksum min0:2 mirror:0 ksum mirror:2 ksum mirror:4,1 ksum mirror:3,5 ksum mirror:6 ksum*2 mirror:7 ksum*2', 'S': '<mask00:1 <xrun0:2 <mask10*2 <xrun0:3 <mask21*2 cab01 moved1*2 count00 count01 cab00 <mask20*2 count11 count10 cab11 moved0*2 cab10 cab21*2 count21 cab20 count20 win0*8 old0 leave1 leave0 xrun1*2 back0 xrun1*2 back0 xrun1*3 zout:0 xrun1 xrun0 zout:1 xrun0 zout:3 xrun0 zout:4 xrun0 zout:2 xsum*6 rows:1 xsum rows:0 xsum*2', 'P': '<row hop01 <row*5 hop00 <mask01 <mask11 <mask00 <mask10 hop01*4 hop00*4 hop01*2 <mask21 moved1 hop00 hop11 cab01 hop00 hop10 moved0 <mask20 cab00 hop11*4 back1 hop10*3 hop11*2 hop10 hop21 check0*2 hop10*2 hop20 check0 back1 cab11 back1*2 hop21*4 cab10 check1*2 hop21*2 check1 cab21 hop20*4 clear win1*3 hop20*2 cab20*2 check21*3 win0*2 win1*2 xoff1*2 win1 xoff1 win0 check20*3 lose1*3 lose0*2 xoff0*3 back0*4 win0 lose0 win0*2 late0*3 lose0 late0*4 zout:0,1,2,3 row zout:7 row*2 zout:4,5,6,8,9 row*3 mirror*4 xsum mirror xsum*2 mirror xsum mirror xsum*4 mirror*2 xsum', 'G': 'column1 column0 rows'}
+ORDER = {'V': 'hop01*4 <min0*4 hop00*4 hop01*2 hop00 hop01 hop00 hop11 hop00 hop11 hop10*2 hop11*2 hop10 hop11 hop10 hop11 hop21 hop10 hop21 hop10 hop20*2 hop21*2 back1*2 hop21*2 win1:2,6,3 hop20*2 win1:0,4,7,1,5,10 hop20*2 win1:9,8,11,14,13 cab20 check21 win1:12 old1*2 lose1 xoff1 win0:0,1 check20 win0:7,3,11 soff1 win0:2,9 xoff0 run1 win0:5,4 run1 win0:6,8,10 run1 late0 run1 late0 run1 late0 lose0 run1 row clear run1 clear*2 run1 soff0 clear run0*4 min1*4', 'S': '<mask10*2 <xrun0 <mask21 cab01 <mask21 count01 count00 cab00 <mask20*2 moved1 count11 count10 cab11 moved1 cab10 cab21*2 count21 moved0*2 cab20 count20 win0*8 old0 leave1 leave0 front1 xrun1 back0 front0 xrun1 back0 xrun1*6 xrun0*2 mask01*2 mask11*2 mask00*2 xrun0', 'P': 'hop01*4 <mask10 hop00*4 hop01*2 hop11 <mask21 hop00 cab01 hop00 hop10 <mask20 hop11*4 cab00 moved1 hop10*4 hop11*2 check0*2 hop10 hop21 hop10 back1 cab11 check0 hop20 back1*2 hop21*4 cab10 check1*2 hop21*2 check1 cab21 hop20*4 moved0 win1*3 hop20*2 cab20*2 check21*3 win0*2 win1*3 win0 xoff1*3 check20*3 lose1*2 lose0*2 lose1 back0 xoff0*3 win0 back0 lose0 front1 back0*2 front0 win0*3 late0 clear lose0 late0*2 row*6 mask01 mask11 mask00', 'G': 'column1 column0 front1 front0 leave1 leave0'}
+ORDER['P'] = 'hop01 hop00 ' + ORDER['P']
+FIRST = {'V': 'hop01*4 hop00*4 hop01*2 hop00*2 hop01 hop11 hop00 hop11 hop10*2 hop11*2 hop10 hop11 hop10 hop11 hop21 hop10 hop21 hop20 hop10 hop20 back1 hop21*2 back1 hop21*2 hop20*2 win1:7,2,6,1,3,0,5,4 hop20*2 cab20 win1:8,9,14 check21 win1:11,12,10,13 old1 xoff1 check20 old1 lose1 xoff0 clear:1 win0:4,3,2 soff1 win0:6 late0:1 win0:10 run1 win0:0,11 run1 win0:1,5 run1 win0:7,9,8 run1 late0:0 run1 lose0 run1 late0:2 run1 clear:0 run1 soff0 row clear:2 run0 clear:3 run0*3 min1*4', 'S': 'cab01 count01 count00 moved1 cab00 moved1 count11 count10 cab11 moved0*2 cab10 cab21*2 count21 cab20 count20 win0*8 leave1 old0 leave0 front1 front0 xrun1*6 back0 xrun1*2 back0 xrun0*2 mask01*2 mask11*2 mask00*2 xrun0', 'P': 'hop01 hop00 hop01*4 hop00*4 hop01*2 hop00 hop10 hop00 cab01 hop11 cab00 hop11*4 moved1 hop10*4 hop11*2 check0*2 hop10 hop21 hop10 back1 cab11 back1 moved0 hop20 back1 hop21*4 cab10 check0 check1*2 hop20 check1 hop21*2 hop20 cab21 hop20*2 clear win1 hop20*2 cab20*2 win1*2 check21*3 win0 win1 xoff1*3 check20*3 win1*2 lose0 xoff0*3 win0*2 lose1*3 back0 lose0 front1 front0 back0 lose0 win0*4 late0 back0*2 lose0 late0*2 row*6 mask01 mask11 mask00', 'G': 'column1 column0 front1 front0 leave1 leave0'}
+LAST = {'V': 'hop01*4 <min0*4 hop00*4 hop01*2 hop00 hop01 hop00 hop11 hop00 hop11 hop10*2 hop11*2 hop10 hop11 hop10 hop11 hop21 hop10*2 hop21 hop20*2 hop21*2 back1*2 hop21*2 win1:2,7,4 hop20*2 win1:5,0,3,1,6,10 hop20*2 win1:8,11,13,12,9 cab20 check21 win1:14 old1*2 lose1 xoff1 win0:0,1 check20 win0:3,7 soff1 win0:10,2 xoff0 run1 win0:5,6,11,4 run1 win0:9,8 run1 late0:0 run1 late0:2 lose0 run1 late0:1 run1 clear*2 run1 clear run1 soff0 clear run0 row run0*3 ksum min0:3 min1:1,3 ksum min1:2,0 ksum min0:2,1 ksum mirror:0 min0:0 ksum mirror:2 ksum mirror:4 ksum mirror:1,3 ksum mirror:6 ksum mirror:5,7 ksum*3', 'S': '<mask10*2 <xrun0:3 <mask21*2 count00 cab00 cab01 count01 <mask20*2 moved1 count11 count10 cab11 moved1 cab10 cab21*2 count21 moved0 cab20 moved0 count20 win0*8 old0 leave1 leave0 back0 xrun1 back0 xrun1*6 zout:0 xrun1 xrun0 zout:1 xrun0 zout:3 xrun0 zout:4 xrun0 zout:2 xsum*6 rows:1 xsum rows:0 xsum*2', 'P': 'hop01 hop00 <mask10 hop01*4 hop00*4 hop01*2 <mask21 hop11 hop00*2 hop10 cab01 <mask20 hop11 cab00 hop11*3 moved1 hop10*4 hop11*2 hop21 check0*2 hop10*2 back1 cab11 check0 back1 hop20 cab10 back1 hop21*4 check1*2 hop21*2 check1 cab21 hop20*4 moved0 win1*3 hop20*2 cab20*2 check21*3 win0*3 win1*3 xoff1*3 check20*3 lose1*3 back0 xoff0*3 back0*3 lose0 win0 lose0 win0 lose0 win0*2 clear late0 zout:0 lose0 late0*2 zout:1,2,3,7,4,5,6 row:3 zout:8,9 row:4,5,0,1,2 mirror*4 xsum mirror xsum*3 mirror*2 xsum*2 mirror*2 xsum*3', 'G': 'column1 column0 rows'}
+EARLY = "hop01 hop00 hop11 hop10 cab01 cab00 count01 count00".split()
+FIRST = {'V': 'hop01*4 hop00*4 hop01*2 hop00*2 hop01 hop11 hop00 hop11 hop10*2 hop11*2 hop10 hop11 hop10 hop11 hop21 hop10 hop21 hop20 hop10 hop20 hop21*2 back1*2 hop21*2 hop20*2 win1:0,2,4,1,6,5,7 hop20*2 win1:3 cab20 win1:8,12,14 check21 win1:10,11,13,9 old1 xoff1 check20 old1 lose1 xoff0 win0:0 soff1 win0:1,6 run1 win0:5,7,8 run1 win0:2,3,4,9 run1 win0:11 late0:1 win0:10 run1 late0:0 run1 lose0 late0:2 run1 clear*2 run1 clear soff0 row run1 run0 clear run0*3 min1*4', 'S': 'cab01 count01 count00 moved1*2 cab00 count11 count10 moved0*2 cab11 cab10 cab21*2 count21 cab20 count20 win0*8 old0 leave1 leave0 front1 front0 back0*2 xrun1*8 xrun0*2 mask01*2 mask11*2 mask00*2 xrun0', 'P': 'hop01 hop00 hop01*4 hop00*4 hop01*2 hop10 hop00*2 cab01 cab00 hop11*5 moved1 hop10*4 hop11*2 check0*2 hop10 hop21 hop10 back1*2 cab11 moved0 hop20 back1 hop21*4 cab10 check0 check1*2 hop20 check1 hop21*2 hop20 cab21 hop20*2 clear win1 hop20*2 cab20*2 win1*2 check21*3 win1 xoff1*3 check20*3 win1*2 xoff0*3 win0*3 lose1*3 front1 lose0*3 back0*2 front0 back0*2 win0*3 row:0 win0 late0 lose0 late0*2 row:3,1,4,2,5 mask01 mask11 mask00', 'G': 'column1 column0 front1 front0 leave1 leave0'}
+ORDER = {'V': 'hop01*4 <min0*4 hop00*4 hop01*2 hop00 hop01 hop00 hop11 hop00 hop11 hop10*2 hop11*2 hop10 hop11 hop10 hop11 hop21 hop10 hop21 hop10 hop20*2 hop21*2 back1*2 hop21*2 win1:4 hop20*2 win1:2,3,1,6,7,0,5 hop20*2 win1:8,14,9,11,10 cab20 win1:13 check21 win1:12 old1*2 xoff1 lose1 win0:0,1 check20 win0:2,3 soff1 win0:9 xoff0 run1 win0:8,4 run1 win0:11,5,6,7 run1 win0:10 late0 run1 late0 run1 late0 lose0 run1 clear*2 run1 clear row run1 soff0 clear run0*4 min1*4', 'S': '<xrun0 <mask10*2 <xrun0 <mask21*2 count01 cab01 count00 <mask20*2 moved1 cab00 moved1 count11 count10 cab11 moved0*2 cab10 cab21*2 count21 cab20 count20 win0*8 old0 leave1 leave0 front1 back0 xrun1 front0 xrun1 back0 xrun1*6 xrun0*2 mask01*2 mask11*2 mask00*2', 'P': 'hop01 hop00 hop01*4 <mask10 hop00*4 hop01*2 <mask21 hop11 hop00 cab01 hop00 hop10 <mask20 hop11*4 moved1 cab00 hop10*4 hop11*2 check0*2 hop21 check0 hop10*2 back1 moved0 cab11 back1*2 hop21*4 hop20 cab10 check1*2 hop21*2 check1 cab21 hop20*4 win1*2 hop20*2 cab20*2 win1 check21*3 win0*2 win1*2 xoff1*3 win1 win0 check20*3 lose1*3 back0 xoff0*3 lose0 back0 lose0 back0 front1 back0 lose0 win0 front0 win0*3 clear late0 lose0 late0*2 row*6 mask01 mask11 mask00', 'G': 'column1 column0 front1 front0 leave1 leave0'}
+FIRST['S'] = FIRST['S'].replace('mask00*2 xrun0', 'mask00*2')
+LAST['S'] = LAST['S'].replace('<mask10*2 <xrun0:3', '<xrun0:2 <mask10*2 <xrun0:3').replace('cab11 moved1 cab10 cab21*2 count21 moved0 cab20 moved0 count20', 'cab11 moved0*2 cab10 cab21*2 count21 cab20 count20').replace('moved1 count11', 'moved1*2 count11')
+LAST['P'] = LAST['P'].replace('hop20*4 moved0 win1*3', 'hop20*4 win1*3').replace('check0 back1 hop20', 'check0 moved0 back1 hop20')
+LAST = {'V': 'hop01*4 <min0*4 hop00*4 hop01*2 hop00 hop01 hop00 hop11 hop00 hop11 hop10*2 hop11*2 hop10 hop11 hop10 hop11 hop21 hop10*2 hop21 hop20*2 hop21*2 back1 hop21*2 back1 win1:2,1 hop20*2 win1:3,4,5,0,6,7 hop20*2 win1:13,11,8 cab20 win1:12 check21 win1:14,10,9 old1 xoff1 old1 check20 lose1 win0:2,1 xoff0 win0:6,0 soff1 win0:5,3 run1 win0:4,7,11 run1 win0:10,9,8 run1 late0:0 run1 late0:2 lose0 run1 late0:1 run1 clear*2 run1 clear soff0 run1 clear run0 row run0*3 ksum min0:3 min1:2,3 ksum min1:0 min0:0 min1:1 ksum min0:1,2 ksum mirror:0 ksum mirror:2,1 ksum mirror:4,3 ksum mirror:6,5 ksum mirror:7 rows ksum*3', 'S': '<xrun0:2 <mask10*2 <xrun0:3 <mask21*2 count01 cab01 count00 cab00 <mask20*2 moved1*2 count11 count10 cab11 moved0 cab10 moved0 cab21*2 count21 cab20 count20 win0*8 old0 leave1 leave0 back0 xrun1*3 back0 xrun1*4 zout:0 xrun1 xrun0 zout:1 xrun0 zout:4 xrun0 zout:2 xrun0 zout:3 xsum*6 rows xsum*3', 'P': 'hop01 hop00 <mask10 hop01*4 hop00*4 hop01*2 <mask21 hop00*2 hop11 cab01 hop10 <mask20 hop11 cab00 hop11*3 moved1 hop10*4 hop11*2 check0*2 hop21 hop10 hop20 hop10 back1 cab11 moved0 check0 back1*2 hop21*4 cab10 check1*2 hop21*2 check1 cab21 hop20*4 win1*2 hop20*2 cab20*2 win1 check21*3 win0*2 win1 xoff1*3 check20*2 win1 check20 win1 win0 back0 xoff0*3 lose0 lose1*3 lose0 back0*3 win0 row:0 win0 zout:0 win0 lose0 win0 late0 clear zout:1 lose0 late0*2 zout:2 row:3 zout:3,7,4,5,6,8,9 row:4,5,1,2 mirror*5 xsum mirror xsum*2 mirror xsum mirror xsum*2 mirror*2 xsum*3', 'G': 'column1 column0 rows'}
+OPT.update(npe=6, tile="VS")
+OPT.update(pclear=False, late=(0, 0))
+ORDER = {'V': 'hop01*4 <min0*4 hop00*4 hop01*2 hop00 hop01 hop00 hop11 hop00 hop11 hop10*2 hop11*2 hop10 hop11 hop10 hop11 hop21 hop10 hop21 hop20 hop10 hop20 hop21*2 back1*2 hop21*2 win1:2 hop20*2 win1:1,4,3,5,6,0,7 hop20*2 win1:9,8,11,14,10 cab20 win1:13 check21 win1:12 old1*2 xoff1 lose1 win0:1,0 check20 win0:2,4 soff1 win0:3 xoff0 run1 win0:13,6,5,7 run1 win0:12,14,11 run1 win0:10,9 run1 win0:8 run1 clear run1 row lose0 run1 clear run1 soff0 clear run0 clear run0*3 min1*4', 'S': '<mask10*2 <xrun0 <mask21*2 count01 <mask20 cab01 count00 <mask20 cab00 moved1*2 count11 count10 cab11 moved0*2 cab10 cab21*2 count21 cab20 count20 win0*8 old0 leave1 leave0 front1 xrun1 back0 front0 xrun1 back0 xrun1*6 xrun0*2 mask01*2 mask11*2 mask00*2 xrun0', 'P': 'hop01 hop00 hop01*4 <mask10 hop00*4 hop01*2 <mask21 hop11 hop00 cab01 hop00 hop10 moved1 cab00 <mask20 hop11*4 hop10*4 hop11*2 hop21 check0*3 hop10*2 back1 cab11 moved0 back1*2 hop21*4 hop20 cab10 check1*2 hop21*2 check1 cab21 hop20*4 win1*2 hop20*2 cab20*2 win1 check21*3 win0*2 win1*2 xoff1*3 win1 win0 check20*3 lose1*3 back0 xoff0*3 win0 front1 back0*3 win0 front0 win0*3 row lose0*4 row*5 mask01 mask11 mask00', 'G': 'column1 column0 front1 front0 leave1 leave0'}
+FIRST = {e: " ".join(w for w in ORDER[e].split() if w[0] != "<") for e in ORDER}
+LAST = {'V': 'hop01*4 <min0*4 hop00*4 hop01*2 hop00 hop01 hop00 hop11 hop00 hop11 hop10*2 hop11*2 hop10 hop11*2 hop10 hop21 hop10*2 hop21 hop20*2 hop21*2 back1*2 hop21*2 win1:3,4 hop20*2 win1:7,2,0,6,5,1 hop20*2 win1:8,10 cab20 win1:11,14,9,12,13 check21 old1*2 xoff1 win0:14 lose1 win0:0,1 check20 win0:3,2 soff1 win0:4,7 xoff0 run1 win0:6,5,11 run1 win0:12,10 run1 win0:9,13 run1 win0:8 run1 clear run1 row lose0 run1 clear run1 soff0 clear run0 clear run0*3 min0:1 ksum min0:3,2,0 ksum min1:1,2 ksum min1:0,3 ksum mirror:2 ksum mirror:0 ksum mirror:3,4 ksum mirror:1,6 ksum mirror:7,5 ksum rows ksum*2', 'S': '<mask10*2 <xrun0:3 <mask21*2 cab01 count01 count00 cab00 <mask20 moved1*2 <mask20 count11 count10 cab10 cab11 moved0*2 cab21*2 count21 cab20 count20 win0*8 old0 leave1 leave0 xrun1*4 back0 xrun1 back0 xrun1 zout:0 xrun1*2 zout:1 xrun0 zout:4 xrun0 zout:2 xrun0 zout:3 xrun0 xsum*6 rows xsum*3', 'P': 'hop01 hop00 <mask10 hop01*4 hop00*4 hop01*2 <mask21 hop00 hop11 hop00 cab01 moved1 hop10 cab00 <mask20 hop11*4 hop10*4 hop11*2 check0 hop21 check0*2 hop10*2 cab11 back1 moved0 back1 cab10 back1 hop21*4 hop20 check1*2 hop21*2 check1 cab21 hop20*4 win1*2 hop20*2 win1 cab20*2 check21*3 win0*3 win1*2 xoff1*3 win1 check20*3 lose1*3 back0 xoff0*3 win0 back0 zout:4 back0 win0*2 back0 row:0 win0*2 zout:0,1,2,3 lose0*4 row:3 zout:7,5,8,6,9 row:4,1,2,5 mirror*4 xsum mirror xsum mirror xsum*3 mirror*2 xsum mirror*2 xsum*3', 'G': 'column1 column0 rows'}
 LEAD = dict(win0=1500.0, clear=-2000.0, soon=30000.0)
 OTHER = ((1.4, 1.3, 1.6, 1.8, 1.3), (0.7, 1.0, 0.8, 0.6, 0.8), (1.5, 1.0, 1.0, 0.9, 1.6))
 
@@ -30,24 +52,26 @@ SB = {
     "K": (KW, f32), "XW": (KW + TH, f32), "CT": (D, bf), "xb": (D, bf), "NC": (TH, f32),
     "ci": (256, i32), "ch": (256, bf), "d0": (256, bf), "d1": (256, bf), "r0": (256, f32), "r1": (256, f32), "z3": (TH, bf),
     "Ga": (TH, f32), "Gb": (TH, f32), "Ab": (TH, f32), "Bb": (TH, f32), "X1": (TH, bf), "X2": (TH, bf),
-    "Cg0": (TH, bf), "Cg1": (TH, bf), "Cg2": (TH, bf), "sq": (512, bf), "hi": (TH, bf),
+    "Cg0": (TH, bf), "Cg1": (TH, bf), "Cg2": (TH, bf), "hi": (TH, bf),
     "T3": (256, f32), "H3": (768, f16), "off": (192, u16), "cab": (192, bf), "P1": (64, f16), "cB": (64, f16),
-    "e01": (64, bf), "nok": (64, bf), "pk": (64, bf), "w": (64, f32), "xoff": (64, u16), "Qn": (64, f16),
-    "XH": (64, f32), "own0": (288, f32), "own1": (288, f32), "eq0": (2048, bf), "eq1": (2048, bf),
-    "nd": (288, bf), "wl": (64, f32), "soff": (64, u16), "Hk": (TH, f16), "Hn": (TH, f16),
+    "e0": (64, bf), "e01": (64, bf), "nok": (64, bf), "pk": (64, bf), "w": (64, f32), "xoff": (64, u16), "Qn": (64, f16),
+    "XH": (64, f32), "own0": (288, f32), "own1": (288, f32), "eq0": (2048, bf), "eq1": (2048, bf), "eq2": (1024, bf),
+    "nd": (432, bf), "wl": (64, f32), "soff": (64, u16), "Hk": (TH, f16), "Hn": (TH, f16),
     "oz": (TH, bf), "okk": (512, f32), "ox": (256, bf), "oc": (512, f32),
     "pi": (48, i32), "pj": (48, i32), "pc": (192, f32), "n256": (256, bf), "io": (480, bf), "JX": (64, f32),
     "SP": (64, f32),
     "Sel": (64, f32), "Mq": (128, f32), "Mh": (128, f32),
     "Rb": (32, f32), "Rh": (64, bf), "IF": (128, f32),
     "crow": (128, bf), "one": (512, bf), "PI": (RO * 128, bf), "WB": (256, bf), "MK": (768, bf),
-    "SQ": (RO * 64, bf), "Y": (288, bf), "Id": (9 * 128, bf), "II": (256, bf), "PK": (128, bf), "Zb": (160, bf), "Z": (16 * 160, bf),
+    "SQ": (RO * 64, bf), "Y": (288, bf), "Id": (10 * 128, bf), "II": (256, bf), "PK": (128, bf), "Zb": (160, bf), "Z": (16 * 160, bf),
     "L": (16 * 128, bf), "SH": (16 * 128, bf), "E": (8 * 128, bf), "HX": (136, bf), "HR": (10 * 128, bf),
 }
 for _t in range(RO):
     SB["s%d" % _t] = (TH, bf)
     for _h in range(2):
         SB["z%d%d" % (_t, _h)] = (TH // 2, bf)
+        SB["q%d%d" % (_t, _h)] = (TH // 4, bf)
+    if _t: SB["u%d" % _t] = (TH // 2, bf)
 SCRATCH = {n: ("sbuf", [128, c], d) for n, (c, d) in SB.items()}
 for _b in range(8):
     SCRATCH["p%d" % _b] = ("psum", [128, 512], f32)
@@ -56,9 +80,10 @@ for _h in range(2):
     DIMS["p%d" % _h] = [512 // RUN[_h], RUN[_h]]
     DIMS["p%d" % BK["win"][_h]] = [32 // RUN[_h], RUN[_h], 16]
     DIMS["own%d" % _h] = [32 // RUN[_h], RUN[_h], 8]
+DIMS["p6"] = [64, 8]
 for _n in DIMS:
     SCRATCH[_n] = (SCRATCH[_n][0], [128] + DIMS[_n], f32)
-SEMAPHORES = ["eV", "eS", "eP", "eG", "sent"] + ["arr%d%d" % (t, h) for t in range(1, RO) for h in range(2)] + ["d%d" % k for k in range(56)]
+SEMAPHORES = ["eV", "eS", "eP", "eG", "sent"] + ["%s%d%d" % (x, t, h) for x in "zq" for t in range(1, RO) for h in range(2)] + ["d%d" % k for k in range(56)]
 DBG = []
 RAW = set()
 LAND = {}
@@ -126,13 +151,14 @@ def free(ops, m, n):
     return ops[m][0] == ops[n][0] and (ops[m][0] == "P" and ops[n][4] is None or ops[m][4] == ops[n][4] == "dma")
 
 
-def sequence(text):
+def sequence(text, last=False):
     words, used = [], {}
     for w in text.split():
         dt, w = -(w[0] == "<"), w.lstrip("<")
         if ":" in w: words += [(w.split(":")[0], int(k), dt) for k in w.split(":")[1].split(",")]
         else: words += [(w.split("*")[0], None, dt)] * int((w + "*1").split("*")[1])
     for want in (0, -1):
+        if last: used = {}
         for i, (step, k, dt) in enumerate(words):
             if k is None and dt == want:
                 words[i] = (step, used.get(step, 0), dt)
@@ -153,7 +179,7 @@ def plan(ops, deps):
     for e in ORDER:
         last = None
         for t in range(RO):
-            for step, k, dt in sequence((FIRST if t == 0 else LAST if t == RO - 1 else ORDER)[e]):
+            for step, k, dt in sequence((FIRST if t == 0 else LAST if t == RO - 1 else ORDER)[e], t == RO - 1):
                 here = calls.get((e, (t + dt, step)), [])
                 if t or step not in FREE:
                     if last is not None: before[here[k]].append((last, 0.0))
@@ -172,16 +198,18 @@ def plan(ops, deps):
         for m, x in before[n]: way[m] = max(way[m], cost[m] + x + way[n])
     kind, seen, one, many = [], {}, {}, {}
     for n, o in enumerate(ops):
-        k, t = (o[7] and o[7][1], o[0], o[3][0][0] if o[3] and o[3][0][0][0] not in "sz" else ""), o[7] and o[7][0]
+        k, t = (o[7] and o[7][1], o[0], o[3][0][0] if o[3] and o[3][0][0][0] not in "szqu" else ""), o[7] and o[7][0]
         seen[k, t] = seen.get((k, t), 0) + 1
         kind.append(k + (seen[k, t],))
         one.setdefault(kind[n], []).append(n)
         many.setdefault(k, []).append(n)
 
     way = [way[n] + LEAD.get(kind[n][0], 0.0) for n in range(N)]
-    tails = [n for n in range(N) if not after[n]]
+    view = [n for n in range(N) if not ops[n][7] or ops[n][7][0] == 0 or ops[n][7][0] == 1 and ops[n][7][1] in EARLY]
+    loose = [n for n in view if not ops[n][7] or ops[n][7][1] in FREE + ["table", "soon"] and ops[n][7][0] == 0]
+    tails = [n for n in view if ops[n][7] and ops[n][7][0] == 1]
 
-    def lay(key, moved=None, up=True):
+    def lay(key, moved=None, up=True, view=view):
         for n in topo[::-1] if moved is None else ():
             for m, x in before[n]:
                 if key[m] <= key[n]: key[m] = key[n] + 1.0
@@ -192,7 +220,7 @@ def plan(ops, deps):
                 key[m] = key[n] + (1.0 if up else -1.0)
                 todo.append(m)
         end, taken = [0.0] * N, {e: ([], []) for e in eng}
-        for n in sorted(range(N), key=lambda n: key[n], reverse=True):
+        for n in sorted(view, key=lambda n: key[n], reverse=True):
             t, c, (s, f) = 0.0, cost[n], taken[eng[n]]
             for m, x in before[n]:
                 x += end[m]
@@ -209,14 +237,14 @@ def plan(ops, deps):
             s.insert(lo, t)
             f.insert(lo, t + c)
             end[n] = t + c
-        return max(end[n] + lag[n] for n in tails), end, key
+        return max(end[n] + lag[n] for n in tails) + sum(end[n] for n in LAND) / len(LAND) / 5, end, key
 
     def bound(end, before=before):
         last, prev, out = {}, {}, []
-        for n in sorted(range(N), key=lambda n: end[n]):
+        for n in sorted(view, key=lambda n: end[n]):
             prev[n] = last.get(eng[n])
             last[eng[n]] = n
-        n = max(range(N), key=lambda n: end[n] + lag[n])
+        n = max(tails, key=lambda n: end[n] + lag[n])
         while n is not None:
             t, m = max([(end[k] + x, k) for k, x in before[n]] + [(-1.0, None)], key=lambda p: p[0])
             if prev[n] is not None and end[prev[n]] > t + 1:
@@ -249,13 +277,13 @@ def plan(ops, deps):
             if y[0] < best[0]: best = y
 
     def shift(now, pairs):
-        key = [cost[n] - now[1][n] - 1e-6 * n for n in range(N)]
+        key = [cost[n] - now[1][n] - 1e-6 * n if now[1][n] else -1e9 - n for n in range(N)]
         m, n = pairs[pick(len(pairs))]
         how = pick(4)
         if how == 0: n, x = m, -(cost[n] + 10, 300, 600, 1200)[pick(4)]
         elif how == 1: x = (cost[m] + 10, 300, 600, 1200)[pick(4)]
-        else: n, x = pick(N), (-1500, -800, -400, -200, 200, 400, 800, 1500)[pick(8)]
-        group = one[kind[n]] if pick(2) else many[kind[n][:3]]
+        else: n, x = loose[pick(len(loose))], (-3000, -1500, -800, -400, -200, 200, 400, 800, 1500, 3000)[pick(10)]
+        group = [k for k in (one[kind[n]] if pick(2) else many[kind[n][:3]]) if now[1][k] and ops[k][7] == ops[n][7]]
         for k in group: key[k] += x
         return lay(key, group, x > 0)
 
@@ -276,7 +304,7 @@ def plan(ops, deps):
                       [[(m, x and x + lag[m] * (fr - 1.0) * (ops[m][4] == "call") + NOM["wake"] * (wake - 1.0)) for m, x in before[n]] for n in range(N)]))
 
     def judge(y):
-        order, ends = sorted(range(N), key=lambda n: (y[1][n] - cost[n], n)), [y[1]]
+        order, ends = sorted(view, key=lambda n: (y[1][n] - cost[n], n)), [y[1]]
         for c, b in other:
             end, busy = [0.0] * N, {e: 0.0 for e in eng}
             for n in order:
@@ -286,7 +314,7 @@ def plan(ops, deps):
                     if x > t: t = x
                 end[n] = busy[eng[n]] = t + c[n]
             ends.append(end)
-        return [max(e[n] + lag[n] for n in tails) for e in ends], ends
+        return [y[0]] + [max(e[n] + lag[n] for n in tails) for e in ends[1:]], ends
 
     bounds = lambda ends: [p for e, b in zip(ends, [before] + [b for c, b in other]) for p in bound(e, b)]
     now = best
@@ -301,6 +329,8 @@ def plan(ops, deps):
         if got <= mark + 0.002 * (1 - it / OPT["polish"]) * pick(1000) / 1000:
             now, mark, pairs = y, got, bounds(ends)
             if got < top: best, top = y, got
+    best = lay([cost[n] - best[1][n] if best[1][n] else way[n] - 1e6 for n in range(N)], view=range(N))
+    best = (max(best[1][n] + lag[n] for n in range(N)),) + best[1:]
     DBG[:] = [ops, before, best]
     return sorted(range(N), key=lambda n: (best[1][n] - cost[n], n))
 
@@ -336,8 +366,10 @@ def emit(g, T, ops):
         if kind == "dma":
             s = "d%d" % nd[0]
             nd[0] += 1
-            fn().then_inc(T.sem[s], 16)
-            sig[n] = (s, 16)
+            made = fn()
+            made = made if isinstance(made, list) else [made]
+            for x in made: x.then_inc(T.sem[s], 16)
+            sig[n] = (s, 16 * len(made))
         elif kind == "call":
             fn()
         elif kind:
@@ -453,8 +485,8 @@ def rank_program(g, core, T, topo):
     iota(ioD, [[0, 8], [1, 4], [0, 4]], 0)
     iota(v("pi", 16, 32), [[-1, 16]], 16, 1)
     iota(v("pi", 32, 40), [[1, 8]], 1, 1)
-    for h in range(2): iota(W("SP", h), [[0, 32 // RUN[h]], [16, RUN[h]]], D // 2, 1)
-    for h in range(2): iota(W("JX", h), [[16, 32]], KW - D // 2 + 512 * h, 1)
+    iota(v("SP"), [[0, 8], [16, 8]], D, 1)
+    for h in range(2): iota(W("JX", h), [[16, 32]], KW - D // 2 * (not OPT["u16"]) + 512 * h, 1)
     bits = [(0, 127), (0, 15), (4, 7), (0, 3), (2, 31), (3, 7), (0, 1), (1, 3), (0, 7), (0, 7)]
     cP, cA, cG, cM3, cP2, cGQ, cDUP, cMQ, c7 = range(9)
     for c, (sh, mk) in enumerate(bits): ts(v("pj", c, c + 1), v("pi", 0, 1), sh, A.arith_shift_right, mk, A.bitwise_and)
@@ -483,6 +515,7 @@ def rank_program(g, core, T, topo):
     ts(col(20), col(18), -BIG, A.mult, BIG, A.add)
     ts(col(23), col(15), 4.0, A.mult, col(cMQ), A.add)
     ts(pcs(56, 7), num(0, 7), col(23), A.is_equal)
+    for c in (58, 62): ts(col(c), col(c), BIG, A.mult)
     ts(blk("WB", 0, 128), ioC, col(16), A.mult, col(17), A.add)
     ts(blk("WB", 1, 128), ioB, col(cGQ), A.is_equal)
     tt(blk("WB", 0, 128), blk("WB", 0, 128), blk("WB", 1, 128), A.mult)
@@ -493,12 +526,13 @@ def rank_program(g, core, T, topo):
     ts(v("Rb"), num(0, 32), col(cP2), A.is_equal)
     ts(blk("Rh", 0, 32), num(0, 32), col(cP2), A.is_equal, -float(D), A.mult)
     ts(blk("Rh", 1, 32), num(0, 32), col(cP2), A.is_equal)
-    ms(v("one", p1=32), 1.0)
+    ms(v("one", p1=64), 1.0)
     ts(pcs(80, 3), num(0, 3), col(cP), A.is_equal)
     ts(col(83), col(80), PB, A.mult)
     ts(col(84), col(81), -float(D // 2), A.mult, col(83), A.add)
     ts(col(85), col(82), 0.5, A.mult, col(84), A.add)
     ts(v("crow"), num(0, 128), 0.0, A.mult, col(85), A.add)
+    ms(v("crow", p0=32, p1=64), float(D // 2))
     ts(col(22), col(cP), 16.0, A.add)
     stage("soon", 0)
     ts(v("Zb"), num(0, 160), col(22), A.is_equal)
@@ -506,8 +540,8 @@ def rank_program(g, core, T, topo):
     for a in range(16): act(blk("Z", a, 160), v("Zb"), scale=col(64 + a))
     ts(col(86), col(21), 16.0, A.add)
     ts(col(88), col(64), -1.0, A.mult, 1.0, A.add)
-    ts(col(89), col(64), 16.0, A.mult)
-    ts(col(91), col(64), 1.0 / 32, A.mult)
+    ts(col(89), col(64), 16384.0, A.mult)
+    ts(col(91), col(64), 32.0, A.mult)
     ts(col(92), col(65), 159.0, A.mult, -128.0, A.add)
     ts(col(95), col(64), 128.0, A.mult, col(92), A.add)
     ts(col(90), col(95), -1.0, A.mult)
@@ -515,7 +549,7 @@ def rank_program(g, core, T, topo):
     ts(col(93), col(64), col(cP), A.add)
     ts(col(94), col(64), 15.0, A.mult, 1.0, A.add)
     ts(Id(0), num(0, 128), col(cP), A.is_equal)
-    for k, wt in enumerate((-1.0 / D, 16.0, 2048.0 / BIG, -512.0 / D, -8192.0)): act(Id(k + 1), Id(0), scale=wt)
+    for k, wt in enumerate((-0.25, 16.0, 16.0, -128.0, -8192.0)): act(Id(k + 1), Id(0), scale=wt)
     act(Id(6), Id(0), scale=col(64))
     ts(Id(7), ioB, col(cG), A.is_equal)
     ts(blk("Y", 0, 144), num(0, 144), col(86), A.is_equal, col(91), A.mult)
@@ -523,7 +557,13 @@ def rank_program(g, core, T, topo):
     for k in range(2): act(blk("II", k, 128), Id(0), scale=col(88))
     ts(v("PK"), num(0, 128), col(93), A.is_equal, col(94), A.mult)
     for a in range(16): act(blk("L", a, 128), Id(7), scale=col(64 + a))
-    act(Id(8), blk("L", 0, 128), scale=128.0)
+    ts(col(132), col(65), col(66), A.add, 1024.0, A.mult)
+    ts(col(133), col(64), 32.0, A.mult, col(132), A.add)
+    ts(col(134), col(65), -BIG / 1024, A.mult)
+    ts(col(135), col(66), -1.5 * D / 1024, A.mult, col(134), A.add)
+    ts(col(136), col(64), 128.0, A.mult, col(135), A.add)
+    act(Id(8), Id(7), scale=col(136))
+    act(Id(9), Id(0), scale=8192.0)
     ts(v("SP"), v("SP"), col(21), A.subtract)
     ts(v("JX"), v("JX"), col(21), A.subtract)
     ts(pcs(170, 8), num(128, 136), 16.0, A.mult, col(cA), A.add)
@@ -558,25 +598,27 @@ def rank_program(g, core, T, topo):
     act(v("IF"), Id(0))
 
     def front(t, h):
-        src = z(t, h) if t else v("z3", 512 * h, 512 * h + 512, p1=24)
-        for q in range(2): mm(ps(7, 256 * h, 256 * h + 256, 1, 64 * q, 64 * q + 64), v("SQ", 64 * t, 64 * t + 64, p1=src[5]), part(src, q, 2), True, True)
-        act(blk("sq", h, 256), ps(7, 256 * h, 256 * h + 256), F.Square, bias=col(169 if t else cDUP))
+        src = R("s%d" % (t - 1), h) if t else v("z3", 512 * h, 512 * h + 512, p1=24)
+        b = BK["front"][h] if t else 7
+        for q in range(2): mm(ps(b, 256 * h, 256 * h + 256, 1, 64 * q, 64 * q + 64), v("SQ", 64 * t, 64 * t + 64, p1=src[5]), part(src, q, 2), True, True)
+        act(blk("u%d" % t, h, 256) if t else v("q0%d" % h), ps(b, 256 * h, 256 * h + 256), F.Square, bias=col(169 if t else cDUP))
 
-    def mask(m, h, bank):
-        for q in range(2): mm(part(ps(bank), q, 2), blk("MK", 2 * m + q, 128), blk("sq", h, 256), True, True)
+    def mask(t, m, h, bank):
+        for q in range(2): mm(part(ps(bank), q, 2), blk("MK", 2 * m + q, 128), v("q%d%d" % (t, h)), True, True)
         for q in range(2):
-            if m < 2: act(part(ps(bank) if m == 0 else R("X1", h), q, 2), part(ps(bank), q, 2), F.Relu, bias=col(19))
-            else: act(part(R("X2", h), q, 2), part(ps(bank), q, 2), F.Relu, bias=col(20), scale=BIG)
+            out, b = part(R("X%d" % m, h) if m else ps(bank), q, 2), col(20 if m == 2 else 19)
+            if OPT["mk"][4 * m + 2 * h + q] == "S" or not now[1]: act(out, part(ps(bank), q, 2), F.Relu, bias=b)
+            else: ts(out, part(ps(bank), q, 2), b, A.add, 0.0, A.max)
 
     def masks(t):
         for h in (1, 0):
             if t: stage("mask0%d" % h)
-            front(t, h)
-            mask(0, h, 2 + h)
+            else: front(t, h)
+            mask(t, 0, h, 2 + h)
         for m in (1, 2):
             for h in (1, 0):
                 if t: stage("mask%d%d" % (m, h))
-                mask(m, h, BK["mask"][h])
+                mask(t, m, h, BK["mask"][h])
 
     def tables():
         stage("table", 0)
@@ -588,20 +630,25 @@ def rank_program(g, core, T, topo):
         for k in range(2): dma("Y", v("d%d" % k), T.xreg[k:128:16, :])
         for h in (1, 0): dma("Y", z(0, h), T.zin[:, 512 * h:512 * h + 512])
         dma("Y", v("XW", 0, D, 1, 0, 1), v("r0"), 0)
+        stage("soon")
         for k in range(8):
             dma("G", v("XW", 0, D, 1, 16 * k + 2, 16 * k + 16), T.xreg[16 * k + 2:16 * k + 16, :],
                 after=[v(x) for x in ("pi", "n256", "io", "SP", "JX", "r0")])
-        mm(ps(4, 0, 256), Id(2), v("d0"), True, False)
-        mm(ps(4, 0, 256), Id(0), v("d1"), False, True)
-        act(v("r1"), ps(4, 0, 256), bias=32.0)
+        mm(ps(6, 0, 256), Id(2), v("d0"), True, False)
+        mm(ps(6, 0, 256), Id(0), v("d1"), False, True)
+        act(v("r1"), ps(6, 0, 256), bias=32.0)
         dma("Y", v("XW", 0, D, 1, 1, 2), v("r1"), 1)
 
     Gs = ["Ga", "Gb", "Ga", "Ab"]
 
     def gather(m, h):
-        if m == 3 and h == 0:
+        if m == 3 and h == 0 and OPT["old0"] == "S":
             act(R("Gb", h), at(v("K", 0, D), W("off", h, 2)))
             stage("clear")
+            if OPT["pclear"]:
+                mm(ps(3), Id(0), R("X2", h), True, True)
+                for i in (3, 2, 1, 0): tt(part(R("Ab", h), i, 4), part(R("Gb", h), i, 4), part(ps(3), i, 4), A.subtract)
+                return
             for i in (3, 2, 1, 0): tt(part(R("Ab", h), i, 4), part(R("Gb", h), i, 4), part(R("X2", h), i, 4), A.subtract)
             return
         for i in range(4 if m == 0 else 2):
@@ -619,58 +666,73 @@ def rank_program(g, core, T, topo):
         mm(o, T3, v("Rb"), True, False, True)
         mm(o, H3, blk("Rh", 0, 32), False, True, True)
         ts(W("off", h, m), o, D // 2 - 0.5, A.add)
-        if m: ts(W(("P1", "Qn")[m - 1], h), o, -0.5, A.add)
+        if m: copy(OPT["sq"][2 * m + h - 2], W(("P1", "Qn")[m - 1], h), o, -0.5)
         stage("cab%d%d" % (m, h))
-        o = ps(BK["cab"][h], 0, 32)
-        mm(o, H3, blk("Rh", 1, 32), True, m < 2)
-        if m == 2: mm(o, Id(0), W("e01", h), False, True)
-        act(W("cab", h, m), o, F.Abs, bias=-(HB - 1.0) * D, scale=float(D))
-        if m == 2: tt(W("XH", h), W("Qn", h), W("cab", h, m), A.add)
+        if m == 2 and h:
+            mm(ps(4, 32, 64), H3, blk("Rh", 1, 32), False, True)
+            act(W("cab", h, m), ps(4, 32, 64), F.Abs, bias=-(HB - 1.0 + GOOD) * D, scale=float(D))
+            if OPT["sq"][4] == "V": ts(W("e01", 0), ps(4, 0, 32), GOOD, A.not_equal, 1024.0, A.mult)
+            else: act(W("e01", 0), ps(4, 0, 32), F.Abs, bias=-GOOD)
+        else:
+            o = ps(BK["cab"][h], 0, 32) if m < 2 else ps(h, 128, 160)
+            mm(o, H3, blk("Rh", 1, 32), True, m < 2)
+            if m == 2: mm(o, Id(0), W("e01", h), False, True)
+            act(W("cab", h, m), o, F.Abs, bias=-(HB - 1.0) * D, scale=float(D))
+        if m == 2 and OPT["own"][h] == "S": tt(W("XH", h), W("Qn", h), W("cab", h, m), A.add)
         stage("count%d%d" % (m, h))
         win, b = (v("XW", 0, D), 32.0) if t else (v("CT"), 0.0)
         if m == 2 and h == 0 and OPT["vcount"]:
             ts(part(R("Cg2", h), 0, 2), at(win, part(W("off", h, m), 0, 2)), b, A.add)
             act(part(R("Cg2", h), 1, 2), at(win, part(W("off", h, m), 1, 2)), bias=b)
+        elif m == 1: act(R("Cg1", h), at(win, W("off", h, m)), bias=col(133 if t else 132), scale=col(64))
         else: act(R("Cg%d" % m, h), at(win, W("off", h, m)), bias=b)
 
     def check(m, h=None):
         c0, c1 = (0, 64) if h is None else (32 * h, 32 * h + 32)
         o = ps(4, c0, c1) if m < 2 else ps(BK["nok"][h or 0], 320 + c0, 320 + c1)
         for a in range(16): mm(o, v("Y", 144 * (m % 2) + 16 - a, 144 * (m % 2) + 144 - a), v("Cg%d" % m, 16 * c0 + a, 16 * c1, 16), a == 0 and m != 1, False)
-        mm(o, Id(4 if m == 1 else 1), v("cab", 64 * m + c0, 64 * m + c1), False, m > 0, True)
-        if m == 1: ts(v("e01"), o, 513.0, A.not_equal, 1024.0, A.mult)
-        if m == 2: ts(v("nok", c0, c1), o, 1.0, A.not_equal, 4 * BIG, A.mult)
+        mm(o, Id(4 if m == 1 else 1), v("cab", 64 * m + c0, 64 * m + c1), False, m == 2, True)
+        if m == 2: ts(v("nok", c0, c1), o, 1024.0, A.not_equal, 2.0 ** 44, A.mult)
 
-    def moved(t, h, stop): mm(ps(2 + h), v("II", 128 - 16 * t, 256 - 16 * t) if t else v("PK"), z(t, h), True, stop)
+    def moved(t, h, stop): mm(ps(2), v("II", 128 - 16 * t, 256 - 16 * t) if t else v("PK"), z(t, h), True, stop)
 
     def leave(t, h=None):
         c0, c1 = (0, 64) if h is None else (32 * h, 32 * h + 32)
-        stage("xoff%s" % h)
+        stage("xoff" if h is None else "xoff%d" % h)
         o = ps(BK["nok"][h or 0], 384 + c0, 384 + c1)
         mm(o, Id(0), v("Qn", c0, c1), True, False)
-        mm(o, Id(3), v("nok", c0, c1), False, True)
-        tt(v("w", c0, c1), o, v("JX", c0, c1), A.min)
-        ts(v("xoff", c0, c1), v("w", c0, c1), float(D // 2), A.add)
-        for x in (1, 0) if h is None else (h,):
-            stage("leave%d" % x)
-            send(t, x)
+        if OPT["u16"]:
+            mm(o, v("crow", p0=32, p1=33), v("one", 0, c1 - c0, p0=32, p1=33), False, False)
+            mm(o, Id(3), v("nok", c0, c1), False, True)
+            tt(v("xoff", c0, c1), o, v("JX", c0, c1), A.min)
+        else:
+            mm(o, Id(3), v("nok", c0, c1), False, True)
+            tt(v("w", c0, c1), o, v("JX", c0, c1), A.min)
+            ts(v("xoff", c0, c1), v("w", c0, c1), float(D // 2), A.add)
 
     def send(t, h):
         so = R("s%d" % t, h)
         act(so, at(v("XW"), W("xoff", h)), bias=col(90))
         if t < RO - 1:
-            sem, to = "arr%d%d" % (t + 1, h), z(t + 1, h)
-            add("G", lambda: g.remote_dma(ap(to), ap(so), T.sem[sem], T.sem.sent, pid, rid, topo.mask(core, nxt)), None, [so], "call", 600.0,
-                NOM["hop"] - 600 + (NOM["once"] if t == 0 else 0))
-            add("X", None, to, [], ("arrival", sem, n_in), 1.0)
+            stage("front%d" % h)
+            front(t + 1, h)
+            write(t, v("q%d%d" % (t + 1, h)), blk("u%d" % (t + 1), h, 256), NOM["less"])
+            stage("leave%d" % h)
+            write(t, z(t + 1, h), so, -NOM["less"] * (2 - h))
+
+    def write(t, to, so, less):
+        add("G", lambda: g.remote_dma(ap(to), ap(so), T.sem[to[0]], T.sem.sent, pid, rid, topo.mask(core, nxt)), None, [so], "call", 600.0,
+            NOM["hop"] - 600 - less + (NOM["once"] if t == 0 else 0))
+        add("X", None, to, [], ("arrival", to[0], n_in), 1.0)
 
     def twin(h):
-        own = v("XW", KW + 512 * h, KW + 512 * h + 512)
-        add("Y", lambda: g.sync.dma_start(ap(R("NC", h)), ap(own)), R("NC", h), [own], "dma", 50.0, NOM["dma"] + 128 * 2048 / NOM["rate"])
+        c = KW + 512 * h
+        add("Y", lambda: [g.sync.dma_start(T.NC[p:p + 15, 512 * h:512 * h + 512], T.XW[p:p + 15, c:c + 512]) for p in range(1, 128, 16)],
+            v("NC", 512 * h, 512 * h + 512, p0=1), [v("XW", c, c + 512)], "dma", 400.0, NOM["dma"] + 120 * 2048 / NOM["rate"])
 
     def column(t, h):
         if OPT["dmacol"]:
-            add("G", lambda: g.dma_start(T.NC[0:128:16, 512 * h:512 * h + 512], T.Cg2[0:128:16, 512 * h:512 * h + 512]), R("NC", h), [R("Cg2", h)],
+            add("G", lambda: g.dma_start(T.NC[0:128:16, 512 * h:512 * h + 512], T.Cg2[0:128:16, 512 * h:512 * h + 512]), v("NC", 512 * h, 512 * h + 512, p1=1), [R("Cg2", h)],
                 "dma", NOM["gdma"], NOM["glag"])
             return
         moved(t, h, False)
@@ -684,7 +746,9 @@ def rank_program(g, core, T, topo):
         sizes = [(c - d) * nr for d in range(1, c)]
         npair = sum(sizes)
         SH = lambda s: blk("SH", s % 16, 128)
-        for k in range(8): act(v("own%d" % h, k, 256, 8), W("XH", h))
+        for k in range(8):
+            if OPT["own"][h] == "S": act(v("own%d" % h, k, 256, 8), W("XH", h))
+            else: tt(v("own%d" % h, k, 256, 8), W("Qn", h), W("cab", h, 2), A.add)
         bank = BK["win"][h]
         own = lambda i0, i1: box("own%d" % h, range(nr), range(i0, i1), range(8))
         far = lambda i0, i1, k0, k1: box("p%d" % bank, range(nr), range(i0, i1), range(k0, k1))
@@ -693,27 +757,83 @@ def rank_program(g, core, T, topo):
             mm(ps(bank, k, 512, 16), SH(k), W("cab", h, 2), False, True)
         tt(v(eq, 0, 256), far(0, c, 1, 9), own(0, c), A.is_equal)
         for k in range(8): mm(ps(h, npair, npair + 32), blk("E", k, 128), v(eq, k, 256, 8), k == 0, k == 7)
-        for r in range(2):
-            e0 = 256 + 8 * npair * r
-            for d in range(1, c):
+        late = OPT["late"][h]
+        for r in (1, 0):
+            e0, d0 = 256 + 8 * npair * r, 1 if r else late + 1
+            for d in range(d0, c):
                 x, a = sizes[d - 1], e0 + 8 * sum(sizes[:d - 1])
                 if r: tt(v(eq, a, a + 8 * x), far(d, c, 0, 8), own(0, c - d), A.is_equal)
                 else: tt(v(eq, a, a + 8 * x), far(0, c - d, 1, 9), own(d, c), A.is_equal)
-            for k in range(8): mm(ps(h, 0, npair), SH(-k * r), v(eq, e0 + k, e0 + 8 * npair, 8), r == 0 and k == 0, r == 1 and k == 7)
+            x = sum(sizes[:d0 - 1])
+            for k in range(8): mm(ps(h, x, npair), SH(-k * r), v(eq, e0 + 8 * x + k, e0 + 8 * npair, 8), r and k == 0, not r and k == 7, k == 0)
         stage("lose%d" % h)
         nd = lambda a, b: v("nd", 144 * h + a, 144 * h + b)
         if OPT["nd"][h] == "V": ts(nd(0, npair + 32), ps(h, 0, npair + 32), 8192.0, A.mult)
         else: act(nd(0, npair + 32), ps(h, 0, npair + 32), scale=8192.0)
-        o = ps(h, 352, 384)
+        ob = 6 if late else h
+        o = ps(ob, 352, 384)
+        high = lambda d: box("p%d" % ob, range(352 // c, 384 // c), range(d, c))
+
+        def straight(ds):
+            stage("late%d" % h)
+            for d in ds:
+                x, a = sizes[d - 1], 256 + 8 * sum(sizes[:d - 1])
+                tt(v(eq, a, a + 8 * x), far(0, c - d, 1, 9), own(d, c), A.is_equal)
+                for k in range(8): mm(high(d), Id(9), v(eq, a + k, a + 8 * x, 8), False, d == late and k == 7, k == 0)
+            stage("lose%d" % h)
+
         mm(o, Id(0), W("Qn", h), True, False)
+        if OPT["u16"]: mm(o, v("crow", p0=32, p1=33), v("one", 0, 32, p0=32, p1=33), False, False)
         mm(o, Id(3), W("nok", h), False, False)
-        for d in range(1, c): mm(box("p%d" % h, range(352 // c, 384 // c), range(d, c)), Id(0), nd(sum(sizes[:d - 1]), sum(sizes[:d])), False, False)
-        mm(o, Id(0), nd(npair, npair + 32), False, True)
+        if late: straight(range(1, OPT["cut"]))
+        for d in range(1, c): mm(high(d), Id(0), nd(sum(sizes[:d - 1]), sum(sizes[:d])), False, False, d == 1 and late)
+        mm(o, Id(0), nd(npair, npair + 32), False, not late)
+        if late: straight(range(OPT["cut"], late + 1))
+        stage("soff%d" % h)
+        if OPT["u16"]: return tt(W("soff", h), o, W("SP", h), A.min)
         if OPT["soff"][h] == "c":
             for i in range(c): ts(v("soff", 32 * h + i, 32 * h + 32, c), ps(h, 352 + i, 384, c), col(170 + i), A.min, float(D // 2), A.add)
         else:
             tt(W("wl", h), o, W("SP", h), A.min)
             ts(W("soff", h), W("wl", h), float(D // 2), A.add)
+
+    def winners3(name, h, r0, nr, pair, bank):
+        eq, nb, c0 = "eq" + name, 4 * nr, 32 * h + 4 * r0
+        SH = lambda s: blk("SH", s % 16, 128)
+        stage("win" + name)
+        if r0 + nr == 8:
+            for k in range(8): act(v("own%d" % h, k, 256, 8), W("XH", h))
+            for k in range(9):
+                mm(ps(BK["win"][h], k, 512, 16), SH(k), W("Qn", h), True, False)
+                mm(ps(BK["win"][h], k, 512, 16), SH(k), W("cab", h, 2), False, True)
+        own = lambda r, i: box("own%d" % h, r, i, range(8))
+        far = lambda r, i, k: box("p%d" % BK["win"][h], r, i, range(k, k + 8))
+        rs = range(r0, r0 + nr)
+        sets = [(rs, range(4 - d), rs, range(d, 4)) for d in range(1, 4)]
+        if pair: sets += [(rs[::2], range(max(-d, 0), 4 - max(d, 0)), rs[1::2], range(max(d, 0), 4 + min(d, 0))) for d in range(-3, 4)]
+        at0 = [sum(len(x[0]) * len(x[1]) for x in sets[:n]) for n in range(len(sets) + 1)]
+        npair = at0[-1]
+        tt(v(eq, 0, 8 * nb), far(rs, range(4), 1), own(rs, range(4)), A.is_equal)
+        for k in range(8): mm(ps(bank, npair, npair + nb), blk("E", k, 128), v(eq, k, 8 * nb, 8), k == 0, k == 7)
+        for r in range(2):
+            e0 = 8 * (nb + npair * r)
+            for n, (rl, il, rh, ih) in enumerate(sets):
+                tt(v(eq, e0 + 8 * at0[n], e0 + 8 * at0[n + 1]), far(rh, ih, 0) if r else far(rl, il, 1), own(rl, il) if r else own(rh, ih), A.is_equal)
+            for k in range(8): mm(ps(bank, 0, npair), SH(-k * r), v(eq, e0 + k, e0 + 8 * npair, 8), r == 0 and k == 0, r == 1 and k == 7)
+        stage("lose" + name)
+        nd = lambda a, b: v("nd", 144 * int(name) + a, 144 * int(name) + b)
+        ts(nd(0, npair + nb), ps(bank, 0, npair + nb), 8192.0, A.mult)
+        o = ps(bank, 352, 352 + nb)
+        mm(o, Id(0), v("Qn", c0, c0 + nb), True, False)
+        mm(o, Id(3), v("nok", c0, c0 + nb), False, False)
+        for n, (rl, il, rh, ih) in enumerate(sets):
+            mm(box("p%d" % bank, range(88 + rh.start - r0, 88 + rh.stop - r0, rh.step), ih), Id(0), nd(at0[n], at0[n + 1]), False, False)
+        mm(o, Id(0), nd(npair, npair + nb), False, True)
+        if name in OPT["soff"]:
+            for i in range(4): ts(v("soff", c0 + i, c0 + nb, 4), ps(bank, 352 + i, 352 + nb, 4), col(170 + i), A.min, float(D // 2), A.add)
+        else:
+            tt(v("wl", c0, c0 + nb), o, v("SP", c0, c0 + nb), A.min)
+            ts(v("soff", c0, c0 + nb), v("wl", c0, c0 + nb), float(D // 2), A.add)
 
     def copy(e, out, a, b):
         if e == "S": act(out, a, bias=b)
@@ -730,10 +850,12 @@ def rank_program(g, core, T, topo):
                 for e in range(2): copy(OPT["bcopy"][2 * x + e], R("Bb", x, e, 2), part(ps(2 + e), x, 2), -BIG - D // 2)
             return
         b = BK["back"][h]
-        mm(ps(b), Id(0), R("X2", h), True, False)
-        for a in range(16): mm(ps(b, a, 512, 16), blk("L", a, 128), W("P1", h), False, False)
+        if not h: mm(ps(b), Id(0), R("X2", h), True, False)
+        for a in range(16): mm(ps(b, a, 512, 16), blk("L", a, 128), W("P1", h), h and a == 0, False)
         mm(ps(b), Id(8), R("Cg1", h), False, True, True)
-        for e in range(2): copy(OPT["bcopy"][2 * h + e], part(R("Bb", h), e, 2), part(ps(b), e, 2), -BIG - 1.5 * D)
+        for e in range(2):
+            if h: tt(part(R("Bb", h), e, 2), part(ps(b), e, 2), part(R("X2", h), e, 2), A.add)
+            else: act(part(R("Bb", h), e, 2), part(ps(b), e, 2))
 
     def new_key(t):
         tt(v("pk"), v("nok"), blk("cab", 2, 64), A.subtract)
@@ -758,11 +880,11 @@ def rank_program(g, core, T, topo):
                 turn(t, m, h)
             stage("check%d" % m)
             if m < 2 or not OPT["split"]: check(m)
-            stage("moved")
             for h in (1, 0) if m == 0 else ():
+                stage("moved%d" % h)
                 moved(t, h, True)
-                act(v("XW", KW + 512 * h, KW + 512 * h + 512), ps(2 + h), bias=col(95 if t else 168))
-                if OPT["dmacol"]: twin(h)
+                for q in range(2): act(part(v("XW", KW + 512 * h, KW + 512 * h + 512), q, 2), part(ps(2), q, 2), bias=col(95 if t else 168))
+                twin(h)
             for h in OPT["back"] if m == 1 else ():
                 stage("back%s" % h)
                 back(h)
@@ -776,18 +898,21 @@ def rank_program(g, core, T, topo):
         if not OPT["split"]: leave(t)
         for h in (1, 0): winners(h)
         for h in (1, 0):
+            stage("leave%d" % h)
+            send(t, h)
+        for h in (1, 0):
             stage("column%d" % h)
             column(t, h)
         stage("row")
         new_key(t)
-        for h in (1, 0):
-            nr = 32 // RUN[h]
-            for r in range(nr - 1, -1, -1):
-                so = part(W("soff", h), r, nr)
-                stage("run%d" % h)
-                tt(at(v("K"), so), part(R("Ab", h), r, nr), part(R("Bb", h), r, nr), A.max)
-                stage("xrun%d" % h)
-                act(at(v("XW", 0, KW), so), part(R("NC", h), r, nr), F.Silu)
+        for name, h, r0, nr, pair, bank in PIECES:
+            c = 4 + 4 * pair
+            for b in range(32 * h + 4 * (r0 + nr) - c, 32 * h + 4 * r0 - 1, -c):
+                so, of = v("soff", b, b + c), lambda x: v(x, 16 * b, 16 * (b + c))
+                stage("run" + name)
+                tt(at(v("K"), so), of("Ab"), of("Bb"), A.max)
+                stage("xrun" + name)
+                act(at(v("XW", 0, KW), so), of("NC"), F.Silu)
         for h in (1, 0):
             stage("min%d" % h)
             for i in range(4): tt(R("K", h, i, 4), R("K", h, i, 4), ps(4 + i % 2, 256 * h + i // 2, 256 * h + 256, 2), A.min)
@@ -828,4 +953,4 @@ def rank_program(g, core, T, topo):
     act(v("ox"), ps(2, 0, 256), bias=col(147))
     dma("Y", T.yx[:], v("ox"))
     emit(g, T, ops)
-    g.wait_ge(T.sem.sent, 2 * n_out * (RO - 1))
+    g.wait_ge(T.sem.sent, 4 * n_out * (RO - 1))

import math
from concourse.mybir import AluOpType as A, ActivationFunctionType as F

D, TH, RO = 4096, 1024, 5
KW = D + 128
BIG = float(1 << 22)
HB = 1600
PB = float(HB * D)
GOOD = 513.0 * 1024
PIECES = (("1", 1, 0, 8, False, 1), ("0", 0, 0, 8, True, 0))
RUN = (8, 4)
NOM = dict(cyc=0.83, pe=0.42, gather=1.5, scatter=3.5, wake=220.0, dma=1800.0, rate=300.0, hop=4500.0, less=700.0, once=2000.0, gdma=1000.0, glag=1500.0)
OPT = dict(npe=3, cap=230, seed=3, turns=800, shifts=6000, polish=1500, heat=100.0, heat2=60.0)
OPT.update(mk="SSSSSSSSSSSS", mv="SSSS", e1=False, tile="SS", u16=True, cut=2, late=(3, 0), own="SV", old0="S", soff="tc", nd="VV", pclear=True, sq="VVVVV", dmacol=True, vcount=False, split=True, back=(1, 0), bcopy="SSSS")
BK = dict(front=(7, 4), two=(5, 7), mask=(6, 6), cab=(5, 7), nok=(7, 6), win=(5, 4), back=(2, 3))
FREE = "hop01 hop00 hop11 hop10 cab01 cab00 cab11 cab10 count01 count00 count11 count10 check0 moved back1 back0".split()
LOOSE = "old1 old0 leave1 leave0 xoff1 xoff0 check21 check20 win1 win0 lose1 lose0 clear row back1 back0 run1 run0 xrun1 xrun0 min1 min0 count20 cab20 column1 column0".split()
ORDER = {
    'V': '<min1:3,1,2 <min0 hop01*4 <min0*2 hop00*4 hop01*2 hop00 hop01 hop00 hop11 hop00 hop11 hop10*2 hop11*2 hop10 hop11 hop10 hop11 hop21:0 hop10 hop21:1 hop10 hop20:0,1 hop21:2,3,5,4 check1 hop20:2,3 old1 cab21 hop20:5,4 old1 win1:0 cab20 win1:3 check21 win1:2,1,4,6 xoff1 win1:5 xoff1 win0:3,1,2,11 check20 lose1:0 win0:13,0 xoff0 win0:14,12,7 xoff0 lose1:1,4,3,2 win0:5,4 run1 win0:8 run1 win0:6,9 run1 win0:10 run1 clear run1 lose0 run1 row run1 lose0 run1 lose0 clear run0 clear run0 clear run0*2 min1:0 min0',
    'S': '<mask10:1,0 <xrun0 <mask21*2 count01 cab00 cab01 <mask20:1 count00 moved <mask20:0 count11 count10 cab11 cab10 moved cab21 count21 win1*8 cab20 count20 win0*8 back1*2 leave1 old0 leave0 back0 xrun1*2 back0 xrun1*6 mask01 xrun0 mask01 xrun0 mask00:0 mask11*2 mask01 mask00:1,2 xrun0',
    'P': 'hop01 <mask11 <mask00*2 hop00 <mask10 hop01*4 hop00*4 hop01*2 <mask21 moved:1 hop00*2 hop11 cab01 <mask20 cab00 moved:0 hop10 hop11*4 hop10*4 hop11*2 check0*2 hop10*2 back1*2 hop21 check0 back1 cab11 hop20 hop21 cab10 hop21*3 check1*2 hop21*2 check1 hop20*4 cab21*2 back1 hop20*2 win1*3 cab20*2 check21*3 win0 win1 xoff1 win0*2 win1 check20*3 win1 back0 xoff0 lose1 back0*2 row:0 back0 win0*5 row:3 lose0*2 row:1,4,2,5 mask01*2',
    'G': 'column1 column0 leave1 leave0'}
ORDER = {'V': '<min0:2 hop01*3 <min0:0 hop01 <min0:3 hop00*4 hop01*2 hop00 hop01 hop00 hop11 hop00 hop11 hop10:1,0 hop11*4 hop10:2,3 hop21:0 hop10:4 hop21:1 hop10:5 hop20:0,1 hop21:2,3 check1 hop21:5,4 hop20:2,3 old1:1 cab21 hop20:5,4 old1:0 win1:0 cab20 check21 win1:3,1,2,5 xoff1 win1:6,4 xoff1 win0:7,1,3,4,11 check20 win0:2 lose1:0 win0:0 xoff0 win0:12,13 xoff0 lose1:1,3,2,4 win0:14,5,6 run1 win0:8 run1 win0:9 run1 win0:10 run1 clear run1 lose0 run1 clear run1 row lose0 run1 lose0 clear run0*2 clear run0*2 min1:0,2,1,3 min0:1', 'S': '<mask21*2 count01 cab01 count00 moved <mask20 cab00 <mask20 count11 count10 cab11 cab10 moved cab21 count21 win1*8 cab20 count20 win0*8 back1:1 leave1 old0 leave0 xrun1 back0:1 xrun1 back1:0 xrun1 back0:0 xrun1*5 mask01 xrun0 mask11 mask01 mask00 mask01 mask11 mask00*2 xrun0 mask10:1,0 xrun0*2', 'P': '<row:5 hop01 <mask00 hop00 <mask10 hop01*4 hop00*4 hop01*2 <mask21 hop00 hop11 hop00 hop10 cab01 moved:1,0 <mask20 hop11*4 cab00 hop10*3 hop11*2 hop10 hop21 check0*3 hop10*2 cab11 back1*3 hop21*4 cab10 check1*3 hop21*2 hop20*5 cab21*2 back1 hop20*2 win1*3 cab20*2 check21*3 win0*2 xoff1 win0 win1*2 check20*3 win1 back0 xoff0 lose1 win0 back0*3 win0*2 row:0 win0*2 row:3 lose0*2 row:1,2 mask01 row:4 mask11 mask01 mask00', 'G': 'column1 column0 leave1 leave0'}
FIRST = {'V': 'hop01*4 hop00:0,1,2,3 hop01*2 hop00:5,4 hop01 hop11 hop00:6 hop11 hop10*2 hop11*4 hop10*2 hop21 hop10 hop21 hop10 hop20*2 hop21*4 check1 hop20*4 old1 cab21 check21 old1 xoff1 cab20 xoff1 win1:0,3,1,6,2 check20 win1:5,4 win0:12,3 xoff0 win0:8,13 xoff0 win0:5 lose1:0 win0:0,10,6,4,7,14 lose1:1,2,4,3 win0:1 run1 win0:2 run1 row win0:11 run1 win0:9 run1 clear run1 lose0 run1 clear run1 lose0 run1 lose0 clear run0 clear run0*3 min1:2,0 min0:1 min1:1,3', 'S': 'count01 count00 cab00 cab01 moved count11 count10 cab11 cab10 moved count21 cab21 count20 cab20 win1*8 back1:1 win0*8 leave1 old0 leave0 xrun1 back1:0 xrun1*5 back0:1 xrun1*2 back0:0 xrun0 mask01 xrun0 mask11:1 mask01 mask00 mask11:0 mask01 mask00*2 mask10:1 xrun0 mask10:0 xrun0', 'P': 'hop01 hop00 hop01*4 hop00*4 hop01*2 hop00 hop10 hop00 cab01 cab00 hop11*5 moved hop10*2 hop11*2 hop10*2 hop21 check0*2 cab11 check0 hop10*2 moved back1*3 hop21*4 hop20 cab10 check1*2 hop21*2 hop20*2 check1 hop20*2 back1 cab21 hop20*2 cab21 check21*3 cab20*2 win1 xoff1 win1*2 win0 check20*3 win0*2 win1 xoff0 win1*2 lose1 back0 win0 row:0 win0 back0 win0 back0 win0*2 row:1 lose0 back0 lose0 row:3,2 mask01 mask11 mask01 mask00 row:4', 'G': 'column1 column0 leave1 leave0'}
LAST = {'V': 'hop01*2 <min0:0 hop01*2 <min0:2,3 hop00*4 hop01*2 hop00 hop01 hop00 hop11:0 hop00 hop11:1 hop10:1,0 hop11:2,3,5,4 hop10:2,3 hop21:0 hop10:4 hop21:1 hop10:5 hop20:1,0 hop21:2,3 check1 hop21:5,4 hop20:2,3 cab21 hop20:5,4 old1*2 win1:0,3 check21 cab20 win1:1,2,6 xoff1 win1:4 xoff1 win1:5 win0:11,2,7,3 check20 win0:13,4 lose1:0 win0:14,0 xoff0 win0:1 xoff0 lose1:2,1,4,3 win0:8 run1 win0:6,9 run1 win0:5,10 run1 win0:12 row run1 clear run1 lose0 run1 clear run1 lose0 run1 lose0 clear run0 clear run0*3 ksum min1:1,0 ksum min1:3,2 ksum min0*2 ksum min0*2 ksum mirror:0 ksum mirror:2,1 ksum mirror:4 ksum mirror:3,5 ksum mirror:6 ksum mirror:7 ksum*2', 'S': '<mask21:1,0 cab01 count01 count00 <mask20:1 cab00 moved <mask20:0 count11 count10 cab11 cab10 moved cab21 count21 win1*8 cab20 count20 win0*8 back1:1 old0 leave1 leave0 xrun1 back0:1 xrun1 back1:0 xrun1 back0:0 xrun1*3 zout:0 xrun1*2 xrun0 zout:1 xrun0 zout:3 xrun0 zout:4 xrun0 zout:2 xsum*6 rows:1 xsum rows:0 xsum*2', 'P': 'hop01 hop00 <row:5 <mask00:1 <mask10 hop01*4 hop00*4 hop01*2 <mask21 hop11 hop00*2 cab01 moved:1 <mask20 hop11*4 hop10 moved:0 cab00 hop10*2 hop11*2 hop10*2 check0*2 hop10*2 back1*2 check0 hop21 cab11 back1 hop20 hop21*3 cab10 hop21 check1*3 hop21*2 hop20*4 cab21*2 back1 hop20*2 win1*3 cab20*2 check21*3 win0*3 xoff1 win1*2 check20*3 win1 xoff0 lose1 row:0 back0*4 zout:0 win0*5 row:3 zout:1,7 lose0*2 zout:2,3,4 row:1,4,2 zout:5,6,8 row:5 zout:9 mirror*4 xsum mirror xsum mirror xsum*4 mirror*2 xsum mirror xsum*2', 'G': 'column1 column0 rows'}
OPT.update(npe=5, bcopy="SSVV", sq="VVVVS")
FREE = "hop01 hop00 hop11 hop10 cab01 cab00 cab11 cab10 count01 count00 count11 count10 check0 moved1 moved0 back1 back0".split()
ORDER = {'V': '<min1*3 hop01 <min0 hop01*3 <min0*3 hop00*4 hop01*2 hop00 hop01 hop00 hop11 hop00 hop11 hop10*2 hop11*2 hop10 hop11 hop10 hop11 hop21 hop10 hop21 hop10 hop20*2 hop21*2 back1*2 hop21*2 win1:4,3,7 hop20*2 win1:2,6,1,0,5,10 hop20*2 win1:11,8 cab20 win1:14,9,12,13 check21 old1*2 lose1 xoff1 win0:0,1 check20 win0:3,7 soff1 win0:4,2 xoff0 run1 win0:5 late0:4 win0:6 run1 late0:5,1 run1 late0:0 run1 late0:2 lose0 run1 late0:3,6 run1 row clear run1 clear*2 run1 soff0 clear run0*4 min1', 'S': '<mask00 <xrun0 <mask10*2 <xrun0 <mask21*2 moved1*2 cab01 count01 count00 cab00 <mask20*2 count11 count10 cab11 moved0*2 cab10 cab21*2 count21 cab20 count20 win0*8 old0 leave1 leave0 front1 xrun1 back0 front0 xrun1 back0 xrun1*6 xrun0*2 mask01*2 mask11*2 mask00', 'P': '<row hop01 hop00 <row*5 <mask01 <mask11 <mask00 <mask10 hop01*4 hop00*4 hop01*2 <mask21 moved1 hop00 hop11 cab01 hop00 moved0 hop10 <mask20 cab00 hop11*4 back1 hop10*4 hop11*2 hop21 check0*3 hop10*2 cab11 back1 hop20 back1*2 hop21*4 cab10 check1*2 hop21*2 check1 cab21 hop20*4 clear win1*3 hop20*2 cab20*2 check21*3 win0*2 win1*2 win0 win1 xoff1*3 check20*3 lose1*2 lose0*2 lose1 back0 xoff0*3 back0*2 lose0 win0 front1 back0 win0 front0 win0 late0*3 lose0 late0*4', 'G': 'column1 column0 front1 front0 leave1 leave0'}
FIRST = {'V': 'hop01*4 hop00*4 hop01*2 hop00*2 hop01 hop11 hop00 hop11 hop10:1,0 hop11*2 hop10:2 hop11 hop10:3 hop11 hop21 hop10:4 hop21 hop10:5 hop20*2 hop21*2 back1*2 hop21*2 hop20*2 win1:2,0,4,7,3,6,1,5 hop20*2 cab20 win1:11,8,10 check21 win1:12,14,13,9 old1 xoff1 check20 old1 lose1 xoff0 clear:1 win0:5,4 late0:0 soff1 win0:2,3 run1 win0:6,0 run1 win0:7,1 run1 late0:2,1 run1 late0:3 lose0 run1 late0:5,6,4 run1 row clear:2 run1 clear:0 soff0 run1 run0 clear:3 run0*3 min1', 'S': 'cab01 count01 cab00 count00 moved1*2 count11 count10 cab11 moved0*2 cab10 cab21*2 count21 cab20 count20 win0*8 old0 leave1 leave0 front1 xrun1 front0 xrun1*4 back0 xrun1*2 back0 xrun1 xrun0*2 mask01*2 mask11*2 mask00', 'P': 'hop00 hop01*5 hop00*4 hop01*2 hop00*2 hop11 cab01 cab00 hop11*4 moved1 hop10*5 hop11*2 moved0 hop21 back1 hop10*2 check0 cab11 check0*2 hop20 back1*2 hop21*4 cab10 back1 check1*2 hop20 hop21*2 hop20 check1 cab21 hop20*2 clear win1 hop20*2 cab20*2 win1*2 check21*3 win0 win1 xoff1*3 check20*3 win1*2 lose0 xoff0*3 win0*2 lose0 lose1*3 front1 back0 lose0 back0 front0 late0 back0 win0*3 back0 late0*2 lose0 late0*4', 'G': 'column1 column0 front1 front0 leave1 leave0'}
LAST = {'V': '<min1:1,2,3 <min0 hop01*4 <min0*3 hop00*4 hop01*2 hop00 hop01 hop00 hop11 hop00 hop11 hop10:1,0 hop11*4 hop10:2,3 hop21 hop10:4 hop21 hop20:1 hop10:5 hop20:0 hop21*2 back1*2 hop21*2 win1:5,4,1 hop20:2,3 win1:2,6,0,3,7,10 hop20:4,5 win1:9,11,8,12 cab20 win1:13,14 check21 old1*2 lose1 xoff1 win0:0,1 check20 win0:3 soff1 xoff0 win0:7,2,4 run1 late0:5,4 win0:5 run1 win0:6 late0:1 run1 late0:0 run1 late0:2 lose0 run1 late0:3 clear run1 row late0:6 run1 clear*2 run1 soff0 clear run0*4 ksum min1:0,1 ksum min0:3 min1:3,2 ksum min0:0,1 ksum min0:2 mirror:0 ksum mirror:2 ksum mirror:4,1 ksum mirror:3,5 ksum mirror:6 ksum*2 mirror:7 ksum*2', 'S': '<mask00:1 <xrun0:2 <mask10*2 <xrun0:3 <mask21*2 cab01 moved1*2 count00 count01 cab00 <mask20*2 count11 count10 cab11 moved0*2 cab10 cab21*2 count21 cab20 count20 win0*8 old0 leave1 leave0 xrun1*2 back0 xrun1*2 back0 xrun1*3 zout:0 xrun1 xrun0 zout:1 xrun0 zout:3 xrun0 zout:4 xrun0 zout:2 xsum*6 rows:1 xsum rows:0 xsum*2', 'P': '<row hop01 <row*5 hop00 <mask01 <mask11 <mask00 <mask10 hop01*4 hop00*4 hop01*2 <mask21 moved1 hop00 hop11 cab01 hop00 hop10 moved0 <mask20 cab00 hop11*4 back1 hop10*3 hop11*2 hop10 hop21 check0*2 hop10*2 hop20 check0 back1 cab11 back1*2 hop21*4 cab10 check1*2 hop21*2 check1 cab21 hop20*4 clear win1*3 hop20*2 cab20*2 check21*3 win0*2 win1*2 xoff1*2 win1 xoff1 win0 check20*3 lose1*3 lose0*2 xoff0*3 back0*4 win0 lose0 win0*2 late0*3 lose0 late0*4 zout:0,1,2,3 row zout:7 row*2 zout:4,5,6,8,9 row*3 mirror*4 xsum mirror xsum*2 mirror xsum mirror xsum*4 mirror*2 xsum', 'G': 'column1 column0 rows'}
ORDER = {'V': 'hop01*4 <min0*4 hop00*4 hop01*2 hop00 hop01 hop00 hop11 hop00 hop11 hop10*2 hop11*2 hop10 hop11 hop10 hop11 hop21 hop10 hop21 hop10 hop20*2 hop21*2 back1*2 hop21*2 win1:2,6,3 hop20*2 win1:0,4,7,1,5,10 hop20*2 win1:9,8,11,14,13 cab20 check21 win1:12 old1*2 lose1 xoff1 win0:0,1 check20 win0:7,3,11 soff1 win0:2,9 xoff0 run1 win0:5,4 run1 win0:6,8,10 run1 late0 run1 late0 run1 late0 lose0 run1 row clear run1 clear*2 run1 soff0 clear run0*4 min1*4', 'S': '<mask10*2 <xrun0 <mask21 cab01 <mask21 count01 count00 cab00 <mask20*2 moved1 count11 count10 cab11 moved1 cab10 cab21*2 count21 moved0*2 cab20 count20 win0*8 old0 leave1 leave0 front1 xrun1 back0 front0 xrun1 back0 xrun1*6 xrun0*2 mask01*2 mask11*2 mask00*2 xrun0', 'P': 'hop01*4 <mask10 hop00*4 hop01*2 hop11 <mask21 hop00 cab01 hop00 hop10 <mask20 hop11*4 cab00 moved1 hop10*4 hop11*2 check0*2 hop10 hop21 hop10 back1 cab11 check0 hop20 back1*2 hop21*4 cab10 check1*2 hop21*2 check1 cab21 hop20*4 moved0 win1*3 hop20*2 cab20*2 check21*3 win0*2 win1*3 win0 xoff1*3 check20*3 lose1*2 lose0*2 lose1 back0 xoff0*3 win0 back0 lose0 front1 back0*2 front0 win0*3 late0 clear lose0 late0*2 row*6 mask01 mask11 mask00', 'G': 'column1 column0 front1 front0 leave1 leave0'}
ORDER['P'] = 'hop01 hop00 ' + ORDER['P']
FIRST = {'V': 'hop01*4 hop00*4 hop01*2 hop00*2 hop01 hop11 hop00 hop11 hop10*2 hop11*2 hop10 hop11 hop10 hop11 hop21 hop10 hop21 hop20 hop10 hop20 back1 hop21*2 back1 hop21*2 hop20*2 win1:7,2,6,1,3,0,5,4 hop20*2 cab20 win1:8,9,14 check21 win1:11,12,10,13 old1 xoff1 check20 old1 lose1 xoff0 clear:1 win0:4,3,2 soff1 win0:6 late0:1 win0:10 run1 win0:0,11 run1 win0:1,5 run1 win0:7,9,8 run1 late0:0 run1 lose0 run1 late0:2 run1 clear:0 run1 soff0 row clear:2 run0 clear:3 run0*3 min1*4', 'S': 'cab01 count01 count00 moved1 cab00 moved1 count11 count10 cab11 moved0*2 cab10 cab21*2 count21 cab20 count20 win0*8 leave1 old0 leave0 front1 front0 xrun1*6 back0 xrun1*2 back0 xrun0*2 mask01*2 mask11*2 mask00*2 xrun0', 'P': 'hop01 hop00 hop01*4 hop00*4 hop01*2 hop00 hop10 hop00 cab01 hop11 cab00 hop11*4 moved1 hop10*4 hop11*2 check0*2 hop10 hop21 hop10 back1 cab11 back1 moved0 hop20 back1 hop21*4 cab10 check0 check1*2 hop20 check1 hop21*2 hop20 cab21 hop20*2 clear win1 hop20*2 cab20*2 win1*2 check21*3 win0 win1 xoff1*3 check20*3 win1*2 lose0 xoff0*3 win0*2 lose1*3 back0 lose0 front1 front0 back0 lose0 win0*4 late0 back0*2 lose0 late0*2 row*6 mask01 mask11 mask00', 'G': 'column1 column0 front1 front0 leave1 leave0'}
LAST = {'V': 'hop01*4 <min0*4 hop00*4 hop01*2 hop00 hop01 hop00 hop11 hop00 hop11 hop10*2 hop11*2 hop10 hop11 hop10 hop11 hop21 hop10*2 hop21 hop20*2 hop21*2 back1*2 hop21*2 win1:2,7,4 hop20*2 win1:5,0,3,1,6,10 hop20*2 win1:8,11,13,12,9 cab20 check21 win1:14 old1*2 lose1 xoff1 win0:0,1 check20 win0:3,7 soff1 win0:10,2 xoff0 run1 win0:5,6,11,4 run1 win0:9,8 run1 late0:0 run1 late0:2 lose0 run1 late0:1 run1 clear*2 run1 clear run1 soff0 clear run0 row run0*3 ksum min0:3 min1:1,3 ksum min1:2,0 ksum min0:2,1 ksum mirror:0 min0:0 ksum mirror:2 ksum mirror:4 ksum mirror:1,3 ksum mirror:6 ksum mirror:5,7 ksum*3', 'S': '<mask10*2 <xrun0:3 <mask21*2 count00 cab00 cab01 count01 <mask20*2 moved1 count11 count10 cab11 moved1 cab10 cab21*2 count21 moved0 cab20 moved0 count20 win0*8 old0 leave1 leave0 back0 xrun1 back0 xrun1*6 zout:0 xrun1 xrun0 zout:1 xrun0 zout:3 xrun0 zout:4 xrun0 zout:2 xsum*6 rows:1 xsum rows:0 xsum*2', 'P': 'hop01 hop00 <mask10 hop01*4 hop00*4 hop01*2 <mask21 hop11 hop00*2 hop10 cab01 <mask20 hop11 cab00 hop11*3 moved1 hop10*4 hop11*2 hop21 check0*2 hop10*2 back1 cab11 check0 back1 hop20 cab10 back1 hop21*4 check1*2 hop21*2 check1 cab21 hop20*4 moved0 win1*3 hop20*2 cab20*2 check21*3 win0*3 win1*3 xoff1*3 check20*3 lose1*3 back0 xoff0*3 back0*3 lose0 win0 lose0 win0 lose0 win0*2 clear late0 zout:0 lose0 late0*2 zout:1,2,3,7,4,5,6 row:3 zout:8,9 row:4,5,0,1,2 mirror*4 xsum mirror xsum*3 mirror*2 xsum*2 mirror*2 xsum*3', 'G': 'column1 column0 rows'}
EARLY = "hop01 hop00 hop11 hop10 cab01 cab00 count01 count00".split()
FIRST = {'V': 'hop01*4 hop00*4 hop01*2 hop00*2 hop01 hop11 hop00 hop11 hop10*2 hop11*2 hop10 hop11 hop10 hop11 hop21 hop10 hop21 hop20 hop10 hop20 hop21*2 back1*2 hop21*2 hop20*2 win1:0,2,4,1,6,5,7 hop20*2 win1:3 cab20 win1:8,12,14 check21 win1:10,11,13,9 old1 xoff1 check20 old1 lose1 xoff0 win0:0 soff1 win0:1,6 run1 win0:5,7,8 run1 win0:2,3,4,9 run1 win0:11 late0:1 win0:10 run1 late0:0 run1 lose0 late0:2 run1 clear*2 run1 clear soff0 row run1 run0 clear run0*3 min1*4', 'S': 'cab01 count01 count00 moved1*2 cab00 count11 count10 moved0*2 cab11 cab10 cab21*2 count21 cab20 count20 win0*8 old0 leave1 leave0 front1 front0 back0*2 xrun1*8 xrun0*2 mask01*2 mask11*2 mask00*2 xrun0', 'P': 'hop01 hop00 hop01*4 hop00*4 hop01*2 hop10 hop00*2 cab01 cab00 hop11*5 moved1 hop10*4 hop11*2 check0*2 hop10 hop21 hop10 back1*2 cab11 moved0 hop20 back1 hop21*4 cab10 check0 check1*2 hop20 check1 hop21*2 hop20 cab21 hop20*2 clear win1 hop20*2 cab20*2 win1*2 check21*3 win1 xoff1*3 check20*3 win1*2 xoff0*3 win0*3 lose1*3 front1 lose0*3 back0*2 front0 back0*2 win0*3 row:0 win0 late0 lose0 late0*2 row:3,1,4,2,5 mask01 mask11 mask00', 'G': 'column1 column0 front1 front0 leave1 leave0'}
ORDER = {'V': 'hop01*4 <min0*4 hop00*4 hop01*2 hop00 hop01 hop00 hop11 hop00 hop11 hop10*2 hop11*2 hop10 hop11 hop10 hop11 hop21 hop10 hop21 hop10 hop20*2 hop21*2 back1*2 hop21*2 win1:4 hop20*2 win1:2,3,1,6,7,0,5 hop20*2 win1:8,14,9,11,10 cab20 win1:13 check21 win1:12 old1*2 xoff1 lose1 win0:0,1 check20 win0:2,3 soff1 win0:9 xoff0 run1 win0:8,4 run1 win0:11,5,6,7 run1 win0:10 late0 run1 late0 run1 late0 lose0 run1 clear*2 run1 clear row run1 soff0 clear run0*4 min1*4', 'S': '<xrun0 <mask10*2 <xrun0 <mask21*2 count01 cab01 count00 <mask20*2 moved1 cab00 moved1 count11 count10 cab11 moved0*2 cab10 cab21*2 count21 cab20 count20 win0*8 old0 leave1 leave0 front1 back0 xrun1 front0 xrun1 back0 xrun1*6 xrun0*2 mask01*2 mask11*2 mask00*2', 'P': 'hop01 hop00 hop01*4 <mask10 hop00*4 hop01*2 <mask21 hop11 hop00 cab01 hop00 hop10 <mask20 hop11*4 moved1 cab00 hop10*4 hop11*2 check0*2 hop21 check0 hop10*2 back1 moved0 cab11 back1*2 hop21*4 hop20 cab10 check1*2 hop21*2 check1 cab21 hop20*4 win1*2 hop20*2 cab20*2 win1 check21*3 win0*2 win1*2 xoff1*3 win1 win0 check20*3 lose1*3 back0 xoff0*3 lose0 back0 lose0 back0 front1 back0 lose0 win0 front0 win0*3 clear late0 lose0 late0*2 row*6 mask01 mask11 mask00', 'G': 'column1 column0 front1 front0 leave1 leave0'}
FIRST['S'] = FIRST['S'].replace('mask00*2 xrun0', 'mask00*2')
LAST['S'] = LAST['S'].replace('<mask10*2 <xrun0:3', '<xrun0:2 <mask10*2 <xrun0:3').replace('cab11 moved1 cab10 cab21*2 count21 moved0 cab20 moved0 count20', 'cab11 moved0*2 cab10 cab21*2 count21 cab20 count20').replace('moved1 count11', 'moved1*2 count11')
LAST['P'] = LAST['P'].replace('hop20*4 moved0 win1*3', 'hop20*4 win1*3').replace('check0 back1 hop20', 'check0 moved0 back1 hop20')
LAST = {'V': 'hop01*4 <min0*4 hop00*4 hop01*2 hop00 hop01 hop00 hop11 hop00 hop11 hop10*2 hop11*2 hop10 hop11 hop10 hop11 hop21 hop10*2 hop21 hop20*2 hop21*2 back1 hop21*2 back1 win1:2,1 hop20*2 win1:3,4,5,0,6,7 hop20*2 win1:13,11,8 cab20 win1:12 check21 win1:14,10,9 old1 xoff1 old1 check20 lose1 win0:2,1 xoff0 win0:6,0 soff1 win0:5,3 run1 win0:4,7,11 run1 win0:10,9,8 run1 late0:0 run1 late0:2 lose0 run1 late0:1 run1 clear*2 run1 clear soff0 run1 clear run0 row run0*3 ksum min0:3 min1:2,3 ksum min1:0 min0:0 min1:1 ksum min0:1,2 ksum mirror:0 ksum mirror:2,1 ksum mirror:4,3 ksum mirror:6,5 ksum mirror:7 rows ksum*3', 'S': '<xrun0:2 <mask10*2 <xrun0:3 <mask21*2 count01 cab01 count00 cab00 <mask20*2 moved1*2 count11 count10 cab11 moved0 cab10 moved0 cab21*2 count21 cab20 count20 win0*8 old0 leave1 leave0 back0 xrun1*3 back0 xrun1*4 zout:0 xrun1 xrun0 zout:1 xrun0 zout:4 xrun0 zout:2 xrun0 zout:3 xsum*6 rows xsum*3', 'P': 'hop01 hop00 <mask10 hop01*4 hop00*4 hop01*2 <mask21 hop00*2 hop11 cab01 hop10 <mask20 hop11 cab00 hop11*3 moved1 hop10*4 hop11*2 check0*2 hop21 hop10 hop20 hop10 back1 cab11 moved0 check0 back1*2 hop21*4 cab10 check1*2 hop21*2 check1 cab21 hop20*4 win1*2 hop20*2 cab20*2 win1 check21*3 win0*2 win1 xoff1*3 check20*2 win1 check20 win1 win0 back0 xoff0*3 lose0 lose1*3 lose0 back0*3 win0 row:0 win0 zout:0 win0 lose0 win0 late0 clear zout:1 lose0 late0*2 zout:2 row:3 zout:3,7,4,5,6,8,9 row:4,5,1,2 mirror*5 xsum mirror xsum*2 mirror xsum mirror xsum*2 mirror*2 xsum*3', 'G': 'column1 column0 rows'}
OPT.update(npe=6, tile="VS")
OPT.update(pclear=False, late=(0, 0))
ORDER = {'V': 'hop01*4 <min0*4 hop00*4 hop01*2 hop00 hop01 hop00 hop11 hop00 hop11 hop10*2 hop11*2 hop10 hop11 hop10 hop11 hop21 hop10 hop21 hop20 hop10 hop20 hop21*2 back1*2 hop21*2 win1:2 hop20*2 win1:1,4,3,5,6,0,7 hop20*2 win1:9,8,11,14,10 cab20 win1:13 check21 win1:12 old1*2 xoff1 lose1 win0:1,0 check20 win0:2,4 soff1 win0:3 xoff0 run1 win0:13,6,5,7 run1 win0:12,14,11 run1 win0:10,9 run1 win0:8 run1 clear run1 row lose0 run1 clear run1 soff0 clear run0 clear run0*3 min1*4', 'S': '<mask10*2 <xrun0 <mask21*2 count01 <mask20 cab01 count00 <mask20 cab00 moved1*2 count11 count10 cab11 moved0*2 cab10 cab21*2 count21 cab20 count20 win0*8 old0 leave1 leave0 front1 xrun1 back0 front0 xrun1 back0 xrun1*6 xrun0*2 mask01*2 mask11*2 mask00*2 xrun0', 'P': 'hop01 hop00 hop01*4 <mask10 hop00*4 hop01*2 <mask21 hop11 hop00 cab01 hop00 hop10 moved1 cab00 <mask20 hop11*4 hop10*4 hop11*2 hop21 check0*3 hop10*2 back1 cab11 moved0 back1*2 hop21*4 hop20 cab10 check1*2 hop21*2 check1 cab21 hop20*4 win1*2 hop20*2 cab20*2 win1 check21*3 win0*2 win1*2 xoff1*3 win1 win0 check20*3 lose1*3 back0 xoff0*3 win0 front1 back0*3 win0 front0 win0*3 row lose0*4 row*5 mask01 mask11 mask00', 'G': 'column1 column0 front1 front0 leave1 leave0'}
FIRST = {e: " ".join(w for w in ORDER[e].split() if w[0] != "<") for e in ORDER}
LAST = {'V': 'hop01*4 <min0*4 hop00*4 hop01*2 hop00 hop01 hop00 hop11 hop00 hop11 hop10*2 hop11*2 hop10 hop11*2 hop10 hop21 hop10*2 hop21 hop20*2 hop21*2 back1*2 hop21*2 win1:3,4 hop20*2 win1:7,2,0,6,5,1 hop20*2 win1:8,10 cab20 win1:11,14,9,12,13 check21 old1*2 xoff1 win0:14 lose1 win0:0,1 check20 win0:3,2 soff1 win0:4,7 xoff0 run1 win0:6,5,11 run1 win0:12,10 run1 win0:9,13 run1 win0:8 run1 clear run1 row lose0 run1 clear run1 soff0 clear run0 clear run0*3 min0:1 ksum min0:3,2,0 ksum min1:1,2 ksum min1:0,3 ksum mirror:2 ksum mirror:0 ksum mirror:3,4 ksum mirror:1,6 ksum mirror:7,5 ksum rows ksum*2', 'S': '<mask10*2 <xrun0:3 <mask21*2 cab01 count01 count00 cab00 <mask20 moved1*2 <mask20 count11 count10 cab10 cab11 moved0*2 cab21*2 count21 cab20 count20 win0*8 old0 leave1 leave0 xrun1*4 back0 xrun1 back0 xrun1 zout:0 xrun1*2 zout:1 xrun0 zout:4 xrun0 zout:2 xrun0 zout:3 xrun0 xsum*6 rows xsum*3', 'P': 'hop01 hop00 <mask10 hop01*4 hop00*4 hop01*2 <mask21 hop00 hop11 hop00 cab01 moved1 hop10 cab00 <mask20 hop11*4 hop10*4 hop11*2 check0 hop21 check0*2 hop10*2 cab11 back1 moved0 back1 cab10 back1 hop21*4 hop20 check1*2 hop21*2 check1 cab21 hop20*4 win1*2 hop20*2 win1 cab20*2 check21*3 win0*3 win1*2 xoff1*3 win1 check20*3 lose1*3 back0 xoff0*3 win0 back0 zout:4 back0 win0*2 back0 row:0 win0*2 zout:0,1,2,3 lose0*4 row:3 zout:7,5,8,6,9 row:4,1,2,5 mirror*4 xsum mirror xsum mirror xsum*3 mirror*2 xsum mirror*2 xsum*3', 'G': 'column1 column0 rows'}
LEAD = dict(win0=1500.0, clear=-2000.0, soon=30000.0)
OTHER = ((1.4, 1.3, 1.6, 1.8, 1.3), (0.7, 1.0, 0.8, 0.6, 0.8), (1.5, 1.0, 1.0, 0.9, 1.6))

f32, bf, i32, u16, f16 = "float32", "bfloat16", "int32", "uint16", "float16"
SB = {
    "K": (KW, f32), "XW": (KW + TH, f32), "CT": (D, bf), "xb": (D, bf), "NC": (TH, f32),
    "ci": (256, i32), "ch": (256, bf), "d0": (256, bf), "d1": (256, bf), "r0": (256, f32), "r1": (256, f32), "z3": (TH, bf),
    "Ga": (TH, f32), "Gb": (TH, f32), "Ab": (TH, f32), "Bb": (TH, f32), "X1": (TH, bf), "X2": (TH, bf),
    "Cg0": (TH, bf), "Cg1": (TH, bf), "Cg2": (TH, bf), "hi": (TH, bf),
    "T3": (256, f32), "H3": (768, f16), "off": (192, u16), "cab": (192, bf), "P1": (64, f16), "cB": (64, f16),
    "e0": (64, bf), "e01": (64, bf), "nok": (64, bf), "pk": (64, bf), "w": (64, f32), "xoff": (64, u16), "Qn": (64, f16),
    "XH": (64, f32), "own0": (288, f32), "own1": (288, f32), "eq0": (2048, bf), "eq1": (2048, bf), "eq2": (1024, bf),
    "nd": (432, bf), "wl": (64, f32), "soff": (64, u16), "Hk": (TH, f16), "Hn": (TH, f16),
    "oz": (TH, bf), "okk": (512, f32), "ox": (256, bf), "oc": (512, f32),
    "pi": (48, i32), "pj": (48, i32), "pc": (192, f32), "n256": (256, bf), "io": (480, bf), "JX": (64, f32),
    "SP": (64, f32),
    "Sel": (64, f32), "Mq": (128, f32), "Mh": (128, f32),
    "Rb": (32, f32), "Rh": (64, bf), "IF": (128, f32),
    "crow": (128, bf), "one": (512, bf), "PI": (RO * 128, bf), "WB": (256, bf), "MK": (768, bf),
    "SQ": (RO * 64, bf), "Y": (288, bf), "Id": (10 * 128, bf), "II": (256, bf), "PK": (128, bf), "Zb": (160, bf), "Z": (16 * 160, bf),
    "L": (16 * 128, bf), "SH": (16 * 128, bf), "E": (8 * 128, bf), "HX": (136, bf), "HR": (10 * 128, bf),
}
for _t in range(RO):
    SB["s%d" % _t] = (TH, bf)
    for _h in range(2):
        SB["z%d%d" % (_t, _h)] = (TH // 2, bf)
        SB["q%d%d" % (_t, _h)] = (TH // 4, bf)
    if _t: SB["u%d" % _t] = (TH // 2, bf)
SCRATCH = {n: ("sbuf", [128, c], d) for n, (c, d) in SB.items()}
for _b in range(8):
    SCRATCH["p%d" % _b] = ("psum", [128, 512], f32)
DIMS = {}
for _h in range(2):
    DIMS["p%d" % _h] = [512 // RUN[_h], RUN[_h]]
    DIMS["p%d" % BK["win"][_h]] = [32 // RUN[_h], RUN[_h], 16]
    DIMS["own%d" % _h] = [32 // RUN[_h], RUN[_h], 8]
DIMS["p6"] = [64, 8]
for _n in DIMS:
    SCRATCH[_n] = (SCRATCH[_n][0], [128] + DIMS[_n], f32)
SEMAPHORES = ["eV", "eS", "eP", "eG", "sent"] + ["%s%d%d" % (x, t, h) for x in "zq" for t in range(1, RO) for h in range(2)] + ["d%d" % k for k in range(56)]
DBG = []
RAW = set()
LAND = {}
PLAN = []


def v(name, c0=0, c1=None, step=1, p0=0, p1=128):
    return (name, c0, math.prod(SCRATCH[name][1][1:]) if c1 is None else c1, step, p0, p1)


def split(x):
    out, cols, inner = [], list(range(x[1], x[2], x[3])), math.prod(DIMS[x[0]])
    for d in DIMS[x[0]]:
        inner //= d
        k = sorted(set(c // inner % d for c in cols))
        out.append(range(k[0], k[-1] + 1, k[1] - k[0] if k[1:] else 1))
    assert math.prod(len(r) for r in out) == len(cols)
    return out


def box(name, *ranges):
    at = lambda f: sum(f(r) * math.prod(DIMS[name][k + 1:]) for k, r in enumerate(ranges))
    return (name, at(min), at(max) + 1, 1, 0, 128, ranges)


def meet(a, b):
    if a[2] <= b[1] or b[2] <= a[1] or a[5] <= b[4] or b[5] <= a[4]: return False
    return (a[1] - b[1]) % math.gcd(a[3], b[3]) == 0


def covers(a, b):
    return a == b or (a[3] == 1 and not a[6:] and a[1] <= b[1] and b[2] <= a[2] and a[4] <= b[4] and b[5] <= a[5])


def needs(ops):
    reads, writes, banks, loads, deps = {}, {}, {}, {}, []
    for n, (e, fn, rd, wr, kind, cost, lag, stage) in enumerate(ops):
        d = set()
        for name in set(x[0] for x in rd + wr if SCRATCH[x[0]][0] == "psum"):
            b = banks.setdefault(name, [e, [], []])
            if b[0] != e: b[:] = [e, [], b[1]]
            d.update(b[2])
            if e == "P":
                d.update(b[1])
                b[1] = []
            b[1].append(n)
        for x in rd: d.update(m for m, old in writes.get(x[0], []) if meet(x, old))
        RAW.update((m, n) for m in d)
        for x in wr:
            for book in (reads, writes):
                d.update(m for m, old in book.get(x[0], []) if meet(x, old))
                book[x[0]] = [(m, old) for m, old in book.get(x[0], []) if not covers(x, old)]
        for x in rd: reads.setdefault(x[0], []).append((n, x))
        for x in wr: writes.setdefault(x[0], []).append((n, x))
        if kind and kind[0] == "arrival": d.add(n - 1)
        if kind == "dma" and wr:
            if e in loads: d.add(loads[e])
            loads[e] = n
        d.discard(n)
        deps.append(d)
    return deps


def free(ops, m, n):
    return ops[m][0] == ops[n][0] and (ops[m][0] == "P" and ops[n][4] is None or ops[m][4] == ops[n][4] == "dma")


def sequence(text, last=False):
    words, used = [], {}
    for w in text.split():
        dt, w = -(w[0] == "<"), w.lstrip("<")
        if ":" in w: words += [(w.split(":")[0], int(k), dt) for k in w.split(":")[1].split(",")]
        else: words += [(w.split("*")[0], None, dt)] * int((w + "*1").split("*")[1])
    for want in (0, -1):
        if last: used = {}
        for i, (step, k, dt) in enumerate(words):
            if k is None and dt == want:
                words[i] = (step, used.get(step, 0), dt)
                used[step] = used.get(step, 0) + 1
    return words


def plan(ops, deps):
    N = len(ops)
    gap = lambda m, n: 0.0 if free(ops, m, n) else ops[m][6] + (0.0 if ops[n][0] == "X" else NOM["wake"])
    before = [[(m, gap(m, n)) for m in sorted(deps[n])] for n in range(N)]
    cost, eng, lag = [o[5] for o in ops], [o[0] for o in ops], [o[6] for o in ops]
    for n in range(N):
        land = [LAND[m] for m in deps[n] if m in LAND and not free(ops, m, n)]
        if land: before[n].append((0, max(land) + NOM["wake"] - cost[0]))
    calls, soft = {}, []
    for n, o in enumerate(ops): calls.setdefault((o[0], o[7]), []).append(n)
    for e in ORDER:
        last = None
        for t in range(RO):
            for step, k, dt in sequence((FIRST if t == 0 else LAST if t == RO - 1 else ORDER)[e], t == RO - 1):
                here = calls.get((e, (t + dt, step)), [])
                if t or step not in FREE:
                    if last is not None: before[here[k]].append((last, 0.0))
                    last = here[k]
    topo, todo, after = [], [len(b) for b in before], [[] for n in range(N)]
    for n in range(N):
        for m, x in before[n]: after[m].append(n)
        if not todo[n]: topo.append(n)
    for n in topo:
        for m in after[n]:
            todo[m] -= 1
            if not todo[m]: topo.append(m)
    assert len(topo) == N
    way = [cost[n] + lag[n] for n in range(N)]
    for n in topo[::-1]:
        for m, x in before[n]: way[m] = max(way[m], cost[m] + x + way[n])
    kind, seen, one, many = [], {}, {}, {}
    for n, o in enumerate(ops):
        k, t = (o[7] and o[7][1], o[0], o[3][0][0] if o[3] and o[3][0][0][0] not in "szqu" else ""), o[7] and o[7][0]
        seen[k, t] = seen.get((k, t), 0) + 1
        kind.append(k + (seen[k, t],))
        one.setdefault(kind[n], []).append(n)
        many.setdefault(k, []).append(n)

    way = [way[n] + LEAD.get(kind[n][0], 0.0) for n in range(N)]
    view = [n for n in range(N) if not ops[n][7] or ops[n][7][0] == 0 or ops[n][7][0] == 1 and ops[n][7][1] in EARLY]
    loose = [n for n in view if not ops[n][7] or ops[n][7][1] in FREE + ["table", "soon"] and ops[n][7][0] == 0]
    tails = [n for n in view if ops[n][7] and ops[n][7][0] == 1]

    def lay(key, moved=None, up=True, view=view):
        for n in topo[::-1] if moved is None else ():
            for m, x in before[n]:
                if key[m] <= key[n]: key[m] = key[n] + 1.0
        todo = list(moved or ())
        while todo:
            n = todo.pop()
            for m in [m for m, x in before[n] if key[m] <= key[n]] if up else [m for m in after[n] if key[m] >= key[n]]:
                key[m] = key[n] + (1.0 if up else -1.0)
                todo.append(m)
        end, taken = [0.0] * N, {e: ([], []) for e in eng}
        for n in sorted(view, key=lambda n: key[n], reverse=True):
            t, c, (s, f) = 0.0, cost[n], taken[eng[n]]
            for m, x in before[n]:
                x += end[m]
                if x > t: t = x
            lo, hi = (len(s), 0) if not f or f[-1] <= t else (0, len(s))
            while lo < hi:
                mid = (lo + hi) // 2
                if f[mid] <= t: lo = mid + 1
                else: hi = mid
            hi = len(s)
            while lo < hi and s[lo] < t + c:
                t = f[lo]
                lo += 1
            s.insert(lo, t)
            f.insert(lo, t + c)
            end[n] = t + c
        return max(end[n] + lag[n] for n in tails) + sum(end[n] for n in LAND) / len(LAND) / 5, end, key

    def bound(end, before=before):
        last, prev, out = {}, {}, []
        for n in sorted(view, key=lambda n: end[n]):
            prev[n] = last.get(eng[n])
            last[eng[n]] = n
        n = max(tails, key=lambda n: end[n] + lag[n])
        while n is not None:
            t, m = max([(end[k] + x, k) for k, x in before[n]] + [(-1.0, None)], key=lambda p: p[0])
            if prev[n] is not None and end[prev[n]] > t + 1:
                m = prev[n]
                out.append((m, n))
            n = m
        return out or [(0, 1)]

    state = [OPT["seed"]]

    def pick(k):
        state[0] = (state[0] * 6364136223846793005 + 1442695040888963407) % (1 << 64)
        return (state[0] >> 33) % k

    lead = {}
    now = best = lay(list(way))
    pairs = bound(now[1])
    for it in range(OPT["turns"]):
        new = dict(lead)
        for k in range(1 + (pick(3) == 0)):
            m, n = pairs[pick(len(pairs))]
            x = now[2][m] - now[2][n]
            if x <= 0: new[kind[n]] = new.get(kind[n], 0.0) + (100, 300, 1000)[pick(3)]
            elif pick(2): new[kind[n]] = new.get(kind[n], 0.0) + x + (10, 100, 300)[pick(3)]
            else: new[kind[m]] = new.get(kind[m], 0.0) - x - (10, 100, 300)[pick(3)]
        y = lay([way[n] + new.get(kind[n], 0.0) for n in range(N)])
        if y[0] <= now[0] + OPT["heat"] * (1 - it / OPT["turns"]) * pick(1000) / 1000:
            now, lead = y, new
            pairs = bound(now[1])
            if y[0] < best[0]: best = y

    def shift(now, pairs):
        key = [cost[n] - now[1][n] - 1e-6 * n if now[1][n] else -1e9 - n for n in range(N)]
        m, n = pairs[pick(len(pairs))]
        how = pick(4)
        if how == 0: n, x = m, -(cost[n] + 10, 300, 600, 1200)[pick(4)]
        elif how == 1: x = (cost[m] + 10, 300, 600, 1200)[pick(4)]
        else: n, x = loose[pick(len(loose))], (-3000, -1500, -800, -400, -200, 200, 400, 800, 1500, 3000)[pick(10)]
        group = [k for k in (one[kind[n]] if pick(2) else many[kind[n][:3]]) if now[1][k] and ops[k][7] == ops[n][7]]
        for k in group: key[k] += x
        return lay(key, group, x > 0)

    now = best
    pairs = bound(now[1])
    for it in range(OPT["shifts"]):
        y = shift(now, pairs)
        if y[0] <= now[0] + OPT["heat2"] * (1 - it / OPT["shifts"]) * pick(1000) / 1000:
            now = y
            pairs = bound(now[1])
            if y[0] < best[0]: best = y

    sort = ["s" if o[7] and "run" in o[7][1] else "g" if o[2][1:] and SCRATCH[o[2][1][0]][2] == u16 else "d" if o[4] else "c" for o in ops]
    other = []
    for wake, fc, fg, fs, fr in OTHER:
        f = dict(s=fs, g=fg, d=1.0, c=fc)
        other.append(([cost[n] * f[sort[n]] for n in range(N)],
                      [[(m, x and x + lag[m] * (fr - 1.0) * (ops[m][4] == "call") + NOM["wake"] * (wake - 1.0)) for m, x in before[n]] for n in range(N)]))

    def judge(y):
        order, ends = sorted(view, key=lambda n: (y[1][n] - cost[n], n)), [y[1]]
        for c, b in other:
            end, busy = [0.0] * N, {e: 0.0 for e in eng}
            for n in order:
                t = busy[eng[n]]
                for m, x in b[n]:
                    x += end[m]
                    if x > t: t = x
                end[n] = busy[eng[n]] = t + c[n]
            ends.append(end)
        return [y[0]] + [max(e[n] + lag[n] for n in tails) for e in ends[1:]], ends

    bounds = lambda ends: [p for e, b in zip(ends, [before] + [b for c, b in other]) for p in bound(e, b)]
    now = best
    unit, ends = judge(now)
    mark = top = float(len(unit))
    pairs = bounds(ends)
    for it in range(OPT["polish"]):
        y = shift(now, pairs)
        if y[0] > now[0] + 600: continue
        times, ends = judge(y)
        got = sum(a / b for a, b in zip(times, unit))
        if got <= mark + 0.002 * (1 - it / OPT["polish"]) * pick(1000) / 1000:
            now, mark, pairs = y, got, bounds(ends)
            if got < top: best, top = y, got
    best = lay([cost[n] - best[1][n] if best[1][n] else way[n] - 1e6 for n in range(N)], view=range(N))
    best = (max(best[1][n] + lag[n] for n in range(N)),) + best[1:]
    DBG[:] = [ops, before, best]
    return sorted(range(N), key=lambda n: (best[1][n] - cost[n], n))


def emit(g, T, ops):
    q = {"V": g.vector, "S": g.scalar, "P": g.tensor, "G": g, "Y": g.sync}
    if not PLAN:
        deps = needs(ops)
        order = plan(ops, deps)
        place = {n: k for k, n in enumerate(order)}
        waits = []
        for n in range(len(ops)):
            last = {}
            for m in deps[n]:
                if free(ops, m, n) or ops[n][0] == "X": continue
                key = ("x", m) if ops[m][4] else ops[m][0]
                if place[m] > place.get(last.get(key), -1): last[key] = m
            waits.append(sorted(last.values(), key=lambda m: -place[m]))
        PLAN.extend([order, waits])
    order, waits = PLAN
    need = set(m for d in waits for m in d)
    sig, cnt, nd, final = {}, {"V": 0, "S": 0, "P": 0, "G": 0}, [0], {}
    seen, knew = {e: {} for e in q}, {}
    for n in order:
        e, fn, kind = ops[n][0], ops[n][1], ops[n][4]
        for m in waits[n]:
            s, val = sig[m]
            if seen[e].get(s, 0) < val:
                q[e].wait_ge(T.sem[s], val)
                seen[e][s] = val
                for s2, v2 in knew[m].items():
                    seen[e][s2] = max(seen[e].get(s2, 0), v2)
        if kind == "dma":
            s = "d%d" % nd[0]
            nd[0] += 1
            made = fn()
            made = made if isinstance(made, list) else [made]
            for x in made: x.then_inc(T.sem[s], 16)
            sig[n] = (s, 16 * len(made))
        elif kind == "call":
            fn()
        elif kind:
            sig[n] = kind[1:]
        else:
            ins = fn()
            if n in need:
                cnt[e] += 1
                ins.then_inc(T.sem["e" + e], 1)
                sig[n] = ("e" + e, cnt[e])
        if n in sig:
            final[sig[n][0]] = sig[n][1]
            knew[n] = dict(seen[e]) if e != "X" else {}
    for s in final:
        g.wait_ge(T.sem[s], final[s])


def rank_program(g, core, T, topo):
    rank = T.rank_of(core)
    if rank is None:
        return
    cores = T.cores
    nxt, prv = cores[(rank + 1) % len(cores)], cores[(rank - 1) % len(cores)]
    rid, pid = topo.addr(nxt)[0], topo.addr(nxt)[1]
    n_out, n_in = len(topo.engines(core, nxt)), len(topo.engines(prv, core))
    ops, loaded, now = [], [0.0], [0, None]
    V, S, P = g.vector, g.scalar, g.tensor

    def ap(x):
        if not isinstance(x, tuple): return x
        if x[0] == "at": return ap(x[1]).indirect(ap(x[2]))
        if x[0] in DIMS: return T[x[0]][(slice(x[4], x[5]),) + tuple(slice(r.start, r.stop, r.step) for r in (x[6] if x[6:] else split(x)))]
        return T[x[0]][x[4]:x[5], x[1]:x[2]:x[3]] if x[3] > 1 else T[x[0]][x[4]:x[5], x[1]:x[2]]

    size = lambda x: 16 * size(x[2]) if x[0] == "at" else math.prod(len(r) for r in x[6]) if x[6:] else len(range(x[1], x[2], x[3]))
    short = lambda x: SCRATCH[x[0]][2] in (bf, f16, u16)

    def add(e, fn, out, ins, kind=None, cost=None, lag=0.0, per=None):
        rd, wr = [], []
        for x in ins:
            if isinstance(x, tuple): rd += [x[1], x[2]] if x[0] == "at" else [x]
        if isinstance(out, tuple):
            if out[0] == "at":
                wr, rd = [out[1]], rd + [out[2]]
            else: wr = [out]
        if cost is None:
            if out[0] == "at": cost = 55 + size(out) * NOM["scatter"] * NOM["cyc"]
            elif ins and ins[0][0] == "at": cost = 55 + size(out) * NOM["gather"] * NOM["cyc"]
            else:
                if per is None: per = 0.5 if e == "V" and all(short(x) for x in [out] + ins[:1]) else 1.0
                cost = max(64, size(out) * per) * NOM["cyc"]
        ops.append((e, fn, rd, wr, kind, cost, lag, now[1] and tuple(now)))

    def stage(name, t=None): now[:] = [now[0] if t is None else t, name]

    def ts(out, a, s1, o0, s2=None, o1=None):
        if o1 is None: add("V", lambda: V.tensor_scalar(ap(out), ap(a), ap(s1), None, o0), out, [a, s1])
        else: add("V", lambda: V.tensor_scalar(ap(out), ap(a), ap(s1), ap(s2), o0, o1), out, [a, s1, s2])

    def tt(out, a, b, op): add("V", lambda: V.tensor_tensor(ap(out), ap(a), ap(b), op), out, [a, b], per=2.0 if a[0] in SB and b[0] in SB else 1.0)
    def cp(out, a): add("V", lambda: V.tensor_copy(ap(out), ap(a)), out, [a])
    def ms(out, c): add("V", lambda: V.memset(ap(out), c), out, [])

    def act(out, a, fn=F.Identity, bias=None, scale=None):
        kw = {k: x for k, x in (("bias", bias), ("scale", scale)) if x is not None}
        add("S", lambda: S.activation(ap(out), ap(a), fn, **{k: ap(x) for k, x in kw.items()}), out, [a, bias, scale])

    def mm(out, l, r, st, sp, alone=False):
        add("P", lambda: P.matmul(ap(out), ap(l), ap(r), bool(st), bool(sp)), out, [l, r], cost=max(64, size(r)) * (1 if short(l) else 4) * NOM["pe"])
        a, b = ops[-2], ops[-1]
        if not alone and a[0] == "P" and a[3][0][0] == out[0] and (a[2][-2][0] == l[0] or a[2][-1][0] == r[0]) and a[5] + b[5] <= (OPT["cap"] if now[1] not in ("zout", "mirror") else 120):
            ops[-2:] = [("P", lambda: (a[1](), b[1]())[1], a[2] + b[2], a[3] + b[3], None, a[5] + b[5], 0.0, a[7])]

    def dma(e, out, a, row=None, after=()):
        x = a if row is not None or not isinstance(out, tuple) else out
        n = size(x) * (x[5] - x[4]) * (2 if short(x) else 4) / NOM["rate"]
        if isinstance(out, tuple):
            loaded[0] += n
            LAND[len(ops)] = NOM["dma"] + loaded[0]
        to = (lambda: ap(out)) if row is None else (lambda: T[out[0]][row:128:16, out[1]:out[2]])
        add(e, lambda: {"Y": g.sync, "S": S, "G": g}[e].dma_start(to(), ap(a)), out, [a] + list(after), "dma", NOM["gdma"] if e == "G" else 50.0,
            NOM["glag" if e == "G" else "dma"] + n)

    def iota(out, pat, base, cm=0):
        kw = {} if SB[out[0]][1] == i32 else {"allow_small_or_imprecise_dtypes": True}
        add("G", lambda: g.iota(ap(out), pat, base, cm, **kw), out, [], cost=130 + 2 * size(out) * NOM["cyc"])

    at = lambda win, off: ("at", win, off)
    ps = lambda b, c0=0, c1=512, step=1, p0=0, p1=128: v("p%d" % b, c0, c1, step, p0, p1)
    R = lambda name, h, i=0, n=1: v(name, 512 * h + i, 512 * h + 512, n)
    W = lambda name, h, m=0: v(name, 64 * m + 32 * h, 64 * m + 32 * h + 32)
    blk = lambda name, k, n: v(name, k * n, k * n + n)
    part = lambda x, i, n: (x[0], x[1] + (x[2] - x[1]) // n * i, x[1] + (x[2] - x[1]) // n * (i + 1)) + x[3:]
    col = lambda c: v("pc", c, c + 1)
    pcs = lambda c, n: v("pc", c, c + n)
    num = lambda a, b: v("n256", a, b)
    z = lambda t, h: v("z%d%d" % (t, h))
    Id = lambda k: blk("Id", k, 128)

    for k in range(3): dma("S", v("z3", p0=8 * k, p1=8 * k + 8), T.zin[k:128:16, :])
    dma("S", v("ci"), T.cnt[:])
    for h in (1, 0): dma("Y", R("K", h), T.nkey[:, 512 * h:512 * h + 512])
    dma("Y", v("K", TH, D), T.nkey[:, TH:D])

    ioA, ioB, ioC, ioD, ioE = v("io", 0, 64), v("io", 64, 192), v("io", 192, 320), v("io", 320, 448), v("io", 448, 480)
    iota(v("pi", 0, 1), [[0, 1]], 0, 1)
    iota(v("pi", 8, 13), [[16, RO]], 0, 1)
    iota(v("n256"), [[1, 256]], 0)
    iota(ioC, [[0, 8], [1, 16]], 0)
    iota(ioB, [[1, 8], [0, 16]], 0)
    iota(ioA, [[1, 32], [0, 2]], 0)
    iota(ioE, [[1, 8], [0, 4]], 0)
    iota(ioD, [[0, 8], [1, 4], [0, 4]], 0)
    iota(v("pi", 16, 32), [[-1, 16]], 16, 1)
    iota(v("pi", 32, 40), [[1, 8]], 1, 1)
    iota(v("SP"), [[0, 8], [16, 8]], D, 1)
    for h in range(2): iota(W("JX", h), [[16, 32]], KW - D // 2 * (not OPT["u16"]) + 512 * h, 1)
    bits = [(0, 127), (0, 15), (4, 7), (0, 3), (2, 31), (3, 7), (0, 1), (1, 3), (0, 7), (0, 7)]
    cP, cA, cG, cM3, cP2, cGQ, cDUP, cMQ, c7 = range(9)
    for c, (sh, mk) in enumerate(bits): ts(v("pj", c, c + 1), v("pi", 0, 1), sh, A.arith_shift_right, mk, A.bitwise_and)
    ts(v("pj", 10, 15), v("pi", 8, 13), 4, A.arith_shift_right, 7, A.bitwise_and)
    ts(v("pj", 15, 16), v("pi", 0, 1), 6, A.arith_shift_right, 1, A.bitwise_and)
    ts(v("pj", 16, 40), v("pi", 16, 40), 15, A.bitwise_and)
    cp(pcs(0, 16), v("pj", 0, 16))
    cp(pcs(96, 24), v("pj", 16, 40))
    ts(pcs(64, 16), num(0, 16), col(cA), A.is_equal)
    ts(col(21), col(cG), 16.0, A.mult)
    ts(pcs(24, 5), num(0, 5), -3.0, A.mult, col(cA), A.add)
    ts(pcs(32, 5), pcs(10, 5), 4.0, A.mult, 300.0, A.add)
    ts(pcs(40, 5), pcs(24, 5), 0.0, A.is_ge)
    ts(pcs(48, 5), pcs(24, 5), 2.0, A.is_le)
    tt(pcs(32, 5), pcs(24, 5), pcs(32, 5), A.add)
    tt(pcs(40, 5), pcs(40, 5), pcs(48, 5), A.mult)
    tt(pcs(32, 5), pcs(32, 5), pcs(40, 5), A.mult)
    ts(pcs(24, 5), pcs(32, 5), -300.0, A.add)
    ts(col(30), col(c7), 4.0, A.mult, col(cGQ), A.add)
    for t in range(RO): ts(blk("SQ", t, 64), ioA, col(24 + t if t else 30), A.is_equal)
    ts(col(16), col(cDUP), 2.0, A.mult, -1.0, A.add)
    ts(col(17), col(cDUP), -1.0, A.add)
    ts(col(169), col(cDUP), -128.0, A.add)
    ts(col(18), col(cA), 1.0, A.add, col(cA), A.mult)
    ts(col(19), col(18), -1.0, A.mult, 1.0, A.add)
    ts(col(20), col(18), -BIG, A.mult, BIG, A.add)
    ts(col(23), col(15), 4.0, A.mult, col(cMQ), A.add)
    ts(pcs(56, 7), num(0, 7), col(23), A.is_equal)
    for c in (58, 62): ts(col(c), col(c), BIG, A.mult)
    ts(blk("WB", 0, 128), ioC, col(16), A.mult, col(17), A.add)
    ts(blk("WB", 1, 128), ioB, col(cGQ), A.is_equal)
    tt(blk("WB", 0, 128), blk("WB", 0, 128), blk("WB", 1, 128), A.mult)
    for m in range(6): act(blk("MK", m, 128), blk("WB", 0, 128), scale=col(56 + m // 2 + 4 * (m % 2)))
    for k, wt in enumerate((1.0, 1.0 / BIG)): ts(blk("Sel", k, 32), ioE, col(cG), A.is_equal, wt, A.mult)
    ts(v("Mq"), ioD, col(cM3), A.is_equal)
    ts(v("Mh"), ioD, col(cM3), A.is_equal, 1.0 / D, A.mult)
    ts(v("Rb"), num(0, 32), col(cP2), A.is_equal)
    ts(blk("Rh", 0, 32), num(0, 32), col(cP2), A.is_equal, -float(D), A.mult)
    ts(blk("Rh", 1, 32), num(0, 32), col(cP2), A.is_equal)
    ms(v("one", p1=64), 1.0)
    ts(pcs(80, 3), num(0, 3), col(cP), A.is_equal)
    ts(col(83), col(80), PB, A.mult)
    ts(col(84), col(81), -float(D // 2), A.mult, col(83), A.add)
    ts(col(85), col(82), 0.5, A.mult, col(84), A.add)
    ts(v("crow"), num(0, 128), 0.0, A.mult, col(85), A.add)
    ms(v("crow", p0=32, p1=64), float(D // 2))
    ts(col(22), col(cP), 16.0, A.add)
    stage("soon", 0)
    ts(v("Zb"), num(0, 160), col(22), A.is_equal)
    stage(None)
    for a in range(16): act(blk("Z", a, 160), v("Zb"), scale=col(64 + a))
    ts(col(86), col(21), 16.0, A.add)
    ts(col(88), col(64), -1.0, A.mult, 1.0, A.add)
    ts(col(89), col(64), 16384.0, A.mult)
    ts(col(91), col(64), 32.0, A.mult)
    ts(col(92), col(65), 159.0, A.mult, -128.0, A.add)
    ts(col(95), col(64), 128.0, A.mult, col(92), A.add)
    ts(col(90), col(95), -1.0, A.mult)
    ts(col(168), col(65), 32.0, A.mult)
    ts(col(93), col(64), col(cP), A.add)
    ts(col(94), col(64), 15.0, A.mult, 1.0, A.add)
    ts(Id(0), num(0, 128), col(cP), A.is_equal)
    for k, wt in enumerate((-0.25, 16.0, 16.0, -128.0, -8192.0)): act(Id(k + 1), Id(0), scale=wt)
    act(Id(6), Id(0), scale=col(64))
    ts(Id(7), ioB, col(cG), A.is_equal)
    ts(blk("Y", 0, 144), num(0, 144), col(86), A.is_equal, col(91), A.mult)
    ts(blk("Y", 1, 144), num(0, 144), col(86), A.is_equal, col(89), A.mult)
    for k in range(2): act(blk("II", k, 128), Id(0), scale=col(88))
    ts(v("PK"), num(0, 128), col(93), A.is_equal, col(94), A.mult)
    for a in range(16): act(blk("L", a, 128), Id(7), scale=col(64 + a))
    ts(col(132), col(65), col(66), A.add, 1024.0, A.mult)
    ts(col(133), col(64), 32.0, A.mult, col(132), A.add)
    ts(col(134), col(65), -BIG / 1024, A.mult)
    ts(col(135), col(66), -1.5 * D / 1024, A.mult, col(134), A.add)
    ts(col(136), col(64), 128.0, A.mult, col(135), A.add)
    act(Id(8), Id(7), scale=col(136))
    act(Id(9), Id(0), scale=8192.0)
    ts(v("SP"), v("SP"), col(21), A.subtract)
    ts(v("JX"), v("JX"), col(21), A.subtract)
    ts(pcs(170, 8), num(128, 136), 16.0, A.mult, col(cA), A.add)
    for t in range(RO): ts(v("PI", 128 * t, 128 * t + 128, p1=32), v("io", 192, 320, p1=32), float(t), A.not_equal, BIG, A.mult)
    ts(v("PI", p1=32), v("PI", p1=32), -1.5 * D, A.add)
    stage("soon", 0)
    add("S", lambda: S.activation(ap(v("XW", D, KW)), ap(num(64, 192)), F.Silu), v("XW", D, KW), [num(64, 192)], cost=1400.0)
    stage(None)
    ts(pcs(96, 16), pcs(96, 16), col(21), A.add)
    ts(pcs(112, 8), pcs(112, 8), col(cA), A.max, col(21), A.add)
    for s in range(16): ts(blk("SH", s, 128), num(0, 128), col(96 + s), A.is_equal)
    for s in range(8): ts(blk("E", s, 128), num(0, 128), col(112 + s), A.is_equal)
    ts(col(124), col(cA), 8.0, A.mult, col(cG), A.add)
    ts(col(124), col(124), 8.0, A.mult, 8.0, A.add)
    ts(v("HX"), num(0, 136), col(124), A.is_equal)
    ts(col(127), col(cGQ), 16.0, A.mult)
    ts(col(128), col(127), 1.0, A.add)
    ts(col(146), col(15), -16.0, A.mult)
    ts(blk("HR", 8, 128), num(0, 128), col(128), A.is_equal, col(146), A.mult)
    ts(blk("HR", 9, 128), num(0, 128), col(127), A.is_equal, col(15), A.mult)
    tt(blk("HR", 8, 128), blk("HR", 8, 128), blk("HR", 9, 128), A.add)
    ts(pcs(148, 8), num(0, 8), col(c7), A.is_equal)
    for b in range(8): act(blk("HR", b, 128), blk("HR", 8, 128), scale=col(148 + b))
    ts(col(129), col(65), 2687.0, A.mult, -128.0, A.add)
    ts(col(131), col(64), -32.0, A.mult, col(129), A.add)
    ts(col(126), col(65), 42992.0, A.mult, -2048.0, A.add)
    ts(col(147), col(64), -512.0, A.mult, col(126), A.add)
    ts(col(125), col(21), 1.0, A.add)
    ts(blk("HR", 9, 128), num(0, 128), col(125), A.is_equal, -16.0, A.mult)
    ts(blk("WB", 1, 128), num(0, 128), col(21), A.is_equal)
    tt(blk("HR", 9, 128), blk("HR", 9, 128), blk("WB", 1, 128), A.add)
    act(v("IF"), Id(0))

    def front(t, h):
        src = R("s%d" % (t - 1), h) if t else v("z3", 512 * h, 512 * h + 512, p1=24)
        b = BK["front"][h] if t else 7
        for q in range(2): mm(ps(b, 256 * h, 256 * h + 256, 1, 64 * q, 64 * q + 64), v("SQ", 64 * t, 64 * t + 64, p1=src[5]), part(src, q, 2), True, True)
        act(blk("u%d" % t, h, 256) if t else v("q0%d" % h), ps(b, 256 * h, 256 * h + 256), F.Square, bias=col(169 if t else cDUP))

    def mask(t, m, h, bank):
        for q in range(2): mm(part(ps(bank), q, 2), blk("MK", 2 * m + q, 128), v("q%d%d" % (t, h)), True, True)
        for q in range(2):
            out, b = part(R("X%d" % m, h) if m else ps(bank), q, 2), col(20 if m == 2 else 19)
            if OPT["mk"][4 * m + 2 * h + q] == "S" or not now[1]: act(out, part(ps(bank), q, 2), F.Relu, bias=b)
            else: ts(out, part(ps(bank), q, 2), b, A.add, 0.0, A.max)

    def masks(t):
        for h in (1, 0):
            if t: stage("mask0%d" % h)
            else: front(t, h)
            mask(t, 0, h, 2 + h)
        for m in (1, 2):
            for h in (1, 0):
                if t: stage("mask%d%d" % (m, h))
                mask(t, m, h, BK["mask"][h])

    def tables():
        stage("table", 0)
        for c in range(6): act(blk("CT", c, 256), v("n256"))
        ms(v("CT", 6 * 256), 0.0)
        ts(v("ch"), v("ci"), 32.0, A.mult, 64.0, A.add)
        add("S", lambda: S.activation(ap(v("r0")), ap(v("ch")), F.Identity, bias=-32.0), v("r0"), [v("ch"), v("CT")])
        dma("Y", v("CT"), v("ch"), 0)
        for k in range(2): dma("Y", v("d%d" % k), T.xreg[k:128:16, :])
        for h in (1, 0): dma("Y", z(0, h), T.zin[:, 512 * h:512 * h + 512])
        dma("Y", v("XW", 0, D, 1, 0, 1), v("r0"), 0)
        stage("soon")
        for k in range(8):
            dma("G", v("XW", 0, D, 1, 16 * k + 2, 16 * k + 16), T.xreg[16 * k + 2:16 * k + 16, :],
                after=[v(x) for x in ("pi", "n256", "io", "SP", "JX", "r0")])
        mm(ps(6, 0, 256), Id(2), v("d0"), True, False)
        mm(ps(6, 0, 256), Id(0), v("d1"), False, True)
        act(v("r1"), ps(6, 0, 256), bias=32.0)
        dma("Y", v("XW", 0, D, 1, 1, 2), v("r1"), 1)

    Gs = ["Ga", "Gb", "Ga", "Ab"]

    def gather(m, h):
        if m == 3 and h == 0 and OPT["old0"] == "S":
            act(R("Gb", h), at(v("K", 0, D), W("off", h, 2)))
            stage("clear")
            if OPT["pclear"]:
                mm(ps(3), Id(0), R("X2", h), True, True)
                for i in (3, 2, 1, 0): tt(part(R("Ab", h), i, 4), part(R("Gb", h), i, 4), part(ps(3), i, 4), A.subtract)
                return
            for i in (3, 2, 1, 0): tt(part(R("Ab", h), i, 4), part(R("Gb", h), i, 4), part(R("X2", h), i, 4), A.subtract)
            return
        for i in range(4 if m == 0 else 2):
            if m == 0: tt(R("Ga", h, i, 4), R("K", h, i, 4), ps(2 + h, i, 512, 4), A.mult)
            else: tt(part(R(Gs[m], h), i, 2), at(v("K", 0, D), part(W("off", h, m - 1), i, 2)), part(R("X1" if m == 1 else "X2", h), i, 2),
                     A.mult if m < 3 else A.subtract)

    def turn(t, m, h):
        mm(ps(h, 0, 128), v("one", 0, 128, p1=3), v("crow", p1=3), True, False)
        for c in range(4): mm(ps(h, c, 128, 4), R(Gs[m], h, c, 4), blk("Sel", m // 2, 32), False, c == 3, True)
        H3, T3 = blk("H3", 2 * m + h, 128), blk("T3", h, 128)
        tt(T3, ps(h, 0, 128), v("Mq"), A.mult)
        tt(H3, ps(h, 0, 128), v("Mh"), A.mult)
        o = ps(BK["two"][h], 256, 288)
        mm(o, T3, v("Rb"), True, False, True)
        mm(o, H3, blk("Rh", 0, 32), False, True, True)
        ts(W("off", h, m), o, D // 2 - 0.5, A.add)
        if m: copy(OPT["sq"][2 * m + h - 2], W(("P1", "Qn")[m - 1], h), o, -0.5)
        stage("cab%d%d" % (m, h))
        if m == 2 and h:
            mm(ps(4, 32, 64), H3, blk("Rh", 1, 32), False, True)
            act(W("cab", h, m), ps(4, 32, 64), F.Abs, bias=-(HB - 1.0 + GOOD) * D, scale=float(D))
            if OPT["sq"][4] == "V": ts(W("e01", 0), ps(4, 0, 32), GOOD, A.not_equal, 1024.0, A.mult)
            else: act(W("e01", 0), ps(4, 0, 32), F.Abs, bias=-GOOD)
        else:
            o = ps(BK["cab"][h], 0, 32) if m < 2 else ps(h, 128, 160)
            mm(o, H3, blk("Rh", 1, 32), True, m < 2)
            if m == 2: mm(o, Id(0), W("e01", h), False, True)
            act(W("cab", h, m), o, F.Abs, bias=-(HB - 1.0) * D, scale=float(D))
        if m == 2 and OPT["own"][h] == "S": tt(W("XH", h), W("Qn", h), W("cab", h, m), A.add)
        stage("count%d%d" % (m, h))
        win, b = (v("XW", 0, D), 32.0) if t else (v("CT"), 0.0)
        if m == 2 and h == 0 and OPT["vcount"]:
            ts(part(R("Cg2", h), 0, 2), at(win, part(W("off", h, m), 0, 2)), b, A.add)
            act(part(R("Cg2", h), 1, 2), at(win, part(W("off", h, m), 1, 2)), bias=b)
        elif m == 1: act(R("Cg1", h), at(win, W("off", h, m)), bias=col(133 if t else 132), scale=col(64))
        else: act(R("Cg%d" % m, h), at(win, W("off", h, m)), bias=b)

    def check(m, h=None):
        c0, c1 = (0, 64) if h is None else (32 * h, 32 * h + 32)
        o = ps(4, c0, c1) if m < 2 else ps(BK["nok"][h or 0], 320 + c0, 320 + c1)
        for a in range(16): mm(o, v("Y", 144 * (m % 2) + 16 - a, 144 * (m % 2) + 144 - a), v("Cg%d" % m, 16 * c0 + a, 16 * c1, 16), a == 0 and m != 1, False)
        mm(o, Id(4 if m == 1 else 1), v("cab", 64 * m + c0, 64 * m + c1), False, m == 2, True)
        if m == 2: ts(v("nok", c0, c1), o, 1024.0, A.not_equal, 2.0 ** 44, A.mult)

    def moved(t, h, stop): mm(ps(2), v("II", 128 - 16 * t, 256 - 16 * t) if t else v("PK"), z(t, h), True, stop)

    def leave(t, h=None):
        c0, c1 = (0, 64) if h is None else (32 * h, 32 * h + 32)
        stage("xoff" if h is None else "xoff%d" % h)
        o = ps(BK["nok"][h or 0], 384 + c0, 384 + c1)
        mm(o, Id(0), v("Qn", c0, c1), True, False)
        if OPT["u16"]:
            mm(o, v("crow", p0=32, p1=33), v("one", 0, c1 - c0, p0=32, p1=33), False, False)
            mm(o, Id(3), v("nok", c0, c1), False, True)
            tt(v("xoff", c0, c1), o, v("JX", c0, c1), A.min)
        else:
            mm(o, Id(3), v("nok", c0, c1), False, True)
            tt(v("w", c0, c1), o, v("JX", c0, c1), A.min)
            ts(v("xoff", c0, c1), v("w", c0, c1), float(D // 2), A.add)

    def send(t, h):
        so = R("s%d" % t, h)
        act(so, at(v("XW"), W("xoff", h)), bias=col(90))
        if t < RO - 1:
            stage("front%d" % h)
            front(t + 1, h)
            write(t, v("q%d%d" % (t + 1, h)), blk("u%d" % (t + 1), h, 256), NOM["less"])
            stage("leave%d" % h)
            write(t, z(t + 1, h), so, -NOM["less"] * (2 - h))

    def write(t, to, so, less):
        add("G", lambda: g.remote_dma(ap(to), ap(so), T.sem[to[0]], T.sem.sent, pid, rid, topo.mask(core, nxt)), None, [so], "call", 600.0,
            NOM["hop"] - 600 - less + (NOM["once"] if t == 0 else 0))
        add("X", None, to, [], ("arrival", to[0], n_in), 1.0)

    def twin(h):
        c = KW + 512 * h
        add("Y", lambda: [g.sync.dma_start(T.NC[p:p + 15, 512 * h:512 * h + 512], T.XW[p:p + 15, c:c + 512]) for p in range(1, 128, 16)],
            v("NC", 512 * h, 512 * h + 512, p0=1), [v("XW", c, c + 512)], "dma", 400.0, NOM["dma"] + 120 * 2048 / NOM["rate"])

    def column(t, h):
        if OPT["dmacol"]:
            add("G", lambda: g.dma_start(T.NC[0:128:16, 512 * h:512 * h + 512], T.Cg2[0:128:16, 512 * h:512 * h + 512]), v("NC", 512 * h, 512 * h + 512, p1=1), [R("Cg2", h)],
                "dma", NOM["gdma"], NOM["glag"])
            return
        moved(t, h, False)
        mm(ps(2 + h), Id(6), R("Cg2", h), False, True)
        act(R("NC", h), ps(2 + h), bias=col(95 if t else 168))

    def winners(h):
        c, eq = RUN[h], "eq%d" % h
        nr = 32 // c
        stage("win%d" % h)
        sizes = [(c - d) * nr for d in range(1, c)]
        npair = sum(sizes)
        SH = lambda s: blk("SH", s % 16, 128)
        for k in range(8):
            if OPT["own"][h] == "S": act(v("own%d" % h, k, 256, 8), W("XH", h))
            else: tt(v("own%d" % h, k, 256, 8), W("Qn", h), W("cab", h, 2), A.add)
        bank = BK["win"][h]
        own = lambda i0, i1: box("own%d" % h, range(nr), range(i0, i1), range(8))
        far = lambda i0, i1, k0, k1: box("p%d" % bank, range(nr), range(i0, i1), range(k0, k1))
        for k in range(9):
            mm(ps(bank, k, 512, 16), SH(k), W("Qn", h), True, False)
            mm(ps(bank, k, 512, 16), SH(k), W("cab", h, 2), False, True)
        tt(v(eq, 0, 256), far(0, c, 1, 9), own(0, c), A.is_equal)
        for k in range(8): mm(ps(h, npair, npair + 32), blk("E", k, 128), v(eq, k, 256, 8), k == 0, k == 7)
        late = OPT["late"][h]
        for r in (1, 0):
            e0, d0 = 256 + 8 * npair * r, 1 if r else late + 1
            for d in range(d0, c):
                x, a = sizes[d - 1], e0 + 8 * sum(sizes[:d - 1])
                if r: tt(v(eq, a, a + 8 * x), far(d, c, 0, 8), own(0, c - d), A.is_equal)
                else: tt(v(eq, a, a + 8 * x), far(0, c - d, 1, 9), own(d, c), A.is_equal)
            x = sum(sizes[:d0 - 1])
            for k in range(8): mm(ps(h, x, npair), SH(-k * r), v(eq, e0 + 8 * x + k, e0 + 8 * npair, 8), r and k == 0, not r and k == 7, k == 0)
        stage("lose%d" % h)
        nd = lambda a, b: v("nd", 144 * h + a, 144 * h + b)
        if OPT["nd"][h] == "V": ts(nd(0, npair + 32), ps(h, 0, npair + 32), 8192.0, A.mult)
        else: act(nd(0, npair + 32), ps(h, 0, npair + 32), scale=8192.0)
        ob = 6 if late else h
        o = ps(ob, 352, 384)
        high = lambda d: box("p%d" % ob, range(352 // c, 384 // c), range(d, c))

        def straight(ds):
            stage("late%d" % h)
            for d in ds:
                x, a = sizes[d - 1], 256 + 8 * sum(sizes[:d - 1])
                tt(v(eq, a, a + 8 * x), far(0, c - d, 1, 9), own(d, c), A.is_equal)
                for k in range(8): mm(high(d), Id(9), v(eq, a + k, a + 8 * x, 8), False, d == late and k == 7, k == 0)
            stage("lose%d" % h)

        mm(o, Id(0), W("Qn", h), True, False)
        if OPT["u16"]: mm(o, v("crow", p0=32, p1=33), v("one", 0, 32, p0=32, p1=33), False, False)
        mm(o, Id(3), W("nok", h), False, False)
        if late: straight(range(1, OPT["cut"]))
        for d in range(1, c): mm(high(d), Id(0), nd(sum(sizes[:d - 1]), sum(sizes[:d])), False, False, d == 1 and late)
        mm(o, Id(0), nd(npair, npair + 32), False, not late)
        if late: straight(range(OPT["cut"], late + 1))
        stage("soff%d" % h)
        if OPT["u16"]: return tt(W("soff", h), o, W("SP", h), A.min)
        if OPT["soff"][h] == "c":
            for i in range(c): ts(v("soff", 32 * h + i, 32 * h + 32, c), ps(h, 352 + i, 384, c), col(170 + i), A.min, float(D // 2), A.add)
        else:
            tt(W("wl", h), o, W("SP", h), A.min)
            ts(W("soff", h), W("wl", h), float(D // 2), A.add)

    def winners3(name, h, r0, nr, pair, bank):
        eq, nb, c0 = "eq" + name, 4 * nr, 32 * h + 4 * r0
        SH = lambda s: blk("SH", s % 16, 128)
        stage("win" + name)
        if r0 + nr == 8:
            for k in range(8): act(v("own%d" % h, k, 256, 8), W("XH", h))
            for k in range(9):
                mm(ps(BK["win"][h], k, 512, 16), SH(k), W("Qn", h), True, False)
                mm(ps(BK["win"][h], k, 512, 16), SH(k), W("cab", h, 2), False, True)
        own = lambda r, i: box("own%d" % h, r, i, range(8))
        far = lambda r, i, k: box("p%d" % BK["win"][h], r, i, range(k, k + 8))
        rs = range(r0, r0 + nr)
        sets = [(rs, range(4 - d), rs, range(d, 4)) for d in range(1, 4)]
        if pair: sets += [(rs[::2], range(max(-d, 0), 4 - max(d, 0)), rs[1::2], range(max(d, 0), 4 + min(d, 0))) for d in range(-3, 4)]
        at0 = [sum(len(x[0]) * len(x[1]) for x in sets[:n]) for n in range(len(sets) + 1)]
        npair = at0[-1]
        tt(v(eq, 0, 8 * nb), far(rs, range(4), 1), own(rs, range(4)), A.is_equal)
        for k in range(8): mm(ps(bank, npair, npair + nb), blk("E", k, 128), v(eq, k, 8 * nb, 8), k == 0, k == 7)
        for r in range(2):
            e0 = 8 * (nb + npair * r)
            for n, (rl, il, rh, ih) in enumerate(sets):
                tt(v(eq, e0 + 8 * at0[n], e0 + 8 * at0[n + 1]), far(rh, ih, 0) if r else far(rl, il, 1), own(rl, il) if r else own(rh, ih), A.is_equal)
            for k in range(8): mm(ps(bank, 0, npair), SH(-k * r), v(eq, e0 + k, e0 + 8 * npair, 8), r == 0 and k == 0, r == 1 and k == 7)
        stage("lose" + name)
        nd = lambda a, b: v("nd", 144 * int(name) + a, 144 * int(name) + b)
        ts(nd(0, npair + nb), ps(bank, 0, npair + nb), 8192.0, A.mult)
        o = ps(bank, 352, 352 + nb)
        mm(o, Id(0), v("Qn", c0, c0 + nb), True, False)
        mm(o, Id(3), v("nok", c0, c0 + nb), False, False)
        for n, (rl, il, rh, ih) in enumerate(sets):
            mm(box("p%d" % bank, range(88 + rh.start - r0, 88 + rh.stop - r0, rh.step), ih), Id(0), nd(at0[n], at0[n + 1]), False, False)
        mm(o, Id(0), nd(npair, npair + nb), False, True)
        if name in OPT["soff"]:
            for i in range(4): ts(v("soff", c0 + i, c0 + nb, 4), ps(bank, 352 + i, 352 + nb, 4), col(170 + i), A.min, float(D // 2), A.add)
        else:
            tt(v("wl", c0, c0 + nb), o, v("SP", c0, c0 + nb), A.min)
            ts(v("soff", c0, c0 + nb), v("wl", c0, c0 + nb), float(D // 2), A.add)

    def copy(e, out, a, b):
        if e == "S": act(out, a, bias=b)
        else: ts(out, a, b, A.add)

    def back(h=None):
        if h is None:
            for e in range(2):
                mm(ps(2 + e), Id(0), v("X2", e, TH, 2), True, False)
                for a in range(e, 16, 2):
                    mm(ps(2 + e, a // 2, 512, 8), blk("L", a, 128), v("P1"), False, False)
                    mm(ps(2 + e, a // 2, 512, 8), blk("L", a, 128), blk("cab", 1, 64), False, a >= 14)
            for x in (1, 0):
                for e in range(2): copy(OPT["bcopy"][2 * x + e], R("Bb", x, e, 2), part(ps(2 + e), x, 2), -BIG - D // 2)
            return
        b = BK["back"][h]
        if not h: mm(ps(b), Id(0), R("X2", h), True, False)
        for a in range(16): mm(ps(b, a, 512, 16), blk("L", a, 128), W("P1", h), h and a == 0, False)
        mm(ps(b), Id(8), R("Cg1", h), False, True, True)
        for e in range(2):
            if h: tt(part(R("Bb", h), e, 2), part(ps(b), e, 2), part(R("X2", h), e, 2), A.add)
            else: act(part(R("Bb", h), e, 2), part(ps(b), e, 2))

    def new_key(t):
        tt(v("pk"), v("nok"), blk("cab", 2, 64), A.subtract)
        for e in range(2):
            mm(ps(4 + e), v("PI", 128 * t, 128 * t + 128, p1=1), v("one", p1=1), True, False)
            for a in range(e, 16, 2):
                l = v("Z", 160 * a + 16 + a - t, 160 * a + 144 + a - t)
                mm(ps(4 + e, a // 2, 512, 8), l, v("Qn"), False, False)
                mm(ps(4 + e, a // 2, 512, 8), l, v("pk"), False, a >= 14)

    def stack(name, n, bank, c0, order):
        for b in order: mm(ps(bank, 0, n), v("HX", 8 - b, 136 - b), blk(name, b, n), b == order[0], b == order[7])
        for i in range(n // 128): act(v("hi", c0 + 128 * i, c0 + 128 * i + 128), part(ps(bank, 0, n), i, n // 128), bias=160.0 - 8.5 / 16, scale=0.0625)

    masks(0)
    tables()
    for t in range(RO):
        for m in range(3):
            for h in (1, 0):
                stage("hop%d%d" % (m, h), t)
                gather(m, h)
                turn(t, m, h)
            stage("check%d" % m)
            if m < 2 or not OPT["split"]: check(m)
            for h in (1, 0) if m == 0 else ():
                stage("moved%d" % h)
                moved(t, h, True)
                for q in range(2): act(part(v("XW", KW + 512 * h, KW + 512 * h + 512), q, 2), part(ps(2), q, 2), bias=col(95 if t else 168))
                twin(h)
            for h in OPT["back"] if m == 1 else ():
                stage("back%s" % h)
                back(h)
        for h in (1, 0):
            stage("old%d" % h)
            gather(3, h)
        for h in (1, 0) if OPT["split"] else ():
            stage("check2%d" % h)
            check(2, h)
            leave(t, h)
        if not OPT["split"]: leave(t)
        for h in (1, 0): winners(h)
        for h in (1, 0):
            stage("leave%d" % h)
            send(t, h)
        for h in (1, 0):
            stage("column%d" % h)
            column(t, h)
        stage("row")
        new_key(t)
        for name, h, r0, nr, pair, bank in PIECES:
            c = 4 + 4 * pair
            for b in range(32 * h + 4 * (r0 + nr) - c, 32 * h + 4 * r0 - 1, -c):
                so, of = v("soff", b, b + c), lambda x: v(x, 16 * b, 16 * (b + c))
                stage("run" + name)
                tt(at(v("K"), so), of("Ab"), of("Bb"), A.max)
                stage("xrun" + name)
                act(at(v("XW", 0, KW), so), of("NC"), F.Silu)
        for h in (1, 0):
            stage("min%d" % h)
            for i in range(4): tt(R("K", h, i, 4), R("K", h, i, 4), ps(4 + i % 2, 256 * h + i // 2, 256 * h + 256, 2), A.min)
        if t < RO - 1: masks(t + 1)

    stage("zout")
    stack("s4", 128, 7, 512, range(8))
    for h in (1, 0):
        mm(ps(2 + h), blk("II", 1, 128), R("s4", h), True, False)
        for b in range(4): mm(part(ps(2 + h), b, 4), blk("HR", 4 * h + b, 128), v("hi", 512, 640), False, b == 3)
        for b in range(2): act(part(R("oz", h), b, 2), part(ps(2 + h), b, 2), bias=col(131))
    dma("Y", T.yz[:], v("oz"))
    stage("ksum")
    top = 16 - OPT["npe"]
    cp(ps(0, 256, 512), blk("K", top - 1, 256))
    for b in range(top - 2, -1, -1): tt(ps(0, 256, 512) if b else blk("okk", 0, 256), blk("K", b, 256), ps(0, 256, 512), A.add)
    stage("mirror")
    for b in (3, 2, 1, 0):
        ts(blk("Hk", b, 256), blk("K", b, 256), 1.0 / D, A.mult, HB - 0.5 + 0.5 / D, A.add)
        ts(blk("Hn", b, 256), blk("Hk", b, 256), 1.0 - HB, A.add, 0.0, A.min)
    for b in range(top, 16): mm(ps(1, 0, 256), v("IF"), blk("K", b, 256), b == top, False)
    for b in (3, 2, 1, 0): mm(ps(1, 0, 256), Id(5), blk("Hn", b, 256), False, b == 0)
    stage("ksum")
    tt(blk("okk", 1, 256), blk("okk", 0, 256), ps(1, 0, 256), A.add)
    dma("Y", T.yk[:], blk("okk", 1, 256))
    stage("rows")
    for k in range(2):
        add("Y", lambda k=k: g.sync.dma_start(ap(v("r%d" % k)), T.XW[k:128:16, 0:D]), v("r%d" % k), [v("XW", 0, D)], "dma", 50.0, NOM["dma"] + 128 * 1024 / NOM["rate"])
    tile = lambda e, out, a, x, y: act(out, a, bias=y, scale=x) if e == "S" else ts(out, a, x, A.mult, y, A.add)
    tile(OPT["tile"][0], v("d1"), v("r1"), 0.0625, 158.0 - 7.5 / 16)
    tile(OPT["tile"][1], v("d0"), v("r0"), 1.0 / 32, -1.0)
    dma("G", T.yc[:], v("d0"))
    stage("xsum")
    for b in range(8): act(blk("xb", b, 512), blk("XW", b, 512), bias=col(90))
    for a in range(16):
        mm(ps(2, 0, 256), blk("II", 1, 128), blk("xb", a, 256), a == 0, a == 15)
        if a == 13: mm(ps(2, 0, 256), blk("HR", 9, 128), v("d1"), False, False, True)
    act(v("ox"), ps(2, 0, 256), bias=col(147))
    dma("Y", T.yx[:], v("ox"))
    emit(g, T, ops)
    g.wait_ge(T.sem.sent, 4 * n_out * (RO - 1))
